import numpy as np, ml_dtypes
CORES = [1,5,17,21,33,37,49,53]
N = 8
import mx_ref
BF = ml_dtypes.bfloat16
def gcols(t, e):
    v = np.concatenate([t.reshape(8, 16, -1, 4), np.zeros((8, 16, 1, 4), BF)], axis=2)
    return np.ascontiguousarray(np.stack([v[g][:, e[g]] for g in range(8)])).reshape(128, -1)
def tile(rs):
    return np.stack(rs, axis=2).reshape(128, -1).astype(BF)
def pick(q, e):
    c = np.concatenate([q[0].reshape(128, -1, 4), np.zeros((128, 1, 4), np.uint8)], axis=1); s = np.concatenate([q[1], np.ones((16, 1), np.uint8)], axis=1)
    return (np.ascontiguousarray(c[:, e].reshape(128, -1)), np.ascontiguousarray(s[:, e]))
def join(*qs):
    return (np.concatenate([q[0] for q in qs], axis=1), np.concatenate([q[1] for q in qs], axis=1))
def put(q, e, v):
    c, s = q[0].reshape(128, -1, 4).copy(), q[1].copy(); c[:, e] = v[0].reshape(128, -1, 4); s[:, e] = v[1]
    return (c.reshape(128, -1), s)
def pk(c, s):
    return (np.ascontiguousarray(c), mx_ref.live(s))
def emit(q):
    return q[0], q[1]
def packed(v, rng):
    q = [mx_ref.quantize(np.ascontiguousarray(v[r])) for r in range(N)]
    return np.stack([a for a, b in q]), np.stack([mx_ref.plane(b, rng) for a, b in q])
def values_of_codes():
    e, c = np.zeros((128, 128, 4), np.float32), np.zeros((128, 2, 4), np.uint8)
    e[np.arange(128), np.arange(128), 0] = 1
    c[:127, :, 0] = np.arange(256).reshape(2, 128).T[:127]
    return mx_ref.matmul(mx_ref.quantize(e.reshape(128, 512).astype(BF)), (c.reshape(128, 8), np.full((16, 2), 127, np.uint8))).T.reshape(-1).astype(np.float64)
CODE_VALUE, SCALE_VALUE = values_of_codes(), 2.0 ** (np.arange(256) - 127.0)
def decode(q):
    return (CODE_VALUE[q[0]].reshape(16, 8, -1, 4) * SCALE_VALUE[q[1]][:, None, :, None] + 0.0).reshape(128, -1).astype(np.float32)
def f(rng, *shape):
    return mx_ref.flush((rng.standard_normal(shape, dtype=np.float32) * np.exp2(rng.integers(-2, 3, shape[:-1] + (1,)))).astype(BF))
def wide(rng, *shape, cols=0):
    v = rng.standard_normal(shape, dtype=np.float32) * np.exp2(rng.integers(-12, 13, shape)).astype(np.float32)
    if cols: v *= np.repeat(np.exp2(rng.integers(-cols, cols + 1, shape[:-2] + (1, shape[-1] // 4))) * (rng.random(shape[:-2] + (1, shape[-1] // 4)) > 0.0625), 4, axis=-1).astype(np.float32)
    return mx_ref.flush(v.astype(BF))
C, K, DEP, R = 256, 128, 32, 3
SOURCE = [7, 0, 1, 1, 2, 2, 3, 3]
LEVEL = [0, 1, 2, 2, 3, 3, 3, 3]
ITEM = 8 * (np.arange(C) % DEP) + np.arange(C) // DEP
def big(v):
    v = v.astype(np.float32)
    v[np.abs(v) < np.float32(2.0 ** -16)] = 0
    return v.astype(BF)
def numbers_of(rng):
    return {"x": big(f(rng, N, 128, 4 * C)), "u": np.array(f(rng, N, 128, 512)), "v": np.array(f(rng, N, 128, 512))}
def layers(rng):
    return big(f(rng, N, 128, 2048).astype(np.float32) * np.float32(0.5)).reshape(N, 8, 16, 4, 8, 16, 4)
def weights(rng, w):
    c, p = packed(np.ascontiguousarray(w).reshape(N, 128, 2048), rng)
    return {"wc": c, "ws": p}
def own_bits(u):
    for b in range(3): u[:, :, b::16] = 0
    for h in range(0, 128, 16):
        for b in range(3): u[:, h, h + b, b] = 1
def setup_inputs(rng):
    return {**numbers_of(rng), **weights(rng, layers(rng))}
def setup_inputs_ties(rng):
    d = numbers_of(rng)
    e = rng.permutation(N)
    k = rng.integers(-1, 2, (N, 8, C, 3)).astype(np.float32)
    k[e[0]] = 0
    k[e[1]] = 1
    for g in range(8): k[e[2], g, :, 0] = 2.0 * (LEVEL[g] % 2) - 1.0
    x = d["x"].reshape(N, 8, 16, C, 4)
    x[:, :, :8] = 0
    x[:, :, 0, :, :3] = k.astype(BF)
    u = d["u"].reshape(N, 128, 128, 4)
    own_bits(u)
    w = layers(rng)
    w[:, :, :, :, :, :8] = 0
    return {"x": x.reshape(N, 128, 4 * C), "u": u.reshape(N, 128, 512), "v": d["v"], **weights(rng, w)}
def setup_inputs_near(rng):
    d = numbers_of(rng)
    x = d["x"].reshape(N, 8, 16, C, 4)
    u = d["u"].reshape(N, 128, 128, 4)
    o = rng.permutation(N) % 4
    x[:, :, :8] = 0
    for b in range(3): u[:, :, b::16] = 0
    for r in range(N):
        a = rng.integers(-1, 2, (8, C, 3)).astype(np.float32)
        b = np.where(rng.random((8, C, 3)) < 0.75, -a, rng.integers(-1, 2, (8, C, 3))).astype(np.float32)
        k = np.float32(2.0 ** -27 if o[r] < 2 else 1.0)
        a, b = a * k, b * k
        for g in rng.permutation(8)[:4]: a[g, rng.integers(C)] = 2.0 ** 18 * rng.choice([-1.0, 1.0], 3)
        x[r, :, 0, :, :3] = a.astype(BF)
        x[r, :, 1, :, :3] = b.astype(BF)
        m = 2.0 ** -30 if o[r] % 2 == 0 else 1.0
        for h in range(0, 128, 16):
            for t in range(3):
                u[r, h, h + t, t] = 1.125 * m
                u[r, h + 1, h + t, t] = m
    w = layers(rng)
    w[:, :, :8] = 0
    w[:, :, :, :, :, :8] = 0
    return {"x": x.reshape(N, 128, 4 * C), "u": u.reshape(N, 128, 512), "v": d["v"], **weights(rng, w)}
def setup_inputs_late(rng):
    d = numbers_of(rng)
    s = rng.integers(6, 8, (N, 8, 8, DEP))
    for g in range(8):
        if g: s[:, g, :, 0] = LEVEL[g] - 1
        s[:, g, :, -1] = LEVEL[g]
    s[:, 7, 7] = 0
    s[:, 7, 7, -1] = 2
    e = int(rng.integers(N))
    s[e] = 7
    for g in range(8):
        if LEVEL[g] > 0: s[e, g, :, 0] = 7 - LEVEL[g]
        if LEVEL[g] < 3: s[e, g, :, -1] = 6 - LEVEL[g]
    s[e, 2:4, :7, -1] = 2
    for h in (0, 1, 6, 7):
        s[e, 4:, h, 0] = 2
        s[e, 4:, h, 1] = 3
    s[e, 4:, 5, 1] = 6
    s = s.reshape(N, 8, C)
    x = d["x"].reshape(N, 8, 16, C, 4)
    x[:, :, :8] = 0
    x[:, :, 0, :, :3] = (2.0 * ((s[..., None] >> np.array([2, 1, 0])) & 1) - 1.0).astype(np.float32).astype(BF)
    k = (1.0 + (2 * rng.integers(0, 64, (N, 8, 8, C, 4)) + 1) / 128.0) * np.exp2(-1.0 * rng.integers(8, 15, (N, 8, 8, C, 4))) * rng.choice([-1.0, 1.0], (N, 8, 8, C, 4))
    k[:, :, 0, :, 0] = 1.96875
    x[:, :, 8:] = k.astype(np.float32).astype(BF)
    u = d["u"].reshape(N, 128, 128, 4)
    own_bits(u)
    w = layers(rng)
    w[:, :, :, :, :, :8] = 0
    return {"x": x.reshape(N, 128, 4 * C), "u": u.reshape(N, 128, 512), "v": d["v"], **weights(rng, w)}
def setup_inputs_ends(rng):
    o = rng.permutation(N)
    x = rng.choice([-1.0, 1.0], (N, 8, 1, C, 1)) * np.ones((1, 1, 16, 1, 4))
    u, v = rng.choice([-1.0, 1.0], (N, 128, 512)), rng.choice([-1.0, 1.0], (N, 128, 512))
    w = np.zeros((N, 128, 2048), np.float32)
    for r in range(N):
        if o[r] == 0: x[r] = 1.0
        if o[r] == 3: x[r] = -1.0
        if o[r] in (0, 3): u[r] = 1.0
        x[r] *= 2.0 ** 19 if o[r] % 2 == 0 else 2.0 ** -27
        u[r] *= 2.0 ** 30 if o[r] % 4 < 2 else 2.0 ** -30
        v[r] *= 2.0 ** 30 if o[r] % 4 in (0, 3) else 2.0 ** -30
        w[r] = (2.0, -2.0, 0.0)[o[r] % 3]
    return {"x": x.astype(np.float32).reshape(N, 128, 4 * C).astype(BF), "u": u.astype(np.float32).astype(BF), "v": v.astype(np.float32).astype(BF), **weights(rng, w.astype(BF))}
def setup_inputs_spread(rng):
    d = setup_inputs(rng)
    d["x"] = big(wide(rng, N, 128, 4 * C, cols=3))
    return d
def check_inputs(d):
    b = []
    for k, m in (("x", 2.0 ** 19), ("u", 2.0 ** 30), ("v", 2.0 ** 30)):
        a = np.abs(d[k].astype(np.float32))
        if not (np.isfinite(a).all() and ((a == 0) | (a >= 2.0 ** -30) & (a <= m)).all()): b.append("a value of " + k)
    none, least, most = [emit(mx_ref.quantize(np.full((128, 16), k, np.float32).astype(BF)))[1][0, 0] for k in (0.0, 2.0 ** -30, 2.0 ** 30)]
    for r in range(N):
        if ((d["wc"][r] == 0x7F) | (d["wc"][r] == 0xFF)).any(): b.append("wc: a code that is no number")
        s = mx_ref.live(d["ws"][r])
        if ((s != none) & ((s < least) | (s > most))).any(): b.append("ws: a scale out of range")
        a = np.abs(decode(pk(d["wc"][r], d["ws"][r])).astype(np.float64)).reshape(128, 512, 4)
        if not (np.sum(a, axis=(0, 2)) <= 1024).all(): b.append("W: a column that adds up to more than 1024")
    return b
def times(sym, wait):
    sym, wait = sym.reshape(8, DEP), wait.reshape(8, DEP)
    t, last = np.zeros((8, DEP), np.int64), np.zeros(8, np.int64)
    for i in range(DEP):
        last = np.maximum(last, wait[:, i]) + (1 + sym[:, i])
        t[:, i] = last
    return t.reshape(C)
def orders(sym):
    o, b = np.zeros((8, C), np.int64), np.zeros((8, K), np.int64)
    first, least = np.full((8, 8), -1), np.zeros((8, 8), np.int64)
    for g in range(8):
        e = SOURCE[g]
        t = times(sym[g], least[e][sym[g]] if g > 0 else np.zeros(C, np.int64))
        o[g] = np.argsort(t, kind="stable")
        for s in range(8):
            p = np.flatnonzero(sym[g][o[g]] == s)
            if len(p) > 0:
                first[g, s] = o[g, p[0]]
                least[g, s] = t[o[g, p[0]]]
        l = o[g, :K]
        p = first[e][sym[g][l]] if g > 0 else l
        b[g] = np.where(p < 0, l, p)
    return o, b
def reference(x, u, v, wc, ws):
    qu = [mx_ref.quantize(u[r]) for r in range(N)]
    lay = [pk(wc[r], ws[r]) for r in range(N)]
    now = [x[r] for r in range(N)]
    order = np.zeros((N, 8, C), np.int64)
    for t in range(R):
        stay, sent = [], []
        for r in range(N):
            q = mx_ref.quantize(now[r])
            full = decode(q)
            s = mx_ref.matmul(qu[r], q)
            order[r], mate = orders(4 * (s[::16] > 0) + 2 * (s[1::16] > 0) + (s[2::16] > 0))
            a = full.reshape(8, 16, C, 4)
            z = np.stack([(a[g][:, order[r, g, :K]] + a[SOURCE[g]][:, mate[g]]) * np.float32(0.5) for g in range(8)])
            sent.append(mx_ref.quantize(np.ascontiguousarray(z.reshape(128, 4 * K).astype(BF))))
            stay.append(gcols(full.astype(BF), order[r][:, K:]))
        for r in range(N):
            q = sent[r - 1]
            d = decode(q)
            h = tile([mx_ref.matmul(pick(lay[r], np.arange(128 * b, 128 * b + 128)), q) * np.float32(0.0078125) + d[:, b::4] for b in range(4)])
            items = np.concatenate([stay[r], h], axis=1).reshape(128, C, 4)
            now[r] = np.ascontiguousarray(items[:, ITEM].reshape(128, 4 * C))
    y, op = np.zeros((N, 128, C), np.float32), np.zeros((N, 8, C), np.float32)
    oc, osc = np.zeros((N, 128, 4 * C), np.uint8), np.zeros((N, 16, C), np.uint8)
    for r in range(N):
        q = mx_ref.quantize(now[r])
        y[r] = mx_ref.matmul(mx_ref.quantize(v[r]), q)
        op[r] = order[r]
        oc[r], osc[r] = emit(q)
    return {"y": y, "op": op, "oc": oc, "osc": osc}

@@ -1,0 +1,490 @@
+import math
+from concourse.mybir import dt, AluOpType as A, AxisListType, ActivationFunctionType as AF
+
+NR = 3
+VUNITS = 4
+BIG = 1 << 20
+TMASK = 0x7FF00
+INTS = ["oi", "oj", "ok1", "ni", "nj", "nk", "fi", "pf", "pg", "ri", "rx"]
+FLTS = ["s1", "sn", "inv", "dif", "own", "ph", "pq", "ka", "kb", "ry", "rz", "of", "srf", "kn"]
+
+SCRATCH = {}
+
+
+def _b(name, n, d="float32"):
+    SCRATCH[name] = ("sbuf", [128, n], d)
+
+
+for _n, _k, _d in (
+        ("xs", 1024, "bfloat16"), ("us", 512, "bfloat16"), ("vs", 512, "bfloat16"),
+        ("one", 128, "bfloat16"), ("zer", 528, "bfloat16"), ("dy", 128, "bfloat16"), ("dy0", 128, "bfloat16"), ("dy1", 128, "bfloat16"),
+        ("dya", 128, "bfloat16"), ("dyb", 128, "bfloat16"), ("dyc", 128, "bfloat16"),
+        ("idn", 128, "bfloat16"), ("prm", 128, "bfloat16"),
+        ("cl", 2560, "bfloat16"), ("ce", 528, "bfloat16"), ("cg", 528, "bfloat16"),
+        ("pI", 1, "int32"), ("pi8", 1, "int32"), ("pi4", 1, "int32"), ("pi16", 1, "int32"), ("pih", 1, "int32"),
+        ("mk", 4, "float32"), ("cm", 2, "float32"), ("c8", 2, "float32"), ("cf", 8, "float32"),
+        ("io8", 8, "float32"), ("dT", 16, "float32"), ("pen", 8, "float32"), ("pwf", 8, "float32"), ("pow", 8, "int32"),
+        ("bp", 128, "float32"), ("br", 256, "float32"),
+        ("ti", 256, "int32"), ("tj", 256, "int32"), ("vrow", 256, "bfloat16"), ("vcol", 256, "float32"),
+        ("ol", 16, "uint16"), ("nl", 16, "uint16"),
+        ("sb", 48, "float32"), ("mt", 512, "bfloat16"),
+        ("l0", 8, "uint16"), ("l1", 8, "uint16"), ("l2", 8, "uint16"), ("lr", 16, "uint16"),
+        ("da", 128, "float32"), ("db", 128, "float32"), ("dc", 128, "float32"), ("dr", 256, "float32"),
+        ("wp", 128, "float32"), ("wr", 256, "float32"), ("tp", 128, "float32"), ("mm", 128, "float32"), ("mv", 1, "float32"),
+        ("rep", 32, "float32"), ("trp", 32, "float32"), ("tab0", 16, "int32"), ("tab1", 16, "int32"), ("tabr", 16, "int32"),
+        ("wt", 8, "int32"), ("wtr", 16, "int32"), ("tin", 32, "float32"), ("tout", 32, "float32"),
+        ("fl", 2, "uint16"), ("prs", 8, "float32"), ("prw", 8, "float32"), ("bb", 1, "float32"), ("gl", 16, "uint16"),
+        ("key", 272, "float32"), ("kt", 512, "float32"), ("acc", 16, "float32"), ("acr", 16, "float32"),
+        ("pl", 16, "uint16"), ("rl", 16, "uint16"),
+        ("win", 512, "bfloat16"), ("wtt", 512, "bfloat16"), ("ou", 16, "uint16"), ("opw", 256, "float32"),
+        ("F", 1024, "bfloat16"), ("G", 1088, "bfloat16"), ("Gp", 1024, "bfloat16"), ("gz", 512, "bfloat16"), ("Z", 512, "bfloat16"),
+        ("X", 1024, "bfloat16"), ("hr", 512, "float32"), ("ysb", 256, "float32")):
+    _b(_n, _k, _d)
+_b("js", 256 * (16 - VUNITS), "bfloat16")
+for _k in range(VUNITS):
+    _b("jv%d" % _k, 256, "bfloat16")
+_b("ints", 16 * len(INTS), "int32")
+_b("flts", 16 * len(FLTS), "float32")
+for _n, _k in (("qx", 256), ("qn", 1024), ("qp", 1024), ("qu", 128), ("qv", 128), ("qw", 512), ("qc", 1664), ("qm", 128),
+               ("qz", 128 * NR), ("qa", 128 * NR)):
+    _b(_n, _k, "float8_e4m3fn_x4")
+    _b("s" + _n, _k, "uint8")
+for _k in range(8):
+    SCRATCH["ps%d" % _k] = ("psum", [128, 512], "float32")
+SEMAPHORES = ["cV", "cS", "cT", "cG", "sent"] + ["arr%d" % k for k in range(NR)] + ["ld%d" % k for k in range(16)]
+
+
+def recorder(g, T):
+    eng = {"V": g.vector, "S": g.scalar, "T": g.tensor, "G": g, "Y": g.sync}
+    count = {"V": 0, "S": 0, "T": 0, "G": 0}
+    known = {q: {} for q in eng}
+    writer, readers = {}, {}
+    nd = [0]
+
+    def need(q, toks):
+        todo = {}
+        for (sem, val, own, snap) in toks:
+            if known[q].get(sem, 0) < val and todo.get(sem, (0, None))[0] < val:
+                todo[sem] = (val, snap)
+        for sem in list(todo):
+            if any(s != sem and todo[s][1].get(sem, 0) >= todo[sem][0] for s in todo):
+                continue
+            eng[q].wait_ge(T.sem[sem], todo[sem][0])
+        for sem, (val, snap) in todo.items():
+            for k, v in list(snap.items()) + [(sem, val)]:
+                if known[q].get(k, 0) < v:
+                    known[q][k] = v
+
+    def toks_of(q, reads, writes):
+        t = []
+        for r in reads:
+            if r in writer:
+                t.append(writer[r])
+            if r[:2] == "ps":
+                t += [x for x in readers.get(r, []) if x[2] != q]
+        for w in writes:
+            t += readers.get(w, [])
+            if w in writer and (writer[w][2] != q or readers.get(w)):
+                t.append(writer[w])
+        return t
+
+    def note(tok, reads, writes):
+        for w in writes:
+            writer[w] = tok
+            readers[w] = []
+        for r in reads:
+            if r not in writes:
+                readers.setdefault(r, []).append(tok)
+
+    def emit(q, make, reads, writes, dma=False):
+        need(q, toks_of(q, reads, writes))
+        ins = make()
+        if dma:
+            sem = "ld%d" % nd[0]
+            nd[0] += 1
+            ins.then_inc(T.sem[sem], 16)
+            tok = (sem, 16, "D" + sem, dict(known[q]))
+        else:
+            sem = "c" + q
+            count[q] += 1
+            ins.then_inc(T.sem[sem], 1)
+            tok = (sem, count[q], q, dict(known[q]))
+        note(tok, reads, writes)
+        return tok
+
+    def landed(sem, val, writes):
+        note((sem, val, "R" + sem, {}), [], writes)
+
+    return emit, need, toks_of, landed, count, nd
+
+
+def rank_program(g, core, T, topo):
+    rank = T.rank_of(core)
+    if rank is None:
+        return
+    nxt = T.cores[(rank + 1) % len(T.cores)]
+    prv = T.cores[(rank - 1) % len(T.cores)]
+    emit, need, toks_of, landed, count, nd = recorder(g, T)
+    v, s = g.vector, g.scalar
+
+    def I(n):
+        k = 16 * INTS.index(n)
+        return T.ints[:, k:k + 16]
+
+    def W(n, p0=0, p1=128, a=0, b=16):
+        k = 16 * FLTS.index(n)
+        return T.flts[p0:p1, k + a:k + b]
+
+    place = {"qcl": ("qc", 0), "qcr": ("qc", 384), "qce": ("qc", 640), "qcg": ("qc", 1152)}
+    for k in range(NR + 1):
+        place["qn%d" % k] = ("qn", 256 * k)
+        place["na%d" % k] = ("qn", 256 * k)
+        place["nb%d" % k] = ("qn", 256 * k + 128)
+        place["qp%d" % k] = ("qp", 256 * k)
+        place["qz%d" % k] = ("qz", 128 * k)
+        place["qa%d" % k] = ("qa", 128 * k)
+
+    def K(n, a, b):
+        q, o = place.get(n, (n, 0))
+        return T[q][:, o + a:o + b], T["s" + q][:, o + a:o + b]
+
+    def pt(n):
+        return n if isinstance(n, (list, tuple)) else [n]
+
+    def TS(o, ok, i, ik, s1, s2, o0, o1=None):
+        if o1 is None:
+            return emit("V", lambda: v.tensor_scalar(o, i, s1, None, o0), pt(ik), pt(ok))
+        return emit("V", lambda: v.tensor_scalar(o, i, s1, s2, o0, o1), pt(ik), pt(ok))
+
+    def TT(o, ok, a, b, ik, op):
+        return emit("V", lambda: v.tensor_tensor(o, a, b, op), pt(ik), pt(ok))
+
+    def CP(o, ok, i, ik):
+        return emit("V", lambda: v.tensor_copy(o, i), pt(ik), pt(ok))
+
+    def ACT(o, ok, i, ik, f=AF.Copy, **kw):
+        return emit("S", lambda: s.activation(o, i, f, **kw), pt(ik), pt(ok))
+
+    def TR(o, ok, i, ik):
+        return emit("V", lambda: v.transpose(o, i), pt(ik), pt(ok))
+
+    def RED(o, ok, i, ik, op):
+        return emit("V", lambda: v.tensor_reduce(o, i, AxisListType.X, op), pt(ik), pt(ok))
+
+    def FILL(ap, ok, c):
+        return emit("V", lambda: v.memset(ap, c), [], pt(ok))
+
+    def QT(q, a, b, i, ik):
+        return emit("V", lambda: v.quantize_mx(*K(q, a, b), i), pt(ik), [q, "s" + q])
+
+    def MM(bank, n, w, wa, m, ma):
+        (wt, ws), (mt, ms) = K(w, wa, wa + 128), K(m, ma, ma + n)
+        o = T["ps%d" % bank][:, 0:n]
+        return emit("T", lambda: g.tensor.matmul_mx(o, wt, ws, mt, ms, True, True), [w, "s" + w, m, "s" + m], ["ps%d" % bank])
+
+    def PICK(o, i, lst, lk, ok, ik):
+        (oc, osc), (ic, isc) = K(o, 0, 256), K(i, 0, 256)
+        emit("V", lambda: v.tensor_copy(oc.bitcast(dt.uint32), ic.bitcast(dt.uint32).indirect(lst)), ik + [lk], ok)
+        emit("S", lambda: s.activation(osc, isc.indirect(lst), AF.Copy), ["s" + k for k in ik] + [lk], ["s" + k for k in ok])
+
+    def IOTA(ap, ok, pat, base, cm, f=True):
+        if f:
+            return emit("G", lambda: g.iota(ap, pat, base, cm, allow_small_or_imprecise_dtypes=True), [], pt(ok))
+        return emit("G", lambda: g.iota(ap, pat, base, cm), [], pt(ok))
+
+    def AFF(o, ok, i, ik, pat, op, base, cm):
+        return emit("G", lambda: g.affine_select(o, i, pat, op, 0.0, base, cm), pt(ik), pt(ok))
+
+    emit("Y", lambda: g.sync.dma_start(T.xs[:], T.x[:]), [], ["xs"], dma=True)
+    emit("S", lambda: s.dma_start(T.us[:], T.u[:]), [], ["us"], dma=True)
+    emit("Y", lambda: g.sync.dma_start(T.qw[:, 0:512].bitcast(dt.uint8), T.wc[:, 0:2048]), [], ["qw"], dma=True)
+    emit("Y", lambda: g.sync.dma_start(T.sqw[:, 0:512], T.ws[:, 0:512]), [], ["sqw"], dma=True)
+    emit("Y", lambda: g.sync.dma_start(T.vs[:], T.v[:]), [], ["vs"], dma=True)
+
+    FILL(T.one[:], "one", 1.0)
+    IOTA(T.pI[:], "pI", [[0, 1]], 0, 1, False)
+    IOTA(T.io8[:], "io8", [[1, 8]], 0, 0)
+    IOTA(I("ni"), "ni", [[16, 16]], 0, 1, False)
+    AFF(T.dyb[:], "dyb", T.one[:], "one", [[0, 8], [-8, 16]], A.is_ge, 0, 1)
+    AFF(T.dy0[:], "dy0", T.dyb[:], "dyb", [[0, 8], [8, 16]], A.is_ge, 3, -1)
+    AFF(T.dyc[:], "dyc", T.one[:], "one", [[0, 8], [-8, 16]], A.is_ge, -4, 1)
+    AFF(T.dy1[:], "dy1", T.dyc[:], "dyc", [[0, 8], [8, 16]], A.is_ge, 7, -1)
+    AFF(T.dya[:], "dya", T.one[:], "one", [[0, 4], [-4, 2], [-8, 16]], A.is_ge, 0, 1)
+    AFF(T.dy[:], "dy", T.dya[:], "dya", [[0, 4], [4, 2], [8, 16]], A.is_ge, 3, -1)
+    IOTA(T.bp[:], "bp0", [[1, 128]], -1, 0)
+    AFF(T.idn[:], "idn", T.one[:], "one", [[-1, 128]], A.is_equal, 0, 1)
+    AFF(T.prm[:], "prm0", T.one[:], "one", [[-16, 4], [0, 2], [-1, 16]], A.is_equal, 0, 1)
+    AFF(T.prm[:, 0:16], "prm", T.one[:, 0:16], ["one", "prm0"], [[-1, 16]], A.is_equal, -112, 1)
+    IOTA(T.br[:], "br", [[1, 256]], -1, 0)
+    IOTA(T.ti[:], "ti", [[16, 2], [32, 8], [1, 16]], 0, 0, False)
+
+    FILL(T.zer[:], "zer", 0.0)
+    ACT(T.cl[:, 1536:2048], "cl0S", T.zer[:, 0:512], "zer")
+    ACT(T.cl[:, 2048:2560], "cl0S", T.zer[:, 0:512], "zer")
+    ACT(T.mt[:], "mt0", T.zer[:, 0:512], "zer")
+    ACT(T.pwf[:], "pwf", T.io8[:], "io8", AF.Exp, scale=math.log(2.0))
+    FILL(T.cl[:, 0:1536], "cl0", 0.0)
+    TS(T.pi16[:], "pi16", T.pI[:], "pI", 15, None, A.bitwise_and)
+    TS(T.pi8[:], "pi8", T.pI[:], "pI", 7, None, A.bitwise_and)
+    TS(T.pi4[:], "pi4", T.pI[:], "pI", 3, None, A.bitwise_and)
+    TS(T.pih[:], "pih", T.pI[:], "pI", 4, 1, A.arith_shift_right, A.bitwise_and)
+    TS(T.cf[:, 5:6], "cf5", T.pI[:], "pI", 1.0, None, A.mult)
+    TS(T.cf[:, 4:5], "cf4", T.pi16[:], "pi16", 1.0, None, A.mult)
+    TT(T.cf[:, 3:4], "cf3", T.cf[:, 4:5], T.cf[:, 5:6], ["cf4", "cf5"], A.subtract)
+    TS(I("nj"), "nj", I("ni"), ["ni", "cf3"], T.cf[:, 3:4], None, A.add)
+    TS(I("nk"), "nk", I("nj"), "nj", 7, None, A.bitwise_and)
+    TS(I("ok1"), "ok1", I("nj"), "nj", 3, None, A.arith_shift_right)
+    TS(I("oi"), "oi", I("nk"), "nk", 32.0, None, A.mult)
+    TT(I("nk"), "nk", I("oi"), I("ok1"), ["oi", "ok1"], A.add)
+    CP(T.nl[:], "nl", I("nk"), "nk")
+    for h in range(4):
+        TS(T.mk[:, h:h + 1], "mk", T.pi4[:], "pi4", float(h), None, A.is_equal)
+    TS(T.c8[:, 0:1], "c80", T.pI[:], "pI", 16.0, 8.0, A.is_lt, A.mult)
+    TS(T.c8[:, 1:2], "c81", T.pI[:], "pI", 16.0, -10.0, A.is_lt, A.mult)
+    for y, nm in ((0, "dy0"), (1, "dy1")):
+        for G in range(8):
+            o = 1536 + 512 * y + 64 * G + G % 4
+            ACT(T.cl[:, o:o + 61:4], "clS", T[nm][:, 16 * G:16 * G + 16], [nm, "cl0S"])
+
+    QT("qx", 0, 256, T.xs[:], "xs")
+    QT("qu", 0, 128, T.us[:], "us")
+    PICK("qn0", "qx", T.nl[:, 0:16], "nl", ["na0", "nb0"], ["qx"])
+    ACT(T.cg[:], "cg0", T.zer[:], "zer")
+    ACT(T.ce[:], "ce0", T.zer[:], "zer")
+    ACT(T.win[:], "win", T.zer[:, 0:512], "zer")
+    CP(T.cl[:, 0:512:4], "clV", T.dy[:], ["dy", "cl0"])
+    CP(T.cl[:, 513:1024:4], "clV", T.dy[:], "dy")
+    for k in range(4):
+        o = 1024 + 128 * k + 2 + k % 2
+        CP(T.cl[:, o:o + 125:4], "clV", T.dy[:, 32 * k:32 * k + 32], "dy")
+    QT("qcl", 0, 384, T.cl[:, 0:1536], "clV")
+    QT("qcr", 0, 256, T.cl[:, 1536:2560], "clS")
+
+    def path_constants():
+        TS(T.dT[:, 0:8], "dT", T.io8[:], "io8", 256.0, 257.0, A.mult, A.add)
+        TS(T.dT[:, 8:16], "dT", T.io8[:], "io8", 256.0, 257.0, A.mult, A.add)
+        TS(T.cf[:, 2:3], "cf2", T.pi8[:], "pi8", 1.0, None, A.mult)
+        TS(T.pen[:], "pen", T.io8[:], ["io8", "cf2"], T.cf[:, 2:3], float(BIG), A.not_equal, A.mult)
+        TS(T.cf[:, 1:2], "cf1", T.pih[:], "pih", 128.0, None, A.mult)
+        TS(T.bp[:], "bp", T.bp[:], ["bp0", "cf1"], T.cf[:, 1:2], None, A.add)
+        emit("V", lambda: v.memset(T.wtr[:], 0), [], ["wtr"])
+        CP(T.pow[:], "pow", T.pwf[:], "pwf")
+
+    def key_constants():
+        TS(T.cm[:, 0:1], "cm", T.pih[:], "pih", 0.0, -1.0, A.is_equal, A.mult)
+        TS(T.cm[:, 1:2], "cm", T.pih[:], "pih", -1.0, None, A.mult)
+        TS(W("own"), "own", I("nj"), "nj", 16.0, None, A.add)
+
+    def order_constants():
+        TS(T.cf[:, 0:1], "cf0", T.pih[:], "pih", 16.0, 255.0, A.mult, A.add)
+        TS(T.cf[:, 6:7], "cf6", T.pih[:], "pih", 16.0, None, A.mult)
+        TS(T.tj[:], "tj", T.ti[:], ["ti", "cf6"], T.cf[:, 6:7], None, A.add)
+        TS(T.ti[:], "ti", T.tj[:], "tj", 255, None, A.bitwise_and)
+        CP(T.vrow[:], "vrow", T.ti[:], "ti")
+
+    def column_constants():
+        CP(T.vcol[:], "vcol", T.ti[:], "ti")
+        TS(I("oi"), "oi", I("nj"), "nj", 31, None, A.bitwise_and)
+        TS(I("oj"), "oj", I("nj"), "nj", 5, None, A.arith_shift_right)
+        TS(I("ok1"), "ok1", I("oi"), "oi", 8.0, None, A.mult)
+        TT(I("oi"), "oi", I("ok1"), I("oj"), ["ok1", "oj"], A.add)
+        CP(T.ol[:], "ol", I("oi"), "oi")
+        QT("qv", 0, 128, T.vs[:], "vs")
+
+    rid, pid, _ = topo.addr(nxt)
+    mask = topo.mask(core, nxt)
+    n_out, n_in = 2 * len(topo.engines(core, nxt)), 2 * len(topo.engines(prv, core))
+
+    def symbols(k, hf):
+        q = ("na%d", "nb%d")[hf] % k
+        if k:
+            QT(q, 0, 128, T.X[:, 512 * hf:512 * hf + 512], [["X0", "XS0"], ["X1"]][hf])
+        if k == NR:
+            MM(hf, 128, "qv", 0, q, 0)
+            return
+        MM(hf, 128, q, 0, "qu", 0)
+        a, b = 8 * hf, 8 * hf + 8
+        for i in range(3):
+            TS(T.sb[:, 16 * i + a:16 * i + b], "sb%d" % hf, T["ps%d" % hf][:, i:128:16], "ps%d" % hf, 0.0, float(4 >> i), A.is_gt, A.mult)
+        TT(W("s1", 0, 128, a, b), "s1%d" % hf, T.sb[:, a:b], T.sb[:, 16 + a:16 + b], "sb%d" % hf, A.add)
+        TT(W("sn", 0, 128, a, b), "sn%d" % hf, W("s1", 0, 128, a, b), T.sb[:, 32 + a:32 + b], ["s1%d" % hf, "sb%d" % hf], A.add)
+        for h in range(4):
+            o, sn = T.mt[:, 16 * h + a:16 * h + b], W("sn", 0, 128, a, b)
+            if h < 2:
+                TS(o, "mt%dv" % hf, sn, ["sn%d" % hf, "mk", "mt0"], T.mk[:, h:h + 1], None, A.mult)
+            else:
+                ACT(o, "mt%ds" % hf, sn, ["sn%d" % hf, "mk", "mt0"], scale=T.mk[:, h:h + 1])
+
+    def y_columns(hf):
+        for h in range(8):
+            CP(T.ysb[:, 32 * h + 16 * hf:32 * h + 16 * hf + 16], "ysb", T["ps%d" % hf][:, h:128:8], "ps%d" % hf)
+
+    def level(w, d, lst):
+        for h in range(4):
+            a = slice(32 * h, 32 * h + 32)
+            emit("V", lambda: v.tensor_tensor_scan(T.tp[:, a], T[w][:, a], T[d][:, a], -1.0, A.max, A.add), [w, d], ["tp"])
+        TT(T.mm[:], "mm", T.pen[:].indirect(T[lst][:, 0:8]), T.tp[:], ["pen", lst, "tp"], A.max)
+        RED(T.mv[:], "mv", T.mm[:], "mm", A.min)
+        TS(T.rep[:], "rep", T.zer[:, 0:32], ["zer", "mv"], T.mv[:, 0:1], None, A.add)
+        TR(T.trp[:], "trp", T.rep[:], "rep")
+
+    def waits(k, lst):
+        tab = "tab%d" % k
+        TT(T[tab][:], tab, T.trp[:, 0:16], T.trp[:, 16:32], "trp", A.min)
+        TS(T.wt[:], "wt", T[tab][:, 0:8], tab, TMASK, None, A.bitwise_and)
+        CP(T.tabr[32 * k:32 * k + 32, :], "tabr%d" % k, T[tab][32 * k:32 * k + 32, :], tab)
+        TT(T.wp[:], "wp", T.wt[:].indirect(T[lst][:, 0:8]), T.bp[:], ["wt", lst, "bp"], A.add)
+
+    for r in range(NR):
+        last = r == NR - 1
+        if r == 0:
+            symbols(0, 0)
+        symbols(r, 1)
+        QT("qm", 0, 128, T.mt[:], ["mt0v", "mt0s", "mt1v", "mt1s"])
+        for k in range(3):
+            MM(2 + k, 128, "qcl", 128 * k, "qm", 0)
+        for k in range(2):
+            MM(5 + k, 128, "qcr", 128 * k, "qm", 0)
+        if r == 0:
+            path_constants()
+            fq = "qx"
+            ACT(T.cg[:, 3:512:4], "cg", T.prm[:], ["prm", "cg0"])
+            ACT(T.ce[:, 3:512:4], "ce", T.idn[:], ["idn", "ce0"])
+        else:
+            fq = "qp%d" % r
+            PICK(fq, "qn%d" % r, T.ol[:, 0:16], "ol", [fq], ["na%d" % r, "nb%d" % r])
+        CP(T.l0[:], "l0", T.ps2[:, 0:16:2], "ps2")
+        CP(T.da[:], "da", T.dT[:, 0:8].indirect(T.l0[:, 0:8]), ["dT", "l0"])
+        CP(T.l1[:], "l1", T.ps3[:, 0:16:2], "ps3")
+        ACT(T.db[:], "db", T.dT[:, 0:8].indirect(T.l1[:, 0:8]), ["dT", "l1"])
+        for y in range(2):
+            for hf in range(2):
+                ACT(W("srf", 64 * hf, 64 * hf + 64, 8 * y, 8 * y + 8), "srf", T["ps%d" % (5 + y)][64 * hf:64 * hf + 64, hf:16:2], ["ps%d" % (5 + y), "c80"],
+                    AF.Identity, bias=T.c8[64 * hf:64 * hf + 64, 0:1])
+        level("bp", "da", "l0")
+        waits(0, "l1")
+        CP(T.l2[:], "l2", T.ps4[:, 0:16:2], "ps4")
+        ACT(T.dc[:], "dc", T.dT[:, 0:8].indirect(T.l2[:, 0:8]), ["dT", "l2"])
+        CP(T.lr[:], "lr", W("srf"), "srf")
+        ACT(T.dr[:], "dr", T.dT[:].indirect(T.lr[:, 0:16]), ["dT", "lr"])
+        ACT(T.dr[:, 31:256:32], "dr", T.dr[:, 31:256:32], "dr", AF.Identity, bias=-float(BIG))
+        ACT(W("inv"), "inv", W("srf"), ["srf", "c81"], AF.Exp, bias=T.c8[:, 1:2], scale=-math.log(2.0))
+        level("wp", "db", "l1")
+        waits(1, "l2")
+        if r == 0:
+            for b in range(4):
+                QT("qcg", 128 * b, 128 * b + 128, T.cg[:, 3 - b:515 - b], "cg")
+            for b in range(4):
+                QT("qce", 128 * b, 128 * b + 128, T.ce[:, 3 - b:515 - b], "ce")
+        for j in range(8):
+            b, src, bk = j % 4, ("qcg", "qce")[j // 4], (7, 0, 1, 2, 3, 4, 5, 6)[j]
+            MM(bk, 256, src, 128 * b, fq, 0)
+            if j < 4:
+                ACT(T.G[:, 272 * b + 16:272 * b + 272], "G%d" % b, T["ps%d" % bk][:, 0:256], "ps%d" % bk, scale=0.5)
+            else:
+                ACT(T.F[:, 256 * b:256 * b + 256], "F%d" % b, T["ps%d" % bk][:, 0:256], "ps%d" % bk, scale=0.5)
+        level("wp", "dc", "l2")
+        TT(T.tabr[64:128, :], "tabr2", T.trp[64:128, 0:16], T.trp[64:128, 16:32], "trp", A.min)
+        tb = ["tabr0", "tabr1", "tabr2"]
+        TS(T.wtr[:, 0:8], "wtr", T.tabr[:, 0:8], tb, TMASK, None, A.bitwise_and)
+        TT(T.wr[:], "wr", T.wtr[:].indirect(T.lr[:, 0:16]), T.br[:], ["wtr", "lr", "br"], A.add)
+        emit("V", lambda: v.tensor_tensor_scan(T.key[:, 0:256], T.wr[:], T.dr[:], -1.0, A.max, A.add), ["wr", "dr"], ["key"])
+        TS(T.key[:, 31:256:32], "key", T.key[:, 31:256:32], "key", float(BIG), None, A.add)
+        CP(T.key[:, 256:272], "keyx", T.key[:, 0:16], "key")
+        TR(T.kt[:, 0:256], "kt", T.key[:, 0:256], "key")
+        TR(T.kt[:, 256:512], "kt", T.key[:, 16:272], ["key", "keyx"])
+        if r == 0:
+            key_constants()
+        TS(W("ka"), "ka", T.kt[:, 0:512:32], ["kt", "cm"], T.cm[:, 0:1], None, A.mult)
+        TS(W("kb"), "kb", T.kt[:, 16:512:32], ["kt", "cm"], T.cm[:, 1:2], None, A.mult)
+        TT(W("kn"), "kn", W("ka"), W("kb"), ["ka", "kb"], A.add)
+        for w in range(VUNITS, 16):
+            j = 256 * (w - VUNITS)
+            ACT(T.js[:, j:j + 256], "accS", T.key[:, 0:256], ["key", "kn"], AF.Sign, bias=W("kn", 0, 128, w, w + 1), accum_out=T.acc[:, w:w + 1])
+        if r == 0:
+            order_constants()
+        pairs = [
+            lambda: TS(I("fi"), "fi", T.tabr[:], tb, 255, None, A.bitwise_and),
+            lambda: TS(T.prs[:], "prs", T.tabr[:, 0:8], tb, float(BIG), None, A.is_lt),
+            lambda: CP(T.tin[:, 0:16], "tin", I("fi"), "fi"),
+            lambda: CP(T.tin[:, 16:32], "tin", I("fi"), "fi"),
+            lambda: TT(T.prw[:], "prw", T.prs[:], T.pow[:], ["prs", "pow"], A.mult),
+            lambda: TR(T.tout[:], "tout", T.tin[:], "tin"),
+            lambda: RED(T.bb[:], "bb", T.prw[:], "prw", A.add),
+            lambda: CP(T.fl[:], "fl", T.tout[:, 0:2], "tout"),
+            lambda: TS(I("pf"), "pf", W("inv"), ["inv", "bb"], T.bb[:, 0:1], -0.495, A.mult, A.add),
+            lambda: TT(W("dif"), "dif", W("srf"), W("own"), ["srf", "own"], A.subtract),
+            lambda: TS(I("pg"), "pg", I("pf"), "pf", 1, None, A.bitwise_and),
+            lambda: TT(W("ph"), "ph", I("pg"), W("dif"), ["pg", "dif"], A.mult),
+            lambda: TT(W("pq"), "pq", W("ph"), W("own"), ["ph", "own"], A.add),
+            lambda: CP(T.gl[:], "gl", W("pq"), "pq"),
+        ]
+        units = []
+        for w in range(VUNITS + 1):
+            if w < VUNITS:
+                units.append(lambda w=w: TS(T["jv%d" % w][:], "jv%d" % w, T.key[:, 0:256], ["key", "kn"], W("kn", 0, 128, w, w + 1), 0.0, A.add, A.is_lt))
+            if w:
+                units.append(lambda w=w - 1: RED(T.acr[:, w:w + 1], "acr", T["jv%d" % w][:], "jv%d" % w, A.add))
+        while units or pairs:
+            for todo, n in ((pairs, 2), (units, 1)):
+                for _ in range(min(n, len(todo))):
+                    todo.pop(0)()
+        for t in range(4):
+            ACT(T.G[:, 272 * t:272 * t + 16], "Gf%d" % t, T.G[:, 272 * t + 16:272 * t + 272].indirect(T.fl[:, 0:1]), ["G%d" % t, "fl"])
+        for t in range(4):
+            ACT(T.Gp[:, 256 * t:256 * t + 256], "Gp%d" % t, T.G[:, 272 * t:272 * t + 272].indirect(T.gl[:, 0:16]), ["G%d" % t, "Gf%d" % t, "gl"])
+        TS(T.acc[:, 0:VUNITS], "accV", T.acr[:, 0:VUNITS], "acr", -2.0, 255.0, A.mult, A.add)
+        ak = ["accV", "accS"]
+        TS(I("ri"), "ri", T.acc[:], ak, -0.5, 127.5, A.mult, A.add)
+        TS(W("ry"), "ry", T.acc[:], ak + ["cf0"], -1.0, T.cf[:, 0:1], A.mult, A.add)
+        TS(I("rx"), "rx", I("ri"), "ri", 15, None, A.bitwise_and)
+        TT(W("rz"), "rz", W("ry"), I("rx"), ["ry", "rx"], A.subtract)
+        CP(T.pl[:], "pl", W("rz"), "rz")
+        emit("V", lambda: v.tensor_copy(T.win[:].indirect(T.pl[:, 0:16]), T.vrow[:]), ["pl", "vrow", "win"], ["win"])
+        TR(T.wtt[:], "wtt", T.win[:], "win")
+        TT(W("of"), "of", T.wtt[:, 0:512:32], T.wtt[:, 16:512:32], "wtt", A.add)
+        CP(T.ou[:], "ou", W("of"), "of")
+        for t in range(4):
+            ACT(T.gz[:, 128 * t:128 * t + 128], "gz%d" % t, T.Gp[:, 256 * t:256 * t + 256].indirect(T.ou[:, 0:8]), ["Gp%d" % t, "ou"])
+        for t in range(4):
+            TT(T.Z[:, t:512:4], "Z", T.F[:, 256 * t:256 * t + 256].indirect(T.ou[:, 0:8]), T.gz[:, 128 * t:128 * t + 128], ["F%d" % t, "ou", "gz%d" % t], A.add)
+        z, a = "qz%d" % r, "qa%d" % r
+        QT(z, 0, 128, T.Z[:], "Z")
+        need("G", toks_of("G", [z], []))
+        (zc, zs), (ac, asc) = K(z, 0, 128), K(a, 0, 128)
+        g.remote_dma(ac.bitcast(dt.uint8), zc.bitcast(dt.uint8), T.sem["arr%d" % r], T.sem.sent, pid, rid, mask)
+        g.remote_dma(asc, zs, T.sem["arr%d" % r], T.sem.sent, pid, rid, mask)
+        landed("arr%d" % r, n_in, [a, "s" + a])
+        for t in range(4):
+            if t < 2:
+                TS(T.X[:, t:512:4], "X0", T.F[:, 256 * t:256 * t + 256].indirect(T.ou[:, 8:16]), ["F%d" % t, "ou"], 2.0, None, A.mult)
+            else:
+                ACT(T.X[:, t:512:4], "XS0", T.F[:, 256 * t:256 * t + 256].indirect(T.ou[:, 8:16]), ["F%d" % t, "ou"], scale=2.0)
+        if r == 0:
+            column_constants()
+        if last:
+            CP(T.rl[:], "rl", I("ri"), "ri")
+            emit("V", lambda: v.tensor_copy(T.opw[:].indirect(T.rl[:, 0:16]), T.vcol[:]), ["rl", "vcol"], ["opw"])
+            emit("Y", lambda: g.sync.dma_start(T.op[:], T.opw[0:128:16, :]), ["opw"], ["op"], dma=True)
+        symbols(r + 1, 0)
+        if last:
+            y_columns(0)
+        for b in range(4):
+            MM(b, 128, "qw", 128 * b, a, 0)
+            MM(4 + b, 128, "qce", 128 * b, a, 0)
+            ACT(T.hr[:, 128 * b:128 * b + 128], "hr%d" % b, T["ps%d" % b][:, 0:128], "ps%d" % b, scale=0.0078125)
+            TT(T.X[:, 512 + b:1024:4], "X1", T.hr[:, 128 * b:128 * b + 128], T["ps%d" % (4 + b)][:, 0:128], ["hr%d" % b, "ps%d" % (4 + b)], A.add)
+    symbols(NR, 1)
+    PICK("qp3", "qn3", T.ol[:, 0:16], "ol", ["qp3"], ["na3", "nb3"])
+    yc, _ = K("qp3", 0, 256)
+    emit("Y", lambda: g.sync.dma_start(T.oc[:, 0:1024], yc.bitcast(dt.uint8)), ["qp3"], ["oc"], dma=True)
+    for k in range(4):
+        emit("Y" if k < 2 else "S", lambda: (g.sync if k < 2 else s).dma_start(T.osc[4 * k:4 * k + 4, 0:256], T.sqp[32 * k:32 * k + 4, 256 * NR:256 * NR + 256]),
+             ["sqp3"], ["osc%d" % k], dma=True)
+    y_columns(1)
+    emit("Y", lambda: g.sync.dma_start(T.y[:], T.ysb[:]), ["ysb"], ["y"], dma=True)
+    for k in range(nd[0]):
+        g.wait_ge(T.sem["ld%d" % k], 16)
+    g.wait_ge(T.sem.sent, NR * n_out)
+    for k in "VSTG":
+        g.wait_ge(T.sem["c" + k], count[k])

@@ -1,57 +1,59 @@
-import math
 from concourse.mybir import dt, AluOpType as A, AxisListType, ActivationFunctionType as AF
 
 NR = 3
-VUNITS = 4
-BIG = 1 << 20
-TMASK = 0x7FF00
-INTS = ["oi", "oj", "ok1", "ni", "nj", "nk", "fi", "pf", "pg", "ri", "rx"]
-FLTS = ["s1", "sn", "inv", "dif", "own", "ph", "pq", "ka", "kb", "ry", "rz", "of", "srf", "kn"]
+U = 2048.0
+GONE = float(1 << 23)
+DROP = float(1 << 22)
+FAR = float(1 << 30)
+ROUND256 = 1.5 * float(1 << 31)
+PIECES = ((0, 1, 2), (3, 4, 5), (6, 7))
+NV = 3
+COLS = ["jj", "us", "w2", "lR", "lD", "lW", "lK", "lO", "l2", "lL", "lS", "xc", "fx"]
+LISTS = {"lO": (0, 1), "lL": (2, 1), "lS": (4, 1), "lK": (6, 1), "lW": (8, 4), "lD0": (12, 4), "lR0": (16, 8), "lP": (24, 16), "lF": (40, 16),
+         "l2": (56, 1), "lD1": (58, 4), "lR1": (62, 8)}
+SMALL = ["pf", "wu", "g0", "nb", "m2", "mn", "fl", "km", "rn"]
 
 SCRATCH = {}
 
 
 def _b(name, n, d="float32"):
-    SCRATCH[name] = ("sbuf", [128, n], d)
+    SCRATCH[name] = ("sbuf", [128] + (list(n) if isinstance(n, tuple) else [n]), d)
 
 
 for _n, _k, _d in (
         ("xs", 1024, "bfloat16"), ("us", 512, "bfloat16"), ("vs", 512, "bfloat16"),
-        ("one", 128, "bfloat16"), ("zer", 528, "bfloat16"), ("dy", 128, "bfloat16"), ("dy0", 128, "bfloat16"), ("dy1", 128, "bfloat16"),
-        ("dya", 128, "bfloat16"), ("dyb", 128, "bfloat16"), ("dyc", 128, "bfloat16"),
-        ("idn", 128, "bfloat16"), ("prm", 128, "bfloat16"),
-        ("cl", 2560, "bfloat16"), ("ce", 528, "bfloat16"), ("cg", 528, "bfloat16"),
-        ("pI", 1, "int32"), ("pi8", 1, "int32"), ("pi4", 1, "int32"), ("pi16", 1, "int32"), ("pih", 1, "int32"),
-        ("mk", 4, "float32"), ("cm", 2, "float32"), ("c8", 2, "float32"), ("cf", 8, "float32"),
-        ("io8", 8, "float32"), ("dT", 16, "float32"), ("pen", 8, "float32"), ("pwf", 8, "float32"), ("pow", 8, "int32"),
-        ("bp", 128, "float32"), ("br", 256, "float32"),
-        ("ti", 256, "int32"), ("tj", 256, "int32"), ("vrow", 256, "bfloat16"), ("vcol", 256, "float32"),
-        ("ol", 16, "uint16"), ("nl", 16, "uint16"),
-        ("sb", 48, "float32"), ("mt", 512, "bfloat16"),
-        ("l0", 8, "uint16"), ("l1", 8, "uint16"), ("l2", 8, "uint16"), ("lr", 16, "uint16"),
-        ("da", 128, "float32"), ("db", 128, "float32"), ("dc", 128, "float32"), ("dr", 256, "float32"),
-        ("wp", 128, "float32"), ("wr", 256, "float32"), ("tp", 128, "float32"), ("mm", 128, "float32"), ("mv", 1, "float32"),
-        ("rep", 32, "float32"), ("trp", 32, "float32"), ("tab0", 16, "int32"), ("tab1", 16, "int32"), ("tabr", 16, "int32"),
-        ("wt", 8, "int32"), ("wtr", 16, "int32"), ("tin", 32, "float32"), ("tout", 32, "float32"),
-        ("fl", 2, "uint16"), ("prs", 8, "float32"), ("prw", 8, "float32"), ("bb", 1, "float32"), ("gl", 16, "uint16"),
-        ("key", 272, "float32"), ("kt", 512, "float32"), ("acc", 16, "float32"), ("acr", 16, "float32"),
-        ("pl", 16, "uint16"), ("rl", 16, "uint16"),
-        ("win", 512, "bfloat16"), ("wtt", 512, "bfloat16"), ("ou", 16, "uint16"), ("opw", 256, "float32"),
-        ("F", 1024, "bfloat16"), ("G", 1088, "bfloat16"), ("Gp", 1024, "bfloat16"), ("gz", 512, "bfloat16"), ("Z", 512, "bfloat16"),
-        ("X", 1024, "bfloat16"), ("hr", 512, "float32"), ("ysb", 256, "float32")):
+        ("one", 128, "bfloat16"), ("zer", 528, "bfloat16"), ("idn", 128, "bfloat16"), ("prm", 128, "bfloat16"),
+        ("ce", 528, "bfloat16"), ("cg", 528, "bfloat16"), ("cs", 1024, "bfloat16"), ("vk", 128, "float32"), ("vg", 128, "float32"),
+        ("zr", 32 * len(COLS), "float32"), ("zc", 32 * len(COLS), "float32"), ("sm", 8 * len(SMALL), "float32"),
+        ("ls", 70, "uint16"), ("rows", 64, "float32"), ("cc", 48, "float32"),
+        ("crow", 384, "float32"), ("wrow", 384, "bfloat16"), ("r16", 128, "bfloat16"), ("dT", 48, "float32"),
+        ("hrow", 256, "float32"), ("rst", 64, "float32"), ("e40", 40, "float32"),
+        ("crep", 32, "float32"), ("c4k", 2, "float32"), ("rsv", 256 * NV, "bfloat16"),
+        ("ng0", 256, "bfloat16"), ("ng1", 256, "bfloat16"), ("ngn", 256, "bfloat16"), ("dlt", 256, "bfloat16"), ("dl2", 256, "bfloat16"),
+        ("B", 1024, "bfloat16"), ("dz", 256, "bfloat16"), ("ab", 256, "bfloat16"), ("dr", 256, "float32"),
+        ("sr", 288, "bfloat16"), ("st", 544, "bfloat16"), ("LG", 32, "uint16"),
+        ("pb", 256, "bfloat16"), ("fs", 256, "bfloat16"), ("e1", 128, "bfloat16"), ("pm", 128, "bfloat16"), ("pt", 128, "float32"),
+        ("pt8", 8, "float32"), ("pkr", 128, "bfloat16"), ("ck", 16, "float32"), ("R", 128, "bfloat16"), ("al", 128, "bfloat16"),
+        ("dif", 64, "float32"), ("neg", 64, "float32"), ("MT", 64, "float32"), ("yi", 64, "float32"), ("Y", 320, "float32"),
+        ("rep", 40, "float32"), ("trp", 32, "float32"), ("trf", 48, "float32"),
+        ("c1", 8, "float32"), ("k2", 8, "float32"), ("pen", 2, "float32"), ("rp2", 32, "float32"), ("tr2", 48, "float32"),
+        ("wr", 256, "float32"), ("key", 288, "float32"), ("kt", 544, "float32"), ("own", 32, "float32"),
+        ("js", 256 * (16 - NV), "bfloat16"), ("jv", 256 * NV, "bfloat16"), ("jo", 256 * NV, "bfloat16"),
+        ("acc", 16 * len(PIECES), "float32"), ("oa", 16 * len(PIECES), "float32"), ("oq", 16 * len(PIECES), "int32"),
+        ("od", 16 * len(PIECES), "float32"), ("pl", 16 * len(PIECES), "uint16"),
+        ("prf", 256, "bfloat16"), ("prb", 256, "bfloat16"), ("win", 272, "bfloat16"), ("wt", 256, "bfloat16"), ("wk", 256, "bfloat16"),
+        ("ll", 16 * NR, "uint16"), ("la", 16 * NR, "uint16"), ("lk", 16, "uint16"), ("opw", 256, "float32"),
+        ("Fo", 1024, "bfloat16"), ("F", 1024, "bfloat16"), ("G", 1024, "bfloat16"), ("gz", 512, "bfloat16"), ("Z", 512, "bfloat16"),
+        ("X", 1024, "bfloat16"), ("ysb", (8, 32), "float32")):
     _b(_n, _k, _d)
-_b("js", 256 * (16 - VUNITS), "bfloat16")
-for _k in range(VUNITS):
-    _b("jv%d" % _k, 256, "bfloat16")
-_b("ints", 16 * len(INTS), "int32")
-_b("flts", 16 * len(FLTS), "float32")
-for _n, _k in (("qx", 256), ("qn", 1024), ("qp", 1024), ("qu", 128), ("qv", 128), ("qw", 512), ("qc", 1664), ("qm", 128),
-               ("qz", 128 * NR), ("qa", 128 * NR)):
+for _n, _k in (("qn", 256 * (NR + 1)), ("qa", 256 * NR), ("qp", 256), ("qu", 128), ("qv", 128), ("qw", 512), ("qc", 1280), ("qb", 256),
+               ("qz", 128 * NR)):
     _b(_n, _k, "float8_e4m3fn_x4")
     _b("s" + _n, _k, "uint8")
 for _k in range(8):
     SCRATCH["ps%d" % _k] = ("psum", [128, 512], "float32")
-SEMAPHORES = ["cV", "cS", "cT", "cG", "sent"] + ["arr%d" % k for k in range(NR)] + ["ld%d" % k for k in range(16)]
+SEMAPHORES = (["cV", "cS", "cT", "cG", "sent"] + ["arc%d" % k for k in range(NR)] + ["arl%d" % k for k in range(NR)]
+              + ["ld%d" % k for k in range(16)])
 
 
 def recorder(g, T):
@@ -127,29 +129,31 @@ def rank_program(g, core, T, topo):
     emit, need, toks_of, landed, count, nd = recorder(g, T)
     v, s = g.vector, g.scalar
 
-    def I(n):
-        k = 16 * INTS.index(n)
-        return T.ints[:, k:k + 16]
+    def C(n, p=128):
+        if n in COLS:
+            k = 32 * COLS.index(n)
+            return T.zc[0:p, k:k + 1]
+        k = 8 * SMALL.index(n)
+        return T.sm[0:p, k:k + 1]
 
-    def W(n, p0=0, p1=128, a=0, b=16):
-        k = 16 * FLTS.index(n)
-        return T.flts[p0:p1, k + a:k + b]
+    def L(n):
+        a, k = LISTS[n]
+        return T.ls[:, a:a + k]
 
-    place = {"qcl": ("qc", 0), "qcr": ("qc", 384), "qce": ("qc", 640), "qcg": ("qc", 1152)}
+    place = {"qcs": ("qc", 0), "qce": ("qc", 256), "qcg": ("qc", 768), "qb0": ("qb", 0), "qb1": ("qb", 128)}
     for k in range(NR + 1):
         place["qn%d" % k] = ("qn", 256 * k)
         place["na%d" % k] = ("qn", 256 * k)
         place["nb%d" % k] = ("qn", 256 * k + 128)
-        place["qp%d" % k] = ("qp", 256 * k)
         place["qz%d" % k] = ("qz", 128 * k)
-        place["qa%d" % k] = ("qa", 128 * k)
+        place["qa%d" % k] = ("qa", 256 * k)
 
     def K(n, a, b):
         q, o = place.get(n, (n, 0))
         return T[q][:, o + a:o + b], T["s" + q][:, o + a:o + b]
 
     def pt(n):
-        return n if isinstance(n, (list, tuple)) else [n]
+        return list(n) if isinstance(n, (list, tuple)) else [n]
 
     def TS(o, ok, i, ik, s1, s2, o0, o1=None):
         if o1 is None:
@@ -171,29 +175,44 @@ def rank_program(g, core, T, topo):
     def RED(o, ok, i, ik, op):
         return emit("V", lambda: v.tensor_reduce(o, i, AxisListType.X, op), pt(ik), pt(ok))
 
-    def FILL(ap, ok, c):
-        return emit("V", lambda: v.memset(ap, c), [], pt(ok))
+    def SCAN(o, ok, a, b, ik, init, o0, o1):
+        return emit("V", lambda: v.tensor_tensor_scan(o, a, b, init, o0, o1), pt(ik), pt(ok))
 
-    def QT(q, a, b, i, ik):
-        return emit("V", lambda: v.quantize_mx(*K(q, a, b), i), pt(ik), [q, "s" + q])
+    def FILL(ap, ok, c, ik=()):
+        return emit("V", lambda: v.memset(ap, c), pt(ik), pt(ok))
 
-    def MM(bank, n, w, wa, m, ma):
-        (wt, ws), (mt, ms) = K(w, wa, wa + 128), K(m, ma, ma + n)
+    def QT(q, a, b, i, ik, ok=None):
+        return emit("V", lambda: v.quantize_mx(*K(q, a, b), i), pt(ik), pt(ok or q))
+
+    def MM(bank, n, w, wa, m, mk=None, start=True, stop=True):
+        (wt, ws), (mt, ms) = K(w, wa, wa + 128), K(m, 0, n)
         o = T["ps%d" % bank][:, 0:n]
-        return emit("T", lambda: g.tensor.matmul_mx(o, wt, ws, mt, ms, True, True), [w, "s" + w, m, "s" + m], ["ps%d" % bank])
+        return emit("T", lambda: g.tensor.matmul_mx(o, wt, ws, mt, ms, start, stop), [w, "s" + w] + pt(mk or m), ["ps%d" % bank])
 
-    def PICK(o, i, lst, lk, ok, ik):
-        (oc, osc), (ic, isc) = K(o, 0, 256), K(i, 0, 256)
-        emit("V", lambda: v.tensor_copy(oc.bitcast(dt.uint32), ic.bitcast(dt.uint32).indirect(lst)), ik + [lk], ok)
-        emit("S", lambda: s.activation(osc, isc.indirect(lst), AF.Copy), ["s" + k for k in ik] + [lk], ["s" + k for k in ok])
-
-    def IOTA(ap, ok, pat, base, cm, f=True):
-        if f:
-            return emit("G", lambda: g.iota(ap, pat, base, cm, allow_small_or_imprecise_dtypes=True), [], pt(ok))
-        return emit("G", lambda: g.iota(ap, pat, base, cm), [], pt(ok))
+    def IOTA(ap, ok, pat, base, cm=0):
+        return emit("G", lambda: g.iota(ap, pat, base, cm, allow_small_or_imprecise_dtypes=True), [], pt(ok))
 
     def AFF(o, ok, i, ik, pat, op, base, cm):
         return emit("G", lambda: g.affine_select(o, i, pat, op, 0.0, base, cm), pt(ik), pt(ok))
+
+    def row(n, a=0, b=32, st=1):
+        k = 32 * COLS.index(n)
+        return T.zr[:, k + a:k + b:st]
+
+    def turn(a, b, ok, ik):
+        i, j = 32 * COLS.index(a), 32 * COLS.index(b) + 32
+        TR(T.zc[:, i:j], ok, T.zr[:, i:j], ik)
+
+    rid, pid, _ = topo.addr(nxt)
+    mask = topo.mask(core, nxt)
+    n_out, n_in = len(topo.engines(core, nxt)), len(topo.engines(prv, core))
+
+    def send_codes(r):
+        need("G", toks_of("G", ["na%d" % r, "nb%d" % r], []))
+        (zc, zs), (ac, asc) = K("qn%d" % r, 0, 256), K("qa%d" % r, 0, 256)
+        g.remote_dma(ac.bitcast(dt.uint8), zc.bitcast(dt.uint8), T.sem["arc%d" % r], T.sem.sent, pid, rid, mask)
+        g.remote_dma(asc, zs, T.sem["arc%d" % r], T.sem.sent, pid, rid, mask)
+        landed("arc%d" % r, 2 * n_in, ["qa%d" % r])
 
     emit("Y", lambda: g.sync.dma_start(T.xs[:], T.x[:]), [], ["xs"], dma=True)
     emit("S", lambda: s.dma_start(T.us[:], T.u[:]), [], ["us"], dma=True)
@@ -201,290 +220,347 @@ def rank_program(g, core, T, topo):
     emit("Y", lambda: g.sync.dma_start(T.sqw[:, 0:512], T.ws[:, 0:512]), [], ["sqw"], dma=True)
     emit("Y", lambda: g.sync.dma_start(T.vs[:], T.v[:]), [], ["vs"], dma=True)
 
-    FILL(T.one[:], "one", 1.0)
-    IOTA(T.pI[:], "pI", [[0, 1]], 0, 1, False)
-    IOTA(T.io8[:], "io8", [[1, 8]], 0, 0)
-    IOTA(I("ni"), "ni", [[16, 16]], 0, 1, False)
-    AFF(T.dyb[:], "dyb", T.one[:], "one", [[0, 8], [-8, 16]], A.is_ge, 0, 1)
-    AFF(T.dy0[:], "dy0", T.dyb[:], "dyb", [[0, 8], [8, 16]], A.is_ge, 3, -1)
-    AFF(T.dyc[:], "dyc", T.one[:], "one", [[0, 8], [-8, 16]], A.is_ge, -4, 1)
-    AFF(T.dy1[:], "dy1", T.dyc[:], "dyc", [[0, 8], [8, 16]], A.is_ge, 7, -1)
-    AFF(T.dya[:], "dya", T.one[:], "one", [[0, 4], [-4, 2], [-8, 16]], A.is_ge, 0, 1)
-    AFF(T.dy[:], "dy", T.dya[:], "dya", [[0, 4], [4, 2], [8, 16]], A.is_ge, 3, -1)
-    IOTA(T.bp[:], "bp0", [[1, 128]], -1, 0)
+    FILL(T.one[:], "one", 128.0)
+    FILL(T.zer[:], "zer", 0.0)
+    FILL(row("w2"), "zr0", 0.0)
+    IOTA(row("jj"), "zrA", [[0, 2], [1, 16]], 0)
+    IOTA(row("us"), "zrA", [[0, 2], [int(U), 8], [0, 2]], int(U))
+    IOTA(T.vg[:], "vg", [[-16, 8], [0, 16]], 0, 1)
+    IOTA(T.vk[:], "vk", [[-16, 4], [0, 32]], 0, 1)
     AFF(T.idn[:], "idn", T.one[:], "one", [[-1, 128]], A.is_equal, 0, 1)
     AFF(T.prm[:], "prm0", T.one[:], "one", [[-16, 4], [0, 2], [-1, 16]], A.is_equal, 0, 1)
     AFF(T.prm[:, 0:16], "prm", T.one[:, 0:16], ["one", "prm0"], [[-1, 16]], A.is_equal, -112, 1)
-    IOTA(T.br[:], "br", [[1, 256]], -1, 0)
-    IOTA(T.ti[:], "ti", [[16, 2], [32, 8], [1, 16]], 0, 0, False)
+    IOTA(row("lR"), "zrB", [[32, 2], [0, 16]], 0)
+    IOTA(row("lD"), "zrB", [[0, 2], [32, 2], [0, 8]], 0)
+    IOTA(row("lW"), "zrB", [[0, 4], [2, 8]], 0)
+    IOTA(row("lK", 0, 16), "zrB", [[32, 8], [288, 2]], 0)
+    IOTA(row("lK", 16, 32), "zrB", [[32, 8], [-256, 2]], 272)
+    IOTA(C("pf"), "pf", [[0, 1]], 0, 1)
+    IOTA(T.rows[:, 0:4], "rows", [[64, 4]], 0)
+    IOTA(T.rows[:, 8:16], "rows", [[64, 4], [0, 2]], 0)
 
-    FILL(T.zer[:], "zer", 0.0)
-    ACT(T.cl[:, 1536:2048], "cl0S", T.zer[:, 0:512], "zer")
-    ACT(T.cl[:, 2048:2560], "cl0S", T.zer[:, 0:512], "zer")
-    ACT(T.mt[:], "mt0", T.zer[:, 0:512], "zer")
-    ACT(T.pwf[:], "pwf", T.io8[:], "io8", AF.Exp, scale=math.log(2.0))
-    FILL(T.cl[:, 0:1536], "cl0", 0.0)
-    TS(T.pi16[:], "pi16", T.pI[:], "pI", 15, None, A.bitwise_and)
-    TS(T.pi8[:], "pi8", T.pI[:], "pI", 7, None, A.bitwise_and)
-    TS(T.pi4[:], "pi4", T.pI[:], "pI", 3, None, A.bitwise_and)
-    TS(T.pih[:], "pih", T.pI[:], "pI", 4, 1, A.arith_shift_right, A.bitwise_and)
-    TS(T.cf[:, 5:6], "cf5", T.pI[:], "pI", 1.0, None, A.mult)
-    TS(T.cf[:, 4:5], "cf4", T.pi16[:], "pi16", 1.0, None, A.mult)
-    TT(T.cf[:, 3:4], "cf3", T.cf[:, 4:5], T.cf[:, 5:6], ["cf4", "cf5"], A.subtract)
-    TS(I("nj"), "nj", I("ni"), ["ni", "cf3"], T.cf[:, 3:4], None, A.add)
-    TS(I("nk"), "nk", I("nj"), "nj", 7, None, A.bitwise_and)
-    TS(I("ok1"), "ok1", I("nj"), "nj", 3, None, A.arith_shift_right)
-    TS(I("oi"), "oi", I("nk"), "nk", 32.0, None, A.mult)
-    TT(I("nk"), "nk", I("oi"), I("ok1"), ["oi", "ok1"], A.add)
-    CP(T.nl[:], "nl", I("nk"), "nk")
-    for h in range(4):
-        TS(T.mk[:, h:h + 1], "mk", T.pi4[:], "pi4", float(h), None, A.is_equal)
-    TS(T.c8[:, 0:1], "c80", T.pI[:], "pI", 16.0, 8.0, A.is_lt, A.mult)
-    TS(T.c8[:, 1:2], "c81", T.pI[:], "pI", 16.0, -10.0, A.is_lt, A.mult)
-    for y, nm in ((0, "dy0"), (1, "dy1")):
-        for G in range(8):
-            o = 1536 + 512 * y + 64 * G + G % 4
-            ACT(T.cl[:, o:o + 61:4], "clS", T[nm][:, 16 * G:16 * G + 16], [nm, "cl0S"])
-
-    QT("qx", 0, 256, T.xs[:], "xs")
-    QT("qu", 0, 128, T.us[:], "us")
-    PICK("qn0", "qx", T.nl[:, 0:16], "nl", ["na0", "nb0"], ["qx"])
-    ACT(T.cg[:], "cg0", T.zer[:], "zer")
+    for a in range(0, 1024, 512):
+        ACT(T.cs[:, a:a + 512], "cs0", T.zer[:, 0:512], "zer")
     ACT(T.ce[:], "ce0", T.zer[:], "zer")
-    ACT(T.win[:], "win", T.zer[:, 0:512], "zer")
-    CP(T.cl[:, 0:512:4], "clV", T.dy[:], ["dy", "cl0"])
-    CP(T.cl[:, 513:1024:4], "clV", T.dy[:], "dy")
-    for k in range(4):
-        o = 1024 + 128 * k + 2 + k % 2
-        CP(T.cl[:, o:o + 125:4], "clV", T.dy[:, 32 * k:32 * k + 32], "dy")
-    QT("qcl", 0, 384, T.cl[:, 0:1536], "clV")
-    QT("qcr", 0, 256, T.cl[:, 1536:2560], "clS")
+    ACT(T.cg[:], "cg0", T.zer[:], "zer")
+    for a in range(0, 1024, 512):
+        ACT(T.B[:, a:a + 512], ["B0", "B1"], T.zer[:, 0:512], "zer")
+    ACT(T.ce[:, 3:512:4], "ce", T.idn[:], ["idn", "ce0"])
+    ACT(T.cg[:, 3:512:4], "cg", T.prm[:], ["prm", "cg0"])
+    ACT(T.sr[:, 0:16], "srp", T.zer[:, 0:16], "zer")
+    ACT(T.sr[:, 272:288], "srp", T.zer[:, 0:16], "zer")
+    ACT(T.key[:], "key", T.zer[:, 0:288], "zer")
+    ACT(T.win[:], "win", T.zer[:, 0:272], "zer")
+    ACT(T.e1[:], "e1", T.zer[:, 0:128], "zer")
+    ACT(T.pm[:], "pm", T.zer[:, 0:128], "zer")
 
-    def path_constants():
-        TS(T.dT[:, 0:8], "dT", T.io8[:], "io8", 256.0, 257.0, A.mult, A.add)
-        TS(T.dT[:, 8:16], "dT", T.io8[:], "io8", 256.0, 257.0, A.mult, A.add)
-        TS(T.cf[:, 2:3], "cf2", T.pi8[:], "pi8", 1.0, None, A.mult)
-        TS(T.pen[:], "pen", T.io8[:], ["io8", "cf2"], T.cf[:, 2:3], float(BIG), A.not_equal, A.mult)
-        TS(T.cf[:, 1:2], "cf1", T.pih[:], "pih", 128.0, None, A.mult)
-        TS(T.bp[:], "bp", T.bp[:], ["bp0", "cf1"], T.cf[:, 1:2], None, A.add)
-        emit("V", lambda: v.memset(T.wtr[:], 0), [], ["wtr"])
-        CP(T.pow[:], "pow", T.pwf[:], "pwf")
+    FILL(T.crow[:], "crow0", U)
+    for i in range(3):
+        FILL(row("w2", i, 32, 16), "zrV", float(8 >> i), "zr0")
+    FILL(T.rst[:], "rst0", 0.0)
+    FILL(T.e40[:], "e400", 0.0)
+    turn("jj", "w2", "zcA", ["zrA", "zrV"])
+    FILL(T.wrow[:], "wrow0", 1.0)
+    FILL(T.crow[:, 31:256:32], "crow", U + GONE, "crow0")
+    TS(C("wu"), "wu", C("w2"), "zcA", U / 2, None, A.mult)
+    TS(T.cs[:, 512:1024:4], "cs", T.vg[:], ["vg", "zcA", "cs0"], C("jj"), C("w2"), A.is_equal, A.mult)
+    TS(T.cs[:, 0:512:4], "cs", T.vk[:], ["vk", "zcA", "wu", "cs0"], C("jj"), C("wu"), A.is_equal, A.mult)
+    TS(C("nb"), "nb", C("us"), "zcA", -U, -GONE / U, A.add, A.mult)
+    FILL(T.crow[:, 271:384:16], "crow", U + GONE)
+    QT("qcs", 0, 256, T.cs[:], "cs")
+    FILL(T.rst[:, 0:64:8], "rst", -FAR, "rst0")
+    FILL(T.wrow[:, 271:384:16], "wrow", 4096.0, "wrow0")
+    FILL(T.Y[:, 79:320:8], "Yc", FAR)
+    FILL(T.trp[:], ["trp1", "trp2"], 0.0)
+    FILL(T.trf[:, 32:48], "trfc", 0.0)
+    TS(T.crep[:], "crep", T.zer[:, 0:32], ["zer", "zcA"], C("us"), None, A.add)
+    CP(T.e40[:, 8:9], "e40", C("us"), ["zcA", "e400"])
+    FILL(T.rp2[:], "rp2", -4096.0)
+    FILL(T.tr2[:, 32:48], "tr2c", -4096.0)
+    FILL(T.c4k[:], "c4k", 4096.0)
+    FILL(T.acc[:], ["acc%d%s" % (k, q) for k in range(len(PIECES)) for q in "VS"], 1.0)
+    FILL(row("fx"), "zr1", 0.0)
+    FILL(row("xc", 0, 16), "zrW", 4080.0)
+    FILL(row("xc", 16, 32), "zrW", 4096.0)
+    FILL(row("fx", 31, 32), "zrW", DROP, "zr1")
+    QT("qu", 0, 128, T.us[:], "us")
+    for b in range(4):
+        QT("qce", 128 * b, 128 * b + 128, T.ce[:, 3 - b:515 - b], "ce")
+    QT("qn0", 0, 256, T.xs[:], "xs", ["na0", "nb0"])
 
-    def key_constants():
-        TS(T.cm[:, 0:1], "cm", T.pih[:], "pih", 0.0, -1.0, A.is_equal, A.mult)
-        TS(T.cm[:, 1:2], "cm", T.pih[:], "pih", -1.0, None, A.mult)
-        TS(W("own"), "own", I("nj"), "nj", 16.0, None, A.add)
+    send_codes(0)
+    IOTA(T.dT[:], "dT", [[0, 3], [int(U) // 2, 16]], int(U))
+    IOTA(T.cc[:, 0:8], "cc0", [[288, 8]], 0)
+    IOTA(T.cc[:, 8:24], "cc0", [[128, 2], [272, 8]], 0)
+    IOTA(T.hrow[:], "hrow", [[1, 8], [0, 32]], 0)
+    IOTA(row("lO"), "zrC", [[16, 2], [0, 2], [32, 8]], 0)
+    IOTA(row("l2"), "zrC", [[-16, 2], [0, 2], [32, 8]], 32)
+    IOTA(row("lL"), "zrC", [[16, 2], [1, 2], [32, 8]], 0)
+    IOTA(row("lS", 0, 16), "zrC", [[1, 16]], 0)
+    IOTA(row("lS", 16, 32), "zrC", [[2, 8], [-1, 2]], 1)
+    IOTA(T.ng0[:], "ng0", [[-1, 256]], 0)
+    IOTA(T.rows[:, 16:32], "rows2", [[2, 16]], 0)
+    IOTA(T.rows[:, 32:48], "rows2", [[16, 8], [128, 2]], 0)
+    IOTA(T.ngn[:], "ngn", [[-16, 8], [-128, 2], [-1, 16]], 0)
+    IOTA(T.dlt[:], "dlt", [[-16, 8], [112, 2], [0, 16]], 0)
 
-    def order_constants():
-        TS(T.cf[:, 0:1], "cf0", T.pih[:], "pih", 16.0, 255.0, A.mult, A.add)
-        TS(T.cf[:, 6:7], "cf6", T.pih[:], "pih", 16.0, None, A.mult)
-        TS(T.tj[:], "tj", T.ti[:], ["ti", "cf6"], T.cf[:, 6:7], None, A.add)
-        TS(T.ti[:], "ti", T.tj[:], "tj", 255, None, A.bitwise_and)
-        CP(T.vrow[:], "vrow", T.ti[:], "ti")
+    def dims(parts):
+        return (256, 0) if len(parts) == 2 else (128, parts[0])
 
-    def column_constants():
-        CP(T.vcol[:], "vcol", T.ti[:], "ti")
-        TS(I("oi"), "oi", I("nj"), "nj", 31, None, A.bitwise_and)
-        TS(I("oj"), "oj", I("nj"), "nj", 5, None, A.arith_shift_right)
-        TS(I("ok1"), "ok1", I("oi"), "oi", 8.0, None, A.mult)
-        TT(I("oi"), "oi", I("ok1"), I("oj"), ["ok1", "oj"], A.add)
-        CP(T.ol[:], "ol", I("oi"), "oi")
-        QT("qv", 0, 128, T.vs[:], "vs")
+    def keys(n, parts):
+        return [n + str(p) for p in parts]
 
-    rid, pid, _ = topo.addr(nxt)
-    mask = topo.mask(core, nxt)
-    n_out, n_in = 2 * len(topo.engines(core, nxt)), 2 * len(topo.engines(prv, core))
+    def back(t, a, b):
+        return t[:, b - 1::-1] if a == 0 else t[:, b - 1:a - 1:-1]
 
-    def symbols(k, hf):
-        q = ("na%d", "nb%d")[hf] % k
-        if k:
-            QT(q, 0, 128, T.X[:, 512 * hf:512 * hf + 512], [["X0", "XS0"], ["X1"]][hf])
-        if k == NR:
-            MM(hf, 128, "qv", 0, q, 0)
-            return
-        MM(hf, 128, q, 0, "qu", 0)
-        a, b = 8 * hf, 8 * hf + 8
-        for i in range(3):
-            TS(T.sb[:, 16 * i + a:16 * i + b], "sb%d" % hf, T["ps%d" % hf][:, i:128:16], "ps%d" % hf, 0.0, float(4 >> i), A.is_gt, A.mult)
-        TT(W("s1", 0, 128, a, b), "s1%d" % hf, T.sb[:, a:b], T.sb[:, 16 + a:16 + b], "sb%d" % hf, A.add)
-        TT(W("sn", 0, 128, a, b), "sn%d" % hf, W("s1", 0, 128, a, b), T.sb[:, 32 + a:32 + b], ["s1%d" % hf, "sb%d" % hf], A.add)
-        for h in range(4):
-            o, sn = T.mt[:, 16 * h + a:16 * h + b], W("sn", 0, 128, a, b)
-            if h < 2:
-                TS(o, "mt%dv" % hf, sn, ["sn%d" % hf, "mk", "mt0"], T.mk[:, h:h + 1], None, A.mult)
-            else:
-                ACT(o, "mt%ds" % hf, sn, ["sn%d" % hf, "mk", "mt0"], scale=T.mk[:, h:h + 1])
+    def scores(k, parts):
+        n, o = dims(parts)
+        q = "qn%d" % k if n == 256 else ("na%d", "nb%d")[o] % k
+        MM(4, n, "qu", 0, q, [("na%d", "nb%d")[p] % k for p in parts])
 
-    def y_columns(hf):
-        for h in range(8):
-            CP(T.ysb[:, 32 * h + 16 * hf:32 * h + 16 * hf + 16], "ysb", T["ps%d" % hf][:, h:128:8], "ps%d" % hf)
+    def bits(parts):
+        n, o = dims(parts)
+        TS(T.B[:, 512 * o:512 * o + 4 * n:4], keys("B", parts), T.ps4[:, 0:n], "ps4", 0.0, None, A.is_gt)
+        QT("qb%d" % o, 0, n, T.B[:, 512 * o:512 * o + 4 * n], keys("B", parts), keys("qb", parts))
+        for bank, c in ((5, 0), (6, 0), (7, 128)):
+            MM(bank, n, "qcs", c, "qb%d" % o, keys("qb", parts))
 
-    def level(w, d, lst):
-        for h in range(4):
-            a = slice(32 * h, 32 * h + 32)
-            emit("V", lambda: v.tensor_tensor_scan(T.tp[:, a], T[w][:, a], T[d][:, a], -1.0, A.max, A.add), [w, d], ["tp"])
-        TT(T.mm[:], "mm", T.pen[:].indirect(T[lst][:, 0:8]), T.tp[:], ["pen", lst, "tp"], A.max)
-        RED(T.mv[:], "mv", T.mm[:], "mm", A.min)
-        TS(T.rep[:], "rep", T.zer[:, 0:32], ["zer", "mv"], T.mv[:, 0:1], None, A.add)
-        TR(T.trp[:], "trp", T.rep[:], "rep")
+    def rows_S(parts):
+        n, o = dims(parts)
+        ACT(T.ab[:, 128 * o:128 * o + n], keys("ab", parts), T.ps5[:, 0:n], ["ps5", "nb"], AF.Abs, bias=C("nb"), scale=GONE / U)
+        ACT(T.sr[:, 16:16 + n], "sr", T.ps7[:, 0:n], "ps7")
 
-    def waits(k, lst):
-        tab = "tab%d" % k
-        TT(T[tab][:], tab, T.trp[:, 0:16], T.trp[:, 16:32], "trp", A.min)
-        TS(T.wt[:], "wt", T[tab][:, 0:8], tab, TMASK, None, A.bitwise_and)
-        CP(T.tabr[32 * k:32 * k + 32, :], "tabr%d" % k, T[tab][32 * k:32 * k + 32, :], tab)
-        TT(T.wp[:], "wp", T.wt[:].indirect(T[lst][:, 0:8]), T.bp[:], ["wt", lst, "bp"], A.add)
+    def rows_V(parts):
+        n, o = dims(parts)
+        c = 0 if n == 256 else 256
+        TT(T.dz[:, 128 * o:128 * o + n], keys("dz", parts), T.ps6[:, 0:n], T.crow[:, c:c + n], ["ps6", "crow"], A.add)
+
+    def firsts(parts):
+        n, o = dims(parts)
+        a, c = 128 * o, 0 if n == 256 else 256
+        return [lambda: SCAN(back(T.pb, a, a + n), keys("pb", parts), back(T.dz, a, a + n), back(T.ab, a, a + n), keys("dz", parts) + keys("ab", parts),
+                             0.0, A.add, A.min),
+                lambda: SCAN(back(T.fs, a, a + n), keys("fs", parts), back(T.wrow, c, c + n), back(T.ab, a, a + n), ["wrow"] + keys("ab", parts),
+                             0.0, A.add, A.min)]
+
+    def list_V(parts):
+        n, o = dims(parts)
+        return [lambda: TR(T.st[:, 0:n], "st", T.sr[:, 16:16 + n], "sr"),
+                lambda: TR(T.st[:, 256:288 + n], "st", T.sr[:, 0:32 + n], ["sr", "srp"]),
+                lambda: TS(T.LG[:, 0:16] if n == 256 else T.LG[:, o:32:2], keys("LG", parts), T.st[:].indirect(L("lK")), ["st", "lsB", "g0"],
+                           C("g0"), None, A.add)]
+
+    def unpack(c, q, qk, o, sc, part="TS"):
+        for b in range(4):
+            if "T" in part:
+                MM(b, 256, c, 128 * b, q, qk)
+            if "S" in part:
+                ACT(T[o][:, 256 * b:256 * b + 256], "%s%d" % (o, b), T["ps%d" % b][:, 0:256], "ps%d" % b, scale=sc)
+
+    def weave(main, fill):
+        fill = list(fill)
+        for m in main:
+            m()
+            if fill:
+                fill.pop(0)()
+        for f in fill:
+            f()
+
+    def level(p0, p1, tk):
+        return [lambda: TT(T.yi[:], "yi", T.trp[:].indirect(L("lW")), T.MT[:], ["trp1", "trp2", "MT", "lsB"], A.add),
+                lambda: SCAN(T.Y[:, 0:64], "Y", T.rst[:], T.yi[:], ["rst", "yi"], -FAR, A.add, A.max),
+                lambda: SCAN(T.rep[p0:p1, :], tk, T.Y[p0:p1, 7:320:8], T.e40[p0:p1, :], ["Y", "Yc", "cap", "e40"], FAR, A.min, A.add)]
+
+    both = (0, 1)
+    scores(0, both)
+    for b in range(2):
+        QT("qcg", 128 * b, 128 * b + 128, T.cg[:, 3 - b:515 - b], "cg")
+    bits(both)
+    for b in range(2, 4):
+        QT("qcg", 128 * b, 128 * b + 128, T.cg[:, 3 - b:515 - b], "cg")
+    turn("lR", "lK", "zcB", "zrB")
+    TS(C("g0"), "g0", C("pf"), "pf", 16.0, 32.0, A.is_lt, A.mult)
+    TS(L("lR0"), "lsB", T.rows[:, 8:16], ["rows", "zcB"], C("lR"), None, A.add)
+    TS(L("lD0"), "lsB", T.rows[:, 0:4], ["rows", "zcB"], C("lD"), None, A.add)
+    TS(L("lW"), "lsB", T.zer[:, 0:4], ["zer", "zcB"], C("lW"), None, A.add)
+    CP(L("lK"), "lsB", C("lK"), "zcB")
+    rows_S(both)
+    rows_V(both)
 
     for r in range(NR):
         last = r == NR - 1
+        parts = both if r == 0 else (1,)
+        lists = list_V(parts)
+        first = firsts(parts)
+        first[0]()
+        unpack("qce", "qn%d" % r, ["na%d" % r, "nb%d" % r], "Fo", 1 / 128)
+        lists[0]()
         if r == 0:
-            symbols(0, 0)
-        symbols(r, 1)
-        QT("qm", 0, 128, T.mt[:], ["mt0v", "mt0s", "mt1v", "mt1s"])
-        for k in range(3):
-            MM(2 + k, 128, "qcl", 128 * k, "qm", 0)
-        for k in range(2):
-            MM(5 + k, 128, "qcr", 128 * k, "qm", 0)
-        if r == 0:
-            path_constants()
-            fq = "qx"
-            ACT(T.cg[:, 3:512:4], "cg", T.prm[:], ["prm", "cg0"])
-            ACT(T.ce[:, 3:512:4], "ce", T.idn[:], ["idn", "ce0"])
+            pb, pk, ends = T.pb, ["pb0", "pb1"], T.pb[:, 0:256:32]
+            head = [lambda: CP(T.R[:], "R", T.pb[:].indirect(L("lR0")), pk + ["lsB"])]
+            fill = []
         else:
-            fq = "qp%d" % r
-            PICK(fq, "qn%d" % r, T.ol[:, 0:16], "ol", [fq], ["na%d" % r, "nb%d" % r])
-        CP(T.l0[:], "l0", T.ps2[:, 0:16:2], "ps2")
-        CP(T.da[:], "da", T.dT[:, 0:8].indirect(T.l0[:, 0:8]), ["dT", "l0"])
-        CP(T.l1[:], "l1", T.ps3[:, 0:16:2], "ps3")
-        ACT(T.db[:], "db", T.dT[:, 0:8].indirect(T.l1[:, 0:8]), ["dT", "l1"])
-        for y in range(2):
-            for hf in range(2):
-                ACT(W("srf", 64 * hf, 64 * hf + 64, 8 * y, 8 * y + 8), "srf", T["ps%d" % (5 + y)][64 * hf:64 * hf + 64, hf:16:2], ["ps%d" % (5 + y), "c80"],
-                    AF.Identity, bias=T.c8[64 * hf:64 * hf + 64, 0:1])
-        level("bp", "da", "l0")
-        waits(0, "l1")
-        CP(T.l2[:], "l2", T.ps4[:, 0:16:2], "ps4")
-        ACT(T.dc[:], "dc", T.dT[:, 0:8].indirect(T.l2[:, 0:8]), ["dT", "l2"])
-        CP(T.lr[:], "lr", W("srf"), "srf")
-        ACT(T.dr[:], "dr", T.dT[:].indirect(T.lr[:, 0:16]), ["dT", "lr"])
-        ACT(T.dr[:, 31:256:32], "dr", T.dr[:, 31:256:32], "dr", AF.Identity, bias=-float(BIG))
-        ACT(W("inv"), "inv", W("srf"), ["srf", "c81"], AF.Exp, bias=T.c8[:, 1:2], scale=-math.log(2.0))
-        level("wp", "db", "l1")
-        waits(1, "l2")
+            pb, pk, ends = T.pm, ["pm"], T.pm[:, 0:128:16]
+            head = [lambda: TT(T.e1[:, 0:128:16], "e1", T.pb[:, 128:256:16], T.pt8[:], ["pb1", "pt8"], A.add),
+                    lambda: TT(T.R[:], "R", T.e1[:].indirect(L("lR1")), T.pkr[:], ["e1", "pkr", "lsD"], A.min)]
+            fill = [lists[1], lambda: TT(ends, "pm", T.e1[:, 0:128:16], T.pb[:, 0:128:16], ["e1", "pb0"], A.min)]
+        weave(head + [lambda: TR(T.al[:], "al", T.R[:], "R"),
+                      lambda: TT(T.dif[:], "dif", pb[:].indirect(L("lD%d" % min(r, 1))), T.al[:, 0:128:2], pk + ["al", "lsB", "lsD"], A.subtract),
+                      lambda: TS(T.neg[:], "neg", T.dif[:], "dif", 0.0, GONE / U, A.min, A.mult),
+                      lambda: TT(T.MT[:], "MT", T.dif[:], T.neg[:], ["dif", "neg"], A.add)],
+              fill + [lambda: RED(C("mn"), "mn", ends, pk, A.min),
+                      lambda: TS(C("fl"), "fl", C("mn"), "mn", DROP, None, A.is_lt),
+                      lambda: TS(T.rep[0:32, 8:40], "rep0", T.crep[0:32, :], ["crep", "mn", "fl"], C("mn", 32), C("fl", 32), A.add, A.mult),
+                      lambda: TR(T.trp[32:64, :], "trp1", T.rep[0:32, 8:40], "rep0"),
+                      lambda: TS(T.Y[:, 71:72], "cap", C("fl"), ["fl", "zcA"], FAR, C("us"), A.mult, A.subtract)])
         if r == 0:
-            for b in range(4):
-                QT("qcg", 128 * b, 128 * b + 128, T.cg[:, 3 - b:515 - b], "cg")
-            for b in range(4):
-                QT("qce", 128 * b, 128 * b + 128, T.ce[:, 3 - b:515 - b], "ce")
-        for j in range(8):
-            b, src, bk = j % 4, ("qcg", "qce")[j // 4], (7, 0, 1, 2, 3, 4, 5, 6)[j]
-            MM(bk, 256, src, 128 * b, fq, 0)
-            if j < 4:
-                ACT(T.G[:, 272 * b + 16:272 * b + 272], "G%d" % b, T["ps%d" % bk][:, 0:256], "ps%d" % bk, scale=0.5)
+            fill = [lists[1], lists[2], first[1], lambda: TS(T.cc[:, 24:48], "cc", T.cc[:, 0:24], "cc0", -127.5, None, A.add),
+                    lambda: TT(T.c1[:], "c1", T.fs[:, 0:256:32], T.cc[:, 24:32], ["fs0", "fs1", "cc"], A.add)]
+        else:
+            fill = [lists[2], first[1], lambda: TT(T.ck[:, 8:16], "ck1", T.fs[:, 128:256:16], T.cc[:, 40:48], ["fs1", "cc"], A.add),
+                    lambda: TT(T.c1[:], "c1", T.ck[:, 0:8], T.ck[:, 8:16], ["ck0", "ck1"], A.min)]
+        weave(level(32, 64, "rep1") + [lambda: (TR(T.trp[64:96, :], "trp2", T.rep[32:64, 8:40], "rep1"), TR(T.trp[96:128, :], "trp2", T.rep[32:64, 8:40], "rep1"))]
+              + level(64, 128, "rep2") + [lambda: TR(T.trf[:, 0:32], "trf", T.rep[:, 8:40], ["rep0", "rep1", "rep2"])],
+              fill + [lambda: TS(T.pen[:], "pen", T.c4k[:], ["c4k", "fl"], C("fl"), 127.5 - 4096.0, A.mult, A.add)])
+        ACT(T.dr[:], "dr", T.dT[:].indirect(T.LG[:, 0:16]), ["dT", "LG0", "LG1"])
+        ACT(T.dr[:, 31:256:32], "dr", T.dr[:, 31:256:32], "dr", AF.Identity, bias=-DROP)
+        unpack("qcg", "qa%d" % r, None, "G", 1 / 256)
+        unpack("qce", "qa%d" % r, None, "F", 1 / 256, "T")
+        if r == 0:
+            turn("lO", "fx", "zcC", ["zrC", "zrW"])
+            FILL(T.rsv[:], "rsv0", 1.0)
+            for n in ("lO", "l2", "lL", "lS"):
+                CP(L(n), "lsC", C(n), "zcC")
+            FILL(T.rsv[:, 0:256 * NV:256], "rsv", 0.0, "rsv0")
+        key = T.key[:, 16:272]
+        weave([lambda: TT(T.wr[:], "wr", T.trf[:].indirect(T.LG[:, 0:16]), T.hrow[:], ["trf", "trfc", "LG0", "LG1", "hrow"], A.add),
+               lambda: SCAN(key, "key", T.wr[:], T.dr[:], ["wr", "dr"], -1.0, A.max, A.add),
+               lambda: TR(T.kt[:, 0:256], "kt0", key, "key")],
+              [lambda: TT(T.k2[:], "k2", T.Y[:, 7:64:8], T.c1[:], ["Y", "c1"], A.add),
+               lambda: RED(C("km"), "km", T.k2[:], "k2", A.min),
+               lambda: TS(C("rn"), "rn", C("km"), "km", ROUND256, -ROUND256, A.add, A.add)])
+        TS(T.own[:, 0:16], "own0", T.kt[:, 0:256].indirect(L("lO")), ["kt0", "lsC", "zcC"], C("fx"), None, A.add)
+        TS(T.key[:, 47:272:32], "key", T.key[:, 47:272:32], "key", DROP, None, A.add)
+        TS(T.rp2[:, 1:32:16], "rp2", T.pen[:], ["pen", "km", "rn"], C("km"), C("rn"), A.add, A.subtract)
+        TR(T.kt[:, 256:544], "kt1", T.key[:], "key")
+        TR(T.tr2[:, 0:32], "tr2", T.rp2[:], "rp2")
+        CP(T.own[:, 16:32], "own1", T.kt[:, 256:544].indirect(L("l2")), ["kt1", "lsC"])
+        ng = ("ng0", "ng1")[min(r, 1)]
+        TT(T.prf[:], "prf", T.tr2[:].indirect(T.LG[:, 0:16]), T[ng][:], ["tr2", "tr2c", "LG0", "LG1", ng], A.max)
+        nj = [0]
+
+        def unit_S(k, i, b, w):
+            j = 256 * nj[0]
+            nj[0] += 1
+            ACT(T.js[:, j:j + 256], "acc%dS" % k, key, ["key", "own%d" % w], AF.Sign, bias=T.own[:, 16 * w + b:16 * w + b + 1], scale=-1.0,
+                accum_out=T.acc[:, 16 * k + 2 * i + w:16 * k + 2 * i + w + 1])
+
+        def scatter(k):
+            n, w0, a = 2 * len(PIECES[k]), 2 * PIECES[k][0], slice(16 * k, 16 * k + 16)
+            ak = ["acc%dV" % k, "acc%dS" % k, "lsC"]
+            TS(T.oa[:, a], "oa%d" % k, T.acc[:, a].indirect(L("lS")), ak, 16 / 255, None, A.mult)
+            TS(T.oq[:, a], "oq%d" % k, T.acc[:, a].indirect(L("lS")), ak, 1 / 16, 15.5, A.mult, A.add)
+            TT(T.od[:, a], "od%d" % k, T.oa[:, a], T.oq[:, a], ["oa%d" % k, "oq%d" % k], A.subtract)
+            TS(T.pl[:, a], "pl%d" % k, T.od[:, a], ["od%d" % k, "zcC"], 255.0, C("xc"), A.mult, A.add)
+            emit("V", lambda: v.tensor_copy(T.win[:].indirect(T.pl[:, 16 * k:16 * k + n]), T.prb[:, 16 * w0:16 * (w0 + n)]), ["pl%d" % k, "prb", "win"], ["win"])
+
+        for k, piece in enumerate(PIECES):
+            for w in range(2):
+                for i, b in enumerate(piece):
+                    if w == 0 or b >= NV:
+                        unit_S(k, i, b, w)
+            if k == 0:
+                ACT(T.prb[:], "prb", T.prf[:], "prf", AF.Abs)
+                for b in range(NV):
+                    TS(T.jv[:, 256 * b:256 * b + 256], "jv", key, ["key", "own1"], T.own[:, 16 + b:17 + b], None, A.is_lt)
+                SCAN(T.jo[:], "jo", T.rsv[:], T.jv[:], ["rsv", "jv"], 0.0, A.mult, A.add)
+                TS(T.acc[:, 1:2 * NV:2], "acc0V", T.jo[:, 255:256 * NV:256], "jo", 2.0, -255.0, A.mult, A.add)
+        unpack("qce", "qa%d" % r, None, "F", 1 / 256, "S")
+        for k in range(len(PIECES)):
+            scatter(k)
+        ll = T.ll[:, 16 * r:16 * r + 16]
+        TR(T.wt[:], "wt", T.win[:, 0:256], "win")
+        CP(ll, "ll%d" % r, T.wt[:].indirect(L("lL")), ["wt", "lsC"])
+        need("G", toks_of("G", ["ll%d" % r], []))
+        g.remote_dma(T.la[:, 16 * r:16 * r + 16], ll, T.sem["arl%d" % r], T.sem.sent, pid, rid, mask)
+        landed("arl%d" % r, n_in, ["la%d" % r])
+        TR(T.wk[:], "wk", T.win[:, 16:272], "win")
+        if r == 0:
+            TS(C("m2"), "m2", C("jj"), "zcA", 2.0, None, A.is_equal)
+        CP(T.lk[:], "lk", T.wk[:].indirect(L("lO")), ["wk", "lsC"])
+        for t in range(4):
+            src = T.Fo[:, 256 * t:256 * t + 256].indirect(T.lk[:, 0:8])
+            (CP if t < 2 else ACT)(T.X[:, t:512:4], "X0" + "VS"[t // 2], src, ["Fo%d" % t, "lk"])
+        QT("na%d" % (r + 1), 0, 128, T.X[:, 0:512], ["X0V", "X0S"])
+        if last:
+            MM(4, 128, "qv", 0, "na3")
+            ACT(T.opw[:], "opw", T.win[:].indirect(L("lP")), ["win", "lsE"])
+            emit("Y", lambda: g.sync.dma_start(T.op[:], T.opw[2:128:16, :]), ["opw"], ["op"], dma=True)
+        else:
+            scores(r + 1, (0,))
+            if r == 0:
+                TS(L("lR1"), "lsD", L("lR0"), "lsB", 0.5, None, A.mult)
+                TS(L("lD1"), "lsD", L("lD0"), "lsB", 0.5, None, A.mult)
+                FILL(T.r16[:], "r160", 1.0)
+                ACT(T.dl2[:], "dl2", T.dlt[:], ["dlt", "m2"], scale=C("m2"))
+            bits((0,))
+            if r == 0:
+                FILL(T.r16[:, 0:128:16], "r16", 0.0, "r160")
+                TT(T.ng1[:], "ng1", T.dl2[:], T.ngn[:], ["dl2", "ngn"], A.add)
             else:
-                ACT(T.F[:, 256 * b:256 * b + 256], "F%d" % b, T["ps%d" % bk][:, 0:256], "ps%d" % bk, scale=0.5)
-        level("wp", "dc", "l2")
-        TT(T.tabr[64:128, :], "tabr2", T.trp[64:128, 0:16], T.trp[64:128, 16:32], "trp", A.min)
-        tb = ["tabr0", "tabr1", "tabr2"]
-        TS(T.wtr[:, 0:8], "wtr", T.tabr[:, 0:8], tb, TMASK, None, A.bitwise_and)
-        TT(T.wr[:], "wr", T.wtr[:].indirect(T.lr[:, 0:16]), T.br[:], ["wtr", "lr", "br"], A.add)
-        emit("V", lambda: v.tensor_tensor_scan(T.key[:, 0:256], T.wr[:], T.dr[:], -1.0, A.max, A.add), ["wr", "dr"], ["key"])
-        TS(T.key[:, 31:256:32], "key", T.key[:, 31:256:32], "key", float(BIG), None, A.add)
-        CP(T.key[:, 256:272], "keyx", T.key[:, 0:16], "key")
-        TR(T.kt[:, 0:256], "kt", T.key[:, 0:256], "key")
-        TR(T.kt[:, 256:512], "kt", T.key[:, 16:272], ["key", "keyx"])
-        if r == 0:
-            key_constants()
-        TS(W("ka"), "ka", T.kt[:, 0:512:32], ["kt", "cm"], T.cm[:, 0:1], None, A.mult)
-        TS(W("kb"), "kb", T.kt[:, 16:512:32], ["kt", "cm"], T.cm[:, 1:2], None, A.mult)
-        TT(W("kn"), "kn", W("ka"), W("kb"), ["ka", "kb"], A.add)
-        for w in range(VUNITS, 16):
-            j = 256 * (w - VUNITS)
-            ACT(T.js[:, j:j + 256], "accS", T.key[:, 0:256], ["key", "kn"], AF.Sign, bias=W("kn", 0, 128, w, w + 1), accum_out=T.acc[:, w:w + 1])
-        if r == 0:
-            order_constants()
-        pairs = [
-            lambda: TS(I("fi"), "fi", T.tabr[:], tb, 255, None, A.bitwise_and),
-            lambda: TS(T.prs[:], "prs", T.tabr[:, 0:8], tb, float(BIG), None, A.is_lt),
-            lambda: CP(T.tin[:, 0:16], "tin", I("fi"), "fi"),
-            lambda: CP(T.tin[:, 16:32], "tin", I("fi"), "fi"),
-            lambda: TT(T.prw[:], "prw", T.prs[:], T.pow[:], ["prs", "pow"], A.mult),
-            lambda: TR(T.tout[:], "tout", T.tin[:], "tin"),
-            lambda: RED(T.bb[:], "bb", T.prw[:], "prw", A.add),
-            lambda: CP(T.fl[:], "fl", T.tout[:, 0:2], "tout"),
-            lambda: TS(I("pf"), "pf", W("inv"), ["inv", "bb"], T.bb[:, 0:1], -0.495, A.mult, A.add),
-            lambda: TT(W("dif"), "dif", W("srf"), W("own"), ["srf", "own"], A.subtract),
-            lambda: TS(I("pg"), "pg", I("pf"), "pf", 1, None, A.bitwise_and),
-            lambda: TT(W("ph"), "ph", I("pg"), W("dif"), ["pg", "dif"], A.mult),
-            lambda: TT(W("pq"), "pq", W("ph"), W("own"), ["ph", "own"], A.add),
-            lambda: CP(T.gl[:], "gl", W("pq"), "pq"),
-        ]
-        units = []
-        for w in range(VUNITS + 1):
-            if w < VUNITS:
-                units.append(lambda w=w: TS(T["jv%d" % w][:], "jv%d" % w, T.key[:, 0:256], ["key", "kn"], W("kn", 0, 128, w, w + 1), 0.0, A.add, A.is_lt))
-            if w:
-                units.append(lambda w=w - 1: RED(T.acr[:, w:w + 1], "acr", T["jv%d" % w][:], "jv%d" % w, A.add))
-        while units or pairs:
-            for todo, n in ((pairs, 2), (units, 1)):
-                for _ in range(min(n, len(todo))):
-                    todo.pop(0)()
+                TS(L("lP"), "lsE", T.rows[:, 16:32], ["rows2", "zcC"], C("lL"), None, A.add)
+                TS(L("lF"), "lsE", T.rows[:, 32:48], ["rows2", "zcA"], C("jj"), None, A.add)
+                QT("qv", 0, 128, T.vs[:], "vs")
+            rows_V((0,))
+            SCAN(T.pt[:], "pt", T.r16[:], T.ps6[:, 0:128], ["r16", "ps6"], 0.0, A.mult, A.add)
+        z = "qz%d" % r
         for t in range(4):
-            ACT(T.G[:, 272 * t:272 * t + 16], "Gf%d" % t, T.G[:, 272 * t + 16:272 * t + 272].indirect(T.fl[:, 0:1]), ["G%d" % t, "fl"])
+            ACT(T.gz[:, 128 * t:128 * t + 128], "gz%d" % t, T.G[:, 256 * t:256 * t + 256].indirect(T.la[:, 16 * r + 8:16 * r + 16]), ["G%d" % t, "la%d" % r])
         for t in range(4):
-            ACT(T.Gp[:, 256 * t:256 * t + 256], "Gp%d" % t, T.G[:, 272 * t:272 * t + 272].indirect(T.gl[:, 0:16]), ["G%d" % t, "Gf%d" % t, "gl"])
-        TS(T.acc[:, 0:VUNITS], "accV", T.acr[:, 0:VUNITS], "acr", -2.0, 255.0, A.mult, A.add)
-        ak = ["accV", "accS"]
-        TS(I("ri"), "ri", T.acc[:], ak, -0.5, 127.5, A.mult, A.add)
-        TS(W("ry"), "ry", T.acc[:], ak + ["cf0"], -1.0, T.cf[:, 0:1], A.mult, A.add)
-        TS(I("rx"), "rx", I("ri"), "ri", 15, None, A.bitwise_and)
-        TT(W("rz"), "rz", W("ry"), I("rx"), ["ry", "rx"], A.subtract)
-        CP(T.pl[:], "pl", W("rz"), "rz")
-        emit("V", lambda: v.tensor_copy(T.win[:].indirect(T.pl[:, 0:16]), T.vrow[:]), ["pl", "vrow", "win"], ["win"])
-        TR(T.wtt[:], "wtt", T.win[:], "win")
-        TT(W("of"), "of", T.wtt[:, 0:512:32], T.wtt[:, 16:512:32], "wtt", A.add)
-        CP(T.ou[:], "ou", W("of"), "of")
-        for t in range(4):
-            ACT(T.gz[:, 128 * t:128 * t + 128], "gz%d" % t, T.Gp[:, 256 * t:256 * t + 256].indirect(T.ou[:, 0:8]), ["Gp%d" % t, "ou"])
-        for t in range(4):
-            TT(T.Z[:, t:512:4], "Z", T.F[:, 256 * t:256 * t + 256].indirect(T.ou[:, 0:8]), T.gz[:, 128 * t:128 * t + 128], ["F%d" % t, "ou", "gz%d" % t], A.add)
-        z, a = "qz%d" % r, "qa%d" % r
+            TT(T.Z[:, t:512:4], "Z", T.F[:, 256 * t:256 * t + 256].indirect(T.la[:, 16 * r:16 * r + 8]), T.gz[:, 128 * t:128 * t + 128],
+               ["F%d" % t, "la%d" % r, "gz%d" % t], A.add)
         QT(z, 0, 128, T.Z[:], "Z")
-        need("G", toks_of("G", [z], []))
-        (zc, zs), (ac, asc) = K(z, 0, 128), K(a, 0, 128)
-        g.remote_dma(ac.bitcast(dt.uint8), zc.bitcast(dt.uint8), T.sem["arr%d" % r], T.sem.sent, pid, rid, mask)
-        g.remote_dma(asc, zs, T.sem["arr%d" % r], T.sem.sent, pid, rid, mask)
-        landed("arr%d" % r, n_in, [a, "s" + a])
-        for t in range(4):
-            if t < 2:
-                TS(T.X[:, t:512:4], "X0", T.F[:, 256 * t:256 * t + 256].indirect(T.ou[:, 8:16]), ["F%d" % t, "ou"], 2.0, None, A.mult)
-            else:
-                ACT(T.X[:, t:512:4], "XS0", T.F[:, 256 * t:256 * t + 256].indirect(T.ou[:, 8:16]), ["F%d" % t, "ou"], scale=2.0)
-        if r == 0:
-            column_constants()
-        if last:
-            CP(T.rl[:], "rl", I("ri"), "ri")
-            emit("V", lambda: v.tensor_copy(T.opw[:].indirect(T.rl[:, 0:16]), T.vcol[:]), ["rl", "vcol"], ["opw"])
-            emit("Y", lambda: g.sync.dma_start(T.op[:], T.opw[0:128:16, :]), ["opw"], ["op"], dma=True)
-        symbols(r + 1, 0)
-        if last:
-            y_columns(0)
         for b in range(4):
-            MM(b, 128, "qw", 128 * b, a, 0)
-            MM(4 + b, 128, "qce", 128 * b, a, 0)
-            ACT(T.hr[:, 128 * b:128 * b + 128], "hr%d" % b, T["ps%d" % b][:, 0:128], "ps%d" % b, scale=0.0078125)
-            TT(T.X[:, 512 + b:1024:4], "X1", T.hr[:, 128 * b:128 * b + 128], T["ps%d" % (4 + b)][:, 0:128], ["hr%d" % b, "ps%d" % (4 + b)], A.add)
-    symbols(NR, 1)
-    PICK("qp3", "qn3", T.ol[:, 0:16], "ol", ["qp3"], ["na3", "nb3"])
-    yc, _ = K("qp3", 0, 256)
-    emit("Y", lambda: g.sync.dma_start(T.oc[:, 0:1024], yc.bitcast(dt.uint8)), ["qp3"], ["oc"], dma=True)
+            MM(b, 128, "qw", 128 * b, z, None, True, False)
+            MM(b, 128, "qce", 128 * b, z, None, False, True)
+        if last:
+            CP(T.ysb[:, :, 0:16], "ysb", T.ps4[:, 0:128], "ps4")
+        else:
+            rows_S((0,))
+            kept, first = list_V((0,)), firsts((0,))
+            TS(T.pt8[:], "pt8", T.pt[:, 15:128:16], "pt", 16 * U, None, A.add)
+            first[0]()
+            first[1]()
+            kept[0]()
+            kept[1]()
+            CP(T.pkr[:], "pkr", T.pb[:, 0:128].indirect(L("lR1")), ["pb0", "lsD"])
+        for b in range(4):
+            o, i = T.X[:, 512 + b:1024:4], T["ps%d" % b][:, 0:128]
+            if b % 2:
+                TS(o, "X1V", i, "ps%d" % b, 0.0078125, None, A.mult)
+            else:
+                ACT(o, "X1S", i, "ps%d" % b, scale=0.0078125)
+        QT("nb%d" % (r + 1), 0, 128, T.X[:, 512:1024], ["X1V", "X1S"])
+        if not last:
+            scores(r + 1, (1,))
+            send_codes(r + 1)
+            kept[2]()
+            TT(T.ck[:, 0:8], "ck0", T.fs[:, 0:128:16], T.cc[:, 32:40], ["fs0", "cc"], A.add)
+            bits((1,))
+            rows_S((1,))
+            rows_V((1,))
+    MM(5, 128, "qv", 0, "nb3")
+    (oc, osc), (ic, isc) = K("qp", 0, 256), K("qn3", 0, 256)
+    emit("V", lambda: v.tensor_copy(oc.bitcast(dt.uint32), ic.bitcast(dt.uint32).indirect(L("lF"))), ["na3", "nb3", "lsE"], ["qp"])
+    emit("S", lambda: s.activation(osc, isc.indirect(L("lF")), AF.Copy), ["na3", "nb3", "lsE"], ["sqp"])
+    emit("Y", lambda: g.sync.dma_start(T.oc[:, 0:1024], oc.bitcast(dt.uint8)), ["qp"], ["oc"], dma=True)
     for k in range(4):
-        emit("Y" if k < 2 else "S", lambda: (g.sync if k < 2 else s).dma_start(T.osc[4 * k:4 * k + 4, 0:256], T.sqp[32 * k:32 * k + 4, 256 * NR:256 * NR + 256]),
-             ["sqp3"], ["osc%d" % k], dma=True)
-    y_columns(1)
+        emit("Y" if k < 2 else "S", lambda: (g.sync if k < 2 else s).dma_start(T.osc[4 * k:4 * k + 4, 0:256], T.sqp[32 * k:32 * k + 4, 0:256]),
+             ["sqp"], ["osc%d" % k], dma=True)
+    CP(T.ysb[:, :, 16:32], "ysb", T.ps5[:, 0:128], "ps5")
     emit("Y", lambda: g.sync.dma_start(T.y[:], T.ysb[:]), ["ysb"], ["y"], dma=True)
     for k in range(nd[0]):
         g.wait_ge(T.sem["ld%d" % k], 16)
-    g.wait_ge(T.sem.sent, NR * n_out)
+    g.wait_ge(T.sem.sent, 3 * NR * n_out)
     for k in "VSTG":
         g.wait_ge(T.sem["c" + k], count[k])

@@ -6,8 +6,8 @@ GONE = float(1 << 23)
 DROP = float(1 << 22)
 FAR = float(1 << 30)
 ROUND256 = 1.5 * float(1 << 31)
-PIECES = ((0, 1, 2), (3, 4, 5), (6, 7))
-NV = 3
+PIECES = ((0, 1, 2, 3, 4, 5), (6, 7))
+NV = 4
 COLS = ["jj", "us", "w2", "lR", "lD", "lW", "lK", "lO", "l2", "lL", "lS", "xc", "fx"]
 LISTS = {"lO": (0, 1), "lL": (2, 1), "lS": (4, 1), "lK": (6, 1), "lW": (8, 4), "lD0": (12, 4), "lR0": (16, 8), "lP": (24, 16), "lF": (40, 16),
          "l2": (56, 1), "lD1": (58, 4), "lR1": (62, 8)}
@@ -239,12 +239,12 @@ def rank_program(g, core, T, topo):
     IOTA(T.rows[:, 0:4], "rows", [[64, 4]], 0)
     IOTA(T.rows[:, 8:16], "rows", [[64, 4], [0, 2]], 0)
 
-    for a in range(0, 1024, 512):
-        ACT(T.cs[:, a:a + 512], "cs0", T.zer[:, 0:512], "zer")
-    ACT(T.ce[:], "ce0", T.zer[:], "zer")
-    ACT(T.cg[:], "cg0", T.zer[:], "zer")
+    FILL(T.cs[:], "cs0", 0.0)
     for a in range(0, 1024, 512):
         ACT(T.B[:, a:a + 512], ["B0", "B1"], T.zer[:, 0:512], "zer")
+    ACT(T.crow[:], "crow0", T.zer[:, 0:384], "zer", AF.Identity, bias=U)
+    ACT(T.ce[:], "ce0", T.zer[:], "zer")
+    ACT(T.cg[:], "cg0", T.zer[:], "zer")
     ACT(T.ce[:, 3:512:4], "ce", T.idn[:], ["idn", "ce0"])
     ACT(T.cg[:, 3:512:4], "cg", T.prm[:], ["prm", "cg0"])
     ACT(T.sr[:, 0:16], "srp", T.zer[:, 0:16], "zer")
@@ -254,19 +254,16 @@ def rank_program(g, core, T, topo):
     ACT(T.e1[:], "e1", T.zer[:, 0:128], "zer")
     ACT(T.pm[:], "pm", T.zer[:, 0:128], "zer")
 
-    FILL(T.crow[:], "crow0", U)
     for i in range(3):
         FILL(row("w2", i, 32, 16), "zrV", float(8 >> i), "zr0")
     FILL(T.rst[:], "rst0", 0.0)
     FILL(T.e40[:], "e400", 0.0)
     turn("jj", "w2", "zcA", ["zrA", "zrV"])
     FILL(T.wrow[:], "wrow0", 1.0)
-    FILL(T.crow[:, 31:256:32], "crow", U + GONE, "crow0")
     TS(C("wu"), "wu", C("w2"), "zcA", U / 2, None, A.mult)
     TS(T.cs[:, 512:1024:4], "cs", T.vg[:], ["vg", "zcA", "cs0"], C("jj"), C("w2"), A.is_equal, A.mult)
     TS(T.cs[:, 0:512:4], "cs", T.vk[:], ["vk", "zcA", "wu", "cs0"], C("jj"), C("wu"), A.is_equal, A.mult)
-    TS(C("nb"), "nb", C("us"), "zcA", -U, -GONE / U, A.add, A.mult)
-    FILL(T.crow[:, 271:384:16], "crow", U + GONE)
+    TS(C("nb"), "nb", C("us"), "zcA", -U, None, A.add)
     QT("qcs", 0, 256, T.cs[:], "cs")
     FILL(T.rst[:, 0:64:8], "rst", -FAR, "rst0")
     FILL(T.wrow[:, 271:384:16], "wrow", 4096.0, "wrow0")
@@ -283,9 +280,9 @@ def rank_program(g, core, T, topo):
     FILL(row("xc", 0, 16), "zrW", 4080.0)
     FILL(row("xc", 16, 32), "zrW", 4096.0)
     FILL(row("fx", 31, 32), "zrW", DROP, "zr1")
+    FILL(T.crow[:, 31:256:32], "crow", U + GONE, "crow0")
+    FILL(T.crow[:, 271:384:16], "crow", U + GONE)
     QT("qu", 0, 128, T.us[:], "us")
-    for b in range(4):
-        QT("qce", 128 * b, 128 * b + 128, T.ce[:, 3 - b:515 - b], "ce")
     QT("qn0", 0, 256, T.xs[:], "xs", ["na0", "nb0"])
 
     send_codes(0)
@@ -322,17 +319,17 @@ def rank_program(g, core, T, topo):
         n, o = dims(parts)
         TS(T.B[:, 512 * o:512 * o + 4 * n:4], keys("B", parts), T.ps4[:, 0:n], "ps4", 0.0, None, A.is_gt)
         QT("qb%d" % o, 0, n, T.B[:, 512 * o:512 * o + 4 * n], keys("B", parts), keys("qb", parts))
-        for bank, c in ((5, 0), (6, 0), (7, 128)):
+        for bank, c in ((6, 0), (7, 128)):
             MM(bank, n, "qcs", c, "qb%d" % o, keys("qb", parts))
 
     def rows_S(parts):
         n, o = dims(parts)
-        ACT(T.ab[:, 128 * o:128 * o + n], keys("ab", parts), T.ps5[:, 0:n], ["ps5", "nb"], AF.Abs, bias=C("nb"), scale=GONE / U)
         ACT(T.sr[:, 16:16 + n], "sr", T.ps7[:, 0:n], "ps7")
 
     def rows_V(parts):
         n, o = dims(parts)
         c = 0 if n == 256 else 256
+        TS(T.ab[:, 128 * o:128 * o + n], keys("ab", parts), T.ps6[:, 0:n], ["ps6", "nb"], C("nb"), GONE, A.not_equal, A.mult)
         TT(T.dz[:, 128 * o:128 * o + n], keys("dz", parts), T.ps6[:, 0:n], T.crow[:, c:c + n], ["ps6", "crow"], A.add)
 
     def firsts(parts):
@@ -350,12 +347,12 @@ def rank_program(g, core, T, topo):
                 lambda: TS(T.LG[:, 0:16] if n == 256 else T.LG[:, o:32:2], keys("LG", parts), T.st[:].indirect(L("lK")), ["st", "lsB", "g0"],
                            C("g0"), None, A.add)]
 
-    def unpack(c, q, qk, o, sc, part="TS"):
+    def unpack(c, q, qk, o, sc, part="TS", k=0):
         for b in range(4):
             if "T" in part:
-                MM(b, 256, c, 128 * b, q, qk)
+                MM(k + b, 256, c, 128 * b, q, qk)
             if "S" in part:
-                ACT(T[o][:, 256 * b:256 * b + 256], "%s%d" % (o, b), T["ps%d" % b][:, 0:256], "ps%d" % b, scale=sc)
+                ACT(T[o][:, 256 * b:256 * b + 256], "%s%d" % (o, b), T["ps%d" % (k + b)][:, 0:256], "ps%d" % (k + b), scale=sc)
 
     def weave(main, fill):
         fill = list(fill)
@@ -373,17 +370,17 @@ def rank_program(g, core, T, topo):
 
     both = (0, 1)
     scores(0, both)
-    for b in range(2):
-        QT("qcg", 128 * b, 128 * b + 128, T.cg[:, 3 - b:515 - b], "cg")
-    bits(both)
-    for b in range(2, 4):
-        QT("qcg", 128 * b, 128 * b + 128, T.cg[:, 3 - b:515 - b], "cg")
+    for b in range(4):
+        QT("qce", 128 * b, 128 * b + 128, T.ce[:, 3 - b:515 - b], "ce")
     turn("lR", "lK", "zcB", "zrB")
+    bits(both)
     TS(C("g0"), "g0", C("pf"), "pf", 16.0, 32.0, A.is_lt, A.mult)
     TS(L("lR0"), "lsB", T.rows[:, 8:16], ["rows", "zcB"], C("lR"), None, A.add)
     TS(L("lD0"), "lsB", T.rows[:, 0:4], ["rows", "zcB"], C("lD"), None, A.add)
     TS(L("lW"), "lsB", T.zer[:, 0:4], ["zer", "zcB"], C("lW"), None, A.add)
     CP(L("lK"), "lsB", C("lK"), "zcB")
+    for b in range(2):
+        QT("qcg", 128 * b, 128 * b + 128, T.cg[:, 3 - b:515 - b], "cg")
     rows_S(both)
     rows_V(both)
 
@@ -394,7 +391,7 @@ def rank_program(g, core, T, topo):
         first = firsts(parts)
         first[0]()
         unpack("qce", "qn%d" % r, ["na%d" % r, "nb%d" % r], "Fo", 1 / 128)
-        lists[0]()
+        first[1]()
         if r == 0:
             pb, pk, ends = T.pb, ["pb0", "pb1"], T.pb[:, 0:256:32]
             head = [lambda: CP(T.R[:], "R", T.pb[:].indirect(L("lR0")), pk + ["lsB"])]
@@ -403,7 +400,8 @@ def rank_program(g, core, T, topo):
             pb, pk, ends = T.pm, ["pm"], T.pm[:, 0:128:16]
             head = [lambda: TT(T.e1[:, 0:128:16], "e1", T.pb[:, 128:256:16], T.pt8[:], ["pb1", "pt8"], A.add),
                     lambda: TT(T.R[:], "R", T.e1[:].indirect(L("lR1")), T.pkr[:], ["e1", "pkr", "lsD"], A.min)]
-            fill = [lists[1], lambda: TT(ends, "pm", T.e1[:, 0:128:16], T.pb[:, 0:128:16], ["e1", "pb0"], A.min)]
+            fill = [lambda: TT(T.ck[:, 8:16], "ck1", T.fs[:, 128:256:16], T.cc[:, 40:48], ["fs1", "cc"], A.add),
+                    lambda: TT(ends, "pm", T.e1[:, 0:128:16], T.pb[:, 0:128:16], ["e1", "pb0"], A.min)]
         weave(head + [lambda: TR(T.al[:], "al", T.R[:], "R"),
                       lambda: TT(T.dif[:], "dif", pb[:].indirect(L("lD%d" % min(r, 1))), T.al[:, 0:128:2], pk + ["al", "lsB", "lsD"], A.subtract),
                       lambda: TS(T.neg[:], "neg", T.dif[:], "dif", 0.0, GONE / U, A.min, A.mult),
@@ -414,25 +412,24 @@ def rank_program(g, core, T, topo):
                       lambda: TR(T.trp[32:64, :], "trp1", T.rep[0:32, 8:40], "rep0"),
                       lambda: TS(T.Y[:, 71:72], "cap", C("fl"), ["fl", "zcA"], FAR, C("us"), A.mult, A.subtract)])
         if r == 0:
-            fill = [lists[1], lists[2], first[1], lambda: TS(T.cc[:, 24:48], "cc", T.cc[:, 0:24], "cc0", -127.5, None, A.add),
-                    lambda: TT(T.c1[:], "c1", T.fs[:, 0:256:32], T.cc[:, 24:32], ["fs0", "fs1", "cc"], A.add)]
+            fill = lists + [lambda: TS(T.cc[:, 24:48], "cc", T.cc[:, 0:24], "cc0", -127.5, None, A.add),
+                    lambda: TT(T.c1[:], "c1", T.fs[:, 0:256:32], T.cc[:, 24:32], ["fs0", "fs1", "cc"], A.add),
+                    lambda: turn("lO", "fx", "zcC", ["zrC", "zrW"])]
         else:
-            fill = [lists[2], first[1], lambda: TT(T.ck[:, 8:16], "ck1", T.fs[:, 128:256:16], T.cc[:, 40:48], ["fs1", "cc"], A.add),
-                    lambda: TT(T.c1[:], "c1", T.ck[:, 0:8], T.ck[:, 8:16], ["ck0", "ck1"], A.min)]
+            fill = lists + [lambda: TT(T.c1[:], "c1", T.ck[:, 0:8], T.ck[:, 8:16], ["ck0", "ck1"], A.min)]
         weave(level(32, 64, "rep1") + [lambda: (TR(T.trp[64:96, :], "trp2", T.rep[32:64, 8:40], "rep1"), TR(T.trp[96:128, :], "trp2", T.rep[32:64, 8:40], "rep1"))]
               + level(64, 128, "rep2") + [lambda: TR(T.trf[:, 0:32], "trf", T.rep[:, 8:40], ["rep0", "rep1", "rep2"])],
               fill + [lambda: TS(T.pen[:], "pen", T.c4k[:], ["c4k", "fl"], C("fl"), 127.5 - 4096.0, A.mult, A.add)])
         ACT(T.dr[:], "dr", T.dT[:].indirect(T.LG[:, 0:16]), ["dT", "LG0", "LG1"])
         ACT(T.dr[:, 31:256:32], "dr", T.dr[:, 31:256:32], "dr", AF.Identity, bias=-DROP)
-        unpack("qcg", "qa%d" % r, None, "G", 1 / 256)
-        unpack("qce", "qa%d" % r, None, "F", 1 / 256, "T")
+        key = T.key[:, 16:272]
         if r == 0:
-            turn("lO", "fx", "zcC", ["zrC", "zrW"])
-            FILL(T.rsv[:], "rsv0", 1.0)
             for n in ("lO", "l2", "lL", "lS"):
                 CP(L(n), "lsC", C(n), "zcC")
-            FILL(T.rsv[:, 0:256 * NV:256], "rsv", 0.0, "rsv0")
-        key = T.key[:, 16:272]
+            for b in range(2, 4):
+                QT("qcg", 128 * b, 128 * b + 128, T.cg[:, 3 - b:515 - b], "cg")
+        unpack("qcg", "qa%d" % r, None, "G", 1 / 256, "T")
+        unpack("qce", "qa%d" % r, None, "F", 1 / 256, "T", 4)
         weave([lambda: TT(T.wr[:], "wr", T.trf[:].indirect(T.LG[:, 0:16]), T.hrow[:], ["trf", "trfc", "LG0", "LG1", "hrow"], A.add),
                lambda: SCAN(key, "key", T.wr[:], T.dr[:], ["wr", "dr"], -1.0, A.max, A.add),
                lambda: TR(T.kt[:, 0:256], "kt0", key, "key")],
@@ -472,10 +469,13 @@ def rank_program(g, core, T, topo):
             if k == 0:
                 ACT(T.prb[:], "prb", T.prf[:], "prf", AF.Abs)
                 for b in range(NV):
-                    TS(T.jv[:, 256 * b:256 * b + 256], "jv", key, ["key", "own1"], T.own[:, 16 + b:17 + b], None, A.is_lt)
-                SCAN(T.jo[:], "jo", T.rsv[:], T.jv[:], ["rsv", "jv"], 0.0, A.mult, A.add)
-                TS(T.acc[:, 1:2 * NV:2], "acc0V", T.jo[:, 255:256 * NV:256], "jo", 2.0, -255.0, A.mult, A.add)
-        unpack("qce", "qa%d" % r, None, "F", 1 / 256, "S")
+                    TS(T.jv[:, 256 * b:256 * b + 256], "jv%d" % b, key, ["key", "own1"], T.own[:, 16 + b:17 + b], None, A.is_lt)
+                for b in range(NV):
+                    a = slice(256 * b, 256 * b + 256)
+                    SCAN(T.jo[:, a], "jo", T.jv[:, a], T.jv[:, a], "jv%d" % b, -255.0, A.add, A.add)
+                CP(T.acc[:, 1:2 * NV:2], "acc0V", T.jo[:, 255:256 * NV:256], "jo")
+        unpack("qcg", "qa%d" % r, None, "G", 1 / 256, "S")
+        unpack("qce", "qa%d" % r, None, "F", 1 / 256, "S", 4)
         for k in range(len(PIECES)):
             scatter(k)
         ll = T.ll[:, 16 * r:16 * r + 16]
@@ -490,8 +490,8 @@ def rank_program(g, core, T, topo):
         CP(T.lk[:], "lk", T.wk[:].indirect(L("lO")), ["wk", "lsC"])
         for t in range(4):
             src = T.Fo[:, 256 * t:256 * t + 256].indirect(T.lk[:, 0:8])
-            (CP if t < 2 else ACT)(T.X[:, t:512:4], "X0" + "VS"[t // 2], src, ["Fo%d" % t, "lk"])
-        QT("na%d" % (r + 1), 0, 128, T.X[:, 0:512], ["X0V", "X0S"])
+            CP(T.X[:, t:512:4], "X0", src, ["Fo%d" % t, "lk"])
+        QT("na%d" % (r + 1), 0, 128, T.X[:, 0:512], "X0")
         if last:
             MM(4, 128, "qv", 0, "na3")
             ACT(T.opw[:], "opw", T.win[:].indirect(L("lP")), ["win", "lsE"])
@@ -506,16 +506,9 @@ def rank_program(g, core, T, topo):
             bits((0,))
             if r == 0:
                 FILL(T.r16[:, 0:128:16], "r16", 0.0, "r160")
-                TT(T.ng1[:], "ng1", T.dl2[:], T.ngn[:], ["dl2", "ngn"], A.add)
-            else:
-                TS(L("lP"), "lsE", T.rows[:, 16:32], ["rows2", "zcC"], C("lL"), None, A.add)
-                TS(L("lF"), "lsE", T.rows[:, 32:48], ["rows2", "zcA"], C("jj"), None, A.add)
-                QT("qv", 0, 128, T.vs[:], "vs")
-            rows_V((0,))
-            SCAN(T.pt[:], "pt", T.r16[:], T.ps6[:, 0:128], ["r16", "ps6"], 0.0, A.mult, A.add)
         z = "qz%d" % r
         for t in range(4):
-            ACT(T.gz[:, 128 * t:128 * t + 128], "gz%d" % t, T.G[:, 256 * t:256 * t + 256].indirect(T.la[:, 16 * r + 8:16 * r + 16]), ["G%d" % t, "la%d" % r])
+            (ACT if t else CP)(T.gz[:, 128 * t:128 * t + 128], "gz%d" % t, T.G[:, 256 * t:256 * t + 256].indirect(T.la[:, 16 * r + 8:16 * r + 16]), ["G%d" % t, "la%d" % r])
         for t in range(4):
             TT(T.Z[:, t:512:4], "Z", T.F[:, 256 * t:256 * t + 256].indirect(T.la[:, 16 * r:16 * r + 8]), T.gz[:, 128 * t:128 * t + 128],
                ["F%d" % t, "la%d" % r, "gz%d" % t], A.add)
@@ -527,16 +520,18 @@ def rank_program(g, core, T, topo):
             CP(T.ysb[:, :, 0:16], "ysb", T.ps4[:, 0:128], "ps4")
         else:
             rows_S((0,))
+            rows_V((0,))
+            SCAN(T.pt[:], "pt", T.r16[:], T.ps6[:, 0:128], ["r16", "ps6"], 0.0, A.mult, A.add)
             kept, first = list_V((0,)), firsts((0,))
-            TS(T.pt8[:], "pt8", T.pt[:, 15:128:16], "pt", 16 * U, None, A.add)
             first[0]()
             first[1]()
+            TS(T.pt8[:], "pt8", T.pt[:, 15:128:16], "pt", 16 * U, None, A.add)
             kept[0]()
             kept[1]()
             CP(T.pkr[:], "pkr", T.pb[:, 0:128].indirect(L("lR1")), ["pb0", "lsD"])
         for b in range(4):
             o, i = T.X[:, 512 + b:1024:4], T["ps%d" % b][:, 0:128]
-            if b % 2:
+            if b >= 2:
                 TS(o, "X1V", i, "ps%d" % b, 0.0078125, None, A.mult)
             else:
                 ACT(o, "X1S", i, "ps%d" % b, scale=0.0078125)
@@ -546,7 +541,14 @@ def rank_program(g, core, T, topo):
             send_codes(r + 1)
             kept[2]()
             TT(T.ck[:, 0:8], "ck0", T.fs[:, 0:128:16], T.cc[:, 32:40], ["fs0", "cc"], A.add)
+            if r == 1:
+                TS(L("lP"), "lsE", T.rows[:, 16:32], ["rows2", "zcC"], C("lL"), None, A.add)
+                TS(L("lF"), "lsE", T.rows[:, 32:48], ["rows2", "zcA"], C("jj"), None, A.add)
             bits((1,))
+            if r == 0:
+                TT(T.ng1[:], "ng1", T.dl2[:], T.ngn[:], ["dl2", "ngn"], A.add)
+            else:
+                QT("qv", 0, 128, T.vs[:], "vs")
             rows_S((1,))
             rows_V((1,))
     MM(5, 128, "qv", 0, "nb3")

@@ -1,13 +1,14 @@
 from concourse.mybir import dt, AluOpType as A, AxisListType, ActivationFunctionType as AF
 
 NR = 3
-U = 2048.0
+U = 8.0
 GONE = float(1 << 23)
 DROP = float(1 << 22)
 FAR = float(1 << 30)
 ROUND256 = 1.5 * float(1 << 31)
-PIECES = ((0, 1, 2, 3, 4, 5), (6, 7))
-NV = 4
+PIECES = ((0, 1, 2, 3, 4, 5, 6, 7),)
+ABS_AT = 10
+NV = 6
 COLS = ["jj", "us", "w2", "lR", "lD", "lW", "lK", "lO", "l2", "lL", "lS", "xc", "fx"]
 LISTS = {"lO": (0, 1), "lL": (2, 1), "lS": (4, 1), "lK": (6, 1), "lW": (8, 4), "lD0": (12, 4), "lR0": (16, 8), "lP": (24, 16), "lF": (40, 16),
          "l2": (56, 1), "lD1": (58, 4), "lR1": (62, 8)}
@@ -28,7 +29,7 @@ for _n, _k, _d in (
         ("ls", 70, "uint16"), ("rows", 64, "float32"), ("cc", 48, "float32"),
         ("crow", 384, "float32"), ("wrow", 384, "bfloat16"), ("r16", 128, "bfloat16"), ("dT", 48, "float32"),
         ("hrow", 256, "float32"), ("rst", 64, "float32"), ("e40", 40, "float32"),
-        ("crep", 32, "float32"), ("c4k", 2, "float32"), ("rsv", 256 * NV, "bfloat16"),
+        ("crep", 32, "float32"), ("c4k", 2, "float32"),
         ("ng0", 256, "bfloat16"), ("ng1", 256, "bfloat16"), ("ngn", 256, "bfloat16"), ("dlt", 256, "bfloat16"), ("dl2", 256, "bfloat16"),
         ("B", 1024, "bfloat16"), ("dz", 256, "bfloat16"), ("ab", 256, "bfloat16"), ("dr", 256, "float32"),
         ("sr", 288, "bfloat16"), ("st", 544, "bfloat16"), ("LG", 32, "uint16"),
@@ -36,7 +37,7 @@ for _n, _k, _d in (
         ("pt8", 8, "float32"), ("pkr", 128, "bfloat16"), ("ck", 16, "float32"), ("R", 128, "bfloat16"), ("al", 128, "bfloat16"),
         ("dif", 64, "float32"), ("neg", 64, "float32"), ("MT", 64, "float32"), ("yi", 64, "float32"), ("Y", 320, "float32"),
         ("rep", 40, "float32"), ("trp", 32, "float32"), ("trf", 48, "float32"),
-        ("c1", 8, "float32"), ("k2", 8, "float32"), ("pen", 2, "float32"), ("rp2", 32, "float32"), ("tr2", 48, "float32"),
+        ("c1", 8, "float32"), ("k1", 8, "float32"), ("k16", 256, "uint16"), ("k2", 8, "float32"), ("pen", 2, "float32"), ("rp2", 32, "float32"), ("tr2", 48, "float32"),
         ("wr", 256, "float32"), ("key", 288, "float32"), ("kt", 544, "float32"), ("own", 32, "float32"),
         ("js", 256 * (16 - NV), "bfloat16"), ("jv", 256 * NV, "bfloat16"), ("jo", 256 * NV, "bfloat16"),
         ("acc", 16 * len(PIECES), "float32"), ("oa", 16 * len(PIECES), "float32"), ("oq", 16 * len(PIECES), "int32"),
@@ -319,7 +320,7 @@ def rank_program(g, core, T, topo):
         n, o = dims(parts)
         TS(T.B[:, 512 * o:512 * o + 4 * n:4], keys("B", parts), T.ps4[:, 0:n], "ps4", 0.0, None, A.is_gt)
         QT("qb%d" % o, 0, n, T.B[:, 512 * o:512 * o + 4 * n], keys("B", parts), keys("qb", parts))
-        for bank, c in ((6, 0), (7, 128)):
+        for bank, c in ((5 + o, 0), (7, 128)):
             MM(bank, n, "qcs", c, "qb%d" % o, keys("qb", parts))
 
     def rows_S(parts):
@@ -329,8 +330,8 @@ def rank_program(g, core, T, topo):
     def rows_V(parts):
         n, o = dims(parts)
         c = 0 if n == 256 else 256
-        TS(T.ab[:, 128 * o:128 * o + n], keys("ab", parts), T.ps6[:, 0:n], ["ps6", "nb"], C("nb"), GONE, A.not_equal, A.mult)
-        TT(T.dz[:, 128 * o:128 * o + n], keys("dz", parts), T.ps6[:, 0:n], T.crow[:, c:c + n], ["ps6", "crow"], A.add)
+        TS(T.ab[:, 128 * o:128 * o + n], keys("ab", parts), T["ps%d" % (5 + o)][:, 0:n], ["ps%d" % (5 + o), "nb"], C("nb"), GONE, A.not_equal, A.mult)
+        TT(T.dz[:, 128 * o:128 * o + n], keys("dz", parts), T["ps%d" % (5 + o)][:, 0:n], T.crow[:, c:c + n], ["ps%d" % (5 + o), "crow"], A.add)
 
     def firsts(parts):
         n, o = dims(parts)
@@ -419,7 +420,8 @@ def rank_program(g, core, T, topo):
             fill = lists + [lambda: TT(T.c1[:], "c1", T.ck[:, 0:8], T.ck[:, 8:16], ["ck0", "ck1"], A.min)]
         weave(level(32, 64, "rep1") + [lambda: (TR(T.trp[64:96, :], "trp2", T.rep[32:64, 8:40], "rep1"), TR(T.trp[96:128, :], "trp2", T.rep[32:64, 8:40], "rep1"))]
               + level(64, 128, "rep2") + [lambda: TR(T.trf[:, 0:32], "trf", T.rep[:, 8:40], ["rep0", "rep1", "rep2"])],
-              fill + [lambda: TS(T.pen[:], "pen", T.c4k[:], ["c4k", "fl"], C("fl"), 127.5 - 4096.0, A.mult, A.add)])
+              fill + [lambda: TS(T.pen[:], "pen", T.c4k[:], ["c4k", "fl"], C("fl"), 127.5 - 4096.0, A.mult, A.add)] + [lambda: None] * (6 - len(fill))
+              + [lambda: TS(T.k1[:], "k1", T.Y[:, 7:64:8], "Y", 256.0, None, A.mult)])
         ACT(T.dr[:], "dr", T.dT[:].indirect(T.LG[:, 0:16]), ["dT", "LG0", "LG1"])
         ACT(T.dr[:, 31:256:32], "dr", T.dr[:, 31:256:32], "dr", AF.Identity, bias=-DROP)
         key = T.key[:, 16:272]
@@ -433,7 +435,7 @@ def rank_program(g, core, T, topo):
         weave([lambda: TT(T.wr[:], "wr", T.trf[:].indirect(T.LG[:, 0:16]), T.hrow[:], ["trf", "trfc", "LG0", "LG1", "hrow"], A.add),
                lambda: SCAN(key, "key", T.wr[:], T.dr[:], ["wr", "dr"], -1.0, A.max, A.add),
                lambda: TR(T.kt[:, 0:256], "kt0", key, "key")],
-              [lambda: TT(T.k2[:], "k2", T.Y[:, 7:64:8], T.c1[:], ["Y", "c1"], A.add),
+              [lambda: TT(T.k2[:], "k2", T.k1[:], T.c1[:], ["k1", "c1"], A.add),
                lambda: RED(C("km"), "km", T.k2[:], "k2", A.min),
                lambda: TS(C("rn"), "rn", C("km"), "km", ROUND256, -ROUND256, A.add, A.add)])
         TS(T.own[:, 0:16], "own0", T.kt[:, 0:256].indirect(L("lO")), ["kt0", "lsC", "zcC"], C("fx"), None, A.add)
@@ -442,6 +444,7 @@ def rank_program(g, core, T, topo):
         TR(T.kt[:, 256:544], "kt1", T.key[:], "key")
         TR(T.tr2[:, 0:32], "tr2", T.rp2[:], "rp2")
         CP(T.own[:, 16:32], "own1", T.kt[:, 256:544].indirect(L("l2")), ["kt1", "lsC"])
+        CP(T.k16[:], "k16", key, "key")
         ng = ("ng0", "ng1")[min(r, 1)]
         TT(T.prf[:], "prf", T.tr2[:].indirect(T.LG[:, 0:16]), T[ng][:], ["tr2", "tr2c", "LG0", "LG1", ng], A.max)
         nj = [0]
@@ -452,32 +455,33 @@ def rank_program(g, core, T, topo):
             ACT(T.js[:, j:j + 256], "acc%dS" % k, key, ["key", "own%d" % w], AF.Sign, bias=T.own[:, 16 * w + b:16 * w + b + 1], scale=-1.0,
                 accum_out=T.acc[:, 16 * k + 2 * i + w:16 * k + 2 * i + w + 1])
 
-        def scatter(k):
-            n, w0, a = 2 * len(PIECES[k]), 2 * PIECES[k][0], slice(16 * k, 16 * k + 16)
+        def places(k):
+            a = slice(16 * k, 16 * k + 16)
             ak = ["acc%dV" % k, "acc%dS" % k, "lsC"]
-            TS(T.oa[:, a], "oa%d" % k, T.acc[:, a].indirect(L("lS")), ak, 16 / 255, None, A.mult)
-            TS(T.oq[:, a], "oq%d" % k, T.acc[:, a].indirect(L("lS")), ak, 1 / 16, 15.5, A.mult, A.add)
-            TT(T.od[:, a], "od%d" % k, T.oa[:, a], T.oq[:, a], ["oa%d" % k, "oq%d" % k], A.subtract)
-            TS(T.pl[:, a], "pl%d" % k, T.od[:, a], ["od%d" % k, "zcC"], 255.0, C("xc"), A.mult, A.add)
-            emit("V", lambda: v.tensor_copy(T.win[:].indirect(T.pl[:, 16 * k:16 * k + n]), T.prb[:, 16 * w0:16 * (w0 + n)]), ["pl%d" % k, "prb", "win"], ["win"])
+            return [lambda: (TS(T.oa[:, a], "oa%d" % k, T.acc[:, a].indirect(L("lS")), ak, 16 / 255, None, A.mult),
+                             TS(T.oq[:, a], "oq%d" % k, T.acc[:, a].indirect(L("lS")), ak, 1 / 16, 15.5, A.mult, A.add)),
+                    lambda: TT(T.od[:, a], "od%d" % k, T.oa[:, a], T.oq[:, a], ["oa%d" % k, "oq%d" % k], A.subtract),
+                    lambda: TS(T.pl[:, a], "pl%d" % k, T.od[:, a], ["od%d" % k, "zcC"], 255.0, C("xc"), A.mult, A.add)]
 
-        for k, piece in enumerate(PIECES):
-            for w in range(2):
-                for i, b in enumerate(piece):
-                    if w == 0 or b >= NV:
-                        unit_S(k, i, b, w)
-            if k == 0:
-                ACT(T.prb[:], "prb", T.prf[:], "prf", AF.Abs)
-                for b in range(NV):
-                    TS(T.jv[:, 256 * b:256 * b + 256], "jv%d" % b, key, ["key", "own1"], T.own[:, 16 + b:17 + b], None, A.is_lt)
-                for b in range(NV):
-                    a = slice(256 * b, 256 * b + 256)
-                    SCAN(T.jo[:, a], "jo", T.jv[:, a], T.jv[:, a], "jv%d" % b, -255.0, A.add, A.add)
-                CP(T.acc[:, 1:2 * NV:2], "acc0V", T.jo[:, 255:256 * NV:256], "jo")
+        def scatter(k, a, b):
+            o = 16 * k + 2 * (a - PIECES[k][0])
+            return lambda: emit("V", lambda: v.tensor_copy(T.win[:].indirect(T.pl[:, o:o + 2 * (b - a)]), T.prb[:, 32 * a:32 * b]),
+                                ["pl%d" % k, "prb", "win"], ["win"])
+
+        units = [(k, i, b, w) for k, piece in enumerate(PIECES) for w in range(2) for i, b in enumerate(piece) if w == 0 or b >= NV]
+        for u in units:
+            unit_S(*u)
+        ACT(T.prb[:], "prb", T.prf[:], "prf", AF.Abs)
         unpack("qcg", "qa%d" % r, None, "G", 1 / 256, "S")
         unpack("qce", "qa%d" % r, None, "F", 1 / 256, "S", 4)
-        for k in range(len(PIECES)):
-            scatter(k)
+        for b in range(NV):
+            TS(T.jv[:, 256 * b:256 * b + 256], "jv%d" % b, T.k16[:], ["k16", "own1"], T.own[:, 16 + b:17 + b], None, A.is_lt)
+        for b in range(NV):
+            a = slice(256 * b, 256 * b + 256)
+            SCAN(T.jo[:, a], "jo", T.jv[:, a], T.jv[:, a], "jv%d" % b, -255.0, A.add, A.add)
+        CP(T.acc[:, 1:2 * NV:2], "acc0V", T.jo[:, 255:256 * NV:256], "jo")
+        weave(places(0), [])
+        scatter(0, 0, 8)()
         ll = T.ll[:, 16 * r:16 * r + 16]
         TR(T.wt[:], "wt", T.win[:, 0:256], "win")
         CP(ll, "ll%d" % r, T.wt[:].indirect(L("lL")), ["wt", "lsC"])
@@ -491,6 +495,11 @@ def rank_program(g, core, T, topo):
         for t in range(4):
             src = T.Fo[:, 256 * t:256 * t + 256].indirect(T.lk[:, 0:8])
             CP(T.X[:, t:512:4], "X0", src, ["Fo%d" % t, "lk"])
+        if r == 0:
+            ACT(T.dl2[:], "dl2", T.dlt[:], ["dlt", "m2"], scale=C("m2"))
+        z = "qz%d" % r
+        for t in range(4):
+            (ACT if t else CP)(T.gz[:, 128 * t:128 * t + 128], "gz%d" % t, T.G[:, 256 * t:256 * t + 256].indirect(T.la[:, 16 * r + 8:16 * r + 16]), ["G%d" % t, "la%d" % r])
         QT("na%d" % (r + 1), 0, 128, T.X[:, 0:512], "X0")
         if last:
             MM(4, 128, "qv", 0, "na3")
@@ -498,17 +507,6 @@ def rank_program(g, core, T, topo):
             emit("Y", lambda: g.sync.dma_start(T.op[:], T.opw[2:128:16, :]), ["opw"], ["op"], dma=True)
         else:
             scores(r + 1, (0,))
-            if r == 0:
-                TS(L("lR1"), "lsD", L("lR0"), "lsB", 0.5, None, A.mult)
-                TS(L("lD1"), "lsD", L("lD0"), "lsB", 0.5, None, A.mult)
-                FILL(T.r16[:], "r160", 1.0)
-                ACT(T.dl2[:], "dl2", T.dlt[:], ["dlt", "m2"], scale=C("m2"))
-            bits((0,))
-            if r == 0:
-                FILL(T.r16[:, 0:128:16], "r16", 0.0, "r160")
-        z = "qz%d" % r
-        for t in range(4):
-            (ACT if t else CP)(T.gz[:, 128 * t:128 * t + 128], "gz%d" % t, T.G[:, 256 * t:256 * t + 256].indirect(T.la[:, 16 * r + 8:16 * r + 16]), ["G%d" % t, "la%d" % r])
         for t in range(4):
             TT(T.Z[:, t:512:4], "Z", T.F[:, 256 * t:256 * t + 256].indirect(T.la[:, 16 * r:16 * r + 8]), T.gz[:, 128 * t:128 * t + 128],
                ["F%d" % t, "la%d" % r, "gz%d" % t], A.add)
@@ -519,16 +517,17 @@ def rank_program(g, core, T, topo):
         if last:
             CP(T.ysb[:, :, 0:16], "ysb", T.ps4[:, 0:128], "ps4")
         else:
-            rows_S((0,))
-            rows_V((0,))
-            SCAN(T.pt[:], "pt", T.r16[:], T.ps6[:, 0:128], ["r16", "ps6"], 0.0, A.mult, A.add)
-            kept, first = list_V((0,)), firsts((0,))
-            first[0]()
-            first[1]()
-            TS(T.pt8[:], "pt8", T.pt[:, 15:128:16], "pt", 16 * U, None, A.add)
-            kept[0]()
-            kept[1]()
-            CP(T.pkr[:], "pkr", T.pb[:, 0:128].indirect(L("lR1")), ["pb0", "lsD"])
+            bits((0,))
+            if r == 0:
+                FILL(T.r16[:], "r160", 1.0)
+                TS(L("lR1"), "lsD", L("lR0"), "lsB", 0.5, None, A.mult)
+                TS(L("lD1"), "lsD", L("lD0"), "lsB", 0.5, None, A.mult)
+                FILL(T.r16[:, 0:128:16], "r16", 0.0, "r160")
+                TT(T.ng1[:], "ng1", T.dl2[:], T.ngn[:], ["dl2", "ngn"], A.add)
+            else:
+                TS(L("lP"), "lsE", T.rows[:, 16:32], ["rows2", "zcC"], C("lL"), None, A.add)
+                TS(L("lF"), "lsE", T.rows[:, 32:48], ["rows2", "zcA"], C("jj"), None, A.add)
+                QT("qv", 0, 128, T.vs[:], "vs")
         for b in range(4):
             o, i = T.X[:, 512 + b:1024:4], T["ps%d" % b][:, 0:128]
             if b >= 2:
@@ -539,16 +538,19 @@ def rank_program(g, core, T, topo):
         if not last:
             scores(r + 1, (1,))
             send_codes(r + 1)
+            rows_S((0,))
+            rows_V((0,))
+            SCAN(T.pt[:], "pt", T.r16[:], T.ps5[:, 0:128], ["r16", "ps5"], 0.0, A.mult, A.add)
+            kept, first = list_V((0,)), firsts((0,))
+            first[0]()
+            bits((1,))
+            first[1]()
+            TS(T.pt8[:], "pt8", T.pt[:, 15:128:16], "pt", 16 * U, None, A.add)
+            kept[0]()
+            kept[1]()
+            CP(T.pkr[:], "pkr", T.pb[:, 0:128].indirect(L("lR1")), ["pb0", "lsD"])
             kept[2]()
             TT(T.ck[:, 0:8], "ck0", T.fs[:, 0:128:16], T.cc[:, 32:40], ["fs0", "cc"], A.add)
-            if r == 1:
-                TS(L("lP"), "lsE", T.rows[:, 16:32], ["rows2", "zcC"], C("lL"), None, A.add)
-                TS(L("lF"), "lsE", T.rows[:, 32:48], ["rows2", "zcA"], C("jj"), None, A.add)
-            bits((1,))
-            if r == 0:
-                TT(T.ng1[:], "ng1", T.dl2[:], T.ngn[:], ["dl2", "ngn"], A.add)
-            else:
-                QT("qv", 0, 128, T.vs[:], "vs")
             rows_S((1,))
             rows_V((1,))
     MM(5, 128, "qv", 0, "nb3")
@@ -556,11 +558,11 @@ def rank_program(g, core, T, topo):
     emit("V", lambda: v.tensor_copy(oc.bitcast(dt.uint32), ic.bitcast(dt.uint32).indirect(L("lF"))), ["na3", "nb3", "lsE"], ["qp"])
     emit("S", lambda: s.activation(osc, isc.indirect(L("lF")), AF.Copy), ["na3", "nb3", "lsE"], ["sqp"])
     emit("Y", lambda: g.sync.dma_start(T.oc[:, 0:1024], oc.bitcast(dt.uint8)), ["qp"], ["oc"], dma=True)
+    ACT(T.ysb[:, :, 16:32], "ysb1", T.ps5[:, 0:128], "ps5")
+    emit("S", lambda: s.dma_start(T.y[:], T.ysb[:]), ["ysb", "ysb1"], ["y"], dma=True)
     for k in range(4):
-        emit("Y" if k < 2 else "S", lambda: (g.sync if k < 2 else s).dma_start(T.osc[4 * k:4 * k + 4, 0:256], T.sqp[32 * k:32 * k + 4, 0:256]),
+        emit("Y" if k < 3 else "S", lambda: (g.sync if k < 3 else s).dma_start(T.osc[4 * k:4 * k + 4, 0:256], T.sqp[32 * k:32 * k + 4, 0:256]),
              ["sqp"], ["osc%d" % k], dma=True)
-    CP(T.ysb[:, :, 16:32], "ysb", T.ps5[:, 0:128], "ps5")
-    emit("Y", lambda: g.sync.dma_start(T.y[:], T.ysb[:]), ["ysb"], ["y"], dma=True)
     for k in range(nd[0]):
         g.wait_ge(T.sem["ld%d" % k], 16)
     g.wait_ge(T.sem.sent, 3 * NR * n_out)

@@ -7,12 +7,13 @@ DROP = float(1 << 22)
 FAR = float(1 << 30)
 ROUND256 = 1.5 * float(1 << 31)
 PIECES = ((0, 1, 2, 3, 4, 5, 6, 7),)
-ABS_AT = 10
-NV = 6
-COLS = ["jj", "us", "w2", "lR", "lD", "lW", "lK", "lO", "l2", "lL", "lS", "xc", "fx"]
-LISTS = {"lO": (0, 1), "lL": (2, 1), "lS": (4, 1), "lK": (6, 1), "lW": (8, 4), "lD0": (12, 4), "lR0": (16, 8), "lP": (24, 16), "lF": (40, 16),
-         "l2": (56, 1), "lD1": (58, 4), "lR1": (62, 8)}
-SMALL = ["pf", "wu", "g0", "nb", "m2", "mn", "fl", "km", "rn"]
+QNA = 0
+NV = 8
+COLS = ["jj", "us", "w2", "fx", "lR", "lD", "lW", "lK", "lO", "l2", "lL", "lS"]
+LISTS = {"lO": (0, 1), "l2": (2, 1), "lL": (4, 1), "lS": (6, 1), "lW": (8, 4), "lD0": (12, 4), "lR0": (16, 8), "lP": (24, 16), "lF": (40, 16),
+         "lK": (56, 1), "lD1": (58, 4), "lR1": (62, 8)}
+SMALL = ["pf", "wu", "g0", "nb", "m2", "mn", "fl", "km", "rn", "xc"]
+RST, E40, TRP, TRF, RP2, TR2 = 0, 64, 104, 136, 184, 216
 
 SCRATCH = {}
 
@@ -28,23 +29,22 @@ for _n, _k, _d in (
         ("zr", 32 * len(COLS), "float32"), ("zc", 32 * len(COLS), "float32"), ("sm", 8 * len(SMALL), "float32"),
         ("ls", 70, "uint16"), ("rows", 64, "float32"), ("cc", 48, "float32"),
         ("crow", 384, "float32"), ("wrow", 384, "bfloat16"), ("r16", 128, "bfloat16"), ("dT", 48, "float32"),
-        ("hrow", 256, "float32"), ("rst", 64, "float32"), ("e40", 40, "float32"),
-        ("crep", 32, "float32"), ("c4k", 2, "float32"),
+        ("hrow", 256, "float32"), ("zf", 264, "float32"), ("crep", 32, "float32"), ("cra", 128, "float32"),
         ("ng0", 256, "bfloat16"), ("ng1", 256, "bfloat16"), ("ngn", 256, "bfloat16"), ("dlt", 256, "bfloat16"), ("dl2", 256, "bfloat16"),
         ("B", 1024, "bfloat16"), ("dz", 256, "bfloat16"), ("ab", 256, "bfloat16"), ("dr", 256, "float32"),
         ("sr", 288, "bfloat16"), ("st", 544, "bfloat16"), ("LG", 32, "uint16"),
         ("pb", 256, "bfloat16"), ("fs", 256, "bfloat16"), ("e1", 128, "bfloat16"), ("pm", 128, "bfloat16"), ("pt", 128, "float32"),
-        ("pt8", 8, "float32"), ("pkr", 128, "bfloat16"), ("ck", 16, "float32"), ("R", 128, "bfloat16"), ("al", 128, "bfloat16"),
+        ("pt8", 24, "float32"), ("pkr", 128, "bfloat16"), ("ck", 16, "float32"), ("R", 128, "bfloat16"), ("al", 128, "bfloat16"),
         ("dif", 64, "float32"), ("neg", 64, "float32"), ("MT", 64, "float32"), ("yi", 64, "float32"), ("Y", 320, "float32"),
-        ("rep", 40, "float32"), ("trp", 32, "float32"), ("trf", 48, "float32"),
-        ("c1", 8, "float32"), ("k1", 8, "float32"), ("k16", 256, "uint16"), ("k2", 8, "float32"), ("pen", 2, "float32"), ("rp2", 32, "float32"), ("tr2", 48, "float32"),
-        ("wr", 256, "float32"), ("key", 288, "float32"), ("kt", 544, "float32"), ("own", 32, "float32"),
+        ("rep", 40, "float32"), ("c1", 8, "float32"), ("k1", 8, "float32"), ("k16", 256, "uint16"), ("k2", 8, "float32"), ("pen", 4, "float32"),
+        ("lf", 16 * NR, "uint16"), ("fa", 16 * NR, "uint16"),
+        ("wr", 256, "float32"), ("key", 288, "float32"), ("kt", 544, "float32"), ("own", 32, "float32"), ("ow2", 32, "bfloat16"),
         ("js", 256 * (16 - NV), "bfloat16"), ("jv", 256 * NV, "bfloat16"), ("jo", 256 * NV, "bfloat16"),
         ("acc", 16 * len(PIECES), "float32"), ("oa", 16 * len(PIECES), "float32"), ("oq", 16 * len(PIECES), "int32"),
         ("od", 16 * len(PIECES), "float32"), ("pl", 16 * len(PIECES), "uint16"),
-        ("prf", 256, "bfloat16"), ("prb", 256, "bfloat16"), ("win", 272, "bfloat16"), ("wt", 256, "bfloat16"), ("wk", 256, "bfloat16"),
+        ("prb", 256, "bfloat16"), ("win", 272, "bfloat16"), ("wt", 256, "bfloat16"), ("wk", 256, "bfloat16"),
         ("ll", 16 * NR, "uint16"), ("la", 16 * NR, "uint16"), ("lk", 16, "uint16"), ("opw", 256, "float32"),
-        ("Fo", 1024, "bfloat16"), ("F", 1024, "bfloat16"), ("G", 1024, "bfloat16"), ("gz", 512, "bfloat16"), ("Z", 512, "bfloat16"),
+        ("Fo", 1024, "bfloat16"), ("F", 1088, "bfloat16"), ("G", 1088, "bfloat16"), ("gz", 512, "bfloat16"), ("Z", 512, "bfloat16"),
         ("X", 1024, "bfloat16"), ("ysb", (8, 32), "float32")):
     _b(_n, _k, _d)
 for _n, _k in (("qn", 256 * (NR + 1)), ("qa", 256 * NR), ("qp", 256), ("qu", 128), ("qv", 128), ("qw", 512), ("qc", 1280), ("qb", 256),
@@ -53,7 +53,7 @@ for _n, _k in (("qn", 256 * (NR + 1)), ("qa", 256 * NR), ("qp", 256), ("qu", 128
     _b("s" + _n, _k, "uint8")
 for _k in range(8):
     SCRATCH["ps%d" % _k] = ("psum", [128, 512], "float32")
-SEMAPHORES = (["cV", "cS", "cT", "cG", "sent"] + ["arc%d" % k for k in range(NR)] + ["arl%d" % k for k in range(NR)]
+SEMAPHORES = (["cV", "cS", "cT", "cG", "sent"] + ["arc%d" % k for k in range(NR)] + ["arl%d" % k for k in range(NR)] + ["arf%d" % k for k in range(NR)]
               + ["ld%d" % k for k in range(16)])
 
 
@@ -215,22 +215,24 @@ def rank_program(g, core, T, topo):
         g.remote_dma(asc, zs, T.sem["arc%d" % r], T.sem.sent, pid, rid, mask)
         landed("arc%d" % r, 2 * n_in, ["qa%d" % r])
 
-    emit("Y", lambda: g.sync.dma_start(T.xs[:], T.x[:]), [], ["xs"], dma=True)
+    emit("Y", lambda: g.sync.dma_start(T.xs[:, 0:512], T.x[:, 0:512]), [], ["xs0"], dma=True)
     emit("S", lambda: s.dma_start(T.us[:], T.u[:]), [], ["us"], dma=True)
-    emit("Y", lambda: g.sync.dma_start(T.qw[:, 0:512].bitcast(dt.uint8), T.wc[:, 0:2048]), [], ["qw"], dma=True)
+    emit("Y", lambda: g.sync.dma_start(T.xs[:, 512:1024], T.x[:, 512:1024]), [], ["xs1"], dma=True)
+    emit("Y", lambda: g.sync.dma_start(T.qw[:, 0:512].bitcast(dt.uint8), T.wc[:, 0:2048]), ["xs0", "xs1", "us"], ["qw"], dma=True)
     emit("Y", lambda: g.sync.dma_start(T.sqw[:, 0:512], T.ws[:, 0:512]), [], ["sqw"], dma=True)
     emit("Y", lambda: g.sync.dma_start(T.vs[:], T.v[:]), [], ["vs"], dma=True)
 
     FILL(T.one[:], "one", 128.0)
     FILL(T.zer[:], "zer", 0.0)
-    FILL(row("w2"), "zr0", 0.0)
+    FILL(row("w2", 0, 64), "zr0", 0.0)
     IOTA(row("jj"), "zrA", [[0, 2], [1, 16]], 0)
     IOTA(row("us"), "zrA", [[0, 2], [int(U), 8], [0, 2]], int(U))
-    IOTA(T.vg[:], "vg", [[-16, 8], [0, 16]], 0, 1)
-    IOTA(T.vk[:], "vk", [[-16, 4], [0, 32]], 0, 1)
     AFF(T.idn[:], "idn", T.one[:], "one", [[-1, 128]], A.is_equal, 0, 1)
-    AFF(T.prm[:], "prm0", T.one[:], "one", [[-16, 4], [0, 2], [-1, 16]], A.is_equal, 0, 1)
-    AFF(T.prm[:, 0:16], "prm", T.one[:, 0:16], ["one", "prm0"], [[-1, 16]], A.is_equal, -112, 1)
+    AFF(T.prm[:, 0:16], "prm", T.one[:, 0:16], "one", [[-1, 16]], A.is_equal, -112, 1)
+    AFF(T.prm[:, 16:32], "prm", T.one[:, 0:16], "one", [[-1, 16]], A.is_equal, 0, 1)
+    AFF(T.prm[:, 32:128], "prm", T.one[:, 0:96], "one", [[-16, 3], [0, 2], [-1, 16]], A.is_equal, -16, 1)
+    IOTA(T.vk[:], "vk", [[-16, 4], [0, 32]], 0, 1)
+    IOTA(T.vg[:], "vg", [[-16, 8], [0, 16]], 0, 1)
     IOTA(row("lR"), "zrB", [[32, 2], [0, 16]], 0)
     IOTA(row("lD"), "zrB", [[0, 2], [32, 2], [0, 8]], 0)
     IOTA(row("lW"), "zrB", [[0, 4], [2, 8]], 0)
@@ -241,50 +243,46 @@ def rank_program(g, core, T, topo):
     IOTA(T.rows[:, 8:16], "rows", [[64, 4], [0, 2]], 0)
 
     FILL(T.cs[:], "cs0", 0.0)
-    for a in range(0, 1024, 512):
-        ACT(T.B[:, a:a + 512], ["B0", "B1"], T.zer[:, 0:512], "zer")
-    ACT(T.crow[:], "crow0", T.zer[:, 0:384], "zer", AF.Identity, bias=U)
     ACT(T.ce[:], "ce0", T.zer[:], "zer")
     ACT(T.cg[:], "cg0", T.zer[:], "zer")
     ACT(T.ce[:, 3:512:4], "ce", T.idn[:], ["idn", "ce0"])
+    ACT(T.B[:, 0:512], "B0", T.zer[:, 0:512], "zer")
     ACT(T.cg[:, 3:512:4], "cg", T.prm[:], ["prm", "cg0"])
+    ACT(T.B[:, 512:1024], "B1", T.zer[:, 0:512], "zer")
+    ACT(T.crow[:], "crow0", T.zer[:, 0:384], "zer", AF.Identity, bias=U)
+    ACT(T.crow[:, 31:256:32], "crow", T.zer[:, 0:8], ["zer", "crow0"], AF.Identity, bias=GONE)
     ACT(T.sr[:, 0:16], "srp", T.zer[:, 0:16], "zer")
     ACT(T.sr[:, 272:288], "srp", T.zer[:, 0:16], "zer")
     ACT(T.key[:], "key", T.zer[:, 0:288], "zer")
     ACT(T.win[:], "win", T.zer[:, 0:272], "zer")
+    for t in range(4):
+        ACT(T.F[:, 272 * t:272 * t + 16], "Fp", T.zer[:, 0:16], "zer")
     ACT(T.e1[:], "e1", T.zer[:, 0:128], "zer")
     ACT(T.pm[:], "pm", T.zer[:, 0:128], "zer")
 
     for i in range(3):
         FILL(row("w2", i, 32, 16), "zrV", float(8 >> i), "zr0")
-    FILL(T.rst[:], "rst0", 0.0)
-    FILL(T.e40[:], "e400", 0.0)
-    turn("jj", "w2", "zcA", ["zrA", "zrV"])
+    FILL(row("fx", 31, 32), "zrV", DROP)
     FILL(T.wrow[:], "wrow0", 1.0)
+    turn("jj", "fx", "zcA", ["zrA", "zrV"])
+    FILL(T.zf[:, 0:RP2], ["zf0", "trp1", "trp2", "trfc"], 0.0)
     TS(C("wu"), "wu", C("w2"), "zcA", U / 2, None, A.mult)
-    TS(T.cs[:, 512:1024:4], "cs", T.vg[:], ["vg", "zcA", "cs0"], C("jj"), C("w2"), A.is_equal, A.mult)
-    TS(T.cs[:, 0:512:4], "cs", T.vk[:], ["vk", "zcA", "wu", "cs0"], C("jj"), C("wu"), A.is_equal, A.mult)
     TS(C("nb"), "nb", C("us"), "zcA", -U, None, A.add)
-    QT("qcs", 0, 256, T.cs[:], "cs")
-    FILL(T.rst[:, 0:64:8], "rst", -FAR, "rst0")
+    FILL(T.zf[:, RST:RST + 64:8], "rst", -FAR, "zf0")
     FILL(T.wrow[:, 271:384:16], "wrow", 4096.0, "wrow0")
     FILL(T.Y[:, 79:320:8], "Yc", FAR)
-    FILL(T.trp[:], ["trp1", "trp2"], 0.0)
-    FILL(T.trf[:, 32:48], "trfc", 0.0)
     TS(T.crep[:], "crep", T.zer[:, 0:32], ["zer", "zcA"], C("us"), None, A.add)
-    CP(T.e40[:, 8:9], "e40", C("us"), ["zcA", "e400"])
-    FILL(T.rp2[:], "rp2", -4096.0)
-    FILL(T.tr2[:, 32:48], "tr2c", -4096.0)
-    FILL(T.c4k[:], "c4k", 4096.0)
-    FILL(T.acc[:], ["acc%d%s" % (k, q) for k in range(len(PIECES)) for q in "VS"], 1.0)
-    FILL(row("fx"), "zr1", 0.0)
-    FILL(row("xc", 0, 16), "zrW", 4080.0)
-    FILL(row("xc", 16, 32), "zrW", 4096.0)
-    FILL(row("fx", 31, 32), "zrW", DROP, "zr1")
-    FILL(T.crow[:, 31:256:32], "crow", U + GONE, "crow0")
-    FILL(T.crow[:, 271:384:16], "crow", U + GONE)
+    CP(T.zf[:, E40 + 8:E40 + 9], "e40", C("us"), ["zcA", "zf0"])
+    FILL(T.zf[:, RP2:264], ["rp2", "tr2c"], 4096.0)
+    FILL(T.pen[:, 2:4], "pen", 127.5)
+    TS(T.pen[:, 0:2], "pen", T.crep[:, 0:2], "crep", 2 / U, -146.0 - 4096.0, A.mult, A.add)
+    for b in range(4):
+        QT("qce", 128 * b, 128 * b + 128, T.ce[:, 3 - b:515 - b], "ce")
+    for b in range(2):
+        QT("qcg", 128 * b, 128 * b + 128, T.cg[:, 3 - b:515 - b], "cg")
     QT("qu", 0, 128, T.us[:], "us")
-    QT("qn0", 0, 256, T.xs[:], "xs", ["na0", "nb0"])
+    QT("na0", 0, 128, T.xs[:, 0:512], "xs0")
+    QT("nb0", 0, 128, T.xs[:, 512:1024], "xs1")
 
     send_codes(0)
     IOTA(T.dT[:], "dT", [[0, 3], [int(U) // 2, 16]], int(U))
@@ -296,11 +294,11 @@ def rank_program(g, core, T, topo):
     IOTA(row("lL"), "zrC", [[16, 2], [1, 2], [32, 8]], 0)
     IOTA(row("lS", 0, 16), "zrC", [[1, 16]], 0)
     IOTA(row("lS", 16, 32), "zrC", [[2, 8], [-1, 2]], 1)
-    IOTA(T.ng0[:], "ng0", [[-1, 256]], 0)
+    IOTA(T.ng0[:], "ng0", [[1, 256]], -128)
     IOTA(T.rows[:, 16:32], "rows2", [[2, 16]], 0)
     IOTA(T.rows[:, 32:48], "rows2", [[16, 8], [128, 2]], 0)
-    IOTA(T.ngn[:], "ngn", [[-16, 8], [-128, 2], [-1, 16]], 0)
-    IOTA(T.dlt[:], "dlt", [[-16, 8], [112, 2], [0, 16]], 0)
+    IOTA(T.ngn[:], "ngn", [[16, 8], [128, 2], [1, 16]], -128)
+    IOTA(T.dlt[:], "dlt", [[16, 8], [-112, 2], [0, 16]], 0)
 
     def dims(parts):
         return (256, 0) if len(parts) == 2 else (128, parts[0])
@@ -327,11 +325,12 @@ def rank_program(g, core, T, topo):
         n, o = dims(parts)
         ACT(T.sr[:, 16:16 + n], "sr", T.ps7[:, 0:n], "ps7")
 
-    def rows_V(parts):
+    def rows_V(parts, c=None):
         n, o = dims(parts)
-        c = 0 if n == 256 else 256
+        if c is None:
+            c = T.cra[:] if o else T.crow[:, 256:384]
         TS(T.ab[:, 128 * o:128 * o + n], keys("ab", parts), T["ps%d" % (5 + o)][:, 0:n], ["ps%d" % (5 + o), "nb"], C("nb"), GONE, A.not_equal, A.mult)
-        TT(T.dz[:, 128 * o:128 * o + n], keys("dz", parts), T["ps%d" % (5 + o)][:, 0:n], T.crow[:, c:c + n], ["ps%d" % (5 + o), "crow"], A.add)
+        TT(T.dz[:, 128 * o:128 * o + n], keys("dz", parts), T["ps%d" % (5 + o)][:, 0:n], c, ["ps%d" % (5 + o), "crow"] + ["cra"] * o, A.add)
 
     def firsts(parts):
         n, o = dims(parts)
@@ -353,7 +352,8 @@ def rank_program(g, core, T, topo):
             if "T" in part:
                 MM(k + b, 256, c, 128 * b, q, qk)
             if "S" in part:
-                ACT(T[o][:, 256 * b:256 * b + 256], "%s%d" % (o, b), T["ps%d" % (k + b)][:, 0:256], "ps%d" % (k + b), scale=sc)
+                a = 256 * b if o == "Fo" else 272 * b + 16
+                ACT(T[o][:, a:a + 256], "%s%d" % (o, b), T["ps%d" % (k + b)][:, 0:256], "ps%d" % (k + b), scale=sc)
 
     def weave(main, fill):
         fill = list(fill)
@@ -365,25 +365,33 @@ def rank_program(g, core, T, topo):
             f()
 
     def level(p0, p1, tk):
-        return [lambda: TT(T.yi[:], "yi", T.trp[:].indirect(L("lW")), T.MT[:], ["trp1", "trp2", "MT", "lsB"], A.add),
-                lambda: SCAN(T.Y[:, 0:64], "Y", T.rst[:], T.yi[:], ["rst", "yi"], -FAR, A.add, A.max),
-                lambda: SCAN(T.rep[p0:p1, :], tk, T.Y[p0:p1, 7:320:8], T.e40[p0:p1, :], ["Y", "Yc", "cap", "e40"], FAR, A.min, A.add)]
+        return [lambda: TT(T.yi[:], "yi", T.zf[:, TRP:TRP + 32].indirect(L("lW")), T.MT[:], ["trp1", "trp2", "MT", "lsB"], A.add),
+                lambda: SCAN(T.Y[:, 0:64], "Y", T.zf[:, RST:RST + 64], T.yi[:], ["rst", "yi"], -FAR, A.add, A.max),
+                lambda: SCAN(T.rep[p0:p1, :], tk, T.Y[p0:p1, 7:320:8], T.zf[p0:p1, E40:E40 + 40], ["Y", "Yc", "cap", "e40"], FAR, A.min, A.add)]
 
     both = (0, 1)
-    scores(0, both)
-    for b in range(4):
-        QT("qce", 128 * b, 128 * b + 128, T.ce[:, 3 - b:515 - b], "ce")
+    for o in both:
+        MM(4 * o, 128, "qu", 0, ("na0", "nb0")[o])
+    TS(T.cs[:, 0:512:4], "cs", T.vk[:], ["vk", "zcA", "wu", "cs0"], C("jj"), C("wu"), A.is_equal, A.mult)
+    TS(T.cs[:, 512:1024:4], "cs", T.vg[:], ["vg", "zcA", "cs0"], C("jj"), C("w2"), A.is_equal, A.mult)
+    QT("qcs", 0, 256, T.cs[:], "cs")
+    for o in both:
+        TS(T.B[:, 512 * o:512 * o + 512:4], "B%d" % o, T["ps%d" % (4 * o)][:, 0:128], "ps%d" % (4 * o), 0.0, None, A.is_gt)
+    for o in both:
+        QT("qb%d" % o, 0, 128, T.B[:, 512 * o:512 * o + 512], "B%d" % o)
+    for bank, c, o in ((5, 0, 0), (6, 0, 1), (7, 128, 0), (1, 128, 1)):
+        MM(bank, 128, "qcs", c, "qb%d" % o)
     turn("lR", "lK", "zcB", "zrB")
-    bits(both)
-    TS(C("g0"), "g0", C("pf"), "pf", 16.0, 32.0, A.is_lt, A.mult)
+    QT("qcg", 256, 384, T.cg[:, 1:513], "cg")
     TS(L("lR0"), "lsB", T.rows[:, 8:16], ["rows", "zcB"], C("lR"), None, A.add)
     TS(L("lD0"), "lsB", T.rows[:, 0:4], ["rows", "zcB"], C("lD"), None, A.add)
     TS(L("lW"), "lsB", T.zer[:, 0:4], ["zer", "zcB"], C("lW"), None, A.add)
     CP(L("lK"), "lsB", C("lK"), "zcB")
-    for b in range(2):
-        QT("qcg", 128 * b, 128 * b + 128, T.cg[:, 3 - b:515 - b], "cg")
-    rows_S(both)
-    rows_V(both)
+    for o in both:
+        ACT(T.sr[:, 16 + 128 * o:144 + 128 * o], "sr", T["ps%d" % (7, 1)[o]][:, 0:128], "ps%d" % (7, 1)[o])
+        rows_V((o,), T.crow[:, 128 * o:128 * o + 128])
+    TS(C("g0"), "g0", C("pf"), "pf", 16.0, 32.0, A.is_lt, A.mult)
+    QT("qcg", 384, 512, T.cg[:, 0:512], "cg")
 
     for r in range(NR):
         last = r == NR - 1
@@ -399,10 +407,9 @@ def rank_program(g, core, T, topo):
             fill = []
         else:
             pb, pk, ends = T.pm, ["pm"], T.pm[:, 0:128:16]
-            head = [lambda: TT(T.e1[:, 0:128:16], "e1", T.pb[:, 128:256:16], T.pt8[:], ["pb1", "pt8"], A.add),
-                    lambda: TT(T.R[:], "R", T.e1[:].indirect(L("lR1")), T.pkr[:], ["e1", "pkr", "lsD"], A.min)]
-            fill = [lambda: TT(T.ck[:, 8:16], "ck1", T.fs[:, 128:256:16], T.cc[:, 40:48], ["fs1", "cc"], A.add),
-                    lambda: TT(ends, "pm", T.e1[:, 0:128:16], T.pb[:, 0:128:16], ["e1", "pb0"], A.min)]
+            head = [lambda: TT(T.R[:], "R", T.pb[:, 128:256].indirect(L("lR1")), T.pkr[:], ["pb1", "pkr", "lsD"], A.max),
+                    lambda: TT(ends, "pm", T.pb[:, 128:256:16], T.e1[:, 0:128:16], ["e1", "pb1"], A.max)]
+            fill = [lambda: None, lambda: None]
         weave(head + [lambda: TR(T.al[:], "al", T.R[:], "R"),
                       lambda: TT(T.dif[:], "dif", pb[:].indirect(L("lD%d" % min(r, 1))), T.al[:, 0:128:2], pk + ["al", "lsB", "lsD"], A.subtract),
                       lambda: TS(T.neg[:], "neg", T.dif[:], "dif", 0.0, GONE / U, A.min, A.mult),
@@ -410,43 +417,46 @@ def rank_program(g, core, T, topo):
               fill + [lambda: RED(C("mn"), "mn", ends, pk, A.min),
                       lambda: TS(C("fl"), "fl", C("mn"), "mn", DROP, None, A.is_lt),
                       lambda: TS(T.rep[0:32, 8:40], "rep0", T.crep[0:32, :], ["crep", "mn", "fl"], C("mn", 32), C("fl", 32), A.add, A.mult),
-                      lambda: TR(T.trp[32:64, :], "trp1", T.rep[0:32, 8:40], "rep0"),
+                      lambda: TR(T.zf[32:64, TRP:TRP + 32], "trp1", T.rep[0:32, 8:40], "rep0"),
                       lambda: TS(T.Y[:, 71:72], "cap", C("fl"), ["fl", "zcA"], FAR, C("us"), A.mult, A.subtract)])
         if r == 0:
             fill = lists + [lambda: TS(T.cc[:, 24:48], "cc", T.cc[:, 0:24], "cc0", -127.5, None, A.add),
                     lambda: TT(T.c1[:], "c1", T.fs[:, 0:256:32], T.cc[:, 24:32], ["fs0", "fs1", "cc"], A.add),
-                    lambda: turn("lO", "fx", "zcC", ["zrC", "zrW"])]
+                    lambda: turn("lO", "lS", "zcC", "zrC")]
         else:
-            fill = lists + [lambda: TT(T.c1[:], "c1", T.ck[:, 0:8], T.ck[:, 8:16], ["ck0", "ck1"], A.min)]
-        weave(level(32, 64, "rep1") + [lambda: (TR(T.trp[64:96, :], "trp2", T.rep[32:64, 8:40], "rep1"), TR(T.trp[96:128, :], "trp2", T.rep[32:64, 8:40], "rep1"))]
-              + level(64, 128, "rep2") + [lambda: TR(T.trf[:, 0:32], "trf", T.rep[:, 8:40], ["rep0", "rep1", "rep2"])],
-              fill + [lambda: TS(T.pen[:], "pen", T.c4k[:], ["c4k", "fl"], C("fl"), 127.5 - 4096.0, A.mult, A.add)] + [lambda: None] * (6 - len(fill))
-              + [lambda: TS(T.k1[:], "k1", T.Y[:, 7:64:8], "Y", 256.0, None, A.mult)])
+            fill = lists + [lambda: TT(T.ck[:, 8:16], "ck1", T.fs[:, 128:256:16], T.cc[:, 40:48], ["fs1", "cc"], A.add),
+                            lambda: TT(T.c1[:], "c1", T.ck[:, 0:8], T.ck[:, 8:16], ["ck0", "ck1"], A.min)]
+        weave(level(32, 64, "rep1") + [lambda: [TR(T.zf[p:p + 32, TRP:TRP + 32], "trp2", T.rep[32:64, 8:40], "rep1") for p in (64, 96)]]
+              + level(64, 128, "rep2") + [lambda: TR(T.zf[:, TRF:TRF + 32], "trf", T.rep[:, 8:40], ["rep0", "rep1", "rep2"])],
+              [lambda: TS(T.zf[:, RP2 + 1:RP2 + 32:16], "rp2", T.pen[:, 0:2], ["pen", "fl"], C("fl"), 4096.0, A.mult, A.add)] + fill
+              + [lambda: TR(T.zf[:, TR2:TR2 + 32], "tr2", T.zf[:, RP2:RP2 + 32], "rp2")] + [lambda: None] * (5 - len(fill))
+              + [lambda: TS(T.k1[:], "k1", T.Y[:, 7:64:8], "Y", 256.0, DROP, A.mult, A.min)])
         ACT(T.dr[:], "dr", T.dT[:].indirect(T.LG[:, 0:16]), ["dT", "LG0", "LG1"])
         ACT(T.dr[:, 31:256:32], "dr", T.dr[:, 31:256:32], "dr", AF.Identity, bias=-DROP)
         key = T.key[:, 16:272]
         if r == 0:
-            for n in ("lO", "l2", "lL", "lS"):
-                CP(L(n), "lsC", C(n), "zcC")
-            for b in range(2, 4):
-                QT("qcg", 128 * b, 128 * b + 128, T.cg[:, 3 - b:515 - b], "cg")
+            k0 = 32 * COLS.index("lO")
+            CP(T.ls[:, 0:8:2], "lsC", T.zc[:, k0:k0 + 128:32], "zcC")
         unpack("qcg", "qa%d" % r, None, "G", 1 / 256, "T")
         unpack("qce", "qa%d" % r, None, "F", 1 / 256, "T", 4)
-        weave([lambda: TT(T.wr[:], "wr", T.trf[:].indirect(T.LG[:, 0:16]), T.hrow[:], ["trf", "trfc", "LG0", "LG1", "hrow"], A.add),
+        weave([lambda: TT(T.wr[:], "wr", T.zf[:, TRF:TRF + 48].indirect(T.LG[:, 0:16]), T.hrow[:], ["trf", "trfc", "LG0", "LG1", "hrow"], A.add),
                lambda: SCAN(key, "key", T.wr[:], T.dr[:], ["wr", "dr"], -1.0, A.max, A.add),
                lambda: TR(T.kt[:, 0:256], "kt0", key, "key")],
               [lambda: TT(T.k2[:], "k2", T.k1[:], T.c1[:], ["k1", "c1"], A.add),
                lambda: RED(C("km"), "km", T.k2[:], "k2", A.min),
                lambda: TS(C("rn"), "rn", C("km"), "km", ROUND256, -ROUND256, A.add, A.add)])
-        TS(T.own[:, 0:16], "own0", T.kt[:, 0:256].indirect(L("lO")), ["kt0", "lsC", "zcC"], C("fx"), None, A.add)
+        TS(T.own[:, 0:16], "own0", T.kt[:, 0:256].indirect(L("lO")), ["kt0", "lsC", "zcA"], C("fx"), None, A.add)
         TS(T.key[:, 47:272:32], "key", T.key[:, 47:272:32], "key", DROP, None, A.add)
-        TS(T.rp2[:, 1:32:16], "rp2", T.pen[:], ["pen", "km", "rn"], C("km"), C("rn"), A.add, A.subtract)
+        TS(T.lf[:, 16 * r:16 * r + 2], "lf%d" % r, T.pen[:, 2:4], ["pen", "km", "rn"], C("km"), C("rn"), A.add, A.subtract)
         TR(T.kt[:, 256:544], "kt1", T.key[:], "key")
-        TR(T.tr2[:, 0:32], "tr2", T.rp2[:], "rp2")
-        CP(T.own[:, 16:32], "own1", T.kt[:, 256:544].indirect(L("l2")), ["kt1", "lsC"])
-        CP(T.k16[:], "k16", key, "key")
+        need("G", toks_of("G", ["lf%d" % r], []))
+        g.remote_dma(T.fa[:, 16 * r:16 * r + 2], T.lf[:, 16 * r:16 * r + 2], T.sem["arf%d" % r], T.sem.sent, pid, rid, mask)
+        landed("arf%d" % r, n_in, ["fa%d" % r])
+        CP(T.k16[:, 0:128], "k16", T.key[:, 16:144], "key")
+        CP(T.ow2[:, 0:16], "owh", T.kt[:, 256:544].indirect(L("l2")), ["kt1", "lsC"])
+        CP(T.k16[:, 128:256], "k16", T.key[:, 144:272], "key")
+        TT(T.ow2[:, 16:32], "owl", T.kt[:, 256:544].indirect(L("l2")), T.ow2[:, 0:16], ["kt1", "lsC", "owh"], A.subtract)
         ng = ("ng0", "ng1")[min(r, 1)]
-        TT(T.prf[:], "prf", T.tr2[:].indirect(T.LG[:, 0:16]), T[ng][:], ["tr2", "tr2c", "LG0", "LG1", ng], A.max)
         nj = [0]
 
         def unit_S(k, i, b, w):
@@ -461,7 +471,7 @@ def rank_program(g, core, T, topo):
             return [lambda: (TS(T.oa[:, a], "oa%d" % k, T.acc[:, a].indirect(L("lS")), ak, 16 / 255, None, A.mult),
                              TS(T.oq[:, a], "oq%d" % k, T.acc[:, a].indirect(L("lS")), ak, 1 / 16, 15.5, A.mult, A.add)),
                     lambda: TT(T.od[:, a], "od%d" % k, T.oa[:, a], T.oq[:, a], ["oa%d" % k, "oq%d" % k], A.subtract),
-                    lambda: TS(T.pl[:, a], "pl%d" % k, T.od[:, a], ["od%d" % k, "zcC"], 255.0, C("xc"), A.mult, A.add)]
+                    lambda: TS(T.pl[:, a], "pl%d" % k, T.od[:, a], ["od%d" % k, "xc"], 255.0, C("xc"), A.mult, A.add)]
 
         def scatter(k, a, b):
             o = 16 * k + 2 * (a - PIECES[k][0])
@@ -471,45 +481,53 @@ def rank_program(g, core, T, topo):
         units = [(k, i, b, w) for k, piece in enumerate(PIECES) for w in range(2) for i, b in enumerate(piece) if w == 0 or b >= NV]
         for u in units:
             unit_S(*u)
-        ACT(T.prb[:], "prb", T.prf[:], "prf", AF.Abs)
         unpack("qcg", "qa%d" % r, None, "G", 1 / 256, "S")
         unpack("qce", "qa%d" % r, None, "F", 1 / 256, "S", 4)
+        for t in range(4):
+            ACT(T.G[:, 272 * t:272 * t + 16], "Gf%d" % t, T.G[:, 272 * t + 16:272 * t + 272].indirect(T.fa[:, 16 * r:16 * r + 1]), ["G%d" % t, "fa%d" % r])
         for b in range(NV):
-            TS(T.jv[:, 256 * b:256 * b + 256], "jv%d" % b, T.k16[:], ["k16", "own1"], T.own[:, 16 + b:17 + b], None, A.is_lt)
+            TS(T.jv[:, 256 * b:256 * b + 256], "jv%d" % b, T.k16[:], ["k16", "owh", "owl"], T.ow2[:, b:b + 1], T.ow2[:, 16 + b:17 + b],
+               A.subtract, A.is_lt)
         for b in range(NV):
-            a = slice(256 * b, 256 * b + 256)
-            SCAN(T.jo[:, a], "jo", T.jv[:, a], T.jv[:, a], "jv%d" % b, -255.0, A.add, A.add)
-        CP(T.acc[:, 1:2 * NV:2], "acc0V", T.jo[:, 255:256 * NV:256], "jo")
-        weave(places(0), [])
+            SCAN(T.jo[:, 128 * b:128 * b + 128], "jo", T.jv[:, 256 * b:256 * b + 128], T.jv[:, 256 * b + 128:256 * b + 256], "jv%d" % b, 0.0, A.add, A.add)
+        if r == 0:
+            TS(C("xc"), "xc", C("lR"), "zcB", 0.5, 4080.0, A.mult, A.add)
+        cuts = (0, 6, 12, 14, 16)
+        vals = [lambda a=a, b=b: TT(T.prb[:, 16 * a:16 * b], "prb", T.zf[:, TR2:TR2 + 48].indirect(T.LG[:, a:b]), T[ng][:, 16 * a:16 * b],
+                                    ["tr2", "tr2c", "LG0", "LG1", ng], A.min) for a, b in zip(cuts, cuts[1:])]
+        vals[0]()
+        weave([lambda: TS(T.acc[:, 1:2 * NV:2], "acc0V", T.jo[:, 127:128 * NV:128], "jo", 2.0, -255.0, A.mult, A.add)] + places(0), vals[1:])
         scatter(0, 0, 8)()
         ll = T.ll[:, 16 * r:16 * r + 16]
         TR(T.wt[:], "wt", T.win[:, 0:256], "win")
-        CP(ll, "ll%d" % r, T.wt[:].indirect(L("lL")), ["wt", "lsC"])
+        TS(ll, "ll%d" % r, T.wt[:].indirect(L("lL")), ["wt", "lsC"], 144.0, None, A.add)
         need("G", toks_of("G", ["ll%d" % r], []))
         g.remote_dma(T.la[:, 16 * r:16 * r + 16], ll, T.sem["arl%d" % r], T.sem.sent, pid, rid, mask)
         landed("arl%d" % r, n_in, ["la%d" % r])
         TR(T.wk[:], "wk", T.win[:, 16:272], "win")
         if r == 0:
             TS(C("m2"), "m2", C("jj"), "zcA", 2.0, None, A.is_equal)
-        CP(T.lk[:], "lk", T.wk[:].indirect(L("lO")), ["wk", "lsC"])
+        TS(T.lk[:], "lk", T.wk[:].indirect(L("lO")), ["wk", "lsC"], 128.0, None, A.add)
         for t in range(4):
             src = T.Fo[:, 256 * t:256 * t + 256].indirect(T.lk[:, 0:8])
-            CP(T.X[:, t:512:4], "X0", src, ["Fo%d" % t, "lk"])
-        if r == 0:
-            ACT(T.dl2[:], "dl2", T.dlt[:], ["dlt", "m2"], scale=C("m2"))
+            (CP if t < 2 else ACT)(T.X[:, t:512:4], "X0" + "VS"[t // 2], src, ["Fo%d" % t, "lk"])
         z = "qz%d" % r
         for t in range(4):
-            (ACT if t else CP)(T.gz[:, 128 * t:128 * t + 128], "gz%d" % t, T.G[:, 256 * t:256 * t + 256].indirect(T.la[:, 16 * r + 8:16 * r + 16]), ["G%d" % t, "la%d" % r])
-        QT("na%d" % (r + 1), 0, 128, T.X[:, 0:512], "X0")
+            (ACT if t else CP)(T.gz[:, 128 * t:128 * t + 128], "gz%d" % t, T.G[:, 272 * t:272 * t + 272].indirect(T.la[:, 16 * r + 8:16 * r + 16]),
+                               ["G%d" % t, "Gf%d" % t, "la%d" % r])
+        if r == 0:
+            ACT(T.dl2[:], "dl2", T.dlt[:], ["dlt", "m2"], scale=C("m2"))
+        for t in range(4):
+            if t == QNA:
+                QT("na%d" % (r + 1), 0, 128, T.X[:, 0:512], ["X0V", "X0S"])
+            TT(T.Z[:, t:512:4], "Z", T.F[:, 272 * t:272 * t + 272].indirect(T.la[:, 16 * r:16 * r + 8]), T.gz[:, 128 * t:128 * t + 128],
+               ["F%d" % t, "Fp", "la%d" % r, "gz%d" % t], A.add)
         if last:
             MM(4, 128, "qv", 0, "na3")
-            ACT(T.opw[:], "opw", T.win[:].indirect(L("lP")), ["win", "lsE"])
+            ACT(T.opw[:], "opw", T.win[:].indirect(L("lP")), ["win", "lsE"], AF.Identity, bias=128.0)
             emit("Y", lambda: g.sync.dma_start(T.op[:], T.opw[2:128:16, :]), ["opw"], ["op"], dma=True)
         else:
             scores(r + 1, (0,))
-        for t in range(4):
-            TT(T.Z[:, t:512:4], "Z", T.F[:, 256 * t:256 * t + 256].indirect(T.la[:, 16 * r:16 * r + 8]), T.gz[:, 128 * t:128 * t + 128],
-               ["F%d" % t, "la%d" % r, "gz%d" % t], A.add)
         QT(z, 0, 128, T.Z[:], "Z")
         for b in range(4):
             MM(b, 128, "qw", 128 * b, z, None, True, False)
@@ -522,7 +540,10 @@ def rank_program(g, core, T, topo):
                 FILL(T.r16[:], "r160", 1.0)
                 TS(L("lR1"), "lsD", L("lR0"), "lsB", 0.5, None, A.mult)
                 TS(L("lD1"), "lsD", L("lD0"), "lsB", 0.5, None, A.mult)
+                FILL(T.cra[:], "cra0", U)
                 FILL(T.r16[:, 0:128:16], "r16", 0.0, "r160")
+                FILL(T.crow[:, 271:384:16], "crow", U + GONE, "crow0")
+                FILL(T.cra[:, 15:128:16], "cra", 16 * GONE, "cra0")
                 TT(T.ng1[:], "ng1", T.dl2[:], T.ngn[:], ["dl2", "ngn"], A.add)
             else:
                 TS(L("lP"), "lsE", T.rows[:, 16:32], ["rows2", "zcC"], C("lL"), None, A.add)
@@ -542,13 +563,17 @@ def rank_program(g, core, T, topo):
             rows_V((0,))
             SCAN(T.pt[:], "pt", T.r16[:], T.ps5[:, 0:128], ["r16", "ps5"], 0.0, A.mult, A.add)
             kept, first = list_V((0,)), firsts((0,))
-            first[0]()
-            bits((1,))
-            first[1]()
-            TS(T.pt8[:], "pt8", T.pt[:, 15:128:16], "pt", 16 * U, None, A.add)
             kept[0]()
+            first[0]()
             kept[1]()
-            CP(T.pkr[:], "pkr", T.pb[:, 0:128].indirect(L("lR1")), ["pb0", "lsD"])
+            TS(T.pt8[:, 0:8], "pt8", T.pt[:, 15:128:16], "pt", 16 * U, None, A.add)
+            TS(T.pt8[:, 8:16], "pt9", T.pt[:, 15:128:16], "pt", 16 * U - 8 * GONE, None, A.add)
+            bits((1,))
+            TS(T.pt8[:, 16:24], "pta", T.pb[:, 0:128:16], "pb0", DROP, 8 * GONE + U, A.is_ge, A.mult)
+            TT(T.e1[:, 0:128:16], "e1", T.pb[:, 0:128:16], T.pt8[:, 0:8], ["pb0", "pt8"], A.min)
+            first[1]()
+            TT(T.cra[:, 0:128:16], "cra", T.pt8[:, 8:16], T.pt8[:, 16:24], ["pt9", "pta"], A.add)
+            CP(T.pkr[:], "pkr", T.e1[:].indirect(L("lR1")), ["e1", "lsD"])
             kept[2]()
             TT(T.ck[:, 0:8], "ck0", T.fs[:, 0:128:16], T.cc[:, 32:40], ["fs0", "cc"], A.add)
             rows_S((1,))
@@ -565,6 +590,6 @@ def rank_program(g, core, T, topo):
              ["sqp"], ["osc%d" % k], dma=True)
     for k in range(nd[0]):
         g.wait_ge(T.sem["ld%d" % k], 16)
-    g.wait_ge(T.sem.sent, 3 * NR * n_out)
+    g.wait_ge(T.sem.sent, 4 * NR * n_out)
     for k in "VSTG":
         g.wait_ge(T.sem["c" + k], count[k])

@@ -7,9 +7,11 @@ DROP = float(1 << 22)
 FAR = float(1 << 30)
 ROUND256 = 1.5 * float(1 << 31)
 PIECES = ((0, 1, 2, 3, 4, 5, 6, 7),)
-QNA = 0
+NCE, NCG = 2, 2
+CUTS = (0, 6, 12, 16)
+XV, GV, QNA = 2, 1, 0
 NV = 8
-COLS = ["jj", "us", "w2", "fx", "lR", "lD", "lW", "lK", "lO", "l2", "lL", "lS"]
+COLS = ["jj", "us", "w2", "lR", "lD", "lW", "lK", "lO", "l2", "lL", "lS"]
 LISTS = {"lO": (0, 1), "l2": (2, 1), "lL": (4, 1), "lS": (6, 1), "lW": (8, 4), "lD0": (12, 4), "lR0": (16, 8), "lP": (24, 16), "lF": (40, 16),
          "lK": (56, 1), "lD1": (58, 4), "lR1": (62, 8)}
 SMALL = ["pf", "wu", "g0", "nb", "m2", "mn", "fl", "km", "rn", "xc"]
@@ -27,22 +29,21 @@ for _n, _k, _d in (
         ("one", 128, "bfloat16"), ("zer", 528, "bfloat16"), ("idn", 128, "bfloat16"), ("prm", 128, "bfloat16"),
         ("ce", 528, "bfloat16"), ("cg", 528, "bfloat16"), ("cs", 1024, "bfloat16"), ("vk", 128, "float32"), ("vg", 128, "float32"),
         ("zr", 32 * len(COLS), "float32"), ("zc", 32 * len(COLS), "float32"), ("sm", 8 * len(SMALL), "float32"),
-        ("ls", 70, "uint16"), ("rows", 64, "float32"), ("cc", 48, "float32"),
+        ("ls", 74, "uint16"), ("rows", 64, "float32"), ("cc", 48, "float32"),
         ("crow", 384, "float32"), ("wrow", 384, "bfloat16"), ("r16", 128, "bfloat16"), ("dT", 48, "float32"),
         ("hrow", 256, "float32"), ("zf", 264, "float32"), ("crep", 32, "float32"), ("cra", 128, "float32"),
         ("ng0", 256, "bfloat16"), ("ng1", 256, "bfloat16"), ("ngn", 256, "bfloat16"), ("dlt", 256, "bfloat16"), ("dl2", 256, "bfloat16"),
         ("B", 1024, "bfloat16"), ("dz", 256, "bfloat16"), ("ab", 256, "bfloat16"), ("dr", 256, "float32"),
-        ("sr", 288, "bfloat16"), ("st", 544, "bfloat16"), ("LG", 32, "uint16"),
-        ("pb", 256, "bfloat16"), ("fs", 256, "bfloat16"), ("e1", 128, "bfloat16"), ("pm", 128, "bfloat16"), ("pt", 128, "float32"),
-        ("pt8", 24, "float32"), ("pkr", 128, "bfloat16"), ("ck", 16, "float32"), ("R", 128, "bfloat16"), ("al", 128, "bfloat16"),
+        ("sr", 288, "bfloat16"), ("st", 544, "bfloat16"), ("sk", 160, "bfloat16"), ("sl", 544, "bfloat16"), ("LG", 32, "uint16"),
+        ("pb", 256, "bfloat16"), ("fs", 256, "bfloat16"), ("e1", 128, "bfloat16"), ("pkr", 128, "bfloat16"), ("pm", 128, "bfloat16"), ("pt", 128, "float32"),
+        ("pt8", 24, "float32"), ("ck", 16, "float32"), ("R", 128, "bfloat16"), ("al", 128, "bfloat16"),
         ("dif", 64, "float32"), ("neg", 64, "float32"), ("MT", 64, "float32"), ("yi", 64, "float32"), ("Y", 320, "float32"),
         ("rep", 40, "float32"), ("c1", 8, "float32"), ("k1", 8, "float32"), ("k16", 256, "uint16"), ("k2", 8, "float32"), ("pen", 4, "float32"),
         ("lf", 16 * NR, "uint16"), ("fa", 16 * NR, "uint16"),
         ("wr", 256, "float32"), ("key", 288, "float32"), ("kt", 544, "float32"), ("own", 32, "float32"), ("ow2", 32, "bfloat16"),
         ("js", 256 * (16 - NV), "bfloat16"), ("jv", 256 * NV, "bfloat16"), ("jo", 256 * NV, "bfloat16"),
-        ("acc", 16 * len(PIECES), "float32"), ("oa", 16 * len(PIECES), "float32"), ("oq", 16 * len(PIECES), "int32"),
-        ("od", 16 * len(PIECES), "float32"), ("pl", 16 * len(PIECES), "uint16"),
-        ("prb", 256, "bfloat16"), ("win", 272, "bfloat16"), ("wt", 256, "bfloat16"), ("wk", 256, "bfloat16"),
+        ("acc", 16, "float32"), ("pl", 16, "uint16"),
+        ("prb", 256, "bfloat16"), ("win", 384, "bfloat16"), ("wt", 256, "bfloat16"), ("wk", 256, "bfloat16"),
         ("ll", 16 * NR, "uint16"), ("la", 16 * NR, "uint16"), ("lk", 16, "uint16"), ("opw", 256, "float32"),
         ("Fo", 1024, "bfloat16"), ("F", 1088, "bfloat16"), ("G", 1088, "bfloat16"), ("gz", 512, "bfloat16"), ("Z", 512, "bfloat16"),
         ("X", 1024, "bfloat16"), ("ysb", (8, 32), "float32")):
@@ -215,6 +216,11 @@ def rank_program(g, core, T, topo):
         g.remote_dma(asc, zs, T.sem["arc%d" % r], T.sem.sent, pid, rid, mask)
         landed("arc%d" % r, 2 * n_in, ["qa%d" % r])
 
+    def send(dst, src, n, k, r):
+        need("G", toks_of("G", ["l%s%d" % (k, r)], []))
+        g.remote_dma(dst[:, 16 * r:16 * r + n], src[:, 16 * r:16 * r + n], T.sem["ar%s%d" % (k, r)], T.sem.sent, pid, rid, mask)
+        landed("ar%s%d" % (k, r), n_in, ["%sa%d" % (k, r)])
+
     emit("Y", lambda: g.sync.dma_start(T.xs[:, 0:512], T.x[:, 0:512]), [], ["xs0"], dma=True)
     emit("S", lambda: s.dma_start(T.us[:], T.u[:]), [], ["us"], dma=True)
     emit("Y", lambda: g.sync.dma_start(T.xs[:, 512:1024], T.x[:, 512:1024]), [], ["xs1"], dma=True)
@@ -224,15 +230,15 @@ def rank_program(g, core, T, topo):
 
     FILL(T.one[:], "one", 128.0)
     FILL(T.zer[:], "zer", 0.0)
-    FILL(row("w2", 0, 64), "zr0", 0.0)
+    FILL(row("w2"), "zr0", 0.0)
     IOTA(row("jj"), "zrA", [[0, 2], [1, 16]], 0)
     IOTA(row("us"), "zrA", [[0, 2], [int(U), 8], [0, 2]], int(U))
     AFF(T.idn[:], "idn", T.one[:], "one", [[-1, 128]], A.is_equal, 0, 1)
+    IOTA(T.vk[:], "vk", [[-16, 4], [0, 32]], 0, 1)
+    IOTA(T.vg[:], "vg", [[-16, 8], [0, 16]], 0, 1)
     AFF(T.prm[:, 0:16], "prm", T.one[:, 0:16], "one", [[-1, 16]], A.is_equal, -112, 1)
     AFF(T.prm[:, 16:32], "prm", T.one[:, 0:16], "one", [[-1, 16]], A.is_equal, 0, 1)
     AFF(T.prm[:, 32:128], "prm", T.one[:, 0:96], "one", [[-16, 3], [0, 2], [-1, 16]], A.is_equal, -16, 1)
-    IOTA(T.vk[:], "vk", [[-16, 4], [0, 32]], 0, 1)
-    IOTA(T.vg[:], "vg", [[-16, 8], [0, 16]], 0, 1)
     IOTA(row("lR"), "zrB", [[32, 2], [0, 16]], 0)
     IOTA(row("lD"), "zrB", [[0, 2], [32, 2], [0, 8]], 0)
     IOTA(row("lW"), "zrB", [[0, 4], [2, 8]], 0)
@@ -244,31 +250,37 @@ def rank_program(g, core, T, topo):
 
     FILL(T.cs[:], "cs0", 0.0)
     ACT(T.ce[:], "ce0", T.zer[:], "zer")
-    ACT(T.cg[:], "cg0", T.zer[:], "zer")
     ACT(T.ce[:, 3:512:4], "ce", T.idn[:], ["idn", "ce0"])
     ACT(T.B[:, 0:512], "B0", T.zer[:, 0:512], "zer")
-    ACT(T.cg[:, 3:512:4], "cg", T.prm[:], ["prm", "cg0"])
     ACT(T.B[:, 512:1024], "B1", T.zer[:, 0:512], "zer")
+    ACT(T.cg[:], "cg0", T.zer[:], "zer")
+    ACT(T.cg[:, 3:512:4], "cg", T.prm[:], ["prm", "cg0"])
     ACT(T.crow[:], "crow0", T.zer[:, 0:384], "zer", AF.Identity, bias=U)
     ACT(T.crow[:, 31:256:32], "crow", T.zer[:, 0:8], ["zer", "crow0"], AF.Identity, bias=GONE)
     ACT(T.sr[:, 0:16], "srp", T.zer[:, 0:16], "zer")
     ACT(T.sr[:, 272:288], "srp", T.zer[:, 0:16], "zer")
     ACT(T.key[:], "key", T.zer[:, 0:288], "zer")
-    ACT(T.win[:], "win", T.zer[:, 0:272], "zer")
+    ACT(T.win[:], "win", T.zer[:, 0:384], "zer")
     for t in range(4):
         ACT(T.F[:, 272 * t:272 * t + 16], "Fp", T.zer[:, 0:16], "zer")
-    ACT(T.e1[:], "e1", T.zer[:, 0:128], "zer")
     ACT(T.pm[:], "pm", T.zer[:, 0:128], "zer")
+    ACT(T.e1[:], "e1", T.zer[:, 0:128], "zer")
+    for a, b in ((128, 256), (416, 544)):
+        ACT(T.sl[:, a:b], "slp", T.zer[:, 0:128], "zer")
+    for a in (0, 144):
+        ACT(T.sk[:, a:a + 16], "srp", T.zer[:, 0:16], "zer")
 
     for i in range(3):
         FILL(row("w2", i, 32, 16), "zrV", float(8 >> i), "zr0")
-    FILL(row("fx", 31, 32), "zrV", DROP)
     FILL(T.wrow[:], "wrow0", 1.0)
-    turn("jj", "fx", "zcA", ["zrA", "zrV"])
+    turn("jj", "w2", "zcA", ["zrA", "zrV"])
     FILL(T.zf[:, 0:RP2], ["zf0", "trp1", "trp2", "trfc"], 0.0)
     TS(C("wu"), "wu", C("w2"), "zcA", U / 2, None, A.mult)
     TS(C("nb"), "nb", C("us"), "zcA", -U, None, A.add)
+    TS(T.cs[:, 0:512:4], "cs", T.vk[:], ["vk", "zcA", "wu", "cs0"], C("jj"), C("wu"), A.is_equal, A.mult)
+    TS(T.cs[:, 512:1024:4], "cs", T.vg[:], ["vg", "zcA", "cs0"], C("jj"), C("w2"), A.is_equal, A.mult)
     FILL(T.zf[:, RST:RST + 64:8], "rst", -FAR, "zf0")
+    QT("qcs", 0, 256, T.cs[:], "cs")
     FILL(T.wrow[:, 271:384:16], "wrow", 4096.0, "wrow0")
     FILL(T.Y[:, 79:320:8], "Yc", FAR)
     TS(T.crep[:], "crep", T.zer[:, 0:32], ["zer", "zcA"], C("us"), None, A.add)
@@ -276,26 +288,24 @@ def rank_program(g, core, T, topo):
     FILL(T.zf[:, RP2:264], ["rp2", "tr2c"], 4096.0)
     FILL(T.pen[:, 2:4], "pen", 127.5)
     TS(T.pen[:, 0:2], "pen", T.crep[:, 0:2], "crep", 2 / U, -146.0 - 4096.0, A.mult, A.add)
-    for b in range(4):
+    for b in range(NCE):
         QT("qce", 128 * b, 128 * b + 128, T.ce[:, 3 - b:515 - b], "ce")
-    for b in range(2):
-        QT("qcg", 128 * b, 128 * b + 128, T.cg[:, 3 - b:515 - b], "cg")
     QT("qu", 0, 128, T.us[:], "us")
     QT("na0", 0, 128, T.xs[:, 0:512], "xs0")
     QT("nb0", 0, 128, T.xs[:, 512:1024], "xs1")
 
-    send_codes(0)
     IOTA(T.dT[:], "dT", [[0, 3], [int(U) // 2, 16]], int(U))
     IOTA(T.cc[:, 0:8], "cc0", [[288, 8]], 0)
     IOTA(T.cc[:, 8:24], "cc0", [[128, 2], [272, 8]], 0)
-    IOTA(T.hrow[:], "hrow", [[1, 8], [0, 32]], 0)
+    IOTA(T.hrow[:], "hrow0", [[1, 8], [0, 32]], 0)
     IOTA(row("lO"), "zrC", [[16, 2], [0, 2], [32, 8]], 0)
     IOTA(row("l2"), "zrC", [[-16, 2], [0, 2], [32, 8]], 32)
     IOTA(row("lL"), "zrC", [[16, 2], [1, 2], [32, 8]], 0)
     IOTA(row("lS", 0, 16), "zrC", [[1, 16]], 0)
     IOTA(row("lS", 16, 32), "zrC", [[2, 8], [-1, 2]], 1)
     IOTA(T.ng0[:], "ng0", [[1, 256]], -128)
-    IOTA(T.rows[:, 16:32], "rows2", [[2, 16]], 0)
+    send_codes(0)
+    IOTA(T.rows[:, 48:64], "rows3", [[16, 16]], 0)
     IOTA(T.rows[:, 32:48], "rows2", [[16, 8], [128, 2]], 0)
     IOTA(T.ngn[:], "ngn", [[16, 8], [128, 2], [1, 16]], -128)
     IOTA(T.dlt[:], "dlt", [[16, 8], [-112, 2], [0, 16]], 0)
@@ -323,12 +333,12 @@ def rank_program(g, core, T, topo):
 
     def rows_S(parts):
         n, o = dims(parts)
-        ACT(T.sr[:, 16:16 + n], "sr", T.ps7[:, 0:n], "ps7")
+        ACT(T[("sk", "sr")[o]][:, 16:16 + n], ("sk", "sr")[o], T.ps7[:, 0:n], "ps7")
 
     def rows_V(parts, c=None):
         n, o = dims(parts)
         if c is None:
-            c = T.cra[:] if o else T.crow[:, 256:384]
+            c = T.cra[:]
         TS(T.ab[:, 128 * o:128 * o + n], keys("ab", parts), T["ps%d" % (5 + o)][:, 0:n], ["ps%d" % (5 + o), "nb"], C("nb"), GONE, A.not_equal, A.mult)
         TT(T.dz[:, 128 * o:128 * o + n], keys("dz", parts), T["ps%d" % (5 + o)][:, 0:n], c, ["ps%d" % (5 + o), "crow"] + ["cra"] * o, A.add)
 
@@ -342,9 +352,10 @@ def rank_program(g, core, T, topo):
 
     def list_V(parts):
         n, o = dims(parts)
-        return [lambda: TR(T.st[:, 0:n], "st", T.sr[:, 16:16 + n], "sr"),
-                lambda: TR(T.st[:, 256:288 + n], "st", T.sr[:, 0:32 + n], ["sr", "srp"]),
-                lambda: TS(T.LG[:, 0:16] if n == 256 else T.LG[:, o:32:2], keys("LG", parts), T.st[:].indirect(L("lK")), ["st", "lsB", "g0"],
+        sr, st = ("sk", "sl") if parts == (0,) else ("sr", "st")
+        return [lambda: TR(T[st][:, 0:n], st, T[sr][:, 16:16 + n], sr),
+                lambda: TR(T[st][:, 256:288 + n], st, T[sr][:, 0:32 + n], [sr, "srp"]),
+                lambda: TS(T.LG[:, 0:16] if n == 256 else T.LG[:, o:32:2], keys("LG", parts), T[st][:].indirect(L("lK")), [st, "slp", "lsB", "g0"],
                            C("g0"), None, A.add)]
 
     def unpack(c, q, qk, o, sc, part="TS", k=0):
@@ -372,9 +383,10 @@ def rank_program(g, core, T, topo):
     both = (0, 1)
     for o in both:
         MM(4 * o, 128, "qu", 0, ("na0", "nb0")[o])
-    TS(T.cs[:, 0:512:4], "cs", T.vk[:], ["vk", "zcA", "wu", "cs0"], C("jj"), C("wu"), A.is_equal, A.mult)
-    TS(T.cs[:, 512:1024:4], "cs", T.vg[:], ["vg", "zcA", "cs0"], C("jj"), C("w2"), A.is_equal, A.mult)
-    QT("qcs", 0, 256, T.cs[:], "cs")
+    for b in range(NCE, 4):
+        QT("qce", 128 * b, 128 * b + 128, T.ce[:, 3 - b:515 - b], "ce")
+    for b in range(NCG):
+        QT("qcg", 128 * b, 128 * b + 128, T.cg[:, 3 - b:515 - b], "cg")
     for o in both:
         TS(T.B[:, 512 * o:512 * o + 512:4], "B%d" % o, T["ps%d" % (4 * o)][:, 0:128], "ps%d" % (4 * o), 0.0, None, A.is_gt)
     for o in both:
@@ -382,7 +394,8 @@ def rank_program(g, core, T, topo):
     for bank, c, o in ((5, 0, 0), (6, 0, 1), (7, 128, 0), (1, 128, 1)):
         MM(bank, 128, "qcs", c, "qb%d" % o)
     turn("lR", "lK", "zcB", "zrB")
-    QT("qcg", 256, 384, T.cg[:, 1:513], "cg")
+    for b in range(NCG, 4):
+        QT("qcg", 128 * b, 128 * b + 128, T.cg[:, 3 - b:515 - b], "cg")
     TS(L("lR0"), "lsB", T.rows[:, 8:16], ["rows", "zcB"], C("lR"), None, A.add)
     TS(L("lD0"), "lsB", T.rows[:, 0:4], ["rows", "zcB"], C("lD"), None, A.add)
     TS(L("lW"), "lsB", T.zer[:, 0:4], ["zer", "zcB"], C("lW"), None, A.add)
@@ -391,7 +404,6 @@ def rank_program(g, core, T, topo):
         ACT(T.sr[:, 16 + 128 * o:144 + 128 * o], "sr", T["ps%d" % (7, 1)[o]][:, 0:128], "ps%d" % (7, 1)[o])
         rows_V((o,), T.crow[:, 128 * o:128 * o + 128])
     TS(C("g0"), "g0", C("pf"), "pf", 16.0, 32.0, A.is_lt, A.mult)
-    QT("qcg", 384, 512, T.cg[:, 0:512], "cg")
 
     for r in range(NR):
         last = r == NR - 1
@@ -402,14 +414,16 @@ def rank_program(g, core, T, topo):
         unpack("qce", "qn%d" % r, ["na%d" % r, "nb%d" % r], "Fo", 1 / 128)
         first[1]()
         if r == 0:
+            ACT(T.hrow[:, 0:256:32], "hrow", T.hrow[:, 0:256:32], "hrow0", AF.Identity, bias=DROP)
             pb, pk, ends = T.pb, ["pb0", "pb1"], T.pb[:, 0:256:32]
             head = [lambda: CP(T.R[:], "R", T.pb[:].indirect(L("lR0")), pk + ["lsB"])]
             fill = []
         else:
             pb, pk, ends = T.pm, ["pm"], T.pm[:, 0:128:16]
-            head = [lambda: TT(T.R[:], "R", T.pb[:, 128:256].indirect(L("lR1")), T.pkr[:], ["pb1", "pkr", "lsD"], A.max),
-                    lambda: TT(ends, "pm", T.pb[:, 128:256:16], T.e1[:, 0:128:16], ["e1", "pb1"], A.max)]
-            fill = [lambda: None, lambda: None]
+            weave(kept, [])
+            TT(ends, "pm", T.pb[:, 128:256:16], T.e1[:, 0:128:16], ["e1", "pb1"], A.max)
+            head = [lambda: TT(T.R[:], "R", T.pb[:, 128:256].indirect(L("lR1")), T.pkr[:], ["pb1", "pkr", "lsD"], A.max)]
+            fill = []
         weave(head + [lambda: TR(T.al[:], "al", T.R[:], "R"),
                       lambda: TT(T.dif[:], "dif", pb[:].indirect(L("lD%d" % min(r, 1))), T.al[:, 0:128:2], pk + ["al", "lsB", "lsD"], A.subtract),
                       lambda: TS(T.neg[:], "neg", T.dif[:], "dif", 0.0, GONE / U, A.min, A.mult),
@@ -421,18 +435,20 @@ def rank_program(g, core, T, topo):
                       lambda: TS(T.Y[:, 71:72], "cap", C("fl"), ["fl", "zcA"], FAR, C("us"), A.mult, A.subtract)])
         if r == 0:
             fill = lists + [lambda: TS(T.cc[:, 24:48], "cc", T.cc[:, 0:24], "cc0", -127.5, None, A.add),
-                    lambda: TT(T.c1[:], "c1", T.fs[:, 0:256:32], T.cc[:, 24:32], ["fs0", "fs1", "cc"], A.add),
-                    lambda: turn("lO", "lS", "zcC", "zrC")]
+                            lambda: TT(T.c1[:], "c1", T.fs[:, 0:256:32], T.cc[:, 24:32], ["fs0", "fs1", "cc"], A.add),
+                            lambda: turn("lO", "lS", "zcC", "zrC")]
         else:
-            fill = lists + [lambda: TT(T.ck[:, 8:16], "ck1", T.fs[:, 128:256:16], T.cc[:, 40:48], ["fs1", "cc"], A.add),
-                            lambda: TT(T.c1[:], "c1", T.ck[:, 0:8], T.ck[:, 8:16], ["ck0", "ck1"], A.min)]
+            fill = lists + [lambda: TT(T.ck[:], "ck", T.fs[:, 0:256:16], T.cc[:, 32:48], ["fs0", "fs1", "cc"], A.add),
+                            lambda: TT(T.c1[:], "c1", T.ck[:, 0:8], T.ck[:, 8:16], "ck", A.min)]
+        fill.append(lambda: TS(T.zf[:, RP2 + 1:RP2 + 32:16], "rp2", T.pen[:, 0:2], ["pen", "fl"], C("fl"), 4096.0, A.mult, A.add))
+        mates = [lambda: TR(T.zf[:, TR2:TR2 + 32], "tr2", T.zf[:, RP2:RP2 + 32], "rp2")]
+        if r:
+            fill.append(mates.pop())
         weave(level(32, 64, "rep1") + [lambda: [TR(T.zf[p:p + 32, TRP:TRP + 32], "trp2", T.rep[32:64, 8:40], "rep1") for p in (64, 96)]]
               + level(64, 128, "rep2") + [lambda: TR(T.zf[:, TRF:TRF + 32], "trf", T.rep[:, 8:40], ["rep0", "rep1", "rep2"])],
-              [lambda: TS(T.zf[:, RP2 + 1:RP2 + 32:16], "rp2", T.pen[:, 0:2], ["pen", "fl"], C("fl"), 4096.0, A.mult, A.add)] + fill
-              + [lambda: TR(T.zf[:, TR2:TR2 + 32], "tr2", T.zf[:, RP2:RP2 + 32], "rp2")] + [lambda: None] * (5 - len(fill))
-              + [lambda: TS(T.k1[:], "k1", T.Y[:, 7:64:8], "Y", 256.0, DROP, A.mult, A.min)])
+              fill + [lambda: TS(T.k1[:], "k1", T.Y[:, 7:64:8], "Y", 256.0, DROP, A.mult, A.min)])
         ACT(T.dr[:], "dr", T.dT[:].indirect(T.LG[:, 0:16]), ["dT", "LG0", "LG1"])
-        ACT(T.dr[:, 31:256:32], "dr", T.dr[:, 31:256:32], "dr", AF.Identity, bias=-DROP)
+        ACT(T.dr[:, 0:256:32], "dr", T.dr[:, 0:256:32], "dr", AF.Identity, bias=-DROP)
         key = T.key[:, 16:272]
         if r == 0:
             k0 = 32 * COLS.index("lO")
@@ -444,18 +460,17 @@ def rank_program(g, core, T, topo):
                lambda: TR(T.kt[:, 0:256], "kt0", key, "key")],
               [lambda: TT(T.k2[:], "k2", T.k1[:], T.c1[:], ["k1", "c1"], A.add),
                lambda: RED(C("km"), "km", T.k2[:], "k2", A.min),
-               lambda: TS(C("rn"), "rn", C("km"), "km", ROUND256, -ROUND256, A.add, A.add)])
-        TS(T.own[:, 0:16], "own0", T.kt[:, 0:256].indirect(L("lO")), ["kt0", "lsC", "zcA"], C("fx"), None, A.add)
-        TS(T.key[:, 47:272:32], "key", T.key[:, 47:272:32], "key", DROP, None, A.add)
-        TS(T.lf[:, 16 * r:16 * r + 2], "lf%d" % r, T.pen[:, 2:4], ["pen", "km", "rn"], C("km"), C("rn"), A.add, A.subtract)
-        TR(T.kt[:, 256:544], "kt1", T.key[:], "key")
-        need("G", toks_of("G", ["lf%d" % r], []))
-        g.remote_dma(T.fa[:, 16 * r:16 * r + 2], T.lf[:, 16 * r:16 * r + 2], T.sem["arf%d" % r], T.sem.sent, pid, rid, mask)
-        landed("arf%d" % r, n_in, ["fa%d" % r])
-        CP(T.k16[:, 0:128], "k16", T.key[:, 16:144], "key")
+               lambda: TR(T.kt[:, 256:544], "kt1", T.key[:], "key")])
+        CP(T.own[:, 0:16], "own0", T.kt[:, 0:256].indirect(L("lO")), ["kt0", "lsC"])
+        TS(C("rn"), "rn", C("km"), "km", ROUND256, -ROUND256, A.add, A.add)
         CP(T.ow2[:, 0:16], "owh", T.kt[:, 256:544].indirect(L("l2")), ["kt1", "lsC"])
-        CP(T.k16[:, 128:256], "k16", T.key[:, 144:272], "key")
+        CP(T.k16[:], "k16", key, "key")
         TT(T.ow2[:, 16:32], "owl", T.kt[:, 256:544].indirect(L("l2")), T.ow2[:, 0:16], ["kt1", "lsC", "owh"], A.subtract)
+        if NV < 8:
+            CP(T.own[:, 16:32], "own1", T.kt[:, 256:544].indirect(L("l2")), ["kt1", "lsC"])
+        TS(T.lf[:, 16 * r:16 * r + 2], "lf%d" % r, T.pen[:, 2:4], ["pen", "km", "rn"], C("km"), C("rn"), A.add, A.subtract)
+        send(T.fa, T.lf, 2, "f", r)
+        weave(mates, [])
         ng = ("ng0", "ng1")[min(r, 1)]
         nj = [0]
 
@@ -466,17 +481,11 @@ def rank_program(g, core, T, topo):
                 accum_out=T.acc[:, 16 * k + 2 * i + w:16 * k + 2 * i + w + 1])
 
         def places(k):
-            a = slice(16 * k, 16 * k + 16)
-            ak = ["acc%dV" % k, "acc%dS" % k, "lsC"]
-            return [lambda: (TS(T.oa[:, a], "oa%d" % k, T.acc[:, a].indirect(L("lS")), ak, 16 / 255, None, A.mult),
-                             TS(T.oq[:, a], "oq%d" % k, T.acc[:, a].indirect(L("lS")), ak, 1 / 16, 15.5, A.mult, A.add)),
-                    lambda: TT(T.od[:, a], "od%d" % k, T.oa[:, a], T.oq[:, a], ["oa%d" % k, "oq%d" % k], A.subtract),
-                    lambda: TS(T.pl[:, a], "pl%d" % k, T.od[:, a], ["od%d" % k, "xc"], 255.0, C("xc"), A.mult, A.add)]
+            return [lambda: TS(T.pl[:], "pl0", T.acc[:].indirect(L("lS")), ["acc0V", "acc0S", "lsC", "xc"], 0.5, C("xc"), A.mult, A.add)]
 
-        def scatter(k, a, b):
-            o = 16 * k + 2 * (a - PIECES[k][0])
-            return lambda: emit("V", lambda: v.tensor_copy(T.win[:].indirect(T.pl[:, o:o + 2 * (b - a)]), T.prb[:, 32 * a:32 * b]),
-                                ["pl%d" % k, "prb", "win"], ["win"])
+        def deal(o, ok, a):
+            for h in range(8):
+                TR(o[:, 32 * h:32 * h + 32], ok, T.win[:, a + h:a + 256:8], "win")
 
         units = [(k, i, b, w) for k, piece in enumerate(PIECES) for w in range(2) for i, b in enumerate(piece) if w == 0 or b >= NV]
         for u in units:
@@ -486,41 +495,35 @@ def rank_program(g, core, T, topo):
         for t in range(4):
             ACT(T.G[:, 272 * t:272 * t + 16], "Gf%d" % t, T.G[:, 272 * t + 16:272 * t + 272].indirect(T.fa[:, 16 * r:16 * r + 1]), ["G%d" % t, "fa%d" % r])
         for b in range(NV):
-            TS(T.jv[:, 256 * b:256 * b + 256], "jv%d" % b, T.k16[:], ["k16", "owh", "owl"], T.ow2[:, b:b + 1], T.ow2[:, 16 + b:17 + b],
-               A.subtract, A.is_lt)
+            TS(T.jv[:, 256 * b:256 * b + 256], "jv%d" % b, T.k16[:], ["k16", "owh", "owl"], T.ow2[:, b:b + 1], T.ow2[:, 16 + b:17 + b], A.subtract, A.is_lt)
         for b in range(NV):
             SCAN(T.jo[:, 128 * b:128 * b + 128], "jo", T.jv[:, 256 * b:256 * b + 128], T.jv[:, 256 * b + 128:256 * b + 256], "jv%d" % b, 0.0, A.add, A.add)
         if r == 0:
-            TS(C("xc"), "xc", C("lR"), "zcB", 0.5, 4080.0, A.mult, A.add)
-        cuts = (0, 6, 12, 14, 16)
+            TS(C("xc"), "xc", C("lR"), "zcB", 4.0, 127.5, A.mult, A.add)
         vals = [lambda a=a, b=b: TT(T.prb[:, 16 * a:16 * b], "prb", T.zf[:, TR2:TR2 + 48].indirect(T.LG[:, a:b]), T[ng][:, 16 * a:16 * b],
-                                    ["tr2", "tr2c", "LG0", "LG1", ng], A.min) for a, b in zip(cuts, cuts[1:])]
+                                    ["tr2", "tr2c", "LG0", "LG1", ng], A.min) for a, b in zip(CUTS, CUTS[1:])]
         vals[0]()
         weave([lambda: TS(T.acc[:, 1:2 * NV:2], "acc0V", T.jo[:, 127:128 * NV:128], "jo", 2.0, -255.0, A.mult, A.add)] + places(0), vals[1:])
-        scatter(0, 0, 8)()
-        ll = T.ll[:, 16 * r:16 * r + 16]
-        TR(T.wt[:], "wt", T.win[:, 0:256], "win")
-        TS(ll, "ll%d" % r, T.wt[:].indirect(L("lL")), ["wt", "lsC"], 144.0, None, A.add)
-        need("G", toks_of("G", ["ll%d" % r], []))
-        g.remote_dma(T.la[:, 16 * r:16 * r + 16], ll, T.sem["arl%d" % r], T.sem.sent, pid, rid, mask)
-        landed("arl%d" % r, n_in, ["la%d" % r])
-        TR(T.wk[:], "wk", T.win[:, 16:272], "win")
+        emit("V", lambda: v.tensor_copy(T.win[:].indirect(T.pl[:, 0:16]), T.prb[:]), ["pl0", "prb", "win"], ["win"])
+        deal(T.wt, "wt", 0)
+        TS(T.ll[:, 16 * r:16 * r + 16], "ll%d" % r, T.wt[:].indirect(L("lL")), ["wt", "lsC"], 144.0, None, A.add)
+        send(T.la, T.ll, 16, "l", r)
+        deal(T.wk, "wk", 128)
         if r == 0:
             TS(C("m2"), "m2", C("jj"), "zcA", 2.0, None, A.is_equal)
         TS(T.lk[:], "lk", T.wk[:].indirect(L("lO")), ["wk", "lsC"], 128.0, None, A.add)
         for t in range(4):
-            src = T.Fo[:, 256 * t:256 * t + 256].indirect(T.lk[:, 0:8])
-            (CP if t < 2 else ACT)(T.X[:, t:512:4], "X0" + "VS"[t // 2], src, ["Fo%d" % t, "lk"])
+            (CP if t < XV else ACT)(T.X[:, t:512:4], "X0" + "VS"[t >= XV], T.Fo[:, 256 * t:256 * t + 256].indirect(T.lk[:, 0:8]), ["Fo%d" % t, "lk"])
         z = "qz%d" % r
         for t in range(4):
-            (ACT if t else CP)(T.gz[:, 128 * t:128 * t + 128], "gz%d" % t, T.G[:, 272 * t:272 * t + 272].indirect(T.la[:, 16 * r + 8:16 * r + 16]),
-                               ["G%d" % t, "Gf%d" % t, "la%d" % r])
+            (CP if t < GV else ACT)(T.gz[:, 128 * t:128 * t + 128], "gz%d" % t, T.G[:, 272 * t:272 * t + 272].indirect(T.la[:, 16 * r + 8:16 * r + 16]),
+                                    ["G%d" % t, "Gf%d" % t, "la%d" % r])
         if r == 0:
             ACT(T.dl2[:], "dl2", T.dlt[:], ["dlt", "m2"], scale=C("m2"))
         for t in range(4):
             if t == QNA:
                 QT("na%d" % (r + 1), 0, 128, T.X[:, 0:512], ["X0V", "X0S"])
-            TT(T.Z[:, t:512:4], "Z", T.F[:, 272 * t:272 * t + 272].indirect(T.la[:, 16 * r:16 * r + 8]), T.gz[:, 128 * t:128 * t + 128],
+            TT(T.Z[:, t:512:4], "ZV", T.F[:, 272 * t:272 * t + 272].indirect(T.la[:, 16 * r:16 * r + 8]), T.gz[:, 128 * t:128 * t + 128],
                ["F%d" % t, "Fp", "la%d" % r, "gz%d" % t], A.add)
         if last:
             MM(4, 128, "qv", 0, "na3")
@@ -528,7 +531,7 @@ def rank_program(g, core, T, topo):
             emit("Y", lambda: g.sync.dma_start(T.op[:], T.opw[2:128:16, :]), ["opw"], ["op"], dma=True)
         else:
             scores(r + 1, (0,))
-        QT(z, 0, 128, T.Z[:], "Z")
+        QT(z, 0, 128, T.Z[:], ["ZV", "ZS"])
         for b in range(4):
             MM(b, 128, "qw", 128 * b, z, None, True, False)
             MM(b, 128, "qce", 128 * b, z, None, False, True)
@@ -538,6 +541,7 @@ def rank_program(g, core, T, topo):
             bits((0,))
             if r == 0:
                 FILL(T.r16[:], "r160", 1.0)
+                TS(T.rows[:, 16:32], "rows2", T.rows[:, 48:64], "rows3", -127.5, None, A.add)
                 TS(L("lR1"), "lsD", L("lR0"), "lsB", 0.5, None, A.mult)
                 TS(L("lD1"), "lsD", L("lD0"), "lsB", 0.5, None, A.mult)
                 FILL(T.cra[:], "cra0", U)
@@ -546,7 +550,7 @@ def rank_program(g, core, T, topo):
                 FILL(T.cra[:, 15:128:16], "cra", 16 * GONE, "cra0")
                 TT(T.ng1[:], "ng1", T.dl2[:], T.ngn[:], ["dl2", "ngn"], A.add)
             else:
-                TS(L("lP"), "lsE", T.rows[:, 16:32], ["rows2", "zcC"], C("lL"), None, A.add)
+                TS(L("lP"), "lsE", T.rows[:, 16:32], ["rows2", "zcA", "xc"], C("jj"), C("xc"), A.add, A.add)
                 TS(L("lF"), "lsE", T.rows[:, 32:48], ["rows2", "zcA"], C("jj"), None, A.add)
                 QT("qv", 0, 128, T.vs[:], "vs")
         for b in range(4):
@@ -560,22 +564,20 @@ def rank_program(g, core, T, topo):
             scores(r + 1, (1,))
             send_codes(r + 1)
             rows_S((0,))
-            rows_V((0,))
+            rows_V((0,), T.crow[:, 256:384])
             SCAN(T.pt[:], "pt", T.r16[:], T.ps5[:, 0:128], ["r16", "ps5"], 0.0, A.mult, A.add)
             kept, first = list_V((0,)), firsts((0,))
-            kept[0]()
             first[0]()
-            kept[1]()
             TS(T.pt8[:, 0:8], "pt8", T.pt[:, 15:128:16], "pt", 16 * U, None, A.add)
-            TS(T.pt8[:, 8:16], "pt9", T.pt[:, 15:128:16], "pt", 16 * U - 8 * GONE, None, A.add)
             bits((1,))
-            TS(T.pt8[:, 16:24], "pta", T.pb[:, 0:128:16], "pb0", DROP, 8 * GONE + U, A.is_ge, A.mult)
             TT(T.e1[:, 0:128:16], "e1", T.pb[:, 0:128:16], T.pt8[:, 0:8], ["pb0", "pt8"], A.min)
-            first[1]()
-            TT(T.cra[:, 0:128:16], "cra", T.pt8[:, 8:16], T.pt8[:, 16:24], ["pt9", "pta"], A.add)
+            TS(T.pt8[:, 16:24], "pta", T.pb[:, 0:128:16], "pb0", DROP, 8 * GONE + U, A.is_ge, A.mult)
+            TS(T.pt8[:, 8:16], "pt9", T.pt[:, 15:128:16], "pt", 16 * U - 8 * GONE, None, A.add)
+            kept[0]()
             CP(T.pkr[:], "pkr", T.e1[:].indirect(L("lR1")), ["e1", "lsD"])
-            kept[2]()
-            TT(T.ck[:, 0:8], "ck0", T.fs[:, 0:128:16], T.cc[:, 32:40], ["fs0", "cc"], A.add)
+            TT(T.cra[:, 0:128:16], "cra", T.pt8[:, 8:16], T.pt8[:, 16:24], ["pt9", "pta"], A.add)
+            kept[1]()
+            kept = [first[1], kept[2]]
             rows_S((1,))
             rows_V((1,))
     MM(5, 128, "qv", 0, "nb3")

@@ -7,14 +7,15 @@ DROP = float(1 << 22)
 FAR = float(1 << 30)
 ROUND256 = 1.5 * float(1 << 31)
 PIECES = ((0, 1, 2, 3, 4, 5, 6, 7),)
-NCE, NCG = 2, 2
-CUTS = (0, 6, 12, 16)
+NCE, NCG = 1, 1
+HV = 2
+CUTS = (0, 6, 16)
 XV, GV, QNA = 2, 1, 0
 NV = 8
-COLS = ["jj", "us", "w2", "lR", "lD", "lW", "lK", "lO", "l2", "lL", "lS"]
-LISTS = {"lO": (0, 1), "l2": (2, 1), "lL": (4, 1), "lS": (6, 1), "lW": (8, 4), "lD0": (12, 4), "lR0": (16, 8), "lP": (24, 16), "lF": (40, 16),
+COLS = ["jj", "us", "w2", "lR", "lD", "lW", "lK", "lO", "l2", "lL", "lU0", "l4", "lU1", "lG1"]
+LISTS = {"lO": (0, 1), "l2": (2, 1), "lL": (4, 1), "lU0": (6, 1), "l4": (8, 1), "lU1": (70, 1), "lG1": (72, 1), "lW": (74, 4), "lD0": (12, 4), "lR0": (16, 8), "lP": (24, 16), "lF": (40, 16),
          "lK": (56, 1), "lD1": (58, 4), "lR1": (62, 8)}
-SMALL = ["pf", "wu", "g0", "nb", "m2", "mn", "fl", "km", "rn", "xc"]
+SMALL = ["pf", "wu", "g0", "nb", "m2", "mn", "fl", "km", "rn", "xc", "x2", "o0", "o1", "o2", "m3"]
 RST, E40, TRP, TRF, RP2, TR2 = 0, 64, 104, 136, 184, 216
 
 SCRATCH = {}
@@ -29,12 +30,12 @@ for _n, _k, _d in (
         ("one", 128, "bfloat16"), ("zer", 528, "bfloat16"), ("idn", 128, "bfloat16"), ("prm", 128, "bfloat16"),
         ("ce", 528, "bfloat16"), ("cg", 528, "bfloat16"), ("cs", 1024, "bfloat16"), ("vk", 128, "float32"), ("vg", 128, "float32"),
         ("zr", 32 * len(COLS), "float32"), ("zc", 32 * len(COLS), "float32"), ("sm", 8 * len(SMALL), "float32"),
-        ("ls", 74, "uint16"), ("rows", 64, "float32"), ("cc", 48, "float32"),
+        ("ls", 78, "uint16"), ("rows", 64, "float32"), ("cc", 48, "float32"),
         ("crow", 384, "float32"), ("wrow", 384, "bfloat16"), ("r16", 128, "bfloat16"), ("dT", 48, "float32"),
         ("hrow", 256, "float32"), ("zf", 264, "float32"), ("crep", 32, "float32"), ("cra", 128, "float32"),
-        ("ng0", 256, "bfloat16"), ("ng1", 256, "bfloat16"), ("ngn", 256, "bfloat16"), ("dlt", 256, "bfloat16"), ("dl2", 256, "bfloat16"),
+        ("ng0", 256, "bfloat16"), ("ng1", 256, "bfloat16"), ("ngn", 256, "bfloat16"), ("dl2", 256, "bfloat16"), ("dl3", 256, "bfloat16"),
         ("B", 1024, "bfloat16"), ("dz", 256, "bfloat16"), ("ab", 256, "bfloat16"), ("dr", 256, "float32"),
-        ("sr", 288, "bfloat16"), ("st", 544, "bfloat16"), ("sk", 160, "bfloat16"), ("sl", 544, "bfloat16"), ("LG", 32, "uint16"),
+        ("sr", 288, "bfloat16"), ("st", 1088, "bfloat16"), ("sk", 160, "bfloat16"), ("LG", 16, "uint16"), ("LU", 16, "uint16"),
         ("pb", 256, "bfloat16"), ("fs", 256, "bfloat16"), ("e1", 128, "bfloat16"), ("pkr", 128, "bfloat16"), ("pm", 128, "bfloat16"), ("pt", 128, "float32"),
         ("pt8", 24, "float32"), ("ck", 16, "float32"), ("R", 128, "bfloat16"), ("al", 128, "bfloat16"),
         ("dif", 64, "float32"), ("neg", 64, "float32"), ("MT", 64, "float32"), ("yi", 64, "float32"), ("Y", 320, "float32"),
@@ -259,14 +260,14 @@ def rank_program(g, core, T, topo):
     ACT(T.crow[:, 31:256:32], "crow", T.zer[:, 0:8], ["zer", "crow0"], AF.Identity, bias=GONE)
     ACT(T.sr[:, 0:16], "srp", T.zer[:, 0:16], "zer")
     ACT(T.sr[:, 272:288], "srp", T.zer[:, 0:16], "zer")
-    ACT(T.key[:], "key", T.zer[:, 0:288], "zer")
+    ACT(T.key[:], ["key0", "key1"], T.zer[:, 0:288], "zer")
     ACT(T.win[:], "win", T.zer[:, 0:384], "zer")
     for t in range(4):
         ACT(T.F[:, 272 * t:272 * t + 16], "Fp", T.zer[:, 0:16], "zer")
     ACT(T.pm[:], "pm", T.zer[:, 0:128], "zer")
     ACT(T.e1[:], "e1", T.zer[:, 0:128], "zer")
     for a, b in ((128, 256), (416, 544)):
-        ACT(T.sl[:, a:b], "slp", T.zer[:, 0:128], "zer")
+        ACT(T.st[:, 544 + a:544 + b], "slp", T.zer[:, 0:128], "zer")
     for a in (0, 144):
         ACT(T.sk[:, a:a + 16], "srp", T.zer[:, 0:16], "zer")
 
@@ -277,17 +278,17 @@ def rank_program(g, core, T, topo):
     FILL(T.zf[:, 0:RP2], ["zf0", "trp1", "trp2", "trfc"], 0.0)
     TS(C("wu"), "wu", C("w2"), "zcA", U / 2, None, A.mult)
     TS(C("nb"), "nb", C("us"), "zcA", -U, None, A.add)
-    TS(T.cs[:, 0:512:4], "cs", T.vk[:], ["vk", "zcA", "wu", "cs0"], C("jj"), C("wu"), A.is_equal, A.mult)
-    TS(T.cs[:, 512:1024:4], "cs", T.vg[:], ["vg", "zcA", "cs0"], C("jj"), C("w2"), A.is_equal, A.mult)
-    FILL(T.zf[:, RST:RST + 64:8], "rst", -FAR, "zf0")
-    QT("qcs", 0, 256, T.cs[:], "cs")
-    FILL(T.wrow[:, 271:384:16], "wrow", 4096.0, "wrow0")
-    FILL(T.Y[:, 79:320:8], "Yc", FAR)
     TS(T.crep[:], "crep", T.zer[:, 0:32], ["zer", "zcA"], C("us"), None, A.add)
     CP(T.zf[:, E40 + 8:E40 + 9], "e40", C("us"), ["zcA", "zf0"])
+    TS(T.cs[:, 0:512:4], "cs", T.vk[:], ["vk", "zcA", "wu", "cs0"], C("jj"), C("wu"), A.is_equal, A.mult)
+    FILL(T.zf[:, RST:RST + 64:8], "rst", -FAR, "zf0")
+    FILL(T.wrow[:, 271:384:16], "wrow", 4096.0, "wrow0")
+    FILL(T.Y[:, 79:320:8], "Yc", FAR)
+    TS(T.cs[:, 512:1024:4], "cs", T.vg[:], ["vg", "zcA", "cs0"], C("jj"), C("w2"), A.is_equal, A.mult)
     FILL(T.zf[:, RP2:264], ["rp2", "tr2c"], 4096.0)
     FILL(T.pen[:, 2:4], "pen", 127.5)
     TS(T.pen[:, 0:2], "pen", T.crep[:, 0:2], "crep", 2 / U, -146.0 - 4096.0, A.mult, A.add)
+    QT("qcs", 0, 256, T.cs[:], "cs")
     for b in range(NCE):
         QT("qce", 128 * b, 128 * b + 128, T.ce[:, 3 - b:515 - b], "ce")
     QT("qu", 0, 128, T.us[:], "us")
@@ -301,14 +302,18 @@ def rank_program(g, core, T, topo):
     IOTA(row("lO"), "zrC", [[16, 2], [0, 2], [32, 8]], 0)
     IOTA(row("l2"), "zrC", [[-16, 2], [0, 2], [32, 8]], 32)
     IOTA(row("lL"), "zrC", [[16, 2], [1, 2], [32, 8]], 0)
-    IOTA(row("lS", 0, 16), "zrC", [[1, 16]], 0)
-    IOTA(row("lS", 16, 32), "zrC", [[2, 8], [-1, 2]], 1)
-    IOTA(T.ng0[:], "ng0", [[1, 256]], -128)
+    IOTA(row("lU0", 0, 16), "zrC", [[288, 2], [32, 8]], 0)
+    IOTA(row("lU0", 16, 32), "zrC", [[256, 2], [32, 8]], 16)
+    IOTA(row("l4"), "zrC", [[16, 2], [0, 4], [32, 4]], 0)
+    IOTA(T.ng0[:], "ng00", [[16, 2], [32, 8], [1, 16]], -128)
     send_codes(0)
     IOTA(T.rows[:, 48:64], "rows3", [[16, 16]], 0)
     IOTA(T.rows[:, 32:48], "rows2", [[16, 8], [128, 2]], 0)
-    IOTA(T.ngn[:], "ngn", [[16, 8], [128, 2], [1, 16]], -128)
-    IOTA(T.dlt[:], "dlt", [[16, 8], [-112, 2], [0, 16]], 0)
+    IOTA(T.ngn[:], "ngn0", [[128, 2], [16, 8], [1, 16]], -128)
+    IOTA(row("lU1", 0, 16), "zrD", [[-544, 2], [32, 4], [288, 2]], 544)
+    IOTA(row("lU1", 16, 32), "zrD", [[544, 2], [32, 4], [-256, 2]], 272)
+    IOTA(row("lG1", 0, 16), "zrD", [[32, 4], [288, 2], [-544, 2]], 544)
+    IOTA(row("lG1", 16, 32), "zrD", [[32, 4], [-256, 2], [-544, 2]], 816)
 
     def dims(parts):
         return (256, 0) if len(parts) == 2 else (128, parts[0])
@@ -335,12 +340,10 @@ def rank_program(g, core, T, topo):
         n, o = dims(parts)
         ACT(T[("sk", "sr")[o]][:, 16:16 + n], ("sk", "sr")[o], T.ps7[:, 0:n], "ps7")
 
-    def rows_V(parts, c=None):
-        n, o = dims(parts)
-        if c is None:
-            c = T.cra[:]
-        TS(T.ab[:, 128 * o:128 * o + n], keys("ab", parts), T["ps%d" % (5 + o)][:, 0:n], ["ps%d" % (5 + o), "nb"], C("nb"), GONE, A.not_equal, A.mult)
-        TT(T.dz[:, 128 * o:128 * o + n], keys("dz", parts), T["ps%d" % (5 + o)][:, 0:n], c, ["ps%d" % (5 + o), "crow"] + ["cra"] * o, A.add)
+    def rows_V(o, c, more=()):
+        a, ps = slice(128 * o, 128 * o + 128), "ps%d" % (5 + o)
+        TS(T.ab[:, a], ["ab%d" % o] + ["a" + k for k in more], T[ps][:, 0:128], [ps, "nb"], C("nb"), GONE, A.not_equal, A.mult)
+        TT(T.dz[:, a], ["dz%d" % o] + ["d" + k for k in more], T[ps][:, 0:128], c, [ps, "crow"], A.add)
 
     def firsts(parts):
         n, o = dims(parts)
@@ -352,11 +355,13 @@ def rank_program(g, core, T, topo):
 
     def list_V(parts):
         n, o = dims(parts)
-        sr, st = ("sk", "sl") if parts == (0,) else ("sr", "st")
-        return [lambda: TR(T[st][:, 0:n], st, T[sr][:, 16:16 + n], sr),
-                lambda: TR(T[st][:, 256:288 + n], st, T[sr][:, 0:32 + n], [sr, "srp"]),
-                lambda: TS(T.LG[:, 0:16] if n == 256 else T.LG[:, o:32:2], keys("LG", parts), T[st][:].indirect(L("lK")), [st, "slp", "lsB", "g0"],
-                           C("g0"), None, A.add)]
+        sr, st, a = ("sk", "sl", 544) if parts == (0,) else ("sr", "st", 0)
+        win, lg, lu = (T.st[:, 0:544], "lK", "lU0") if n == 256 else (T.st[:], "lG1", "lU1")
+        ik = ["st", "sl", "slp", "lsB", "lsD", "g0"]
+        return [lambda: TR(T.st[:, a:a + n], st, T[sr][:, 16:16 + n], sr),
+                lambda: TR(T.st[:, a + 256:a + 288 + n], st, T[sr][:, 0:32 + n], [sr, "srp"]),
+                lambda: TS(T.LG[:], "LG", win.indirect(L(lg)), ik, C("g0"), None, A.add),
+                lambda: TS(T.LU[:], "LU", win.indirect(L(lu)), ik + ["lsC"], C("g0"), None, A.add)]
 
     def unpack(c, q, qk, o, sc, part="TS", k=0):
         for b in range(4):
@@ -402,7 +407,7 @@ def rank_program(g, core, T, topo):
     CP(L("lK"), "lsB", C("lK"), "zcB")
     for o in both:
         ACT(T.sr[:, 16 + 128 * o:144 + 128 * o], "sr", T["ps%d" % (7, 1)[o]][:, 0:128], "ps%d" % (7, 1)[o])
-        rows_V((o,), T.crow[:, 128 * o:128 * o + 128])
+        rows_V(o, T.crow[:, 128 * o:128 * o + 128], ["c%d" % o])
     TS(C("g0"), "g0", C("pf"), "pf", 16.0, 32.0, A.is_lt, A.mult)
 
     for r in range(NR):
@@ -410,105 +415,127 @@ def rank_program(g, core, T, topo):
         parts = both if r == 0 else (1,)
         lists = list_V(parts)
         first = firsts(parts)
-        first[0]()
+        p0, n = (128, 64) if r else (0, 128)
+        for o in both:
+            a = p0 + n * o
+            SCAN(back(T.pb, a, a + n), ["pb%d" % (o | min(r, 1)), "pc%d" % o], back(T.dz, a, a + n), back(T.ab, a, a + n), ["dc%d" % o, "ac%d" % o], 0.0, A.add, A.min)
         unpack("qce", "qn%d" % r, ["na%d" % r, "nb%d" % r], "Fo", 1 / 128)
         first[1]()
+        lR, lD = LISTS["lR%d" % min(r, 1)][0], LISTS["lD%d" % min(r, 1)][0]
         if r == 0:
             ACT(T.hrow[:, 0:256:32], "hrow", T.hrow[:, 0:256:32], "hrow0", AF.Identity, bias=DROP)
-            pb, pk, ends = T.pb, ["pb0", "pb1"], T.pb[:, 0:256:32]
-            head = [lambda: CP(T.R[:], "R", T.pb[:].indirect(L("lR0")), pk + ["lsB"])]
-            fill = []
+            for c, sc, bi in (("xc", 4.0, 127.5), ("x2", 4.0, 0.0), ("o0", 0.5, 0.0), ("o1", -0.5, 0.0), ("o2", -4.0, 0.0)):
+                ACT(C(c), c, C("lR"), "zcB", AF.Identity, bias=bi, scale=sc)
+            pb, pk, ends = T.pb, ["pc0", "pc1"], T.pb[:, 0:256:32]
+            for o in both:
+                CP(T.R[:, 64 * o:64 * o + 64], "R%d" % o, T.pb[:, 128 * o:128 * o + 128].indirect(T.ls[:, lR:lR + 4]), ["pc%d" % o, "lsB"])
         else:
             pb, pk, ends = T.pm, ["pm"], T.pm[:, 0:128:16]
-            weave(kept, [])
-            TT(ends, "pm", T.pb[:, 128:256:16], T.e1[:, 0:128:16], ["e1", "pb1"], A.max)
-            head = [lambda: TT(T.R[:], "R", T.pb[:, 128:256].indirect(L("lR1")), T.pkr[:], ["pb1", "pkr", "lsD"], A.max)]
-            fill = []
-        weave(head + [lambda: TR(T.al[:], "al", T.R[:], "R"),
-                      lambda: TT(T.dif[:], "dif", pb[:].indirect(L("lD%d" % min(r, 1))), T.al[:, 0:128:2], pk + ["al", "lsB", "lsD"], A.subtract),
-                      lambda: TS(T.neg[:], "neg", T.dif[:], "dif", 0.0, GONE / U, A.min, A.mult),
-                      lambda: TT(T.MT[:], "MT", T.dif[:], T.neg[:], ["dif", "neg"], A.add)],
-              fill + [lambda: RED(C("mn"), "mn", ends, pk, A.min),
+            for o in both:
+                TT(T.R[:, 64 * o:64 * o + 64], "R%d" % o, T.pb[:, 128 + 64 * o:192 + 64 * o].indirect(T.ls[:, lR:lR + 4]), T.pkr[:, 64 * o:64 * o + 64],
+                   ["pc%d" % o, "pkr", "lsD"], A.max)
+                if o == 0:
+                    TT(ends, "pm", T.pb[:, 128:256:16], T.e1[:, 0:128:16], ["e1", "pc0", "pc1"], A.max)
+
+        def two(f):
+            return [lambda o=o: f(o, slice(32 * o, 32 * o + 32)) for o in both]
+
+        def pairs(steps, fill):
+            for (a, b), f in zip(steps, fill):
+                a()
+                f()
+                b()
+            weave(fill[len(steps):], [])
+
+        pairs([two(lambda o, a: TR(T.al[:, 64 * o:64 * o + 64], "al%d" % o, T.R[:, 64 * o:64 * o + 64], "R%d" % o)),
+               two(lambda o, a: TT(T.dif[:, a], "dif%d" % o, pb[:, n * o:n * o + n].indirect(T.ls[:, lD:lD + 2]), T.al[:, 64 * o:64 * o + 64:2],
+                                   pk + ["al%d" % o, "lsB", "lsD"], A.subtract)),
+               two(lambda o, a: TS(T.neg[:, a], "neg%d" % o, T.dif[:, a], "dif%d" % o, 0.0, GONE / U, A.min, A.mult)),
+               two(lambda o, a: TT(T.MT[:, a], "MT", T.dif[:, a], T.neg[:, a], ["dif%d" % o, "neg%d" % o], A.add))],
+                     [lambda: RED(C("mn"), "mn", ends, pk, A.min),
                       lambda: TS(C("fl"), "fl", C("mn"), "mn", DROP, None, A.is_lt),
                       lambda: TS(T.rep[0:32, 8:40], "rep0", T.crep[0:32, :], ["crep", "mn", "fl"], C("mn", 32), C("fl", 32), A.add, A.mult),
                       lambda: TR(T.zf[32:64, TRP:TRP + 32], "trp1", T.rep[0:32, 8:40], "rep0"),
                       lambda: TS(T.Y[:, 71:72], "cap", C("fl"), ["fl", "zcA"], FAR, C("us"), A.mult, A.subtract)])
         if r == 0:
-            fill = lists + [lambda: TS(T.cc[:, 24:48], "cc", T.cc[:, 0:24], "cc0", -127.5, None, A.add),
-                            lambda: TT(T.c1[:], "c1", T.fs[:, 0:256:32], T.cc[:, 24:32], ["fs0", "fs1", "cc"], A.add),
-                            lambda: turn("lO", "lS", "zcC", "zrC")]
+            fill = lists[0:3] + [lambda: TS(T.cc[:, 24:48], "cc", T.cc[:, 0:24], "cc0", -127.5, None, A.add),
+                                 lambda: TT(T.c1[:], "c1", T.fs[:, 0:256:32], T.cc[:, 24:32], ["fs0", "fs1", "cc"], A.add),
+                                 lambda: turn("lO", "l4", "zcC", "zrC")]
         else:
-            fill = lists + [lambda: TT(T.ck[:], "ck", T.fs[:, 0:256:16], T.cc[:, 32:48], ["fs0", "fs1", "cc"], A.add),
-                            lambda: TT(T.c1[:], "c1", T.ck[:, 0:8], T.ck[:, 8:16], "ck", A.min)]
+            fill = lists[0:2] + [lambda: (lists[2](), lists[3]()),
+                                 lambda: TT(T.ck[:], "ck", T.fs[:, 0:256:16], T.cc[:, 32:48], ["fs0", "fs1", "cc"], A.add),
+                                 lambda: TT(T.c1[:], "c1", T.ck[:, 0:8], T.ck[:, 8:16], "ck", A.min)]
         fill.append(lambda: TS(T.zf[:, RP2 + 1:RP2 + 32:16], "rp2", T.pen[:, 0:2], ["pen", "fl"], C("fl"), 4096.0, A.mult, A.add))
         mates = [lambda: TR(T.zf[:, TR2:TR2 + 32], "tr2", T.zf[:, RP2:RP2 + 32], "rp2")]
         if r:
             fill.append(mates.pop())
+        else:
+            mates.append(lists[3])
         weave(level(32, 64, "rep1") + [lambda: [TR(T.zf[p:p + 32, TRP:TRP + 32], "trp2", T.rep[32:64, 8:40], "rep1") for p in (64, 96)]]
               + level(64, 128, "rep2") + [lambda: TR(T.zf[:, TRF:TRF + 32], "trf", T.rep[:, 8:40], ["rep0", "rep1", "rep2"])],
               fill + [lambda: TS(T.k1[:], "k1", T.Y[:, 7:64:8], "Y", 256.0, DROP, A.mult, A.min)])
-        ACT(T.dr[:], "dr", T.dT[:].indirect(T.LG[:, 0:16]), ["dT", "LG0", "LG1"])
+        ACT(T.dr[:], "dr", T.dT[:].indirect(T.LG[:, 0:16]), ["dT", "LG"])
         ACT(T.dr[:, 0:256:32], "dr", T.dr[:, 0:256:32], "dr", AF.Identity, bias=-DROP)
+        if r == 0:
+            for n, a, c in (("ng0", 0, "o0"), ("ng0", 128, "o1"), ("ngn", 0, "x2"), ("ngn", 128, "o2")):
+                ACT(T[n][:, a:a + 128], n, T[n][:, a:a + 128], [n + "0", c], AF.Identity, bias=C(c))
         key = T.key[:, 16:272]
         if r == 0:
             k0 = 32 * COLS.index("lO")
-            CP(T.ls[:, 0:8:2], "lsC", T.zc[:, k0:k0 + 128:32], "zcC")
+            CP(T.ls[:, 0:10:2], "lsC", T.zc[:, k0:k0 + 160:32], "zcC")
         unpack("qcg", "qa%d" % r, None, "G", 1 / 256, "T")
         unpack("qce", "qa%d" % r, None, "F", 1 / 256, "T", 4)
-        weave([lambda: TT(T.wr[:], "wr", T.zf[:, TRF:TRF + 48].indirect(T.LG[:, 0:16]), T.hrow[:], ["trf", "trfc", "LG0", "LG1", "hrow"], A.add),
-               lambda: SCAN(key, "key", T.wr[:], T.dr[:], ["wr", "dr"], -1.0, A.max, A.add),
-               lambda: TR(T.kt[:, 0:256], "kt0", key, "key")],
-              [lambda: TT(T.k2[:], "k2", T.k1[:], T.c1[:], ["k1", "c1"], A.add),
-               lambda: RED(C("km"), "km", T.k2[:], "k2", A.min),
-               lambda: TR(T.kt[:, 256:544], "kt1", T.key[:], "key")])
-        CP(T.own[:, 0:16], "own0", T.kt[:, 0:256].indirect(L("lO")), ["kt0", "lsC"])
+        for o in both:
+            TT(T.wr[:, 128 * o:128 * o + 128], "wr%d" % o, T.zf[:, TRF:TRF + 48].indirect(T.LG[:, 8 * o:8 * o + 8]), T.hrow[:, 128 * o:128 * o + 128],
+               ["trf", "trfc", "LG", "hrow"], A.add)
+        for o in both:
+            SCAN(T.key[:, 16 + 128 * o:144 + 128 * o], "key%d" % o, T.wr[:, 128 * o:128 * o + 128], T.dr[:, 128 * o:128 * o + 128], ["wr%d" % o, "dr"],
+                 -1.0, A.max, A.add)
+            if o == 0:
+                TT(T.k2[:], "k2", T.k1[:], T.c1[:], ["k1", "c1"], A.add)
+        for o in both:
+            TR(T.kt[:, 128 * o:128 * o + 128], "kt%d" % o, T.key[:, 16 + 128 * o:144 + 128 * o], "key%d" % o)
+            if o == 0:
+                RED(C("km"), "km", T.k2[:], "k2", A.min)
+        CP(T.own[:, 0:16], "own0", T.kt[:, 0:128].indirect(L("l4")), ["kt0", "lsC"])
+        TR(T.kt[:, 256:544], "kt2", T.key[:], ["key0", "key1"])
+        CP(T.own[:, 16:32], "own1", T.kt[:, 128:256].indirect(L("l4")), ["kt1", "lsC"])
         TS(C("rn"), "rn", C("km"), "km", ROUND256, -ROUND256, A.add, A.add)
-        CP(T.ow2[:, 0:16], "owh", T.kt[:, 256:544].indirect(L("l2")), ["kt1", "lsC"])
-        CP(T.k16[:], "k16", key, "key")
-        TT(T.ow2[:, 16:32], "owl", T.kt[:, 256:544].indirect(L("l2")), T.ow2[:, 0:16], ["kt1", "lsC", "owh"], A.subtract)
-        if NV < 8:
-            CP(T.own[:, 16:32], "own1", T.kt[:, 256:544].indirect(L("l2")), ["kt1", "lsC"])
+        weave(mates, [])
+        CP(T.ow2[:, 0:16], "owh", T.kt[:, 256:544].indirect(L("l2")), ["kt2", "lsC"])
+        CP(T.k16[:], "k16", key, ["key0", "key1"])
+        TT(T.ow2[:, 16:32], "owl", T.kt[:, 256:544].indirect(L("l2")), T.ow2[:, 0:16], ["kt2", "lsC", "owh"], A.subtract)
         TS(T.lf[:, 16 * r:16 * r + 2], "lf%d" % r, T.pen[:, 2:4], ["pen", "km", "rn"], C("km"), C("rn"), A.add, A.subtract)
         send(T.fa, T.lf, 2, "f", r)
-        weave(mates, [])
         ng = ("ng0", "ng1")[min(r, 1)]
-        nj = [0]
-
-        def unit_S(k, i, b, w):
-            j = 256 * nj[0]
-            nj[0] += 1
-            ACT(T.js[:, j:j + 256], "acc%dS" % k, key, ["key", "own%d" % w], AF.Sign, bias=T.own[:, 16 * w + b:16 * w + b + 1], scale=-1.0,
-                accum_out=T.acc[:, 16 * k + 2 * i + w:16 * k + 2 * i + w + 1])
-
-        def places(k):
-            return [lambda: TS(T.pl[:], "pl0", T.acc[:].indirect(L("lS")), ["acc0V", "acc0S", "lsC", "xc"], 0.5, C("xc"), A.mult, A.add)]
-
-        def deal(o, ok, a):
-            for h in range(8):
+        def deal(o, ok, a, h0, h1):
+            for h in range(h0, h1):
                 TR(o[:, 32 * h:32 * h + 32], ok, T.win[:, a + h:a + 256:8], "win")
 
-        units = [(k, i, b, w) for k, piece in enumerate(PIECES) for w in range(2) for i, b in enumerate(piece) if w == 0 or b >= NV]
-        for u in units:
-            unit_S(*u)
+        for b in range(8):
+            j = 16 * (b // 4) + b % 4
+            ACT(T.js[:, 256 * b:256 * b + 256], "acc", key, ["key0", "key1", "own%d" % (b // 4)], AF.Sign, bias=T.own[:, j:j + 1], scale=-1.0,
+                accum_out=T.acc[:, b:b + 1])
         unpack("qcg", "qa%d" % r, None, "G", 1 / 256, "S")
         unpack("qce", "qa%d" % r, None, "F", 1 / 256, "S", 4)
         for t in range(4):
             ACT(T.G[:, 272 * t:272 * t + 16], "Gf%d" % t, T.G[:, 272 * t + 16:272 * t + 272].indirect(T.fa[:, 16 * r:16 * r + 1]), ["G%d" % t, "fa%d" % r])
-        for b in range(NV):
-            TS(T.jv[:, 256 * b:256 * b + 256], "jv%d" % b, T.k16[:], ["k16", "owh", "owl"], T.ow2[:, b:b + 1], T.ow2[:, 16 + b:17 + b], A.subtract, A.is_lt)
-        for b in range(NV):
-            SCAN(T.jo[:, 128 * b:128 * b + 128], "jo", T.jv[:, 256 * b:256 * b + 128], T.jv[:, 256 * b + 128:256 * b + 256], "jv%d" % b, 0.0, A.add, A.add)
-        if r == 0:
-            TS(C("xc"), "xc", C("lR"), "zcB", 4.0, 127.5, A.mult, A.add)
-        vals = [lambda a=a, b=b: TT(T.prb[:, 16 * a:16 * b], "prb", T.zf[:, TR2:TR2 + 48].indirect(T.LG[:, a:b]), T[ng][:, 16 * a:16 * b],
-                                    ["tr2", "tr2c", "LG0", "LG1", ng], A.min) for a, b in zip(CUTS, CUTS[1:])]
+        vals = [lambda a=a, b=b: TT(T.prb[:, 16 * a:16 * b], "prb", T.zf[:, TR2:TR2 + 48].indirect(T.LU[:, a:b]), T[ng][:, 16 * a:16 * b],
+                                    ["tr2", "tr2c", "LU", ng], A.min) for a, b in zip(CUTS, CUTS[1:])]
         vals[0]()
-        weave([lambda: TS(T.acc[:, 1:2 * NV:2], "acc0V", T.jo[:, 127:128 * NV:128], "jo", 2.0, -255.0, A.mult, A.add)] + places(0), vals[1:])
-        emit("V", lambda: v.tensor_copy(T.win[:].indirect(T.pl[:, 0:16]), T.prb[:]), ["pl0", "prb", "win"], ["win"])
-        deal(T.wt, "wt", 0)
+        for b in range(8):
+            TS(T.jv[:, 256 * b:256 * b + 256], "jv%d" % b, T.k16[:], ["k16", "owh", "owl"], T.ow2[:, b:b + 1], T.ow2[:, 16 + b:17 + b], A.subtract, A.is_lt)
+        for b in range(8):
+            SCAN(T.jo[:, 128 * b:128 * b + 128], "jo", T.jv[:, 256 * b:256 * b + 128], T.jv[:, 256 * b + 128:256 * b + 256], "jv%d" % b, 0.0, A.add, A.add)
+        weave(vals[1:], [])
+        TS(T.pl[:, 0:8], "pl", T.acc[:, 0:8], ["acc", "xc"], 0.5, C("xc"), A.mult, A.add)
+        TS(T.pl[:, 8:16], "pl", T.jo[:, 127:1024:128], ["jo", "x2"], C("x2"), None, A.add)
+        emit("V", lambda: v.tensor_copy(T.win[:].indirect(T.pl[:, 0:16]), T.prb[:]), ["pl", "prb", "win"], ["win"])
+        deal(T.wt, "wt", 0, 0, 8)
+        deal(T.wk, "wk", 128, 0, 3)
         TS(T.ll[:, 16 * r:16 * r + 16], "ll%d" % r, T.wt[:].indirect(L("lL")), ["wt", "lsC"], 144.0, None, A.add)
         send(T.la, T.ll, 16, "l", r)
-        deal(T.wk, "wk", 128)
+        deal(T.wk, "wk", 128, 3, 8)
         if r == 0:
             TS(C("m2"), "m2", C("jj"), "zcA", 2.0, None, A.is_equal)
         TS(T.lk[:], "lk", T.wk[:].indirect(L("lO")), ["wk", "lsC"], 128.0, None, A.add)
@@ -519,7 +546,9 @@ def rank_program(g, core, T, topo):
             (CP if t < GV else ACT)(T.gz[:, 128 * t:128 * t + 128], "gz%d" % t, T.G[:, 272 * t:272 * t + 272].indirect(T.la[:, 16 * r + 8:16 * r + 16]),
                                     ["G%d" % t, "Gf%d" % t, "la%d" % r])
         if r == 0:
-            ACT(T.dl2[:], "dl2", T.dlt[:], ["dlt", "m2"], scale=C("m2"))
+            ACT(C("m3"), "m3", C("m2"), "m2", AF.Identity, bias=1.0, scale=-1.0)
+            ACT(T.dl2[:], "dl2", T.ng0[:], ["ng0", "m2"], scale=C("m2"))
+            ACT(T.dl3[:], "dl3", T.ngn[:], ["ngn", "m3"], scale=C("m3"))
         for t in range(4):
             if t == QNA:
                 QT("na%d" % (r + 1), 0, 128, T.X[:, 0:512], ["X0V", "X0S"])
@@ -540,7 +569,9 @@ def rank_program(g, core, T, topo):
         else:
             bits((0,))
             if r == 0:
+                turn("lU1", "lG1", "zcD", "zrD")
                 FILL(T.r16[:], "r160", 1.0)
+                CP(T.ls[:, 70:74:2], "lsD", T.zc[:, 32 * COLS.index("lU1"):32 * len(COLS):32], "zcD")
                 TS(T.rows[:, 16:32], "rows2", T.rows[:, 48:64], "rows3", -127.5, None, A.add)
                 TS(L("lR1"), "lsD", L("lR0"), "lsB", 0.5, None, A.mult)
                 TS(L("lD1"), "lsD", L("lD0"), "lsB", 0.5, None, A.mult)
@@ -548,14 +579,14 @@ def rank_program(g, core, T, topo):
                 FILL(T.r16[:, 0:128:16], "r16", 0.0, "r160")
                 FILL(T.crow[:, 271:384:16], "crow", U + GONE, "crow0")
                 FILL(T.cra[:, 15:128:16], "cra", 16 * GONE, "cra0")
-                TT(T.ng1[:], "ng1", T.dl2[:], T.ngn[:], ["dl2", "ngn"], A.add)
+                TT(T.ng1[:], "ng1", T.dl2[:], T.dl3[:], ["dl2", "dl3"], A.add)
             else:
                 TS(L("lP"), "lsE", T.rows[:, 16:32], ["rows2", "zcA", "xc"], C("jj"), C("xc"), A.add, A.add)
                 TS(L("lF"), "lsE", T.rows[:, 32:48], ["rows2", "zcA"], C("jj"), None, A.add)
                 QT("qv", 0, 128, T.vs[:], "vs")
         for b in range(4):
             o, i = T.X[:, 512 + b:1024:4], T["ps%d" % b][:, 0:128]
-            if b >= 2:
+            if b >= HV:
                 TS(o, "X1V", i, "ps%d" % b, 0.0078125, None, A.mult)
             else:
                 ACT(o, "X1S", i, "ps%d" % b, scale=0.0078125)
@@ -564,22 +595,25 @@ def rank_program(g, core, T, topo):
             scores(r + 1, (1,))
             send_codes(r + 1)
             rows_S((0,))
-            rows_V((0,), T.crow[:, 256:384])
+            rows_V(0, T.crow[:, 256:384])
             SCAN(T.pt[:], "pt", T.r16[:], T.ps5[:, 0:128], ["r16", "ps5"], 0.0, A.mult, A.add)
             kept, first = list_V((0,)), firsts((0,))
             first[0]()
             TS(T.pt8[:, 0:8], "pt8", T.pt[:, 15:128:16], "pt", 16 * U, None, A.add)
             bits((1,))
-            TT(T.e1[:, 0:128:16], "e1", T.pb[:, 0:128:16], T.pt8[:, 0:8], ["pb0", "pt8"], A.min)
             TS(T.pt8[:, 16:24], "pta", T.pb[:, 0:128:16], "pb0", DROP, 8 * GONE + U, A.is_ge, A.mult)
             TS(T.pt8[:, 8:16], "pt9", T.pt[:, 15:128:16], "pt", 16 * U - 8 * GONE, None, A.add)
+            TT(T.e1[:, 0:128:16], "e1", T.pb[:, 0:128:16], T.pt8[:, 0:8], ["pb0", "pt8"], A.min)
             kept[0]()
-            CP(T.pkr[:], "pkr", T.e1[:].indirect(L("lR1")), ["e1", "lsD"])
-            TT(T.cra[:, 0:128:16], "cra", T.pt8[:, 8:16], T.pt8[:, 16:24], ["pt9", "pta"], A.add)
             kept[1]()
-            kept = [first[1], kept[2]]
+            TT(T.cra[:, 0:128:16], "cra", T.pt8[:, 8:16], T.pt8[:, 16:24], ["pt9", "pta"], A.add)
+            CP(T.pkr[:], "pkr", T.e1[:].indirect(L("lR1")), ["e1", "lsD"])
             rows_S((1,))
-            rows_V((1,))
+            for o in both:
+                a = slice(64 * o, 64 * o + 64)
+                TS(T.ab[:, 128 + 64 * o:192 + 64 * o], ["ab1", "ac%d" % o], T.ps6[:, a], ["ps6", "nb"], C("nb"), GONE, A.not_equal, A.mult)
+                TT(T.dz[:, 128 + 64 * o:192 + 64 * o], ["dz1", "dc%d" % o], T.ps6[:, a], T.cra[:, a], ["ps6", "cra"], A.add)
+            first[1]()
     MM(5, 128, "qv", 0, "nb3")
     (oc, osc), (ic, isc) = K("qp", 0, 256), K("qn3", 0, 256)
     emit("V", lambda: v.tensor_copy(oc.bitcast(dt.uint32), ic.bitcast(dt.uint32).indirect(L("lF"))), ["na3", "nb3", "lsE"], ["qp"])

@@ -8,15 +8,15 @@ FAR = float(1 << 30)
 ROUND256 = 1.5 * float(1 << 31)
 PIECES = ((0, 1, 2, 3, 4, 5, 6, 7),)
 NCE, NCG = 1, 1
-HV = 2
-CUTS = (0, 6, 16)
+HV = 3
+CUTS = ((0, 16), (0, 4, 8, 12, 16))
 XV, GV, QNA = 2, 1, 0
 NV = 8
 COLS = ["jj", "us", "w2", "lR", "lD", "lW", "lK", "lO", "l2", "lL", "lU0", "l4", "lU1", "lG1"]
 LISTS = {"lO": (0, 1), "l2": (2, 1), "lL": (4, 1), "lU0": (6, 1), "l4": (8, 1), "lU1": (70, 1), "lG1": (72, 1), "lW": (74, 4), "lD0": (12, 4), "lR0": (16, 8), "lP": (24, 16), "lF": (40, 16),
          "lK": (56, 1), "lD1": (58, 4), "lR1": (62, 8)}
 SMALL = ["pf", "wu", "g0", "nb", "m2", "mn", "fl", "km", "rn", "xc", "x2", "o0", "o1", "o2", "m3"]
-RST, E40, TRP, TRF, RP2, TR2 = 0, 64, 104, 136, 184, 216
+E40, TRP, TRF, RP2, TR2 = 0, 104, 136, 184, 216
 
 SCRATCH = {}
 
@@ -30,20 +30,20 @@ for _n, _k, _d in (
         ("one", 128, "bfloat16"), ("zer", 528, "bfloat16"), ("idn", 128, "bfloat16"), ("prm", 128, "bfloat16"),
         ("ce", 528, "bfloat16"), ("cg", 528, "bfloat16"), ("cs", 1024, "bfloat16"), ("vk", 128, "float32"), ("vg", 128, "float32"),
         ("zr", 32 * len(COLS), "float32"), ("zc", 32 * len(COLS), "float32"), ("sm", 8 * len(SMALL), "float32"),
-        ("ls", 78, "uint16"), ("rows", 64, "float32"), ("cc", 48, "float32"),
+        ("ls", 78, "uint16"), ("rows", 64, "float32"), ("cc", 56, "float32"),
         ("crow", 384, "float32"), ("wrow", 384, "bfloat16"), ("r16", 128, "bfloat16"), ("dT", 48, "float32"),
         ("hrow", 256, "float32"), ("zf", 264, "float32"), ("crep", 32, "float32"), ("cra", 128, "float32"),
         ("ng0", 256, "bfloat16"), ("ng1", 256, "bfloat16"), ("ngn", 256, "bfloat16"), ("dl2", 256, "bfloat16"), ("dl3", 256, "bfloat16"),
-        ("B", 1024, "bfloat16"), ("dz", 256, "bfloat16"), ("ab", 256, "bfloat16"), ("dr", 256, "float32"),
+        ("B", 1024, "bfloat16"), ("dz", 256, "bfloat16"), ("ab", 258, "bfloat16"), ("dr", 256, "float32"),
         ("sr", 288, "bfloat16"), ("st", 1088, "bfloat16"), ("sk", 160, "bfloat16"), ("LG", 16, "uint16"), ("LU", 16, "uint16"),
-        ("pb", 256, "bfloat16"), ("fs", 256, "bfloat16"), ("e1", 128, "bfloat16"), ("pkr", 128, "bfloat16"), ("pm", 128, "bfloat16"), ("pt", 128, "float32"),
+        ("pb", 1312, "bfloat16"), ("fs", 256, "bfloat16"), ("e1", 128, "bfloat16"), ("pkr", 128, "bfloat16"), ("pm", 656, "bfloat16"), ("pt", 128, "float32"),
         ("pt8", 24, "float32"), ("ck", 16, "float32"), ("R", 128, "bfloat16"), ("al", 128, "bfloat16"),
-        ("dif", 64, "float32"), ("neg", 64, "float32"), ("MT", 64, "float32"), ("yi", 64, "float32"), ("Y", 320, "float32"),
-        ("rep", 40, "float32"), ("c1", 8, "float32"), ("k1", 8, "float32"), ("k16", 256, "uint16"), ("k2", 8, "float32"), ("pen", 4, "float32"),
+        ("dif", 64, "float32"), ("val", 64, "float32"), ("bd", 64, "float32"), ("yi", 64, "float32"), ("Y", 336, "float32"),
+        ("pr", 256, "float32"), ("be", 8, "float32"), ("er", 41, "float32"), ("k0", 8, "float32"), ("rep", 41, "float32"), ("c1", 8, "float32"), ("k1", 8, "float32"), ("k16", 256, "uint16"), ("k2", 8, "float32"), ("pen", 4, "float32"),
         ("lf", 16 * NR, "uint16"), ("fa", 16 * NR, "uint16"),
         ("wr", 256, "float32"), ("key", 288, "float32"), ("kt", 544, "float32"), ("own", 32, "float32"), ("ow2", 32, "bfloat16"),
-        ("js", 256 * (16 - NV), "bfloat16"), ("jv", 256 * NV, "bfloat16"), ("jo", 256 * NV, "bfloat16"),
-        ("acc", 16, "float32"), ("pl", 16, "uint16"),
+        ("js", 256 * (16 - NV), "bfloat16"), ("jv", 256 * NV, "bfloat16"),
+        ("acc", 16, "float32"), ("pl", 2048, "uint16"), ("xb", 2, "bfloat16"),
         ("prb", 256, "bfloat16"), ("win", 384, "bfloat16"), ("wt", 256, "bfloat16"), ("wk", 256, "bfloat16"),
         ("ll", 16 * NR, "uint16"), ("la", 16 * NR, "uint16"), ("lk", 16, "uint16"), ("opw", 256, "float32"),
         ("Fo", 1024, "bfloat16"), ("F", 1088, "bfloat16"), ("G", 1088, "bfloat16"), ("gz", 512, "bfloat16"), ("Z", 512, "bfloat16"),
@@ -264,7 +264,9 @@ def rank_program(g, core, T, topo):
     ACT(T.win[:], "win", T.zer[:, 0:384], "zer")
     for t in range(4):
         ACT(T.F[:, 272 * t:272 * t + 16], "Fp", T.zer[:, 0:16], "zer")
-    ACT(T.pm[:], "pm", T.zer[:, 0:128], "zer")
+    ACT(T.er[:], "er0", T.zer[:, 0:41], "zer")
+    ACT(T.pr[:], "pr", T.zer[:, 0:256], "zer")
+    ACT(T.pm[:, 0:128], "pm", T.zer[:, 0:128], "zer")
     ACT(T.e1[:], "e1", T.zer[:, 0:128], "zer")
     for a, b in ((128, 256), (416, 544)):
         ACT(T.st[:, 544 + a:544 + b], "slp", T.zer[:, 0:128], "zer")
@@ -281,13 +283,14 @@ def rank_program(g, core, T, topo):
     TS(T.crep[:], "crep", T.zer[:, 0:32], ["zer", "zcA"], C("us"), None, A.add)
     CP(T.zf[:, E40 + 8:E40 + 9], "e40", C("us"), ["zcA", "zf0"])
     TS(T.cs[:, 0:512:4], "cs", T.vk[:], ["vk", "zcA", "wu", "cs0"], C("jj"), C("wu"), A.is_equal, A.mult)
-    FILL(T.zf[:, RST:RST + 64:8], "rst", -FAR, "zf0")
+    FILL(T.bd[:, 0:64:32], "bd0", -FAR)
     FILL(T.wrow[:, 271:384:16], "wrow", 4096.0, "wrow0")
-    FILL(T.Y[:, 79:320:8], "Yc", FAR)
+    FILL(T.Y[:, 71:336:8], ["Yc", "cap"], FAR)
+    FILL(T.pb[:, 256:1312:32], ["pfar", "cap0"], FAR)
     TS(T.cs[:, 512:1024:4], "cs", T.vg[:], ["vg", "zcA", "cs0"], C("jj"), C("w2"), A.is_equal, A.mult)
     FILL(T.zf[:, RP2:264], ["rp2", "tr2c"], 4096.0)
     FILL(T.pen[:, 2:4], "pen", 127.5)
-    TS(T.pen[:, 0:2], "pen", T.crep[:, 0:2], "crep", 2 / U, -146.0 - 4096.0, A.mult, A.add)
+    TS(T.pen[:, 0:2], "pen", T.crep[:, 0:2], "crep", 2 / U / FAR, (-146.0 - 4096.0) / FAR, A.mult, A.add)
     QT("qcs", 0, 256, T.cs[:], "cs")
     for b in range(NCE):
         QT("qce", 128 * b, 128 * b + 128, T.ce[:, 3 - b:515 - b], "ce")
@@ -295,6 +298,8 @@ def rank_program(g, core, T, topo):
     QT("na0", 0, 128, T.xs[:, 0:512], "xs0")
     QT("nb0", 0, 128, T.xs[:, 512:1024], "xs1")
 
+    IOTA(T.be[:], "be", [[1, 8]], 0)
+    ACT(T.cc[:, 48:56], "ramp", T.be[:], "be", scale=2 * GONE)
     IOTA(T.dT[:], "dT", [[0, 3], [int(U) // 2, 16]], int(U))
     IOTA(T.cc[:, 0:8], "cc0", [[288, 8]], 0)
     IOTA(T.cc[:, 8:24], "cc0", [[128, 2], [272, 8]], 0)
@@ -381,9 +386,9 @@ def rank_program(g, core, T, topo):
             f()
 
     def level(p0, p1, tk):
-        return [lambda: TT(T.yi[:], "yi", T.zf[:, TRP:TRP + 32].indirect(L("lW")), T.MT[:], ["trp1", "trp2", "MT", "lsB"], A.add),
-                lambda: SCAN(T.Y[:, 0:64], "Y", T.zf[:, RST:RST + 64], T.yi[:], ["rst", "yi"], -FAR, A.add, A.max),
-                lambda: SCAN(T.rep[p0:p1, :], tk, T.Y[p0:p1, 7:320:8], T.zf[p0:p1, E40:E40 + 40], ["Y", "Yc", "cap", "e40"], FAR, A.min, A.add)]
+        return [lambda: TT(T.yi[:], "yi", T.zf[:, TRP:TRP + 32].indirect(L("lW")), T.val[:], ["trp1", "trp2", "val", "lsB"], A.mult),
+                lambda: SCAN(T.Y[:, 0:64], "Y", T.bd[:], T.yi[:], ["bd", "bd0", "yi"], -FAR, A.add, A.max),
+                lambda: SCAN(T.rep[p0:p1, :], tk, T.er[p0:p1, :], T.Y[p0:p1, 7:335:8], ["Y", "Yc", "cap", "er", "er8"], FAR, A.add, A.min)]
 
     both = (0, 1)
     for o in both:
@@ -399,8 +404,7 @@ def rank_program(g, core, T, topo):
     for bank, c, o in ((5, 0, 0), (6, 0, 1), (7, 128, 0), (1, 128, 1)):
         MM(bank, 128, "qcs", c, "qb%d" % o)
     turn("lR", "lK", "zcB", "zrB")
-    for b in range(NCG, 4):
-        QT("qcg", 128 * b, 128 * b + 128, T.cg[:, 3 - b:515 - b], "cg")
+    TS(C("g0"), "g0", C("pf"), "pf", 16.0, 32.0, A.is_lt, A.mult)
     TS(L("lR0"), "lsB", T.rows[:, 8:16], ["rows", "zcB"], C("lR"), None, A.add)
     TS(L("lD0"), "lsB", T.rows[:, 0:4], ["rows", "zcB"], C("lD"), None, A.add)
     TS(L("lW"), "lsB", T.zer[:, 0:4], ["zer", "zcB"], C("lW"), None, A.add)
@@ -408,7 +412,7 @@ def rank_program(g, core, T, topo):
     for o in both:
         ACT(T.sr[:, 16 + 128 * o:144 + 128 * o], "sr", T["ps%d" % (7, 1)[o]][:, 0:128], "ps%d" % (7, 1)[o])
         rows_V(o, T.crow[:, 128 * o:128 * o + 128], ["c%d" % o])
-    TS(C("g0"), "g0", C("pf"), "pf", 16.0, 32.0, A.is_lt, A.mult)
+    RED(T.ab[:, 256:257], "abk", T.ab[:, 0:128], "ab0", A.min)
 
     for r in range(NR):
         last = r == NR - 1
@@ -419,70 +423,85 @@ def rank_program(g, core, T, topo):
         for o in both:
             a = p0 + n * o
             SCAN(back(T.pb, a, a + n), ["pb%d" % (o | min(r, 1)), "pc%d" % o], back(T.dz, a, a + n), back(T.ab, a, a + n), ["dc%d" % o, "ac%d" % o], 0.0, A.add, A.min)
+        RED(C("mn"), "mn", T.ab[:, 128:257], ["ab1", "abk"], A.min)
+        for o, ok in ((T.pm[:, 144:145] if r else T.pb[:, 288:289], "cap0"), (T.Y[:, 79:80], "cap")):
+            ACT(o, ok, C("mn"), "mn", AF.Relu, bias=FAR, scale=-FAR / GONE)
         unpack("qce", "qn%d" % r, ["na%d" % r, "nb%d" % r], "Fo", 1 / 128)
-        first[1]()
         lR, lD = LISTS["lR%d" % min(r, 1)][0], LISTS["lD%d" % min(r, 1)][0]
         if r == 0:
             ACT(T.hrow[:, 0:256:32], "hrow", T.hrow[:, 0:256:32], "hrow0", AF.Identity, bias=DROP)
             for c, sc, bi in (("xc", 4.0, 127.5), ("x2", 4.0, 0.0), ("o0", 0.5, 0.0), ("o1", -0.5, 0.0), ("o2", -4.0, 0.0)):
                 ACT(C(c), c, C("lR"), "zcB", AF.Identity, bias=bi, scale=sc)
-            pb, pk, ends = T.pb, ["pc0", "pc1"], T.pb[:, 0:256:32]
-            for o in both:
-                CP(T.R[:, 64 * o:64 * o + 64], "R%d" % o, T.pb[:, 128 * o:128 * o + 128].indirect(T.ls[:, lR:lR + 4]), ["pc%d" % o, "lsB"])
+            ACT(T.xb[:, 0:1], "xb", C("lR"), "zcB", scale=4.0)
+            pb, pk, st = T.pb, ["pc0", "pc1"], 32
         else:
-            pb, pk, ends = T.pm, ["pm"], T.pm[:, 0:128:16]
-            for o in both:
+            pb, pk, st = T.pm, ["pm"], 16
+        ends = pb[:, 0:8 * st:st]
+        for o in both:
+            if r == 0:
+                CP(T.R[:, 64 * o:64 * o + 64], "R%d" % o, T.pb[:, 128 * o:128 * o + 128].indirect(T.ls[:, lR:lR + 4]), ["pc%d" % o, "lsB"])
+            else:
                 TT(T.R[:, 64 * o:64 * o + 64], "R%d" % o, T.pb[:, 128 + 64 * o:192 + 64 * o].indirect(T.ls[:, lR:lR + 4]), T.pkr[:, 64 * o:64 * o + 64],
                    ["pc%d" % o, "pkr", "lsD"], A.max)
                 if o == 0:
                     TT(ends, "pm", T.pb[:, 128:256:16], T.e1[:, 0:128:16], ["e1", "pc0", "pc1"], A.max)
 
-        def two(f):
-            return [lambda o=o: f(o, slice(32 * o, 32 * o + 32)) for o in both]
+        def turn_al(o):
+            TR(T.al[:, 64 * o:64 * o + 64], "al%d" % o, T.R[:, 64 * o:64 * o + 64], "R%d" % o)
 
-        def pairs(steps, fill):
-            for (a, b), f in zip(steps, fill):
-                a()
-                f()
-                b()
-            weave(fill[len(steps):], [])
+        def above(o):
+            a, al, ik = slice(32 * o, 32 * o + 32), T.al[:, 64 * o:64 * o + 64:2], ["al%d" % o, "lsB", "lsD"]
+            TT(T.val[:, a], "val", pb[:, n * o:n * o + n].indirect(T.ls[:, lD:lD + 2]), al, pk + ik, A.is_ge)
+            TT(T.dif[:, a], "dif%d" % o, T.pr[:, n * o:n * o + n].indirect(T.ls[:, lD:lD + 2]), al, ["pr"] + ik, A.subtract)
 
-        pairs([two(lambda o, a: TR(T.al[:, 64 * o:64 * o + 64], "al%d" % o, T.R[:, 64 * o:64 * o + 64], "R%d" % o)),
-               two(lambda o, a: TT(T.dif[:, a], "dif%d" % o, pb[:, n * o:n * o + n].indirect(T.ls[:, lD:lD + 2]), T.al[:, 64 * o:64 * o + 64:2],
-                                   pk + ["al%d" % o, "lsB", "lsD"], A.subtract)),
-               two(lambda o, a: TS(T.neg[:, a], "neg%d" % o, T.dif[:, a], "dif%d" % o, 0.0, GONE / U, A.min, A.mult)),
-               two(lambda o, a: TT(T.MT[:, a], "MT", T.dif[:, a], T.neg[:, a], ["dif%d" % o, "neg%d" % o], A.add))],
-                     [lambda: RED(C("mn"), "mn", ends, pk, A.min),
-                      lambda: TS(C("fl"), "fl", C("mn"), "mn", DROP, None, A.is_lt),
-                      lambda: TS(T.rep[0:32, 8:40], "rep0", T.crep[0:32, :], ["crep", "mn", "fl"], C("mn", 32), C("fl", 32), A.add, A.mult),
-                      lambda: TR(T.zf[32:64, TRP:TRP + 32], "trp1", T.rep[0:32, 8:40], "rep0"),
-                      lambda: TS(T.Y[:, 71:72], "cap", C("fl"), ["fl", "zcA"], FAR, C("us"), A.mult, A.subtract)])
+        def steps(o):
+            a = 32 * o
+            TT(T.bd[:, a + 1:a + 32], "bd", T.dif[:, a:a + 31], T.dif[:, a + 1:a + 32], "dif%d" % o, A.subtract)
+
+        turn_al(0)
+        TT(T.pr[:, 0:8 * st:st], "pr", ends, T.cc[:, 48:56], pk + ["ramp"], A.add)
+        SCAN(T.rep[0:32, :], "rep0", pb[0:32, 0:41 * st:st], T.zf[0:32, E40:E40 + 41], pk + ["cap0", "pfar", "e40"], FAR, A.min, A.add)
+        turn_al(1)
+        above(0)
+        TR(T.zf[32:64, TRP:TRP + 32], "trp1", T.rep[0:32, 9:41], "rep0")
+        above(1)
+        TT(T.be[:], "be", ends, T.al[:, 14:128:16], pk + ["al0", "al1"], A.subtract)
+        steps(0)
+        ng = ("ng0", "ng1")[min(r, 1)]
+        cuts = CUTS[min(r, 1)]
+        vals = [lambda a=a, b=b: TT(T.prb[:, 16 * a:16 * b], "prb", T.zf[:, TR2:TR2 + 48].indirect(T.LU[:, a:b]), T[ng][:, 16 * a:16 * b],
+                                    ["tr2", "tr2c", "LU", ng], A.min) for a, b in zip(cuts, cuts[1:])]
+        flags = [lambda: TS(T.zf[:, RP2 + 1:RP2 + 32:16], "rp2", T.pen[:, 0:2], ["pen", "cap"], T.Y[:, 79:80], 4096.0, A.mult, A.add),
+                 lambda: TR(T.zf[:, TR2:TR2 + 32], "tr2", T.zf[:, RP2:RP2 + 32], "rp2")]
+
+        def then(*fs):
+            return lambda: [f() for f in fs]
+
         if r == 0:
-            fill = lists[0:3] + [lambda: TS(T.cc[:, 24:48], "cc", T.cc[:, 0:24], "cc0", -127.5, None, A.add),
-                                 lambda: TT(T.c1[:], "c1", T.fs[:, 0:256:32], T.cc[:, 24:32], ["fs0", "fs1", "cc"], A.add),
-                                 lambda: turn("lO", "l4", "zcC", "zrC")]
+            late = [lambda b=b: QT("qcg", 128 * b, 128 * b + 128, T.cg[:, 3 - b:515 - b], "cg") for b in range(NCG, 4)]
+            fill = [flags[0], then(lists[0], lists[1]), then(flags[1], late[0], lists[2]),
+                    then(first[1], lambda: TS(T.cc[:, 24:48], "cc", T.cc[:, 0:24], "cc0", -127.5, None, A.add)),
+                    then(lambda: TT(T.c1[:], "c1", T.fs[:, 0:256:32], T.cc[:, 24:32], ["fs0", "fs1", "cc"], A.add), late[1]),
+                    lambda: turn("lO", "l4", "zcC", "zrC"),
+                    then(late[2], lambda: CP(T.ls[:, 0:10:2], "lsC", T.zc[:, 32 * COLS.index("lO"):32 * COLS.index("lU1"):32], "zcC"))]
+            mates = [lists[3]]
         else:
-            fill = lists[0:2] + [lambda: (lists[2](), lists[3]()),
-                                 lambda: TT(T.ck[:], "ck", T.fs[:, 0:256:16], T.cc[:, 32:48], ["fs0", "fs1", "cc"], A.add),
-                                 lambda: TT(T.c1[:], "c1", T.ck[:, 0:8], T.ck[:, 8:16], "ck", A.min)]
-        fill.append(lambda: TS(T.zf[:, RP2 + 1:RP2 + 32:16], "rp2", T.pen[:, 0:2], ["pen", "fl"], C("fl"), 4096.0, A.mult, A.add))
-        mates = [lambda: TR(T.zf[:, TR2:TR2 + 32], "tr2", T.zf[:, RP2:RP2 + 32], "rp2")]
-        if r:
-            fill.append(mates.pop())
-        else:
-            mates.append(lists[3])
-        weave(level(32, 64, "rep1") + [lambda: [TR(T.zf[p:p + 32, TRP:TRP + 32], "trp2", T.rep[32:64, 8:40], "rep1") for p in (64, 96)]]
-              + level(64, 128, "rep2") + [lambda: TR(T.zf[:, TRF:TRF + 32], "trf", T.rep[:, 8:40], ["rep0", "rep1", "rep2"])],
-              fill + [lambda: TS(T.k1[:], "k1", T.Y[:, 7:64:8], "Y", 256.0, DROP, A.mult, A.min)])
+            fill = [flags[0], then(lists[0], lists[1], first[1]), then(lists[2], flags[1]),
+                    then(lists[3], lambda: TT(T.ck[:], "ck", T.fs[:, 0:256:16], T.cc[:, 32:48], ["fs0", "fs1", "cc"], A.add)),
+                    then(lambda: TT(T.c1[:], "c1", T.ck[:, 0:8], T.ck[:, 8:16], "ck", A.min), vals[0]), vals[1], vals[2]]
+            mates, vals = [], vals[3:]
+        fill[0] = then(lambda: steps(1), lambda: TT(T.er[:, 1:8], "er", T.be[:, 0:7], T.be[:, 1:8], ["be", "er0"], A.subtract),
+                       lambda: TS(T.er[:, 8:9], "er8", T.be[:, 7:8], ["be", "zcA", "er0"], C("us"), None, A.add), fill[0])
+        fill[6] = then(lambda: TT(T.k0[:], "k0", T.Y[:, 7:64:8], T.be[:], ["Y", "be"], A.add), fill[6])
+        weave(level(32, 64, "rep1") + [lambda: [TR(T.zf[p:p + 32, TRP:TRP + 32], "trp2", T.rep[32:64, 9:41], "rep1") for p in (64, 96)]]
+              + level(64, 128, "rep2") + [lambda: TR(T.zf[:, TRF:TRF + 32], "trf", T.rep[:, 9:41], ["rep0", "rep1", "rep2"])],
+              fill + [lambda: TS(T.k1[:], "k1", T.k0[:], "k0", 256.0, DROP, A.mult, A.min)])
         ACT(T.dr[:], "dr", T.dT[:].indirect(T.LG[:, 0:16]), ["dT", "LG"])
         ACT(T.dr[:, 0:256:32], "dr", T.dr[:, 0:256:32], "dr", AF.Identity, bias=-DROP)
         if r == 0:
             for n, a, c in (("ng0", 0, "o0"), ("ng0", 128, "o1"), ("ngn", 0, "x2"), ("ngn", 128, "o2")):
                 ACT(T[n][:, a:a + 128], n, T[n][:, a:a + 128], [n + "0", c], AF.Identity, bias=C(c))
         key = T.key[:, 16:272]
-        if r == 0:
-            k0 = 32 * COLS.index("lO")
-            CP(T.ls[:, 0:10:2], "lsC", T.zc[:, k0:k0 + 160:32], "zcC")
         unpack("qcg", "qa%d" % r, None, "G", 1 / 256, "T")
         unpack("qce", "qa%d" % r, None, "F", 1 / 256, "T", 4)
         for o in both:
@@ -499,15 +518,13 @@ def rank_program(g, core, T, topo):
                 RED(C("km"), "km", T.k2[:], "k2", A.min)
         CP(T.own[:, 0:16], "own0", T.kt[:, 0:128].indirect(L("l4")), ["kt0", "lsC"])
         TR(T.kt[:, 256:544], "kt2", T.key[:], ["key0", "key1"])
+        CP(T.k16[:, 0:128], "k16", T.key[:, 16:144], "key0")
         CP(T.own[:, 16:32], "own1", T.kt[:, 128:256].indirect(L("l4")), ["kt1", "lsC"])
-        TS(C("rn"), "rn", C("km"), "km", ROUND256, -ROUND256, A.add, A.add)
         weave(mates, [])
         CP(T.ow2[:, 0:16], "owh", T.kt[:, 256:544].indirect(L("l2")), ["kt2", "lsC"])
-        CP(T.k16[:], "k16", key, ["key0", "key1"])
+        CP(T.k16[:, 128:256], "k16", T.key[:, 144:272], "key1")
+        TS(C("rn"), "rn", C("km"), "km", ROUND256, -ROUND256, A.add, A.add)
         TT(T.ow2[:, 16:32], "owl", T.kt[:, 256:544].indirect(L("l2")), T.ow2[:, 0:16], ["kt2", "lsC", "owh"], A.subtract)
-        TS(T.lf[:, 16 * r:16 * r + 2], "lf%d" % r, T.pen[:, 2:4], ["pen", "km", "rn"], C("km"), C("rn"), A.add, A.subtract)
-        send(T.fa, T.lf, 2, "f", r)
-        ng = ("ng0", "ng1")[min(r, 1)]
         def deal(o, ok, a, h0, h1):
             for h in range(h0, h1):
                 TR(o[:, 32 * h:32 * h + 32], ok, T.win[:, a + h:a + 256:8], "win")
@@ -518,18 +535,16 @@ def rank_program(g, core, T, topo):
                 accum_out=T.acc[:, b:b + 1])
         unpack("qcg", "qa%d" % r, None, "G", 1 / 256, "S")
         unpack("qce", "qa%d" % r, None, "F", 1 / 256, "S", 4)
-        for t in range(4):
-            ACT(T.G[:, 272 * t:272 * t + 16], "Gf%d" % t, T.G[:, 272 * t + 16:272 * t + 272].indirect(T.fa[:, 16 * r:16 * r + 1]), ["G%d" % t, "fa%d" % r])
-        vals = [lambda a=a, b=b: TT(T.prb[:, 16 * a:16 * b], "prb", T.zf[:, TR2:TR2 + 48].indirect(T.LU[:, a:b]), T[ng][:, 16 * a:16 * b],
-                                    ["tr2", "tr2c", "LU", ng], A.min) for a, b in zip(CUTS, CUTS[1:])]
-        vals[0]()
+        weave(vals, [])
         for b in range(8):
             TS(T.jv[:, 256 * b:256 * b + 256], "jv%d" % b, T.k16[:], ["k16", "owh", "owl"], T.ow2[:, b:b + 1], T.ow2[:, 16 + b:17 + b], A.subtract, A.is_lt)
         for b in range(8):
-            SCAN(T.jo[:, 128 * b:128 * b + 128], "jo", T.jv[:, 256 * b:256 * b + 128], T.jv[:, 256 * b + 128:256 * b + 256], "jv%d" % b, 0.0, A.add, A.add)
-        weave(vals[1:], [])
+            SCAN(T.pl[:, 2040 + b::-16], "pl", T.jv[:, 256 * b:256 * b + 128], T.jv[:, 256 * b + 128:256 * b + 256], ["jv%d" % b, "xb"], T.xb[:, 0:1], A.add, A.add)
         TS(T.pl[:, 0:8], "pl", T.acc[:, 0:8], ["acc", "xc"], 0.5, C("xc"), A.mult, A.add)
-        TS(T.pl[:, 8:16], "pl", T.jo[:, 127:1024:128], ["jo", "x2"], C("x2"), None, A.add)
+        TS(T.lf[:, 16 * r:16 * r + 2], "lf%d" % r, T.pen[:, 2:4], ["pen", "km", "rn"], C("km"), C("rn"), A.add, A.subtract)
+        send(T.fa, T.lf, 2, "f", r)
+        for t in range(4):
+            ACT(T.G[:, 272 * t:272 * t + 16], "Gf%d" % t, T.G[:, 272 * t + 16:272 * t + 272].indirect(T.fa[:, 16 * r:16 * r + 1]), ["G%d" % t, "fa%d" % r])
         emit("V", lambda: v.tensor_copy(T.win[:].indirect(T.pl[:, 0:16]), T.prb[:]), ["pl", "prb", "win"], ["win"])
         deal(T.wt, "wt", 0, 0, 8)
         deal(T.wk, "wk", 128, 0, 3)
@@ -576,6 +591,7 @@ def rank_program(g, core, T, topo):
                 TS(L("lR1"), "lsD", L("lR0"), "lsB", 0.5, None, A.mult)
                 TS(L("lD1"), "lsD", L("lD0"), "lsB", 0.5, None, A.mult)
                 FILL(T.cra[:], "cra0", U)
+                FILL(T.pm[:, 128:656:16], ["pfar", "cap0"], FAR)
                 FILL(T.r16[:, 0:128:16], "r16", 0.0, "r160")
                 FILL(T.crow[:, 271:384:16], "crow", U + GONE, "crow0")
                 FILL(T.cra[:, 15:128:16], "cra", 16 * GONE, "cra0")
@@ -599,15 +615,16 @@ def rank_program(g, core, T, topo):
             SCAN(T.pt[:], "pt", T.r16[:], T.ps5[:, 0:128], ["r16", "ps5"], 0.0, A.mult, A.add)
             kept, first = list_V((0,)), firsts((0,))
             first[0]()
-            TS(T.pt8[:, 0:8], "pt8", T.pt[:, 15:128:16], "pt", 16 * U, None, A.add)
+            ACT(T.pt8[:, 0:8], "pt8", T.pt[:, 15:128:16], "pt", AF.Identity, bias=16 * U)
+            ACT(T.pt8[:, 8:16], "pt9", T.pt[:, 15:128:16], "pt", AF.Identity, bias=16 * U - 8 * GONE)
             bits((1,))
-            TS(T.pt8[:, 16:24], "pta", T.pb[:, 0:128:16], "pb0", DROP, 8 * GONE + U, A.is_ge, A.mult)
-            TS(T.pt8[:, 8:16], "pt9", T.pt[:, 15:128:16], "pt", 16 * U - 8 * GONE, None, A.add)
             TT(T.e1[:, 0:128:16], "e1", T.pb[:, 0:128:16], T.pt8[:, 0:8], ["pb0", "pt8"], A.min)
+            TS(T.pt8[:, 16:24], "pta", T.pb[:, 0:128:16], "pb0", DROP, 8 * GONE + U, A.is_ge, A.mult)
             kept[0]()
             kept[1]()
             TT(T.cra[:, 0:128:16], "cra", T.pt8[:, 8:16], T.pt8[:, 16:24], ["pt9", "pta"], A.add)
-            CP(T.pkr[:], "pkr", T.e1[:].indirect(L("lR1")), ["e1", "lsD"])
+            RED(T.ab[:, 256:257], "abk", T.pt8[:, 16:24], "pta", A.min)
+            ACT(T.pkr[:], "pkr", T.e1[:].indirect(L("lR1")), ["e1", "lsD"])
             rows_S((1,))
             for o in both:
                 a = slice(64 * o, 64 * o + 64)

@@ -4,19 +4,20 @@ NR = 3
 U = 8.0
 GONE = float(1 << 23)
 DROP = float(1 << 22)
+DK = 16384.0
+HOLD = 512.0
 FAR = float(1 << 30)
 ROUND256 = 1.5 * float(1 << 31)
-PIECES = ((0, 1, 2, 3, 4, 5, 6, 7),)
 NCE, NCG = 1, 1
 HV = 3
-CUTS = ((0, 16), (0, 4, 8, 12, 16))
-XV, GV, QNA = 2, 1, 0
+XV, ZV = 1, 2
+GE = (0, 2, 2)
 NV = 8
-COLS = ["jj", "us", "w2", "lR", "lD", "lW", "lK", "lO", "l2", "lL", "lU0", "l4", "lU1", "lG1"]
-LISTS = {"lO": (0, 1), "l2": (2, 1), "lL": (4, 1), "lU0": (6, 1), "l4": (8, 1), "lU1": (70, 1), "lG1": (72, 1), "lW": (74, 4), "lD0": (12, 4), "lR0": (16, 8), "lP": (24, 16), "lF": (40, 16),
-         "lK": (56, 1), "lD1": (58, 4), "lR1": (62, 8)}
-SMALL = ["pf", "wu", "g0", "nb", "m2", "mn", "fl", "km", "rn", "xc", "x2", "o0", "o1", "o2", "m3"]
-E40, TRP, TRF, RP2, TR2 = 0, 104, 136, 184, 216
+COLS = ["jj", "us", "w2", "lR", "lD", "lW", "k4", "lp"]
+LISTS = {"lW": (0, 4), "lD0": (4, 4), "lR0": (8, 8), "lP": (16, 16), "lF": (32, 16), "lD1": (48, 4), "lR1": (52, 8)}
+SMALL = ["pf", "wu", "g0", "nb", "mn", "km", "rn", "pn", "q5", "q6", "jq", "t0", "g1"]
+E40, TRP = 0, 48
+GG, FO, HS = 0, 1088, 2112
 
 SCRATCH = {}
 
@@ -30,23 +31,25 @@ for _n, _k, _d in (
         ("one", 128, "bfloat16"), ("zer", 528, "bfloat16"), ("idn", 128, "bfloat16"), ("prm", 128, "bfloat16"),
         ("ce", 528, "bfloat16"), ("cg", 528, "bfloat16"), ("cs", 1024, "bfloat16"), ("vk", 128, "float32"), ("vg", 128, "float32"),
         ("zr", 32 * len(COLS), "float32"), ("zc", 32 * len(COLS), "float32"), ("sm", 8 * len(SMALL), "float32"),
-        ("ls", 78, "uint16"), ("rows", 64, "float32"), ("cc", 56, "float32"),
-        ("crow", 384, "float32"), ("wrow", 384, "bfloat16"), ("r16", 128, "bfloat16"), ("dT", 48, "float32"),
-        ("hrow", 256, "float32"), ("zf", 264, "float32"), ("crep", 32, "float32"), ("cra", 128, "float32"),
-        ("ng0", 256, "bfloat16"), ("ng1", 256, "bfloat16"), ("ngn", 256, "bfloat16"), ("dl2", 256, "bfloat16"), ("dl3", 256, "bfloat16"),
+        ("ls", 60, "uint16"), ("rows", 112, "float32"), ("cc", 56, "float32"),
+        ("crow", 384, "float32"), ("wrow", 384, "bfloat16"), ("r16", 128, "bfloat16"), ("dT", 128, "float32"),
+        ("hrow", 128, "float32"), ("zf", 80, "float32"), ("cra", 128, "float32"),
+        ("i16", 144, "bfloat16"), ("eq", 144, "bfloat16"), ("a1", 128, "bfloat16"), ("a2", 128, "bfloat16"), ("ar", 128, "bfloat16"), ("mk", 128, "bfloat16"),
+        ("lc", 16, "float32"), ("pc", 32, "float32"), ("tie", 64, "float32"), ("tf", 128, "float32"), ("rp2", 64, "float32"), ("tr2", 128, "float32"),
+        ("rq", 74, "float32"), ("pl0", 256, "float32"), ("pl1", 256, "float32"), ("colw", 768, "bfloat16"),
         ("B", 1024, "bfloat16"), ("dz", 256, "bfloat16"), ("ab", 258, "bfloat16"), ("dr", 256, "float32"),
-        ("sr", 288, "bfloat16"), ("st", 1088, "bfloat16"), ("sk", 160, "bfloat16"), ("LG", 16, "uint16"), ("LU", 16, "uint16"),
+        ("sd", 256, "float32"), ("LG", 16, "uint16"), ("fr", 256, "bfloat16"), ("fd", 256, "float32"), ("fb", 16, "float32"),
         ("pb", 1312, "bfloat16"), ("fs", 256, "bfloat16"), ("e1", 128, "bfloat16"), ("pkr", 128, "bfloat16"), ("pm", 656, "bfloat16"), ("pt", 128, "float32"),
         ("pt8", 24, "float32"), ("ck", 16, "float32"), ("R", 128, "bfloat16"), ("al", 128, "bfloat16"),
-        ("dif", 64, "float32"), ("val", 64, "float32"), ("bd", 64, "float32"), ("yi", 64, "float32"), ("Y", 336, "float32"),
-        ("pr", 256, "float32"), ("be", 8, "float32"), ("er", 41, "float32"), ("k0", 8, "float32"), ("rep", 41, "float32"), ("c1", 8, "float32"), ("k1", 8, "float32"), ("k16", 256, "uint16"), ("k2", 8, "float32"), ("pen", 4, "float32"),
-        ("lf", 16 * NR, "uint16"), ("fa", 16 * NR, "uint16"),
-        ("wr", 256, "float32"), ("key", 288, "float32"), ("kt", 544, "float32"), ("own", 32, "float32"), ("ow2", 32, "bfloat16"),
+        ("dif", 64, "float32"), ("val", 64, "float32"), ("bd", 64, "float32"), ("yi", 64, "float32"), ("Y", 592, "float32"),
+        ("pr", 256, "float32"), ("be", 8, "float32"), ("er", 74, "float32"), ("k0", 8, "float32"), ("rep", 41, "float32"), ("c1", 8, "float32"),
+        ("k1", 8, "float32"), ("k16", 256, "uint16"), ("k2", 8, "float32"), ("pen", 2, "float32"),
+        ("lf", 32 * NR, "uint16"), ("fa", 32 * NR, "uint16"),
+        ("wr", 256, "float32"), ("key", 256, "float32"), ("od", 256, "float32"), ("oh", 128, "bfloat16"), ("ol", 8, "bfloat16"),
         ("js", 256 * (16 - NV), "bfloat16"), ("jv", 256 * NV, "bfloat16"),
         ("acc", 16, "float32"), ("pl", 2048, "uint16"), ("xb", 2, "bfloat16"),
-        ("prb", 256, "bfloat16"), ("win", 384, "bfloat16"), ("wt", 256, "bfloat16"), ("wk", 256, "bfloat16"),
-        ("ll", 16 * NR, "uint16"), ("la", 16 * NR, "uint16"), ("lk", 16, "uint16"), ("opw", 256, "float32"),
-        ("Fo", 1024, "bfloat16"), ("F", 1088, "bfloat16"), ("G", 1088, "bfloat16"), ("gz", 512, "bfloat16"), ("Z", 512, "bfloat16"),
+        ("win", 256, "float32"), ("dl", 256 * NR, "uint16"), ("la", 16 * NR, "uint16"), ("ow", 256, "float32"), ("opw", 256, "float32"),
+        ("D", 3136, "bfloat16"), ("gz", 1024, "bfloat16"), ("Z", 512, "bfloat16"),
         ("X", 1024, "bfloat16"), ("ysb", (8, 32), "float32")):
     _b(_n, _k, _d)
 for _n, _k in (("qn", 256 * (NR + 1)), ("qa", 256 * NR), ("qp", 256), ("qu", 128), ("qv", 128), ("qw", 512), ("qc", 1280), ("qb", 256),
@@ -132,12 +135,12 @@ def rank_program(g, core, T, topo):
     emit, need, toks_of, landed, count, nd = recorder(g, T)
     v, s = g.vector, g.scalar
 
-    def C(n, p=128):
+    def C(n, a=0, b=128):
         if n in COLS:
             k = 32 * COLS.index(n)
-            return T.zc[0:p, k:k + 1]
+            return T.zc[a:b, k:k + 1]
         k = 8 * SMALL.index(n)
-        return T.sm[0:p, k:k + 1]
+        return T.sm[a:b, k:k + 1]
 
     def L(n):
         a, k = LISTS[n]
@@ -209,25 +212,25 @@ def rank_program(g, core, T, topo):
     rid, pid, _ = topo.addr(nxt)
     mask = topo.mask(core, nxt)
     n_out, n_in = len(topo.engines(core, nxt)), len(topo.engines(prv, core))
+    calls = [0]
 
-    def send_codes(r):
-        need("G", toks_of("G", ["na%d" % r, "nb%d" % r], []))
-        (zc, zs), (ac, asc) = K("qn%d" % r, 0, 256), K("qa%d" % r, 0, 256)
+    def send_codes(r, a, b, keys, got):
+        need("G", toks_of("G", keys, []))
+        (zc, zs), (ac, asc) = K("qn%d" % r, a, b), K("qa%d" % r, a, b)
         g.remote_dma(ac.bitcast(dt.uint8), zc.bitcast(dt.uint8), T.sem["arc%d" % r], T.sem.sent, pid, rid, mask)
         g.remote_dma(asc, zs, T.sem["arc%d" % r], T.sem.sent, pid, rid, mask)
-        landed("arc%d" % r, 2 * n_in, ["qa%d" % r])
+        calls[0] += 2
+        landed("arc%d" % r, got * n_in, ["qa%d" % r])
 
-    def send(dst, src, n, k, r):
+    def send(dst, src, k, r):
         need("G", toks_of("G", ["l%s%d" % (k, r)], []))
-        g.remote_dma(dst[:, 16 * r:16 * r + n], src[:, 16 * r:16 * r + n], T.sem["ar%s%d" % (k, r)], T.sem.sent, pid, rid, mask)
+        g.remote_dma(dst, src, T.sem["ar%s%d" % (k, r)], T.sem.sent, pid, rid, mask)
+        calls[0] += 1
         landed("ar%s%d" % (k, r), n_in, ["%sa%d" % (k, r)])
 
     emit("Y", lambda: g.sync.dma_start(T.xs[:, 0:512], T.x[:, 0:512]), [], ["xs0"], dma=True)
     emit("S", lambda: s.dma_start(T.us[:], T.u[:]), [], ["us"], dma=True)
     emit("Y", lambda: g.sync.dma_start(T.xs[:, 512:1024], T.x[:, 512:1024]), [], ["xs1"], dma=True)
-    emit("Y", lambda: g.sync.dma_start(T.qw[:, 0:512].bitcast(dt.uint8), T.wc[:, 0:2048]), ["xs0", "xs1", "us"], ["qw"], dma=True)
-    emit("Y", lambda: g.sync.dma_start(T.sqw[:, 0:512], T.ws[:, 0:512]), [], ["sqw"], dma=True)
-    emit("Y", lambda: g.sync.dma_start(T.vs[:], T.v[:]), [], ["vs"], dma=True)
 
     FILL(T.one[:], "one", 128.0)
     FILL(T.zer[:], "zer", 0.0)
@@ -237,88 +240,86 @@ def rank_program(g, core, T, topo):
     AFF(T.idn[:], "idn", T.one[:], "one", [[-1, 128]], A.is_equal, 0, 1)
     IOTA(T.vk[:], "vk", [[-16, 4], [0, 32]], 0, 1)
     IOTA(T.vg[:], "vg", [[-16, 8], [0, 16]], 0, 1)
-    AFF(T.prm[:, 0:16], "prm", T.one[:, 0:16], "one", [[-1, 16]], A.is_equal, -112, 1)
-    AFF(T.prm[:, 16:32], "prm", T.one[:, 0:16], "one", [[-1, 16]], A.is_equal, 0, 1)
-    AFF(T.prm[:, 32:128], "prm", T.one[:, 0:96], "one", [[-16, 3], [0, 2], [-1, 16]], A.is_equal, -16, 1)
+    IOTA(T.i16[:], "i16", [[0, 9], [1, 16]], 0)
     IOTA(row("lR"), "zrB", [[32, 2], [0, 16]], 0)
     IOTA(row("lD"), "zrB", [[0, 2], [32, 2], [0, 8]], 0)
     IOTA(row("lW"), "zrB", [[0, 4], [2, 8]], 0)
-    IOTA(row("lK", 0, 16), "zrB", [[32, 8], [288, 2]], 0)
-    IOTA(row("lK", 16, 32), "zrB", [[32, 8], [-256, 2]], 272)
+    IOTA(row("k4"), "zrB", [[2, 2], [0, 8], [1, 2]], 4)
     IOTA(C("pf"), "pf", [[0, 1]], 0, 1)
     IOTA(T.rows[:, 0:4], "rows", [[64, 4]], 0)
     IOTA(T.rows[:, 8:16], "rows", [[64, 4], [0, 2]], 0)
+    IOTA(T.rows[:, 72:80], "rowl", [[16, 2], [1, 2], [0, 2]], 0)
+    AFF(T.prm[:, 0:16], "prm", T.one[:, 0:16], "one", [[-1, 16]], A.is_equal, -112, 1)
+    AFF(T.prm[:, 16:32], "prm", T.one[:, 0:16], "one", [[-1, 16]], A.is_equal, 0, 1)
+    AFF(T.prm[:, 32:128], "prm", T.one[:, 0:96], "one", [[-16, 3], [0, 2], [-1, 16]], A.is_equal, -16, 1)
 
     FILL(T.cs[:], "cs0", 0.0)
     ACT(T.ce[:], "ce0", T.zer[:], "zer")
     ACT(T.ce[:, 3:512:4], "ce", T.idn[:], ["idn", "ce0"])
     ACT(T.B[:, 0:512], "B0", T.zer[:, 0:512], "zer")
     ACT(T.B[:, 512:1024], "B1", T.zer[:, 0:512], "zer")
-    ACT(T.cg[:], "cg0", T.zer[:], "zer")
-    ACT(T.cg[:, 3:512:4], "cg", T.prm[:], ["prm", "cg0"])
     ACT(T.crow[:], "crow0", T.zer[:, 0:384], "zer", AF.Identity, bias=U)
     ACT(T.crow[:, 31:256:32], "crow", T.zer[:, 0:8], ["zer", "crow0"], AF.Identity, bias=GONE)
-    ACT(T.sr[:, 0:16], "srp", T.zer[:, 0:16], "zer")
-    ACT(T.sr[:, 272:288], "srp", T.zer[:, 0:16], "zer")
-    ACT(T.key[:], ["key0", "key1"], T.zer[:, 0:288], "zer")
-    ACT(T.win[:], "win", T.zer[:, 0:384], "zer")
-    for t in range(4):
-        ACT(T.F[:, 272 * t:272 * t + 16], "Fp", T.zer[:, 0:16], "zer")
-    ACT(T.er[:], "er0", T.zer[:, 0:41], "zer")
+    ACT(T.er[:], "er0", T.zer[:, 0:74], "zer")
     ACT(T.pr[:], "pr", T.zer[:, 0:256], "zer")
-    ACT(T.pm[:, 0:128], "pm", T.zer[:, 0:128], "zer")
-    ACT(T.e1[:], "e1", T.zer[:, 0:128], "zer")
-    for a, b in ((128, 256), (416, 544)):
-        ACT(T.st[:, 544 + a:544 + b], "slp", T.zer[:, 0:128], "zer")
-    for a in (0, 144):
-        ACT(T.sk[:, a:a + 16], "srp", T.zer[:, 0:16], "zer")
+    ACT(T.tr2[:, 64:128], "tr2c", T.zer[:, 0:64], "zer")
+    ACT(T.rows[:, 64:72], "rowz", T.zer[:, 0:8], "zer")
+    ACT(T.xb[:, 0:1], "xb", T.zer[:, 0:1], "zer")
+    for k in range(4):
+        ACT(T.dT[:, 32 * k:32 * k + 32], "dT", row("us"), "zrA", AF.Identity, bias=-DK * (k % 2))
+    ACT(T.cg[:], "cg0", T.zer[:], "zer")
 
     for i in range(3):
         FILL(row("w2", i, 32, 16), "zrV", float(8 >> i), "zr0")
     FILL(T.wrow[:], "wrow0", 1.0)
     turn("jj", "w2", "zcA", ["zrA", "zrV"])
-    FILL(T.zf[:, 0:RP2], ["zf0", "trp1", "trp2", "trfc"], 0.0)
+    FILL(T.zf[:], ["zf0", "trp1", "trp2"], 0.0)
     TS(C("wu"), "wu", C("w2"), "zcA", U / 2, None, A.mult)
     TS(C("nb"), "nb", C("us"), "zcA", -U, None, A.add)
-    TS(T.crep[:], "crep", T.zer[:, 0:32], ["zer", "zcA"], C("us"), None, A.add)
+    TS(C("q5"), "q5", C("jj"), "zcA", 15.0, HOLD, A.is_lt, A.mult)
     CP(T.zf[:, E40 + 8:E40 + 9], "e40", C("us"), ["zcA", "zf0"])
     TS(T.cs[:, 0:512:4], "cs", T.vk[:], ["vk", "zcA", "wu", "cs0"], C("jj"), C("wu"), A.is_equal, A.mult)
     FILL(T.bd[:, 0:64:32], "bd0", -FAR)
     FILL(T.wrow[:, 271:384:16], "wrow", 4096.0, "wrow0")
-    FILL(T.Y[:, 71:336:8], ["Yc", "cap"], FAR)
+    FILL(T.Y[:, 71:592:8], ["Yc", "cap"], FAR)
     FILL(T.pb[:, 256:1312:32], ["pfar", "cap0"], FAR)
     TS(T.cs[:, 512:1024:4], "cs", T.vg[:], ["vg", "zcA", "cs0"], C("jj"), C("w2"), A.is_equal, A.mult)
-    FILL(T.zf[:, RP2:264], ["rp2", "tr2c"], 4096.0)
-    FILL(T.pen[:, 2:4], "pen", 127.5)
-    TS(T.pen[:, 0:2], "pen", T.crep[:, 0:2], "crep", 2 / U / FAR, (-146.0 - 4096.0) / FAR, A.mult, A.add)
+    TS(T.eq[:], "eq", T.i16[:], ["i16", "zcA"], C("jj"), None, A.is_equal)
+    FILL(T.pen[:], "pen", 127.5)
+    TS(C("pn"), "pn", C("us"), "zcA", 2 / U / FAR, 254.0 / FAR, A.mult, A.add)
     QT("qcs", 0, 256, T.cs[:], "cs")
+    ACT(T.a1[:], "a1", T.eq[:, 15:143], "eq", scale=HOLD)
+    ACT(T.a2[:], "a2", T.eq[:, 16:144], "eq", scale=-4 * HOLD)
+    ACT(T.mk[:], "mk", T.eq[:, 16:144], "eq", AF.Identity, bias=1.0, scale=-1.0)
+    ACT(C("q6"), "q6", C("q5"), "q5", AF.Identity, bias=HOLD, scale=-1.0)
+    ACT(C("jq"), "jq", C("jj"), ["zcA", "q5"], AF.Identity, bias=C("q5"))
+    ACT(T.cg[:, 3:512:4], "cg", T.prm[:], ["prm", "cg0"])
+    ACT(T.win[:], "win", T.zer[:, 0:256], "zer")
+    ACT(T.pm[:, 0:128], "pm", T.zer[:, 0:128], "zer")
+    ACT(T.e1[:], "e1", T.zer[:, 0:128], "zer")
     for b in range(NCE):
         QT("qce", 128 * b, 128 * b + 128, T.ce[:, 3 - b:515 - b], "ce")
+    TS(C("g0"), "g0", C("pf"), "pf", 16.0, 64.0, A.is_lt, A.mult)
+    TS(C("t0"), "t0", C("jj"), "zcA", 0.0, 32.0, A.is_equal, A.mult)
     QT("qu", 0, 128, T.us[:], "us")
     QT("na0", 0, 128, T.xs[:, 0:512], "xs0")
     QT("nb0", 0, 128, T.xs[:, 512:1024], "xs1")
 
     IOTA(T.be[:], "be", [[1, 8]], 0)
     ACT(T.cc[:, 48:56], "ramp", T.be[:], "be", scale=2 * GONE)
-    IOTA(T.dT[:], "dT", [[0, 3], [int(U) // 2, 16]], int(U))
     IOTA(T.cc[:, 0:8], "cc0", [[288, 8]], 0)
     IOTA(T.cc[:, 8:24], "cc0", [[128, 2], [272, 8]], 0)
-    IOTA(T.hrow[:], "hrow0", [[1, 8], [0, 32]], 0)
-    IOTA(row("lO"), "zrC", [[16, 2], [0, 2], [32, 8]], 0)
-    IOTA(row("l2"), "zrC", [[-16, 2], [0, 2], [32, 8]], 32)
-    IOTA(row("lL"), "zrC", [[16, 2], [1, 2], [32, 8]], 0)
-    IOTA(row("lU0", 0, 16), "zrC", [[288, 2], [32, 8]], 0)
-    IOTA(row("lU0", 16, 32), "zrC", [[256, 2], [32, 8]], 16)
-    IOTA(row("l4"), "zrC", [[16, 2], [0, 4], [32, 4]], 0)
-    IOTA(T.ng0[:], "ng00", [[16, 2], [32, 8], [1, 16]], -128)
-    send_codes(0)
-    IOTA(T.rows[:, 48:64], "rows3", [[16, 16]], 0)
-    IOTA(T.rows[:, 32:48], "rows2", [[16, 8], [128, 2]], 0)
-    IOTA(T.ngn[:], "ngn0", [[128, 2], [16, 8], [1, 16]], -128)
-    IOTA(row("lU1", 0, 16), "zrD", [[-544, 2], [32, 4], [288, 2]], 544)
-    IOTA(row("lU1", 16, 32), "zrD", [[544, 2], [32, 4], [-256, 2]], 272)
-    IOTA(row("lG1", 0, 16), "zrD", [[32, 4], [288, 2], [-544, 2]], 544)
-    IOTA(row("lG1", 16, 32), "zrD", [[32, 4], [-256, 2], [-544, 2]], 816)
+    IOTA(T.hrow[:], "hrow", [[1, 4], [0, 32]], -4)
+    IOTA(T.rows[:, 80:96], "rowp", [[16, 16]], 0)
+    send_codes(0, 0, 256, ["na0", "nb0"], 2)
+    emit("Y", lambda: g.sync.dma_start(T.qw[:, 0:512].bitcast(dt.uint8), T.wc[:, 0:2048]), ["qa0"], ["qw"], dma=True)
+    emit("Y", lambda: g.sync.dma_start(T.sqw[:, 0:512], T.ws[:, 0:512]), [], ["sqw"], dma=True)
+    emit("Y", lambda: g.sync.dma_start(T.vs[:], T.v[:]), [], ["vs"], dma=True)
+    IOTA(T.pl0[:], "pl00", [[1, 256]], 0)
+    IOTA(T.rows[:, 96:112], "rowq", [[16, 8], [128, 2]], 0)
+    IOTA(T.pl1[:], "pl10", [[16, 8], [128, 2], [1, 16]], 0)
+    IOTA(T.rows[:, 16:32], "rows2", [[128, 2], [2, 8]], 0)
+    IOTA(row("lp"), "zrD", [[0, 2], [1, 2], [16, 8]], 0)
 
     def dims(parts):
         return (256, 0) if len(parts) == 2 else (128, parts[0])
@@ -329,21 +330,14 @@ def rank_program(g, core, T, topo):
     def back(t, a, b):
         return t[:, b - 1::-1] if a == 0 else t[:, b - 1:a - 1:-1]
 
-    def scores(k, parts):
-        n, o = dims(parts)
-        q = "qn%d" % k if n == 256 else ("na%d", "nb%d")[o] % k
-        MM(4, n, "qu", 0, q, [("na%d", "nb%d")[p] % k for p in parts])
+    def scores(k, o):
+        MM(4, 128, "qu", 0, ("na%d", "nb%d")[o] % k)
 
-    def bits(parts):
-        n, o = dims(parts)
-        TS(T.B[:, 512 * o:512 * o + 4 * n:4], keys("B", parts), T.ps4[:, 0:n], "ps4", 0.0, None, A.is_gt)
-        QT("qb%d" % o, 0, n, T.B[:, 512 * o:512 * o + 4 * n], keys("B", parts), keys("qb", parts))
+    def bits(o):
+        TS(T.B[:, 512 * o:512 * o + 512:4], "B%d" % o, T.ps4[:, 0:128], "ps4", 0.0, None, A.is_gt)
+        QT("qb%d" % o, 0, 128, T.B[:, 512 * o:512 * o + 512], "B%d" % o)
         for bank, c in ((5 + o, 0), (7, 128)):
-            MM(bank, n, "qcs", c, "qb%d" % o, keys("qb", parts))
-
-    def rows_S(parts):
-        n, o = dims(parts)
-        ACT(T[("sk", "sr")[o]][:, 16:16 + n], ("sk", "sr")[o], T.ps7[:, 0:n], "ps7")
+            MM(bank, 128, "qcs", c, "qb%d" % o)
 
     def rows_V(o, c, more=()):
         a, ps = slice(128 * o, 128 * o + 128), "ps%d" % (5 + o)
@@ -358,23 +352,13 @@ def rank_program(g, core, T, topo):
                 lambda: SCAN(back(T.fs, a, a + n), keys("fs", parts), back(T.wrow, c, c + n), back(T.ab, a, a + n), ["wrow"] + keys("ab", parts),
                              0.0, A.add, A.min)]
 
-    def list_V(parts):
-        n, o = dims(parts)
-        sr, st, a = ("sk", "sl", 544) if parts == (0,) else ("sr", "st", 0)
-        win, lg, lu = (T.st[:, 0:544], "lK", "lU0") if n == 256 else (T.st[:], "lG1", "lU1")
-        ik = ["st", "sl", "slp", "lsB", "lsD", "g0"]
-        return [lambda: TR(T.st[:, a:a + n], st, T[sr][:, 16:16 + n], sr),
-                lambda: TR(T.st[:, a + 256:a + 288 + n], st, T[sr][:, 0:32 + n], [sr, "srp"]),
-                lambda: TS(T.LG[:], "LG", win.indirect(L(lg)), ik, C("g0"), None, A.add),
-                lambda: TS(T.LU[:], "LU", win.indirect(L(lu)), ik + ["lsC"], C("g0"), None, A.add)]
+    def symbols(o, bank, cols):
+        return [lambda: SCAN(T.sd[:, 128 * o:128 * o + 128], "sd%d" % o, T.ar[:], T["ps%d" % bank][:, 0:128], ["ar", "ps%d" % bank], 0.0, A.add, A.max),
+                lambda: TT(T.LG[:, cols], "LG%d" % o, T.sd[:, 128 * o + 15:128 * o + 128:16], T.lc[:, cols], ["sd%d" % o, "lc"], A.add)]
 
-    def unpack(c, q, qk, o, sc, part="TS", k=0):
+    def unpack(c, q, qk, k=0):
         for b in range(4):
-            if "T" in part:
-                MM(k + b, 256, c, 128 * b, q, qk)
-            if "S" in part:
-                a = 256 * b if o == "Fo" else 272 * b + 16
-                ACT(T[o][:, a:a + 256], "%s%d" % (o, b), T["ps%d" % (k + b)][:, 0:256], "ps%d" % (k + b), scale=sc)
+            MM(k + b, 256, c, 128 * b, q, qk)
 
     def weave(main, fill):
         fill = list(fill)
@@ -385,66 +369,70 @@ def rank_program(g, core, T, topo):
         for f in fill:
             f()
 
-    def level(p0, p1, tk):
+    def then(*fs):
+        return lambda: [f() for f in fs]
+
+    def level(o, n, p0, p1, tk):
         return [lambda: TT(T.yi[:], "yi", T.zf[:, TRP:TRP + 32].indirect(L("lW")), T.val[:], ["trp1", "trp2", "val", "lsB"], A.mult),
                 lambda: SCAN(T.Y[:, 0:64], "Y", T.bd[:], T.yi[:], ["bd", "bd0", "yi"], -FAR, A.add, A.max),
-                lambda: SCAN(T.rep[p0:p1, :], tk, T.er[p0:p1, :], T.Y[p0:p1, 7:335:8], ["Y", "Yc", "cap", "er", "er8"], FAR, A.add, A.min)]
+                lambda: SCAN(o[p0:p1, 0:n], tk, T.er[p0:p1, 0:n], T.Y[p0:p1, 7:8 * n:8], ["Y", "Yc", "cap", "er", "er8", "erc"], FAR, A.add, A.min)]
 
     both = (0, 1)
     for o in both:
         MM(4 * o, 128, "qu", 0, ("na0", "nb0")[o])
     for b in range(NCE, 4):
         QT("qce", 128 * b, 128 * b + 128, T.ce[:, 3 - b:515 - b], "ce")
-    for b in range(NCG):
-        QT("qcg", 128 * b, 128 * b + 128, T.cg[:, 3 - b:515 - b], "cg")
     for o in both:
         TS(T.B[:, 512 * o:512 * o + 512:4], "B%d" % o, T["ps%d" % (4 * o)][:, 0:128], "ps%d" % (4 * o), 0.0, None, A.is_gt)
+    for b in range(NCG):
+        QT("qcg", 128 * b, 128 * b + 128, T.cg[:, 3 - b:515 - b], "cg")
     for o in both:
         QT("qb%d" % o, 0, 128, T.B[:, 512 * o:512 * o + 512], "B%d" % o)
     for bank, c, o in ((5, 0, 0), (6, 0, 1), (7, 128, 0), (1, 128, 1)):
         MM(bank, 128, "qcs", c, "qb%d" % o)
-    turn("lR", "lK", "zcB", "zrB")
-    TS(C("g0"), "g0", C("pf"), "pf", 16.0, 32.0, A.is_lt, A.mult)
+    turn("lR", "k4", "zcB", "zrB")
+    TT(T.ar[:], "ar", T.a1[:], T.a2[:], ["a1", "a2"], A.add)
+    TS(T.lc[:], "lc0", T.rows[:, 64:80], ["rowl", "rowz", "g0", "q5"], C("g0"), C("q5"), A.add, A.subtract)
+    ACT(T.lc[:, 0:16:2], "lc", T.lc[:, 0:16:2], ["lc0", "t0"], AF.Identity, bias=C("t0"))
     TS(L("lR0"), "lsB", T.rows[:, 8:16], ["rows", "zcB"], C("lR"), None, A.add)
     TS(L("lD0"), "lsB", T.rows[:, 0:4], ["rows", "zcB"], C("lD"), None, A.add)
     TS(L("lW"), "lsB", T.zer[:, 0:4], ["zer", "zcB"], C("lW"), None, A.add)
-    CP(L("lK"), "lsB", C("lK"), "zcB")
+    for k in both:
+        ACT(T.tie[:, 32 * k:32 * k + 32], "tie", T.zer[:, 0:32], ["zer", "zcB"], AF.Identity, bias=C("k4"))
+    ACT(T.tie[:, 32:64], "tie", T.tie[:, 32:64], "tie", AF.Identity, bias=DK)
+    ACT(T.er[64:128, 10:11], "erc", C("k4", 64), ["zcB", "er0"])
+    ACT(T.er[64:128, 42:43], "erc", T.zer[64:128, 0:1], ["zer", "er0"], AF.Identity, bias=DK)
     for o in both:
-        ACT(T.sr[:, 16 + 128 * o:144 + 128 * o], "sr", T["ps%d" % (7, 1)[o]][:, 0:128], "ps%d" % (7, 1)[o])
         rows_V(o, T.crow[:, 128 * o:128 * o + 128], ["c%d" % o])
     RED(T.ab[:, 256:257], "abk", T.ab[:, 0:128], "ab0", A.min)
 
     for r in range(NR):
         last = r == NR - 1
         parts = both if r == 0 else (1,)
-        lists = list_V(parts)
         first = firsts(parts)
         p0, n = (128, 64) if r else (0, 128)
         for o in both:
             a = p0 + n * o
             SCAN(back(T.pb, a, a + n), ["pb%d" % (o | min(r, 1)), "pc%d" % o], back(T.dz, a, a + n), back(T.ab, a, a + n), ["dc%d" % o, "ac%d" % o], 0.0, A.add, A.min)
         RED(C("mn"), "mn", T.ab[:, 128:257], ["ab1", "abk"], A.min)
+        sy = [symbols(o, (7, 1)[o], slice(8 * o, 8 * o + 8)) for o in both] if r == 0 else [symbols(1, 7, slice(1, 16, 2))]
         for o, ok in ((T.pm[:, 144:145] if r else T.pb[:, 288:289], "cap0"), (T.Y[:, 79:80], "cap")):
             ACT(o, ok, C("mn"), "mn", AF.Relu, bias=FAR, scale=-FAR / GONE)
-        unpack("qce", "qn%d" % r, ["na%d" % r, "nb%d" % r], "Fo", 1 / 128)
         lR, lD = LISTS["lR%d" % min(r, 1)][0], LISTS["lD%d" % min(r, 1)][0]
-        if r == 0:
-            ACT(T.hrow[:, 0:256:32], "hrow", T.hrow[:, 0:256:32], "hrow0", AF.Identity, bias=DROP)
-            for c, sc, bi in (("xc", 4.0, 127.5), ("x2", 4.0, 0.0), ("o0", 0.5, 0.0), ("o1", -0.5, 0.0), ("o2", -4.0, 0.0)):
-                ACT(C(c), c, C("lR"), "zcB", AF.Identity, bias=bi, scale=sc)
-            ACT(T.xb[:, 0:1], "xb", C("lR"), "zcB", scale=4.0)
-            pb, pk, st = T.pb, ["pc0", "pc1"], 32
-        else:
-            pb, pk, st = T.pm, ["pm"], 16
+        pb, pk, st = (T.pb, ["pc0", "pc1"], 32) if r == 0 else (T.pm, ["pm"], 16)
         ends = pb[:, 0:8 * st:st]
         for o in both:
             if r == 0:
                 CP(T.R[:, 64 * o:64 * o + 64], "R%d" % o, T.pb[:, 128 * o:128 * o + 128].indirect(T.ls[:, lR:lR + 4]), ["pc%d" % o, "lsB"])
+                sy[o][0]()
             else:
                 TT(T.R[:, 64 * o:64 * o + 64], "R%d" % o, T.pb[:, 128 + 64 * o:192 + 64 * o].indirect(T.ls[:, lR:lR + 4]), T.pkr[:, 64 * o:64 * o + 64],
                    ["pc%d" % o, "pkr", "lsD"], A.max)
                 if o == 0:
                     TT(ends, "pm", T.pb[:, 128:256:16], T.e1[:, 0:128:16], ["e1", "pc0", "pc1"], A.max)
+        unpack("qce", "qn%d" % r, ["na%d" % r, "nb%d" % r])
+        for b in range(4):
+            ACT(T.D[:, FO + 256 * b:FO + 256 * b + 256], "Fo%d" % b, T["ps%d" % b][:, 0:256], "ps%d" % b, scale=1 / 128)
 
         def turn_al(o):
             TR(T.al[:, 64 * o:64 * o + 64], "al%d" % o, T.R[:, 64 * o:64 * o + 64], "R%d" % o)
@@ -467,127 +455,145 @@ def rank_program(g, core, T, topo):
         above(1)
         TT(T.be[:], "be", ends, T.al[:, 14:128:16], pk + ["al0", "al1"], A.subtract)
         steps(0)
-        ng = ("ng0", "ng1")[min(r, 1)]
-        cuts = CUTS[min(r, 1)]
-        vals = [lambda a=a, b=b: TT(T.prb[:, 16 * a:16 * b], "prb", T.zf[:, TR2:TR2 + 48].indirect(T.LU[:, a:b]), T[ng][:, 16 * a:16 * b],
-                                    ["tr2", "tr2c", "LU", ng], A.min) for a, b in zip(cuts, cuts[1:])]
-        flags = [lambda: TS(T.zf[:, RP2 + 1:RP2 + 32:16], "rp2", T.pen[:, 0:2], ["pen", "cap"], T.Y[:, 79:80], 4096.0, A.mult, A.add),
-                 lambda: TR(T.zf[:, TR2:TR2 + 32], "tr2", T.zf[:, RP2:RP2 + 32], "rp2")]
-
-        def then(*fs):
-            return lambda: [f() for f in fs]
+        lf = 32 * r
+        flags = [lambda: TS(T.rp2[:], "rp2", T.zer[:, 0:64], ["zer", "pn", "cap"], C("pn"), T.Y[:, 79:80], A.add, A.mult),
+                 lambda: TR(T.tr2[:, 0:64], "tr2", T.rp2[:], "rp2"),
+                 lambda: [ACT(T.dr[:], "dr", T.dT[:].indirect(T.LG[:]), ["dT", "LG0", "LG1"]),
+                          ACT(T.fr[:], "fr", T.tr2[:].indirect(T.LG[:]), ["tr2", "tr2c", "LG0", "LG1"])]]
+        mate = [lambda o=o: SCAN(T.fd[:, 128 * o:128 * o + 128], "fd", T.ar[:], T.fr[:, 128 * o:128 * o + 128], ["ar", "fr"], 0.0, A.add, A.max) for o in both]
+        pc = T.pc[:, 16 * min(r, 1):16 * min(r, 1) + 16]
+        mate.append(lambda: TT(T.fb[:], "fb", T.fd[:, 15:256:16], pc, ["fd", "pc"], A.max))
+        if r == 0:
+            mate.append(lambda: TS(T.lf[:, lf:lf + 16], "lf%d" % r, T.fb[:], ["fb", "q5"], C("q5"), None, A.subtract))
+        else:
+            mate.append(lambda: [TS(T.lf[:, lf + 8 * y:lf + 8 * y + 8], "lf%d" % r, T.fb[:, y:16:2], ["fb", "q5"], C("q5"), None, A.subtract) for y in both])
+        ties = lambda: TS(T.rq[0:64, 10:74], "rq1", T.tie[0:64, :], ["tie", "rep0", "rep1"], T.rep[0:64, 9:10], None, A.add)
 
         if r == 0:
             late = [lambda b=b: QT("qcg", 128 * b, 128 * b + 128, T.cg[:, 3 - b:515 - b], "cg") for b in range(NCG, 4)]
-            fill = [flags[0], then(lists[0], lists[1]), then(flags[1], late[0], lists[2]),
+            fill = [flags[0], then(sy[0][1], sy[1][1], flags[1], flags[2]), then(late[0], lambda: TR(T.tf[:, 64:128], "tfc", T.tie[:], "tie")),
                     then(first[1], lambda: TS(T.cc[:, 24:48], "cc", T.cc[:, 0:24], "cc0", -127.5, None, A.add)),
                     then(lambda: TT(T.c1[:], "c1", T.fs[:, 0:256:32], T.cc[:, 24:32], ["fs0", "fs1", "cc"], A.add), late[1]),
-                    lambda: turn("lO", "l4", "zcC", "zrC"),
-                    then(late[2], lambda: CP(T.ls[:, 0:10:2], "lsC", T.zc[:, 32 * COLS.index("lO"):32 * COLS.index("lU1"):32], "zcC"))]
-            mates = [lists[3]]
+                    then(ties, late[2]), then()]
         else:
-            fill = [flags[0], then(lists[0], lists[1], first[1]), then(lists[2], flags[1]),
-                    then(lists[3], lambda: TT(T.ck[:], "ck", T.fs[:, 0:256:16], T.cc[:, 32:48], ["fs0", "fs1", "cc"], A.add)),
-                    then(lambda: TT(T.c1[:], "c1", T.ck[:, 0:8], T.ck[:, 8:16], "ck", A.min), vals[0]), vals[1], vals[2]]
-            mates, vals = [], vals[3:]
+            fill = [then(flags[0]), then(sy[0][0], flags[1]), then(sy[0][1], flags[2], first[1]),
+                    then(lambda: TT(T.ck[:], "ck", T.fs[:, 0:256:16], T.cc[:, 32:48], ["fs0", "fs1", "cc"], A.add)),
+                    then(lambda: TT(T.c1[:], "c1", T.ck[:, 0:8], T.ck[:, 8:16], "ck", A.min), ties), then(), then()]
         fill[0] = then(lambda: steps(1), lambda: TT(T.er[:, 1:8], "er", T.be[:, 0:7], T.be[:, 1:8], ["be", "er0"], A.subtract),
                        lambda: TS(T.er[:, 8:9], "er8", T.be[:, 7:8], ["be", "zcA", "er0"], C("us"), None, A.add), fill[0])
-        fill[6] = then(lambda: TT(T.k0[:], "k0", T.Y[:, 7:64:8], T.be[:], ["Y", "be"], A.add), fill[6])
-        weave(level(32, 64, "rep1") + [lambda: [TR(T.zf[p:p + 32, TRP:TRP + 32], "trp2", T.rep[32:64, 9:41], "rep1") for p in (64, 96)]]
-              + level(64, 128, "rep2") + [lambda: TR(T.zf[:, TRF:TRF + 32], "trf", T.rep[:, 9:41], ["rep0", "rep1", "rep2"])],
-              fill + [lambda: TS(T.k1[:], "k1", T.k0[:], "k0", 256.0, DROP, A.mult, A.min)])
-        ACT(T.dr[:], "dr", T.dT[:].indirect(T.LG[:, 0:16]), ["dT", "LG"])
-        ACT(T.dr[:, 0:256:32], "dr", T.dr[:, 0:256:32], "dr", AF.Identity, bias=-DROP)
+        fill[6] = then(lambda: TT(T.k0[:], "k0", T.Y[:, 7:64:8], T.be[:], ["Y", "be"], A.add), fill[6], mate[0])
+        weave(level(T.rep, 41, 32, 64, "rep1") + [lambda: [TR(T.zf[p:p + 32, TRP:TRP + 32], "trp2", T.rep[32:64, 9:41], "rep1") for p in (64, 96)]]
+              + level(T.rq, 74, 64, 128, "rq2") + [lambda: TR(T.tf[:, 0:64], "tf", T.rq[:, 10:74], ["rq1", "rq2"])],
+              fill + [then(lambda: TS(T.k1[:], "k1", T.k0[:], "k0", 256.0, DROP, A.mult, A.min), mate[1])])
         if r == 0:
-            for n, a, c in (("ng0", 0, "o0"), ("ng0", 128, "o1"), ("ngn", 0, "x2"), ("ngn", 128, "o2")):
-                ACT(T[n][:, a:a + 128], n, T[n][:, a:a + 128], [n + "0", c], AF.Identity, bias=C(c))
-        key = T.key[:, 16:272]
-        unpack("qcg", "qa%d" % r, None, "G", 1 / 256, "T")
-        unpack("qce", "qa%d" % r, None, "F", 1 / 256, "T", 4)
-        for o in both:
-            TT(T.wr[:, 128 * o:128 * o + 128], "wr%d" % o, T.zf[:, TRF:TRF + 48].indirect(T.LG[:, 8 * o:8 * o + 8]), T.hrow[:, 128 * o:128 * o + 128],
-               ["trf", "trfc", "LG", "hrow"], A.add)
-        for o in both:
-            SCAN(T.key[:, 16 + 128 * o:144 + 128 * o], "key%d" % o, T.wr[:, 128 * o:128 * o + 128], T.dr[:, 128 * o:128 * o + 128], ["wr%d" % o, "dr"],
-                 -1.0, A.max, A.add)
-            if o == 0:
-                TT(T.k2[:], "k2", T.k1[:], T.c1[:], ["k1", "c1"], A.add)
-        for o in both:
-            TR(T.kt[:, 128 * o:128 * o + 128], "kt%d" % o, T.key[:, 16 + 128 * o:144 + 128 * o], "key%d" % o)
-            if o == 0:
-                RED(C("km"), "km", T.k2[:], "k2", A.min)
-        CP(T.own[:, 0:16], "own0", T.kt[:, 0:128].indirect(L("l4")), ["kt0", "lsC"])
-        TR(T.kt[:, 256:544], "kt2", T.key[:], ["key0", "key1"])
-        CP(T.k16[:, 0:128], "k16", T.key[:, 16:144], "key0")
-        CP(T.own[:, 16:32], "own1", T.kt[:, 128:256].indirect(L("l4")), ["kt1", "lsC"])
-        weave(mates, [])
-        CP(T.ow2[:, 0:16], "owh", T.kt[:, 256:544].indirect(L("l2")), ["kt2", "lsC"])
-        CP(T.k16[:, 128:256], "k16", T.key[:, 144:272], "key1")
-        TS(C("rn"), "rn", C("km"), "km", ROUND256, -ROUND256, A.add, A.add)
-        TT(T.ow2[:, 16:32], "owl", T.kt[:, 256:544].indirect(L("l2")), T.ow2[:, 0:16], ["kt2", "lsC", "owh"], A.subtract)
-        def deal(o, ok, a, h0, h1):
-            for h in range(h0, h1):
-                TR(o[:, 32 * h:32 * h + 32], ok, T.win[:, a + h:a + 256:8], "win")
+            ACT(T.pc[:, 0:16], "pc", T.rows[:, 80:96], ["rowp", "jq"], AF.Identity, bias=C("jq"))
+            ACT(T.pl0[:], "pl0", T.pl0[:], ["pl00", "q6"], AF.Identity, bias=C("q6"))
+        unpack("qcg", "qa%d" % r, None)
+        unpack("qce", "qa%d" % r, None, 4)
 
+        def copy_G(t):
+            ACT(T.D[:, GG + 272 * t:GG + 272 * t + 256], "G%d" % t, T["ps%d" % t][:, 0:256], "ps%d" % t)
+
+        for t in range(GE[r]):
+            copy_G(t)
+        TT(T.wr[:, 0:128], "wr0", T.tf[:].indirect(T.LG[:, 0:8]), T.hrow[:], ["tf", "tfc", "LG0", "LG1", "hrow"], A.add)
+        ACT(T.wr[:, 128:256], "wr1", T.tf[:].indirect(T.LG[:, 8:16]), ["tf", "tfc", "LG0", "LG1"])
+        for t in range(GE[r], 4):
+            copy_G(t)
+        TT(T.k2[:], "k2", T.k1[:], T.c1[:], ["k1", "c1"], A.add)
+        mate[2]()
+        for o in both:
+            a = slice(128 * o, 128 * o + 128)
+            SCAN(T.key[:, a], "key%d" % o, T.wr[:, a], T.dr[:, a], ["wr%d" % o, "dr"], -1.0, A.max, A.add)
+        RED(C("km"), "km", T.k2[:], "k2", A.min)
+
+        def own(o, ok, a, h):
+            SCAN(back(o, a, a + 128), ok, back(T.mk, 0, 128), back(T.key, 128 * h, 128 * h + 128), ["mk", "key%d" % h], 0.0, A.mult, A.max)
+
+        own(T.od, "od0", 0, 0)
+        own(T.od, "od1", 128, 1)
+        own(T.oh, "oh", 0, 1)
+        CP(T.k16[:, 0:128], "k16", T.key[:, 0:128], "key0")
+        TS(C("rn"), "rn", C("km"), "km", ROUND256, -ROUND256, A.add, A.add)
+        CP(T.k16[:, 128:256], "k16", T.key[:, 128:256], "key1")
+        TT(T.ol[:], "ol", T.od[:, 128:256:16], T.oh[:, 0:128:16], ["od1", "oh"], A.subtract)
+        mate[3]()
+        TS(T.lf[:, lf + 16:lf + 18], "lf%d" % r, T.pen[:], ["pen", "km", "rn"], C("km"), C("rn"), A.add, A.subtract)
+        send(T.fa[:, lf:lf + 18], T.lf[:, lf:lf + 18], "f", r)
         for b in range(8):
-            j = 16 * (b // 4) + b % 4
-            ACT(T.js[:, 256 * b:256 * b + 256], "acc", key, ["key0", "key1", "own%d" % (b // 4)], AF.Sign, bias=T.own[:, j:j + 1], scale=-1.0,
+            ACT(T.js[:, 256 * b:256 * b + 256], "acc", T.key[:], ["key0", "key1", "od0"], AF.Sign, bias=T.od[:, 16 * b:16 * b + 1], scale=-1.0,
                 accum_out=T.acc[:, b:b + 1])
-        unpack("qcg", "qa%d" % r, None, "G", 1 / 256, "S")
-        unpack("qce", "qa%d" % r, None, "F", 1 / 256, "S", 4)
-        weave(vals, [])
         for b in range(8):
-            TS(T.jv[:, 256 * b:256 * b + 256], "jv%d" % b, T.k16[:], ["k16", "owh", "owl"], T.ow2[:, b:b + 1], T.ow2[:, 16 + b:17 + b], A.subtract, A.is_lt)
+            TS(T.jv[:, 256 * b:256 * b + 256], "jv%d" % b, T.k16[:], ["k16", "oh", "ol"], T.oh[:, 16 * b:16 * b + 1], T.ol[:, b:b + 1], A.subtract, A.is_lt)
         for b in range(8):
             SCAN(T.pl[:, 2040 + b::-16], "pl", T.jv[:, 256 * b:256 * b + 128], T.jv[:, 256 * b + 128:256 * b + 256], ["jv%d" % b, "xb"], T.xb[:, 0:1], A.add, A.add)
-        TS(T.pl[:, 0:8], "pl", T.acc[:, 0:8], ["acc", "xc"], 0.5, C("xc"), A.mult, A.add)
-        TS(T.lf[:, 16 * r:16 * r + 2], "lf%d" % r, T.pen[:, 2:4], ["pen", "km", "rn"], C("km"), C("rn"), A.add, A.subtract)
-        send(T.fa, T.lf, 2, "f", r)
+        TS(T.pl[:, 0:8], "pl", T.acc[:, 0:8], "acc", 0.5, 127.5, A.mult, A.add)
         for t in range(4):
-            ACT(T.G[:, 272 * t:272 * t + 16], "Gf%d" % t, T.G[:, 272 * t + 16:272 * t + 272].indirect(T.fa[:, 16 * r:16 * r + 1]), ["G%d" % t, "fa%d" % r])
-        emit("V", lambda: v.tensor_copy(T.win[:].indirect(T.pl[:, 0:16]), T.prb[:]), ["pl", "prb", "win"], ["win"])
-        deal(T.wt, "wt", 0, 0, 8)
-        deal(T.wk, "wk", 128, 0, 3)
-        TS(T.ll[:, 16 * r:16 * r + 16], "ll%d" % r, T.wt[:].indirect(L("lL")), ["wt", "lsC"], 144.0, None, A.add)
-        send(T.la, T.ll, 16, "l", r)
-        deal(T.wk, "wk", 128, 3, 8)
+            a = GG + 272 * t
+            ACT(T.D[:, a + 256:a + 272], "Gf%d" % t, T.D[:, a:a + 256].indirect(T.fa[:, lf + 16:lf + 17]), ["G%d" % t, "fa%d" % r])
+        for t in range(4):
+            a = GG + 272 * t
+            ACT(T.gz[:, 256 * t:256 * t + 256], "gz%d" % t, T.D[:, a:a + 272].indirect(T.fa[:, lf:lf + 16]), ["G%d" % t, "Gf%d" % t, "fa%d" % r])
+
+        def pairs(t):
+            TT(T.D[:, HS + 256 * t:HS + 256 * t + 256], "H%d" % t, T["ps%d" % (4 + t)][:, 0:256], T.gz[:, 256 * t:256 * t + 256], ["ps%d" % (4 + t), "gz%d" % t], A.add)
+
+        pl = ("pl0", "pl1")[min(r, 1)]
+        emit("V", lambda: v.tensor_copy(T.win[:].indirect(T.pl[:, 0:16]), T[pl][:]), ["pl", pl, "win"], ["win"])
+        if r:
+            pairs(0)
+        for h in range(8):
+            SCAN(T.dl[:, 256 * r + h:256 * r + 256:8], "ll%d" % r, T.ar[:, 0:32], T.win[:, h:256:8], ["ar", "win"], 0.0, A.add, A.max)
+        la, laid, kept = T.la[:, 16 * r:16 * r + 8], T.dl[:, 256 * r + 120:256 * r + 128], T.dl[:, 256 * r + 248:256 * r + 256]
+        send(la, laid, "l", r)
+        before = ["G%d" % t for t in range(4)] + ["Gf%d" % t for t in range(4)] + ["Fo%d" % t for t in range(4)]
+
+        def stay(t):
+            a = FO + 256 * t
+            (CP if t < XV else ACT)(T.X[:, t:512:4], "X0" + "VS"[t >= XV], T.D[:, a - 512:a + 256].indirect(kept), before + ["ll%d" % r])
+
         if r == 0:
-            TS(C("m2"), "m2", C("jj"), "zcA", 2.0, None, A.is_equal)
-        TS(T.lk[:], "lk", T.wk[:].indirect(L("lO")), ["wk", "lsC"], 128.0, None, A.add)
+            pairs(0)
+        pairs(1)
         for t in range(4):
-            (CP if t < XV else ACT)(T.X[:, t:512:4], "X0" + "VS"[t >= XV], T.Fo[:, 256 * t:256 * t + 256].indirect(T.lk[:, 0:8]), ["Fo%d" % t, "lk"])
-        z = "qz%d" % r
-        for t in range(4):
-            (CP if t < GV else ACT)(T.gz[:, 128 * t:128 * t + 128], "gz%d" % t, T.G[:, 272 * t:272 * t + 272].indirect(T.la[:, 16 * r + 8:16 * r + 16]),
-                                    ["G%d" % t, "Gf%d" % t, "la%d" % r])
+            stay(t)
+        pairs(2)
+        pairs(3)
         if r == 0:
-            ACT(C("m3"), "m3", C("m2"), "m2", AF.Identity, bias=1.0, scale=-1.0)
-            ACT(T.dl2[:], "dl2", T.ng0[:], ["ng0", "m2"], scale=C("m2"))
-            ACT(T.dl3[:], "dl3", T.ngn[:], ["ngn", "m3"], scale=C("m3"))
-        for t in range(4):
-            if t == QNA:
-                QT("na%d" % (r + 1), 0, 128, T.X[:, 0:512], ["X0V", "X0S"])
-            TT(T.Z[:, t:512:4], "ZV", T.F[:, 272 * t:272 * t + 272].indirect(T.la[:, 16 * r:16 * r + 8]), T.gz[:, 128 * t:128 * t + 128],
-               ["F%d" % t, "Fp", "la%d" % r, "gz%d" % t], A.add)
+            IOTA(T.colw[:], "colw", [[16, 6], [32, 8], [1, 16]], -64)
+        QT("na%d" % (r + 1), 0, 128, T.X[:, 0:512], ["X0V", "X0S"])
         if last:
             MM(4, 128, "qv", 0, "na3")
-            ACT(T.opw[:], "opw", T.win[:].indirect(L("lP")), ["win", "lsE"], AF.Identity, bias=128.0)
-            emit("Y", lambda: g.sync.dma_start(T.op[:], T.opw[2:128:16, :]), ["opw"], ["op"], dma=True)
         else:
-            scores(r + 1, (0,))
+            scores(r + 1, 0)
+            send_codes(r + 1, 0, 128, ["na%d" % (r + 1)], 2)
+        z = "qz%d" % r
+        for t in range(4):
+            a = HS + 256 * t
+            o, i, ik = T.Z[:, t:512:4], T.D[:, a - 512:a + 256].indirect(la), ["Fo2", "Fo3"] + ["H%d" % k for k in range(t + 1)] + ["la%d" % r]
+            if t < ZV:
+                TS(o, "ZV", i, ik, 1 / 256, None, A.mult)
+            else:
+                ACT(o, "ZS", i, ik, scale=1 / 256)
+        if last:
+            CP(T.ysb[:, :, 0:16], "ysb", T.ps4[:, 0:128], "ps4")
+        else:
+            TS(T.B[:, 0:512:4], "B0", T.ps4[:, 0:128], "ps4", 0.0, None, A.is_gt)
         QT(z, 0, 128, T.Z[:], ["ZV", "ZS"])
         for b in range(4):
             MM(b, 128, "qw", 128 * b, z, None, True, False)
             MM(b, 128, "qce", 128 * b, z, None, False, True)
         if last:
-            CP(T.ysb[:, :, 0:16], "ysb", T.ps4[:, 0:128], "ps4")
+            for k, li in enumerate((laid, kept)):
+                ACT(T.ow[:, 128 * k:128 * k + 128], "ow", T.colw[:].indirect(li), ["colw", "ll%d" % r])
+            ACT(T.opw[:], "opw", T.ow[:].indirect(L("lP")), ["ow", "lsE"])
+            emit("Y", lambda: g.sync.dma_start(T.op[:], T.opw[0:128:16, :]), ["opw"], ["op"], dma=True)
         else:
-            bits((0,))
+            QT("qb0", 0, 128, T.B[:, 0:512], "B0")
+            for bank, c in ((5, 0), (7, 128)):
+                MM(bank, 128, "qcs", c, "qb0")
             if r == 0:
-                turn("lU1", "lG1", "zcD", "zrD")
                 FILL(T.r16[:], "r160", 1.0)
-                CP(T.ls[:, 70:74:2], "lsD", T.zc[:, 32 * COLS.index("lU1"):32 * len(COLS):32], "zcD")
-                TS(T.rows[:, 16:32], "rows2", T.rows[:, 48:64], "rows3", -127.5, None, A.add)
                 TS(L("lR1"), "lsD", L("lR0"), "lsB", 0.5, None, A.mult)
                 TS(L("lD1"), "lsD", L("lD0"), "lsB", 0.5, None, A.mult)
                 FILL(T.cra[:], "cra0", U)
@@ -595,42 +601,46 @@ def rank_program(g, core, T, topo):
                 FILL(T.r16[:, 0:128:16], "r16", 0.0, "r160")
                 FILL(T.crow[:, 271:384:16], "crow", U + GONE, "crow0")
                 FILL(T.cra[:, 15:128:16], "cra", 16 * GONE, "cra0")
-                TT(T.ng1[:], "ng1", T.dl2[:], T.dl3[:], ["dl2", "dl3"], A.add)
+                ACT(T.pc[:, 16:32], "pc", T.rows[:, 96:112], ["rowq", "jq"], AF.Identity, bias=C("jq"))
+                ACT(T.pl1[:], "pl1", T.pl1[:], ["pl10", "q6"], AF.Identity, bias=C("q6"))
             else:
-                TS(L("lP"), "lsE", T.rows[:, 16:32], ["rows2", "zcA", "xc"], C("jj"), C("xc"), A.add, A.add)
-                TS(L("lF"), "lsE", T.rows[:, 32:48], ["rows2", "zcA"], C("jj"), None, A.add)
+                turn("lp", "lp", "zcD", "zrD")
                 QT("qv", 0, 128, T.vs[:], "vs")
+                TS(L("lF"), "lsE", T.rows[:, 96:112], ["rowq", "zcA"], C("jj"), None, A.add)
+                TS(L("lP"), "lsE", T.rows[:, 16:32], ["rows2", "zcD"], C("lp"), None, A.add)
         for b in range(4):
             o, i = T.X[:, 512 + b:1024:4], T["ps%d" % b][:, 0:128]
             if b >= HV:
                 TS(o, "X1V", i, "ps%d" % b, 0.0078125, None, A.mult)
             else:
                 ACT(o, "X1S", i, "ps%d" % b, scale=0.0078125)
+        if not last:
+            rows_V(0, T.crow[:, 256:384])
         QT("nb%d" % (r + 1), 0, 128, T.X[:, 512:1024], ["X1V", "X1S"])
         if not last:
-            scores(r + 1, (1,))
-            send_codes(r + 1)
-            rows_S((0,))
-            rows_V(0, T.crow[:, 256:384])
+            scores(r + 1, 1)
+            send_codes(r + 1, 128, 256, ["nb%d" % (r + 1)], 4)
+            sy, first = symbols(0, 7, slice(0, 16, 2)), firsts((0,))
             SCAN(T.pt[:], "pt", T.r16[:], T.ps5[:, 0:128], ["r16", "ps5"], 0.0, A.mult, A.add)
-            kept, first = list_V((0,)), firsts((0,))
             first[0]()
+            sy[0]()
+            first[1]()
             ACT(T.pt8[:, 0:8], "pt8", T.pt[:, 15:128:16], "pt", AF.Identity, bias=16 * U)
             ACT(T.pt8[:, 8:16], "pt9", T.pt[:, 15:128:16], "pt", AF.Identity, bias=16 * U - 8 * GONE)
-            bits((1,))
+            sy[1]()
+            TS(T.B[:, 512:1024:4], "B1", T.ps4[:, 0:128], "ps4", 0.0, None, A.is_gt)
             TT(T.e1[:, 0:128:16], "e1", T.pb[:, 0:128:16], T.pt8[:, 0:8], ["pb0", "pt8"], A.min)
             TS(T.pt8[:, 16:24], "pta", T.pb[:, 0:128:16], "pb0", DROP, 8 * GONE + U, A.is_ge, A.mult)
-            kept[0]()
-            kept[1]()
+            QT("qb1", 0, 128, T.B[:, 512:1024], "B1")
+            for bank, c in ((6, 0), (7, 128)):
+                MM(bank, 128, "qcs", c, "qb1")
             TT(T.cra[:, 0:128:16], "cra", T.pt8[:, 8:16], T.pt8[:, 16:24], ["pt9", "pta"], A.add)
             RED(T.ab[:, 256:257], "abk", T.pt8[:, 16:24], "pta", A.min)
             ACT(T.pkr[:], "pkr", T.e1[:].indirect(L("lR1")), ["e1", "lsD"])
-            rows_S((1,))
             for o in both:
                 a = slice(64 * o, 64 * o + 64)
                 TS(T.ab[:, 128 + 64 * o:192 + 64 * o], ["ab1", "ac%d" % o], T.ps6[:, a], ["ps6", "nb"], C("nb"), GONE, A.not_equal, A.mult)
                 TT(T.dz[:, 128 + 64 * o:192 + 64 * o], ["dz1", "dc%d" % o], T.ps6[:, a], T.cra[:, a], ["ps6", "cra"], A.add)
-            first[1]()
     MM(5, 128, "qv", 0, "nb3")
     (oc, osc), (ic, isc) = K("qp", 0, 256), K("qn3", 0, 256)
     emit("V", lambda: v.tensor_copy(oc.bitcast(dt.uint32), ic.bitcast(dt.uint32).indirect(L("lF"))), ["na3", "nb3", "lsE"], ["qp"])
@@ -643,6 +653,6 @@ def rank_program(g, core, T, topo):
              ["sqp"], ["osc%d" % k], dma=True)
     for k in range(nd[0]):
         g.wait_ge(T.sem["ld%d" % k], 16)
-    g.wait_ge(T.sem.sent, 4 * NR * n_out)
+    g.wait_ge(T.sem.sent, calls[0] * n_out)
     for k in "VSTG":
         g.wait_ge(T.sem["c" + k], count[k])

@@ -8,16 +8,17 @@ DK = 16384.0
 HOLD = 512.0
 FAR = float(1 << 30)
 ROUND256 = 1.5 * float(1 << 31)
-NCE, NCG = 1, 1
 HV = 3
 XV, ZV = 1, 2
 GE = (0, 2, 2)
-NV = 8
+FE = 1
+NV = 9
+NS = 16 - NV
 COLS = ["jj", "us", "w2", "lR", "lD", "lW", "k4", "lp"]
 LISTS = {"lW": (0, 4), "lD0": (4, 4), "lR0": (8, 8), "lP": (16, 16), "lF": (32, 16), "lD1": (48, 4), "lR1": (52, 8)}
-SMALL = ["pf", "wu", "g0", "nb", "mn", "km", "rn", "pn", "q5", "q6", "jq", "t0", "g1"]
-E40, TRP = 0, 48
-GG, FO, HS = 0, 1088, 2112
+SMALL = ["pf", "wu", "g0", "nb", "mn", "km", "rn", "pn", "q5", "q6", "jq", "ku", "kb", "gp", "jr"]
+E40, TRP = 0, 80
+GG, FO, HS = 512, 1600, 2624
 
 SCRATCH = {}
 
@@ -28,28 +29,27 @@ def _b(name, n, d="float32"):
 
 for _n, _k, _d in (
         ("xs", 1024, "bfloat16"), ("us", 512, "bfloat16"), ("vs", 512, "bfloat16"),
-        ("one", 128, "bfloat16"), ("zer", 528, "bfloat16"), ("idn", 128, "bfloat16"), ("prm", 128, "bfloat16"),
-        ("ce", 528, "bfloat16"), ("cg", 528, "bfloat16"), ("cs", 1024, "bfloat16"), ("vk", 128, "float32"), ("vg", 128, "float32"),
+        ("one", 128, "bfloat16"), ("idn", 128, "bfloat16"), ("prm", 128, "bfloat16"),
+        ("ce", 516, "bfloat16"), ("cg", 516, "bfloat16"), ("cs", 1024, "bfloat16"), ("vg", 128, "float32"),
         ("zr", 32 * len(COLS), "float32"), ("zc", 32 * len(COLS), "float32"), ("sm", 8 * len(SMALL), "float32"),
-        ("ls", 60, "uint16"), ("rows", 112, "float32"), ("cc", 56, "float32"),
-        ("crow", 384, "float32"), ("wrow", 384, "bfloat16"), ("r16", 128, "bfloat16"), ("dT", 128, "float32"),
-        ("hrow", 128, "float32"), ("zf", 80, "float32"), ("cra", 128, "float32"),
-        ("i16", 144, "bfloat16"), ("eq", 144, "bfloat16"), ("a1", 128, "bfloat16"), ("a2", 128, "bfloat16"), ("ar", 128, "bfloat16"), ("mk", 128, "bfloat16"),
+        ("ls", 60, "uint16"), ("rows", 56, "float32"), ("cc", 32, "float32"),
+        ("crow", 256, "bfloat16"), ("wrow", 384, "bfloat16"), ("r16", 128, "bfloat16"), ("dT", 128, "bfloat16"),
+        ("r15", 64, "float32"), ("zf", 144, "float32"), ("cra", 128, "float32"),
+        ("i16", 160, "bfloat16"), ("eq", 160, "bfloat16"), ("a1", 128, "bfloat16"), ("a2", 128, "bfloat16"), ("ar", 128, "bfloat16"), ("mk", 160, "bfloat16"),
         ("lc", 16, "float32"), ("pc", 32, "float32"), ("tie", 64, "float32"), ("tf", 128, "float32"), ("rp2", 64, "float32"), ("tr2", 128, "float32"),
         ("rq", 74, "float32"), ("pl0", 256, "float32"), ("pl1", 256, "float32"), ("colw", 768, "bfloat16"),
-        ("B", 1024, "bfloat16"), ("dz", 256, "bfloat16"), ("ab", 258, "bfloat16"), ("dr", 256, "float32"),
-        ("sd", 256, "float32"), ("LG", 16, "uint16"), ("fr", 256, "bfloat16"), ("fd", 256, "float32"), ("fb", 16, "float32"),
-        ("pb", 1312, "bfloat16"), ("fs", 256, "bfloat16"), ("e1", 128, "bfloat16"), ("pkr", 128, "bfloat16"), ("pm", 656, "bfloat16"), ("pt", 128, "float32"),
+        ("B", 1024, "bfloat16"), ("dz", 256, "bfloat16"), ("ab", 258, "bfloat16"), ("dr", 256, "bfloat16"),
+        ("sd", 256, "float32"), ("LG", 16, "uint16"), ("fr", 256, "uint16"), ("fd", 256, "uint16"),
+        ("pb", 2368, "bfloat16"), ("fs", 256, "bfloat16"), ("e1", 128, "bfloat16"), ("pkr", 128, "bfloat16"), ("pm", 1184, "bfloat16"), ("pt", 128, "float32"),
         ("pt8", 24, "float32"), ("ck", 16, "float32"), ("R", 128, "bfloat16"), ("al", 128, "bfloat16"),
-        ("dif", 64, "float32"), ("val", 64, "float32"), ("bd", 64, "float32"), ("yi", 64, "float32"), ("Y", 592, "float32"),
-        ("pr", 256, "float32"), ("be", 8, "float32"), ("er", 74, "float32"), ("k0", 8, "float32"), ("rep", 41, "float32"), ("c1", 8, "float32"),
-        ("k1", 8, "float32"), ("k16", 256, "uint16"), ("k2", 8, "float32"), ("pen", 2, "float32"),
+        ("val", 64, "float32"), ("bd", 64, "float32"), ("yi", 64, "float32"), ("Y", 592, "float32"),
+        ("pr", 8, "float32"), ("be", 9, "float32"), ("er", 74, "float32"), ("k0", 8, "float32"), ("rep", 74, "float32"), ("c1", 8, "float32"),
+        ("k1", 8, "float32"), ("k16", 480, "uint16"), ("jb", 4, "bfloat16"), ("k2", 8, "float32"), ("pen", 2, "float32"),
         ("lf", 32 * NR, "uint16"), ("fa", 32 * NR, "uint16"),
-        ("wr", 256, "float32"), ("key", 256, "float32"), ("od", 256, "float32"), ("oh", 128, "bfloat16"), ("ol", 8, "bfloat16"),
-        ("js", 256 * (16 - NV), "bfloat16"), ("jv", 256 * NV, "bfloat16"),
-        ("acc", 16, "float32"), ("pl", 2048, "uint16"), ("xb", 2, "bfloat16"),
+        ("wr", 256, "uint16"), ("od", 256, "float32"), ("oh", 16 * NV, "bfloat16"), ("ol", 16, "bfloat16"),
+        ("js", 256 * NS, "bfloat16"), ("jv", 256 * NV, "bfloat16"), ("acc", 16, "float32"), ("pl", 2048, "uint16"),
         ("win", 256, "float32"), ("dl", 256 * NR, "uint16"), ("la", 16 * NR, "uint16"), ("ow", 256, "float32"), ("opw", 256, "float32"),
-        ("D", 3136, "bfloat16"), ("gz", 1024, "bfloat16"), ("Z", 512, "bfloat16"),
+        ("D", 3648, "bfloat16"), ("gz", 1024, "bfloat16"), ("Z", 512, "bfloat16"),
         ("X", 1024, "bfloat16"), ("ysb", (8, 32), "float32")):
     _b(_n, _k, _d)
 for _n, _k in (("qn", 256 * (NR + 1)), ("qa", 256 * NR), ("qp", 256), ("qu", 128), ("qv", 128), ("qw", 512), ("qc", 1280), ("qb", 256),
@@ -175,6 +175,9 @@ def rank_program(g, core, T, topo):
     def ACT(o, ok, i, ik, f=AF.Copy, **kw):
         return emit("S", lambda: s.activation(o, i, f, **kw), pt(ik), pt(ok))
 
+    def SET(o, ok, n, c, ik=(), a=0, b=128):
+        return ACT(o, ok, T.B[a:b, 1:2 * n:2], ["zer"] + pt(ik), AF.Identity, bias=c)
+
     def TR(o, ok, i, ik):
         return emit("V", lambda: v.transpose(o, i), pt(ik), pt(ok))
 
@@ -201,9 +204,9 @@ def rank_program(g, core, T, topo):
     def AFF(o, ok, i, ik, pat, op, base, cm):
         return emit("G", lambda: g.affine_select(o, i, pat, op, 0.0, base, cm), pt(ik), pt(ok))
 
-    def row(n, a=0, b=32, st=1):
+    def row(n, a=0, b=32, st=1, p=128):
         k = 32 * COLS.index(n)
-        return T.zr[:, k + a:k + b:st]
+        return T.zr[0:p, k + a:k + b:st]
 
     def turn(a, b, ok, ik):
         i, j = 32 * COLS.index(a), 32 * COLS.index(b) + 32
@@ -228,320 +231,299 @@ def rank_program(g, core, T, topo):
         calls[0] += 1
         landed("ar%s%d" % (k, r), n_in, ["%sa%d" % (k, r)])
 
-    emit("Y", lambda: g.sync.dma_start(T.xs[:, 0:512], T.x[:, 0:512]), [], ["xs0"], dma=True)
-    emit("S", lambda: s.dma_start(T.us[:], T.u[:]), [], ["us"], dma=True)
-    emit("Y", lambda: g.sync.dma_start(T.xs[:, 512:1024], T.x[:, 512:1024]), [], ["xs1"], dma=True)
-
-    FILL(T.one[:], "one", 128.0)
-    FILL(T.zer[:], "zer", 0.0)
-    FILL(row("w2"), "zr0", 0.0)
-    IOTA(row("jj"), "zrA", [[0, 2], [1, 16]], 0)
-    IOTA(row("us"), "zrA", [[0, 2], [int(U), 8], [0, 2]], int(U))
-    AFF(T.idn[:], "idn", T.one[:], "one", [[-1, 128]], A.is_equal, 0, 1)
-    IOTA(T.vk[:], "vk", [[-16, 4], [0, 32]], 0, 1)
-    IOTA(T.vg[:], "vg", [[-16, 8], [0, 16]], 0, 1)
-    IOTA(T.i16[:], "i16", [[0, 9], [1, 16]], 0)
-    IOTA(row("lR"), "zrB", [[32, 2], [0, 16]], 0)
-    IOTA(row("lD"), "zrB", [[0, 2], [32, 2], [0, 8]], 0)
-    IOTA(row("lW"), "zrB", [[0, 4], [2, 8]], 0)
-    IOTA(row("k4"), "zrB", [[2, 2], [0, 8], [1, 2]], 4)
-    IOTA(C("pf"), "pf", [[0, 1]], 0, 1)
-    IOTA(T.rows[:, 0:4], "rows", [[64, 4]], 0)
-    IOTA(T.rows[:, 8:16], "rows", [[64, 4], [0, 2]], 0)
-    IOTA(T.rows[:, 72:80], "rowl", [[16, 2], [1, 2], [0, 2]], 0)
-    AFF(T.prm[:, 0:16], "prm", T.one[:, 0:16], "one", [[-1, 16]], A.is_equal, -112, 1)
-    AFF(T.prm[:, 16:32], "prm", T.one[:, 0:16], "one", [[-1, 16]], A.is_equal, 0, 1)
-    AFF(T.prm[:, 32:128], "prm", T.one[:, 0:96], "one", [[-16, 3], [0, 2], [-1, 16]], A.is_equal, -16, 1)
-
-    FILL(T.cs[:], "cs0", 0.0)
-    ACT(T.ce[:], "ce0", T.zer[:], "zer")
-    ACT(T.ce[:, 3:512:4], "ce", T.idn[:], ["idn", "ce0"])
-    ACT(T.B[:, 0:512], "B0", T.zer[:, 0:512], "zer")
-    ACT(T.B[:, 512:1024], "B1", T.zer[:, 0:512], "zer")
-    ACT(T.crow[:], "crow0", T.zer[:, 0:384], "zer", AF.Identity, bias=U)
-    ACT(T.crow[:, 31:256:32], "crow", T.zer[:, 0:8], ["zer", "crow0"], AF.Identity, bias=GONE)
-    ACT(T.er[:], "er0", T.zer[:, 0:74], "zer")
-    ACT(T.pr[:], "pr", T.zer[:, 0:256], "zer")
-    ACT(T.tr2[:, 64:128], "tr2c", T.zer[:, 0:64], "zer")
-    ACT(T.rows[:, 64:72], "rowz", T.zer[:, 0:8], "zer")
-    ACT(T.xb[:, 0:1], "xb", T.zer[:, 0:1], "zer")
-    for k in range(4):
-        ACT(T.dT[:, 32 * k:32 * k + 32], "dT", row("us"), "zrA", AF.Identity, bias=-DK * (k % 2))
-    ACT(T.cg[:], "cg0", T.zer[:], "zer")
-
-    for i in range(3):
-        FILL(row("w2", i, 32, 16), "zrV", float(8 >> i), "zr0")
-    FILL(T.wrow[:], "wrow0", 1.0)
-    turn("jj", "w2", "zcA", ["zrA", "zrV"])
-    FILL(T.zf[:], ["zf0", "trp1", "trp2"], 0.0)
-    TS(C("wu"), "wu", C("w2"), "zcA", U / 2, None, A.mult)
-    TS(C("nb"), "nb", C("us"), "zcA", -U, None, A.add)
-    TS(C("q5"), "q5", C("jj"), "zcA", 15.0, HOLD, A.is_lt, A.mult)
-    CP(T.zf[:, E40 + 8:E40 + 9], "e40", C("us"), ["zcA", "zf0"])
-    TS(T.cs[:, 0:512:4], "cs", T.vk[:], ["vk", "zcA", "wu", "cs0"], C("jj"), C("wu"), A.is_equal, A.mult)
-    FILL(T.bd[:, 0:64:32], "bd0", -FAR)
-    FILL(T.wrow[:, 271:384:16], "wrow", 4096.0, "wrow0")
-    FILL(T.Y[:, 71:592:8], ["Yc", "cap"], FAR)
-    FILL(T.pb[:, 256:1312:32], ["pfar", "cap0"], FAR)
-    TS(T.cs[:, 512:1024:4], "cs", T.vg[:], ["vg", "zcA", "cs0"], C("jj"), C("w2"), A.is_equal, A.mult)
-    TS(T.eq[:], "eq", T.i16[:], ["i16", "zcA"], C("jj"), None, A.is_equal)
-    FILL(T.pen[:], "pen", 127.5)
-    TS(C("pn"), "pn", C("us"), "zcA", 2 / U / FAR, 254.0 / FAR, A.mult, A.add)
-    QT("qcs", 0, 256, T.cs[:], "cs")
-    ACT(T.a1[:], "a1", T.eq[:, 15:143], "eq", scale=HOLD)
-    ACT(T.a2[:], "a2", T.eq[:, 16:144], "eq", scale=-4 * HOLD)
-    ACT(T.mk[:], "mk", T.eq[:, 16:144], "eq", AF.Identity, bias=1.0, scale=-1.0)
-    ACT(C("q6"), "q6", C("q5"), "q5", AF.Identity, bias=HOLD, scale=-1.0)
-    ACT(C("jq"), "jq", C("jj"), ["zcA", "q5"], AF.Identity, bias=C("q5"))
-    ACT(T.cg[:, 3:512:4], "cg", T.prm[:], ["prm", "cg0"])
-    ACT(T.win[:], "win", T.zer[:, 0:256], "zer")
-    ACT(T.pm[:, 0:128], "pm", T.zer[:, 0:128], "zer")
-    ACT(T.e1[:], "e1", T.zer[:, 0:128], "zer")
-    for b in range(NCE):
-        QT("qce", 128 * b, 128 * b + 128, T.ce[:, 3 - b:515 - b], "ce")
-    TS(C("g0"), "g0", C("pf"), "pf", 16.0, 64.0, A.is_lt, A.mult)
-    TS(C("t0"), "t0", C("jj"), "zcA", 0.0, 32.0, A.is_equal, A.mult)
-    QT("qu", 0, 128, T.us[:], "us")
-    QT("na0", 0, 128, T.xs[:, 0:512], "xs0")
-    QT("nb0", 0, 128, T.xs[:, 512:1024], "xs1")
-
-    IOTA(T.be[:], "be", [[1, 8]], 0)
-    ACT(T.cc[:, 48:56], "ramp", T.be[:], "be", scale=2 * GONE)
-    IOTA(T.cc[:, 0:8], "cc0", [[288, 8]], 0)
-    IOTA(T.cc[:, 8:24], "cc0", [[128, 2], [272, 8]], 0)
-    IOTA(T.hrow[:], "hrow", [[1, 4], [0, 32]], -4)
-    IOTA(T.rows[:, 80:96], "rowp", [[16, 16]], 0)
-    send_codes(0, 0, 256, ["na0", "nb0"], 2)
-    emit("Y", lambda: g.sync.dma_start(T.qw[:, 0:512].bitcast(dt.uint8), T.wc[:, 0:2048]), ["qa0"], ["qw"], dma=True)
-    emit("Y", lambda: g.sync.dma_start(T.sqw[:, 0:512], T.ws[:, 0:512]), [], ["sqw"], dma=True)
-    emit("Y", lambda: g.sync.dma_start(T.vs[:], T.v[:]), [], ["vs"], dma=True)
-    IOTA(T.pl0[:], "pl00", [[1, 256]], 0)
-    IOTA(T.rows[:, 96:112], "rowq", [[16, 8], [128, 2]], 0)
-    IOTA(T.pl1[:], "pl10", [[16, 8], [128, 2], [1, 16]], 0)
-    IOTA(T.rows[:, 16:32], "rows2", [[128, 2], [2, 8]], 0)
-    IOTA(row("lp"), "zrD", [[0, 2], [1, 2], [16, 8]], 0)
-
-    def dims(parts):
-        return (256, 0) if len(parts) == 2 else (128, parts[0])
-
-    def keys(n, parts):
-        return [n + str(p) for p in parts]
-
     def back(t, a, b):
         return t[:, b - 1::-1] if a == 0 else t[:, b - 1:a - 1:-1]
 
-    def scores(k, o):
-        MM(4, 128, "qu", 0, ("na%d", "nb%d")[o] % k)
+    def signs(o, bank=4):
+        TS(T.B[:, 512 * o:512 * o + 512:4], "B%d" % o, T["ps%d" % bank][:, 0:128], "ps%d" % bank, 0.0, None, A.is_gt)
 
-    def bits(o):
-        TS(T.B[:, 512 * o:512 * o + 512:4], "B%d" % o, T.ps4[:, 0:128], "ps4", 0.0, None, A.is_gt)
+    def spread(o):
         QT("qb%d" % o, 0, 128, T.B[:, 512 * o:512 * o + 512], "B%d" % o)
-        for bank, c in ((5 + o, 0), (7, 128)):
+        for bank, c in ((5 + o, 0), ((7, 4)[o], 128)):
             MM(bank, 128, "qcs", c, "qb%d" % o)
 
-    def rows_V(o, c, more=()):
+    def rows_V(o, c, ck="crow"):
         a, ps = slice(128 * o, 128 * o + 128), "ps%d" % (5 + o)
-        TS(T.ab[:, a], ["ab%d" % o] + ["a" + k for k in more], T[ps][:, 0:128], [ps, "nb"], C("nb"), GONE, A.not_equal, A.mult)
-        TT(T.dz[:, a], ["dz%d" % o] + ["d" + k for k in more], T[ps][:, 0:128], c, [ps, "crow"], A.add)
+        TS(T.ab[:, a], "ab%d" % o, T[ps][:, 0:128], [ps, "nb"], C("nb"), GONE, A.not_equal, A.mult)
+        TT(T.dz[:, a], "dz%d" % o, T[ps][:, 0:128], c, [ps, ck], A.add)
 
-    def firsts(parts):
-        n, o = dims(parts)
-        a, c = 128 * o, 0 if n == 256 else 256
-        return [lambda: SCAN(back(T.pb, a, a + n), keys("pb", parts), back(T.dz, a, a + n), back(T.ab, a, a + n), keys("dz", parts) + keys("ab", parts),
-                             0.0, A.add, A.min),
-                lambda: SCAN(back(T.fs, a, a + n), keys("fs", parts), back(T.wrow, c, c + n), back(T.ab, a, a + n), ["wrow"] + keys("ab", parts),
-                             0.0, A.add, A.min)]
+    def above(o, ok, w, wk, a, n):
+        SCAN(back(o, a, a + n), ok, w, back(T.ab, a, a + n), pt(wk) + ["ab%d" % h for h in range(a // 128, (a + n) // 128)], 0.0, A.add, A.min)
 
-    def symbols(o, bank, cols):
-        return [lambda: SCAN(T.sd[:, 128 * o:128 * o + 128], "sd%d" % o, T.ar[:], T["ps%d" % bank][:, 0:128], ["ar", "ps%d" % bank], 0.0, A.add, A.max),
+    def symbols(o, cols):
+        ps = "ps%d" % (7, 4)[o]
+        return [lambda: SCAN(T.sd[:, 128 * o:128 * o + 128], "sd%d" % o, T.ar[:], T[ps][:, 0:128], ["ar", ps], 0.0, A.add, A.max),
                 lambda: TT(T.LG[:, cols], "LG%d" % o, T.sd[:, 128 * o + 15:128 * o + 128:16], T.lc[:, cols], ["sd%d" % o, "lc"], A.add)]
 
-    def unpack(c, q, qk, k=0):
-        for b in range(4):
-            MM(k + b, 256, c, 128 * b, q, qk)
+    def own_state(r, a, b):
+        for t in range(a, b):
+            MM(t, 256, "qce", 128 * t, "qn%d" % r, ["na%d" % r, "nb%d" % r, "qce%d" % t])
+            ACT(T.D[:, FO + 256 * t:FO + 256 * t + 256], "Fo%d" % t, T["ps%d" % t][:, 0:256], "ps%d" % t, scale=1 / 128)
 
     def weave(main, fill):
-        fill = list(fill)
-        for m in main:
+        for m, fs in zip(main, fill):
             m()
-            if fill:
-                fill.pop(0)()
-        for f in fill:
-            f()
+            for f in fs:
+                f()
 
-    def then(*fs):
-        return lambda: [f() for f in fs]
-
-    def level(o, n, p0, p1, tk):
-        return [lambda: TT(T.yi[:], "yi", T.zf[:, TRP:TRP + 32].indirect(L("lW")), T.val[:], ["trp1", "trp2", "val", "lsB"], A.mult),
+    def level(o, p0, p1, tk):
+        return [lambda: TT(T.yi[:], "yi", T.zf[:, TRP:TRP + 64].indirect(L("lW")), T.val[:], ["trp0", "trp1", "trp2", "val", "lsW"], A.mult),
                 lambda: SCAN(T.Y[:, 0:64], "Y", T.bd[:], T.yi[:], ["bd", "bd0", "yi"], -FAR, A.add, A.max),
-                lambda: SCAN(o[p0:p1, 0:n], tk, T.er[p0:p1, 0:n], T.Y[p0:p1, 7:8 * n:8], ["Y", "Yc", "cap", "er", "er8", "erc"], FAR, A.add, A.min)]
+                lambda: SCAN(o[p0:p1, :], tk, T.er[p0:p1, :], T.Y[p0:p1, 7:592:8], ["Y", "Yc", "cap", "er", "erc"], FAR, A.add, A.min)]
 
     both = (0, 1)
+    emit("Y", lambda: g.sync.dma_start(T.xs[:, 0:512], T.x[:, 0:512]), [], ["xs0"], dma=True)
+    emit("S", lambda: s.dma_start(T.us[:], T.u[:]), [], ["us"], dma=True)
+    emit("Y", lambda: g.sync.dma_start(T.xs[:, 512:1024], T.x[:, 512:1024]), [], ["xs1"], dma=True)
+    emit("Y", lambda: g.sync.dma_start(T.qw[:, 0:512].bitcast(dt.uint8), T.wc[:, 0:2048]), ["xs1", "us"], ["qw"], dma=True)
+    emit("Y", lambda: g.sync.dma_start(T.sqw[:, 0:512], T.ws[:, 0:512]), [], ["sqw"], dma=True)
+
+    FILL(T.one[:], "one", 128.0)
+    FILL(row("w2"), "zr0", 0.0)
+    FILL(T.B[:], ["zer", "B0", "B1"], 0.0)
+    IOTA(row("jj"), "zrA", [[0, 2], [1, 16]], 0)
+    IOTA(row("us"), "zrA", [[0, 2], [int(U), 8], [0, 2]], int(U))
+    IOTA(C("pf"), "pf", [[0, 1]], 0, 1)
+    IOTA(T.vg[:], "vg", [[16, 8], [0, 16]], 0)
+    AFF(T.idn[:], "idn", T.one[:], "one", [[-1, 128]], A.is_equal, 0, 1)
+    IOTA(T.i16[:], "i16", [[0, 10], [1, 16]], 0)
+    IOTA(row("lR"), "zrB", [[32, 2], [0, 16]], 0)
+    IOTA(row("lD"), "zrB", [[0, 2], [32, 2], [0, 8]], 0)
+    IOTA(row("lW"), "zrB", [[0, 2], [1, 2], [2, 8]], 0)
+    IOTA(row("k4"), "zrB", [[2, 2], [0, 8], [1, 2]], 0)
+    IOTA(T.rows[:, 0:8], "rows", [[64, 4], [0, 2]], 0)
+    for k in both:
+        IOTA(T.rows[:, 8 + 8 * k:16 + 8 * k], "rowl", [[16, 2], [1, 2], [0, 2]], 32 * k)
+    for i in range(3):
+        FILL(row("w2", i, 32, 16), "zrV", float(8 >> i), "zr0")
+    FILL(T.cs[:], "cs0", 0.0)
+    turn("jj", "w2", "zcA", ["zrA", "zrV"])
+    SET(T.ce[:, 0:512], "ce0", 512, 0.0)
+    SET(T.ce[:, 512:516], "ce0", 4, 0.0)
+    SET(T.crow[:], "crow0", 256, U)
+    ACT(T.ce[:, 3:512:4], "ce", T.idn[:], ["idn", "ce0"])
+    SET(T.crow[:, 31:128:32], "crow", 4, GONE, "crow0")
+    ACT(C("nb"), "nb", C("us"), "zcA", AF.Identity, bias=-U)
+    SET(T.cg[:, 0:512], "cg0", 512, 0.0)
+    SET(T.cg[:, 512:516], "cg0", 4, 0.0)
+    FILL(T.zf[:], ["zf0", "trp1", "trp2"], 0.0)
+    QT("qu", 0, 128, T.us[:], "us")
+    TS(C("wu"), "wu", C("w2"), "zcA", U / 2, None, A.mult)
+    TS(C("gp"), "gp", C("pf"), ["pf", "zcA"], C("jj"), None, A.subtract)
+    TS(C("q5"), "q5", C("jj"), "zcA", 15.0, HOLD, A.is_lt, A.mult)
+    FILL(T.Y[:, 71:592:8], ["Yc", "cap"], FAR)
+    FILL(T.pb[:, 256:2368:32], ["pfar", "cap0"], FAR)
+    QT("na0", 0, 128, T.xs[:, 0:512], "xs0")
+    for k in both:
+        TS(T.cs[:, 4 * k:512:8], "cs", T.vg[:, 0:64], ["vg", "gp", "wu", "cs0"], C("gp"), C("wu"), A.is_equal, A.mult)
+    TS(T.cs[:, 512:1024:4], "cs", T.vg[:], ["vg", "gp", "zcA", "cs0"], C("gp"), C("w2"), A.is_equal, A.mult)
+    QT("nb0", 0, 128, T.xs[:, 512:1024], "xs1")
+    QT("qcs", 0, 256, T.cs[:], "cs")
     for o in both:
         MM(4 * o, 128, "qu", 0, ("na0", "nb0")[o])
-    for b in range(NCE, 4):
-        QT("qce", 128 * b, 128 * b + 128, T.ce[:, 3 - b:515 - b], "ce")
-    for o in both:
-        TS(T.B[:, 512 * o:512 * o + 512:4], "B%d" % o, T["ps%d" % (4 * o)][:, 0:128], "ps%d" % (4 * o), 0.0, None, A.is_gt)
-    for b in range(NCG):
-        QT("qcg", 128 * b, 128 * b + 128, T.cg[:, 3 - b:515 - b], "cg")
-    for o in both:
-        QT("qb%d" % o, 0, 128, T.B[:, 512 * o:512 * o + 512], "B%d" % o)
-    for bank, c, o in ((5, 0, 0), (6, 0, 1), (7, 128, 0), (1, 128, 1)):
-        MM(bank, 128, "qcs", c, "qb%d" % o)
+    tiles = [lambda b=b: QT("qce", 128 * b, 128 * b + 128, T.ce[:, 3 - b:515 - b], "ce", "qce%d" % b) for b in range(4)]
+    signs(0, 0)
+    TS(T.eq[:], "eq", T.i16[:], ["i16", "zcA"], C("jj"), None, A.is_equal)
+    TS(C("g0"), "g0", C("pf"), "pf", 16.0, 64.0, A.is_lt, A.mult)
+    spread(0)
+    signs(1)
     turn("lR", "k4", "zcB", "zrB")
-    TT(T.ar[:], "ar", T.a1[:], T.a2[:], ["a1", "a2"], A.add)
-    TS(T.lc[:], "lc0", T.rows[:, 64:80], ["rowl", "rowz", "g0", "q5"], C("g0"), C("q5"), A.add, A.subtract)
-    ACT(T.lc[:, 0:16:2], "lc", T.lc[:, 0:16:2], ["lc0", "t0"], AF.Identity, bias=C("t0"))
-    TS(L("lR0"), "lsB", T.rows[:, 8:16], ["rows", "zcB"], C("lR"), None, A.add)
-    TS(L("lD0"), "lsB", T.rows[:, 0:4], ["rows", "zcB"], C("lD"), None, A.add)
-    TS(L("lW"), "lsB", T.zer[:, 0:4], ["zer", "zcB"], C("lW"), None, A.add)
+    tiles[0]()
+    spread(1)
+    ACT(T.a1[:], "a1", T.eq[:, 15:143], "eq", scale=-0.25)
+    ACT(T.a2[:], "a2", T.eq[:, 16:144], "eq", scale=-4 * HOLD)
+    ACT(T.zf[:, E40 + 8:E40 + 9], "e40", C("us"), ["zcA", "zf0"])
+    ACT(T.cc[:, 24:32], "ramp", T.i16[:, 0:8], "i16", scale=2 * GONE)
+    SET(T.er[:], "er0", 74, 0.0)
+    SET(T.bd[:, 0:1], "bd0", 1, 0.0)
+    ACT(T.be[:, 8:9], "be8", C("us"), "zcA", scale=-1.0)
+    ACT(C("pn"), "pn", C("us"), "zcA", AF.Identity, bias=254.0 / FAR, scale=2 / U / FAR)
+    for k in range(4):
+        ACT(T.dT[:, 32 * k:32 * k + 32], "dT", row("us"), "zrA")
+    SET(T.tr2[:, 64:128], "tr2c", 64, 0.0)
+    SET(T.r15[:], "r150", 64, 0.0)
+    SET(T.r15[:, 15:64:16], "r15", 4, HOLD / FAR, "r150")
+    SET(T.wrow[:, 0:256], "wrow", 256, 1.0)
+    AFF(T.prm[:, 0:16], "prm", T.one[:, 0:16], "one", [[-1, 16]], A.is_equal, -112, 1)
+    AFF(T.prm[:, 16:32], "prm", T.one[:, 0:16], "one", [[-1, 16]], A.is_equal, 0, 1)
+    AFF(T.prm[:, 32:128], "prm", T.one[:, 0:96], "one", [[-16, 3], [0, 2], [-1, 16]], A.is_equal, -16, 1)
+    send_codes(0, 0, 256, ["na0", "nb0"], 2)
+    IOTA(T.pl0[:], "pl00", [[1, 256]], 0)
+    IOTA(T.win[:], "win", [[0, 256]], 0)
+    IOTA(T.D[:, 0:512], "Dp", [[0, 512]], 0)
+    IOTA(T.rows[:, 40:56], "rowq", [[16, 8], [128, 2]], 0)
+    IOTA(T.pl1[:], "pl10", [[16, 8], [128, 2], [1, 16]], 0)
+    IOTA(T.rows[:, 24:40], "rows2", [[128, 2], [2, 8]], 0)
+    IOTA(row("lp"), "zrD", [[0, 2], [1, 2], [16, 8]], 0)
+    tiles[1]()
+    rows_V(0, T.crow[:, 0:128])
+    SCAN(T.ar[:], "ar", T.a1[:], T.a2[:], ["a1", "a2"], 0.0, A.mult, A.add)
+    TS(L("lR0"), "lsB", T.rows[:, 0:8], ["rows", "zcB"], C("lR"), None, A.add)
+    TS(L("lD0"), "lsB", T.i16[:, 0:4], ["i16", "zcB"], 64.0, C("lD"), A.mult, A.add)
+    TS(T.lc[:], "lc", T.rows[:, 8:24], ["rowl", "g0", "q5"], C("g0"), C("q5"), A.add, A.subtract)
+    ACT(C("kb"), "kb", C("k4"), "zcB", scale=2 * GONE)
+    ACT(C("ku"), "ku", C("k4"), ["zcA", "zcB"], AF.Identity, bias=C("us"))
     for k in both:
-        ACT(T.tie[:, 32 * k:32 * k + 32], "tie", T.zer[:, 0:32], ["zer", "zcB"], AF.Identity, bias=C("k4"))
-    ACT(T.tie[:, 32:64], "tie", T.tie[:, 32:64], "tie", AF.Identity, bias=DK)
-    ACT(T.er[64:128, 10:11], "erc", C("k4", 64), ["zcB", "er0"])
-    ACT(T.er[64:128, 42:43], "erc", T.zer[64:128, 0:1], ["zer", "er0"], AF.Identity, bias=DK)
-    for o in both:
-        rows_V(o, T.crow[:, 128 * o:128 * o + 128], ["c%d" % o])
+        ACT(T.zf[0:32, TRP + 32 * k:TRP + 32 * k + 32], "trp0", row("k4", p=32), ["zrB", "zf0"], AF.Identity, bias=8 * GONE * k, scale=2 * GONE)
+    for o, a, ok in ((T.zf, 0, "e40"), (T.er, 32, "erc")):
+        SET(o[a:a + 32, 42:43], ok, 1, 8 * GONE, ["zf0", "er0"], a, a + 32)
+        ACT(o[a:a + 32, 10:11], ok, C("kb", a, a + 32), ["kb", "zf0", "er0"])
+    rows_V(1, T.crow[:, 0:128])
     RED(T.ab[:, 256:257], "abk", T.ab[:, 0:128], "ab0", A.min)
+    s0 = symbols(0, slice(0, 8))
+    s0[0]()
+
+    def later():
+        SET(T.er[64:128, 42:43], "erc", 1, 4.0, "er0", 64)
+        SET(T.tie[:, 0:32], "tie0", 32, C("ku"), "ku")
+        ACT(T.er[64:128, 10:11], "erc", C("ku", 64), ["ku", "er0"])
+        for k, (sc, bi) in enumerate(((288.0, -127.5), (272.0, -127.5), (272.0, 0.5))):
+            ACT(T.cc[:, 8 * k:8 * k + 8], "cc", T.i16[:, 0:8], "i16", AF.Identity, bias=bi, scale=sc)
+        ACT(T.tie[:, 32:64], "tie", T.tie[:, 0:32], "tie0", AF.Identity, bias=4.0)
+        ACT(C("jq"), "jq", C("jj"), "zcA", AF.Identity, bias=HOLD)
+        ACT(C("q6"), "q6", C("q5"), "q5", AF.Identity, bias=HOLD, scale=-1.0)
+        ACT(T.mk[:], "mk", T.eq[:], "eq", AF.Identity, bias=1.0, scale=-1.0)
+        SET(T.pen[:], "pen", 2, 127.5)
+        ACT(C("jr"), "jr", C("jj"), "zcA", AF.Identity, bias=120.0)
+        for y in both:
+            ACT(T.jb[:, 2 * y:2 * y + 1], "jb", C("jj"), "zcA", AF.Identity, bias=16.0 * y)
+        ACT(T.pc[:, 0:16], "pc", T.i16[:, 0:16], ["i16", "jq"], AF.Identity, bias=C("jq"), scale=16.0)
 
     for r in range(NR):
         last = r == NR - 1
-        parts = both if r == 0 else (1,)
-        first = firsts(parts)
-        p0, n = (128, 64) if r else (0, 128)
-        for o in both:
-            a = p0 + n * o
-            SCAN(back(T.pb, a, a + n), ["pb%d" % (o | min(r, 1)), "pc%d" % o], back(T.dz, a, a + n), back(T.ab, a, a + n), ["dc%d" % o, "ac%d" % o], 0.0, A.add, A.min)
+        p0, n = (128, 128) if r else (0, 256)
+        sy = symbols(1, slice(1, 16, 2) if r else slice(8, 16))
+        lR, lD = L("lR%d" % min(r, 1)), L("lD%d" % min(r, 1))
+        pb, pk, st = (T.pb, ["pbc"], 32) if r == 0 else (T.pm, ["pm"], 16)
+        ends = pb[:, 0:8 * st:st]
+        if r:
+            sy[0]()
+        above(T.pb, ["pb1", "pbc"] + ["pb0"] * (r == 0), back(T.dz, p0, p0 + n), ["dz0", "dz1"], p0, n)
         RED(C("mn"), "mn", T.ab[:, 128:257], ["ab1", "abk"], A.min)
-        sy = [symbols(o, (7, 1)[o], slice(8 * o, 8 * o + 8)) for o in both] if r == 0 else [symbols(1, 7, slice(1, 16, 2))]
         for o, ok in ((T.pm[:, 144:145] if r else T.pb[:, 288:289], "cap0"), (T.Y[:, 79:80], "cap")):
             ACT(o, ok, C("mn"), "mn", AF.Relu, bias=FAR, scale=-FAR / GONE)
-        lR, lD = LISTS["lR%d" % min(r, 1)][0], LISTS["lD%d" % min(r, 1)][0]
-        pb, pk, st = (T.pb, ["pc0", "pc1"], 32) if r == 0 else (T.pm, ["pm"], 16)
-        ends = pb[:, 0:8 * st:st]
-        for o in both:
-            if r == 0:
-                CP(T.R[:, 64 * o:64 * o + 64], "R%d" % o, T.pb[:, 128 * o:128 * o + 128].indirect(T.ls[:, lR:lR + 4]), ["pc%d" % o, "lsB"])
-                sy[o][0]()
-            else:
-                TT(T.R[:, 64 * o:64 * o + 64], "R%d" % o, T.pb[:, 128 + 64 * o:192 + 64 * o].indirect(T.ls[:, lR:lR + 4]), T.pkr[:, 64 * o:64 * o + 64],
-                   ["pc%d" % o, "pkr", "lsD"], A.max)
-                if o == 0:
-                    TT(ends, "pm", T.pb[:, 128:256:16], T.e1[:, 0:128:16], ["e1", "pc0", "pc1"], A.max)
-        unpack("qce", "qn%d" % r, ["na%d" % r, "nb%d" % r])
-        for b in range(4):
-            ACT(T.D[:, FO + 256 * b:FO + 256 * b + 256], "Fo%d" % b, T["ps%d" % b][:, 0:256], "ps%d" % b, scale=1 / 128)
-
-        def turn_al(o):
-            TR(T.al[:, 64 * o:64 * o + 64], "al%d" % o, T.R[:, 64 * o:64 * o + 64], "R%d" % o)
-
-        def above(o):
-            a, al, ik = slice(32 * o, 32 * o + 32), T.al[:, 64 * o:64 * o + 64:2], ["al%d" % o, "lsB", "lsD"]
-            TT(T.val[:, a], "val", pb[:, n * o:n * o + n].indirect(T.ls[:, lD:lD + 2]), al, pk + ik, A.is_ge)
-            TT(T.dif[:, a], "dif%d" % o, T.pr[:, n * o:n * o + n].indirect(T.ls[:, lD:lD + 2]), al, ["pr"] + ik, A.subtract)
-
-        def steps(o):
-            a = 32 * o
-            TT(T.bd[:, a + 1:a + 32], "bd", T.dif[:, a:a + 31], T.dif[:, a + 1:a + 32], "dif%d" % o, A.subtract)
-
-        turn_al(0)
-        TT(T.pr[:, 0:8 * st:st], "pr", ends, T.cc[:, 48:56], pk + ["ramp"], A.add)
-        SCAN(T.rep[0:32, :], "rep0", pb[0:32, 0:41 * st:st], T.zf[0:32, E40:E40 + 41], pk + ["cap0", "pfar", "e40"], FAR, A.min, A.add)
-        turn_al(1)
-        above(0)
-        TR(T.zf[32:64, TRP:TRP + 32], "trp1", T.rep[0:32, 9:41], "rep0")
-        above(1)
-        TT(T.be[:], "be", ends, T.al[:, 14:128:16], pk + ["al0", "al1"], A.subtract)
-        steps(0)
+        if r == 0:
+            CP(T.R[:], "R", T.pb[:, 0:256].indirect(lR), ["pbc", "lsB"])
+            own_state(0, 0, 2)
+            later()
+            ACT(T.cg[:, 3:512:4], "cg", T.prm[:], ["prm", "cg0"])
+            sy[0]()
+            s0[1]()
+        else:
+            TT(T.R[:], "R", T.pb[:, 128:256].indirect(lR), T.pkr[:], ["pbc", "pkr", "lsD"], A.max)
+            TT(ends, "pm", T.pb[:, 128:256:16], T.e1[:, 0:128:16], ["e1", "pbc"], A.max)
+            own_state(r, FE, 4)
+            sy[1]()
+        zero = [lambda: SCAN(T.rep[0:32, :], "rep0", pb[0:32, 0:74 * st:st], T.zf[0:32, E40:E40 + 74], pk + ["cap0", "pfar", "e40"], FAR, A.min, A.add),
+                lambda: TR(T.zf[32:64, TRP:TRP + 64], "trp1", T.rep[0:32, 10:74], "rep0")]
+        if r == 0:
+            zero[0]()
+            TS(L("lW"), "lsW", T.i16[:, 0:4], ["i16", "zcB"], 16.0, C("lW"), A.mult, A.add)
+        TR(T.al[:], "al", T.R[:], "R")
+        if r:
+            zero[0]()
+        TT(T.pr[:], "pr", ends, T.cc[:, 24:32], pk + ["ramp"], A.subtract)
+        if r == 0:
+            zero[1]()
+            sy[1]()
+        TT(T.val[:], "val", pb[:, 0:n].indirect(lD), T.al[:, 0:128:2], pk + ["al", "lsB", "lsD"], A.is_ge)
+        if r:
+            zero[1]()
+        TT(T.bd[:, 1:64], "bd", T.al[:, 2:128:2], T.al[:, 0:126:2], "al", A.subtract)
+        TT(T.be[:, 0:8], "be", T.pr[:], T.al[:, 14:128:16], ["pr", "al"], A.subtract)
+        ACT(T.dr[:], "dr", T.dT[:].indirect(T.LG[:]), ["dT", "LG0", "LG1"])
         lf = 32 * r
-        flags = [lambda: TS(T.rp2[:], "rp2", T.zer[:, 0:64], ["zer", "pn", "cap"], C("pn"), T.Y[:, 79:80], A.add, A.mult),
+        flags = [lambda: TS(T.rp2[:], "rp2", T.r15[:], ["r15", "pn", "cap"], C("pn"), T.Y[:, 79:80], A.add, A.mult),
                  lambda: TR(T.tr2[:, 0:64], "tr2", T.rp2[:], "rp2"),
-                 lambda: [ACT(T.dr[:], "dr", T.dT[:].indirect(T.LG[:]), ["dT", "LG0", "LG1"]),
+                 lambda: [SET(T.dr[:, 0:256:32], "dr", 8, -DK, "dr"),
                           ACT(T.fr[:], "fr", T.tr2[:].indirect(T.LG[:]), ["tr2", "tr2c", "LG0", "LG1"])]]
         mate = [lambda o=o: SCAN(T.fd[:, 128 * o:128 * o + 128], "fd", T.ar[:], T.fr[:, 128 * o:128 * o + 128], ["ar", "fr"], 0.0, A.add, A.max) for o in both]
-        pc = T.pc[:, 16 * min(r, 1):16 * min(r, 1) + 16]
-        mate.append(lambda: TT(T.fb[:], "fb", T.fd[:, 15:256:16], pc, ["fd", "pc"], A.max))
-        if r == 0:
-            mate.append(lambda: TS(T.lf[:, lf:lf + 16], "lf%d" % r, T.fb[:], ["fb", "q5"], C("q5"), None, A.subtract))
-        else:
-            mate.append(lambda: [TS(T.lf[:, lf + 8 * y:lf + 8 * y + 8], "lf%d" % r, T.fb[:, y:16:2], ["fb", "q5"], C("q5"), None, A.subtract) for y in both])
+        down = lambda: TT(T.er[:, 1:9], "er", T.be[:, 0:8], T.be[:, 1:9], ["be", "be8", "er0"], A.subtract)
         ties = lambda: TS(T.rq[0:64, 10:74], "rq1", T.tie[0:64, :], ["tie", "rep0", "rep1"], T.rep[0:64, 9:10], None, A.add)
+        least = [lambda: TT(T.k0[:], "k0", T.Y[:, 7:64:8], T.be[:, 0:8], ["Y", "be"], A.add),
+                 lambda: TS(T.k1[:], "k1", T.k0[:], "k0", 256.0, DROP, A.mult, A.min)]
+        depth = lambda: above(T.fs, ["fs1"] + ["fs0"] * (r == 0), back(T.wrow, 256 - p0 - n + 256 * (r > 0), 256 + 128 * (r > 0)), "wrow", p0, n)
 
         if r == 0:
-            late = [lambda b=b: QT("qcg", 128 * b, 128 * b + 128, T.cg[:, 3 - b:515 - b], "cg") for b in range(NCG, 4)]
-            fill = [flags[0], then(sy[0][1], sy[1][1], flags[1], flags[2]), then(late[0], lambda: TR(T.tf[:, 64:128], "tfc", T.tie[:], "tie")),
-                    then(first[1], lambda: TS(T.cc[:, 24:48], "cc", T.cc[:, 0:24], "cc0", -127.5, None, A.add)),
-                    then(lambda: TT(T.c1[:], "c1", T.fs[:, 0:256:32], T.cc[:, 24:32], ["fs0", "fs1", "cc"], A.add), late[1]),
-                    then(ties, late[2]), then()]
+            late = [lambda b=b: QT("qcg", 128 * b, 128 * b + 128, T.cg[:, 3 - b:515 - b], "cg", "qcg%d" % b) for b in range(4)]
+            fill = [[down, flags[0], tiles[2]], [depth, tiles[3]], flags[1:] + [lambda: own_state(0, 2, 4), late[0]], [late[3]],
+                    [late[1], lambda: TT(T.c1[:], "c1", T.fs[:, 0:256:32], T.cc[:, 0:8], ["fs0", "fs1", "cc"], A.add), ties],
+                    [late[2], lambda: TR(T.tf[:, 64:128], "tfc", T.tie[:], "tie")]]
         else:
-            fill = [then(flags[0]), then(sy[0][0], flags[1]), then(sy[0][1], flags[2], first[1]),
-                    then(lambda: TT(T.ck[:], "ck", T.fs[:, 0:256:16], T.cc[:, 32:48], ["fs0", "fs1", "cc"], A.add)),
-                    then(lambda: TT(T.c1[:], "c1", T.ck[:, 0:8], T.ck[:, 8:16], "ck", A.min), ties), then(), then()]
-        fill[0] = then(lambda: steps(1), lambda: TT(T.er[:, 1:8], "er", T.be[:, 0:7], T.be[:, 1:8], ["be", "er0"], A.subtract),
-                       lambda: TS(T.er[:, 8:9], "er8", T.be[:, 7:8], ["be", "zcA", "er0"], C("us"), None, A.add), fill[0])
-        fill[6] = then(lambda: TT(T.k0[:], "k0", T.Y[:, 7:64:8], T.be[:], ["Y", "be"], A.add), fill[6], mate[0])
-        weave(level(T.rep, 41, 32, 64, "rep1") + [lambda: [TR(T.zf[p:p + 32, TRP:TRP + 32], "trp2", T.rep[32:64, 9:41], "rep1") for p in (64, 96)]]
-              + level(T.rq, 74, 64, 128, "rq2") + [lambda: TR(T.tf[:, 0:64], "tf", T.rq[:, 10:74], ["rq1", "rq2"])],
-              fill + [then(lambda: TS(T.k1[:], "k1", T.k0[:], "k0", 256.0, DROP, A.mult, A.min), mate[1])])
-        if r == 0:
-            ACT(T.pc[:, 0:16], "pc", T.rows[:, 80:96], ["rowp", "jq"], AF.Identity, bias=C("jq"))
-            ACT(T.pl0[:], "pl0", T.pl0[:], ["pl00", "q6"], AF.Identity, bias=C("q6"))
-        unpack("qcg", "qa%d" % r, None)
-        unpack("qce", "qa%d" % r, None, 4)
+            fill = [[down, flags[0]], [depth], flags[1:],
+                    [lambda: TT(T.ck[:], "ck", T.fs[:, 0:256:16], T.cc[:, 8:24], ["fs0", "fs1", "cc"], A.add)],
+                    [lambda: TT(T.c1[:], "c1", T.ck[:, 0:8], T.ck[:, 8:16], "ck", A.min), ties], []]
+        weave(level(T.rep, 32, 64, "rep1") + [lambda: [TR(T.zf[p:p + 32, TRP:TRP + 64], "trp2", T.rep[32:64, 10:74], "rep1") for p in (64, 96)]]
+              + level(T.rq, 64, 128, "rq2") + [lambda: TR(T.tf[:, 0:64], "tf", T.rq[:, 10:74], ["rq1", "rq2"])],
+              fill + [least[0:1], least[1:] + mate])
+        for c, k in (("qcg", 0), ("qce", 4)):
+            for b in range(4):
+                MM(k + b, 256, c, 128 * b, "qa%d" % r, ["qa%d" % r, "%s%d" % (c, b)])
 
         def copy_G(t):
             ACT(T.D[:, GG + 272 * t:GG + 272 * t + 256], "G%d" % t, T["ps%d" % t][:, 0:256], "ps%d" % t)
 
         for t in range(GE[r]):
             copy_G(t)
-        TT(T.wr[:, 0:128], "wr0", T.tf[:].indirect(T.LG[:, 0:8]), T.hrow[:], ["tf", "tfc", "LG0", "LG1", "hrow"], A.add)
+        CP(T.wr[:, 0:128], "wr0", T.tf[:].indirect(T.LG[:, 0:8]), ["tf", "tfc", "LG0", "LG1"])
         ACT(T.wr[:, 128:256], "wr1", T.tf[:].indirect(T.LG[:, 8:16]), ["tf", "tfc", "LG0", "LG1"])
         for t in range(GE[r], 4):
             copy_G(t)
         TT(T.k2[:], "k2", T.k1[:], T.c1[:], ["k1", "c1"], A.add)
-        mate[2]()
+        if r == 0:
+            TT(T.lf[:, lf:lf + 16], "lf%d" % r, T.fd[:, 15:256:16], T.pc[:, 0:16], ["fd", "pc"], A.max)
+        else:
+            for y in both:
+                TT(T.lf[:, lf + 8 * y:lf + 8 * y + 8], "lf%d" % r, T.fd[:, 15 + 16 * y:256:32], T.pc[:, 16 + y:32:2], ["fd", "pc"], A.max)
         for o in both:
             a = slice(128 * o, 128 * o + 128)
-            SCAN(T.key[:, a], "key%d" % o, T.wr[:, a], T.dr[:, a], ["wr%d" % o, "dr"], -1.0, A.max, A.add)
+            SCAN(T.k16[:, a], "key%d" % o, T.dr[:, a], T.wr[:, a], ["wr%d" % o, "dr"], 0.0, A.add, A.max)
         RED(C("km"), "km", T.k2[:], "k2", A.min)
 
-        def own(o, ok, a, h):
-            SCAN(back(o, a, a + 128), ok, back(T.mk, 0, 128), back(T.key, 128 * h, 128 * h + 128), ["mk", "key%d" % h], 0.0, A.mult, A.max)
+        def own(o, ok, c, a, b):
+            SCAN(back(o, c, c + b - a), ok, back(T.mk, 0, b - a), back(T.k16, a, b), ["mk"] + ["key%d" % h for h in range(a // 128, (b - 1) // 128 + 1)],
+                 0.0, A.mult, A.max)
 
-        own(T.od, "od0", 0, 0)
-        own(T.od, "od1", 128, 1)
-        own(T.oh, "oh", 0, 1)
-        CP(T.k16[:, 0:128], "k16", T.key[:, 0:128], "key0")
+        def again(a, b):
+            SCAN(T.k16[:, 256 + a:256 + b], "key%d" % (2 + (a > 0)), T.dr[:, a:b], T.wr[:, a:b], ["wr0", "wr1", "dr"], 0.0, A.add, A.max)
+
+        own(T.od, "od0", 0, 0, 16 * NS)
+        again(0, 128)
+        own(T.oh, "oh", 0, 16 * NS, 256)
+        own(T.od, "od1", 16 * NS, 16 * NS, 256)
+        again(128, 224)
         TS(C("rn"), "rn", C("km"), "km", ROUND256, -ROUND256, A.add, A.add)
-        CP(T.k16[:, 128:256], "k16", T.key[:, 128:256], "key1")
-        TT(T.ol[:], "ol", T.od[:, 128:256:16], T.oh[:, 0:128:16], ["od1", "oh"], A.subtract)
-        mate[3]()
+        TT(T.ol[:, 0:NV], "ol", T.od[:, 16 * NS:256:16], T.oh[:, 0:16 * NV:16], ["od0", "od1", "oh"], A.subtract)
         TS(T.lf[:, lf + 16:lf + 18], "lf%d" % r, T.pen[:], ["pen", "km", "rn"], C("km"), C("rn"), A.add, A.subtract)
         send(T.fa[:, lf:lf + 18], T.lf[:, lf:lf + 18], "f", r)
-        for b in range(8):
-            ACT(T.js[:, 256 * b:256 * b + 256], "acc", T.key[:], ["key0", "key1", "od0"], AF.Sign, bias=T.od[:, 16 * b:16 * b + 1], scale=-1.0,
-                accum_out=T.acc[:, b:b + 1])
-        for b in range(8):
-            TS(T.jv[:, 256 * b:256 * b + 256], "jv%d" % b, T.k16[:], ["k16", "oh", "ol"], T.oh[:, 16 * b:16 * b + 1], T.ol[:, b:b + 1], A.subtract, A.is_lt)
-        for b in range(8):
-            SCAN(T.pl[:, 2040 + b::-16], "pl", T.jv[:, 256 * b:256 * b + 128], T.jv[:, 256 * b + 128:256 * b + 256], ["jv%d" % b, "xb"], T.xb[:, 0:1], A.add, A.add)
-        TS(T.pl[:, 0:8], "pl", T.acc[:, 0:8], "acc", 0.5, 127.5, A.mult, A.add)
+        for b in range(NS):
+            a = 32 * (b // 2) + 16 + 16 * (b % 2)
+            ACT(T.js[:, 256 * b:256 * b + 240], "acc", T.k16[:, a:a + 240], ["key0", "key1", "od0"] + ["key2"] * (b > 0), AF.Sign,
+                bias=T.od[:, 16 * b:16 * b + 1], scale=-1.0, accum_out=T.acc[:, b:b + 1])
+        if r == 0:
+            ACT(T.pl0[:], "pl0", T.pl0[:], ["pl00", "q6"], AF.Identity, bias=C("q6"))
+        for b in range(NV):
+            a = 32 * ((NS + b) // 2) + 32
+            TS(T.jv[:, 256 * b:256 * b + 224], "jv%d" % b, T.k16[:, a:a + 224], ["key0", "key1", "key2", "key3", "oh", "ol"], T.oh[:, 16 * b:16 * b + 1], T.ol[:, b:b + 1],
+               A.subtract, A.is_lt)
+        for b in range(NV):
+            y = (NS + b) % 2
+            SCAN(T.pl[:, 1776 + NS + b::-16], "pl", T.jv[:, 256 * b:256 * b + 112], T.jv[:, 256 * b + 112:256 * b + 224], ["jv%d" % b, "jb"], T.jb[:, 2 * y:2 * y + 1],
+                 A.add, A.add)
+        TS(T.pl[:, 0:NS], "pl", T.acc[:, 0:NS], ["acc", "jr"], 0.5, C("jr"), A.mult, A.add)
         for t in range(4):
             a = GG + 272 * t
             ACT(T.D[:, a + 256:a + 272], "Gf%d" % t, T.D[:, a:a + 256].indirect(T.fa[:, lf + 16:lf + 17]), ["G%d" % t, "fa%d" % r])
         for t in range(4):
             a = GG + 272 * t
-            ACT(T.gz[:, 256 * t:256 * t + 256], "gz%d" % t, T.D[:, a:a + 272].indirect(T.fa[:, lf:lf + 16]), ["G%d" % t, "Gf%d" % t, "fa%d" % r])
+            ACT(T.gz[:, 256 * t:256 * t + 256], "gz%d" % t, T.D[:, a - 512:a + 272].indirect(T.fa[:, lf:lf + 16]),
+                ["Dp", "fa%d" % r] + [k + str(j) for k in ("G", "Gf") for j in range(t + 1)])
 
         def pairs(t):
             TT(T.D[:, HS + 256 * t:HS + 256 * t + 256], "H%d" % t, T["ps%d" % (4 + t)][:, 0:256], T.gz[:, 256 * t:256 * t + 256], ["ps%d" % (4 + t), "gz%d" % t], A.add)
 
         pl = ("pl0", "pl1")[min(r, 1)]
         emit("V", lambda: v.tensor_copy(T.win[:].indirect(T.pl[:, 0:16]), T[pl][:]), ["pl", pl, "win"], ["win"])
-        if r:
-            pairs(0)
         for h in range(8):
             SCAN(T.dl[:, 256 * r + h:256 * r + 256:8], "ll%d" % r, T.ar[:, 0:32], T.win[:, h:256:8], ["ar", "win"], 0.0, A.add, A.max)
         la, laid, kept = T.la[:, 16 * r:16 * r + 8], T.dl[:, 256 * r + 120:256 * r + 128], T.dl[:, 256 * r + 248:256 * r + 256]
@@ -552,20 +534,18 @@ def rank_program(g, core, T, topo):
             a = FO + 256 * t
             (CP if t < XV else ACT)(T.X[:, t:512:4], "X0" + "VS"[t >= XV], T.D[:, a - 512:a + 256].indirect(kept), before + ["ll%d" % r])
 
-        if r == 0:
-            pairs(0)
+        pairs(0)
         pairs(1)
         for t in range(4):
             stay(t)
         pairs(2)
         pairs(3)
         if r == 0:
+            emit("Y", lambda: g.sync.dma_start(T.vs[:], T.v[:]), ["la0"], ["vs"], dma=True)
             IOTA(T.colw[:], "colw", [[16, 6], [32, 8], [1, 16]], -64)
         QT("na%d" % (r + 1), 0, 128, T.X[:, 0:512], ["X0V", "X0S"])
-        if last:
-            MM(4, 128, "qv", 0, "na3")
-        else:
-            scores(r + 1, 0)
+        MM(4, 128, "qv" if last else "qu", 0, "na%d" % (r + 1))
+        if not last:
             send_codes(r + 1, 0, 128, ["na%d" % (r + 1)], 2)
         z = "qz%d" % r
         for t in range(4):
@@ -578,75 +558,72 @@ def rank_program(g, core, T, topo):
         if last:
             CP(T.ysb[:, :, 0:16], "ysb", T.ps4[:, 0:128], "ps4")
         else:
-            TS(T.B[:, 0:512:4], "B0", T.ps4[:, 0:128], "ps4", 0.0, None, A.is_gt)
+            signs(0)
         QT(z, 0, 128, T.Z[:], ["ZV", "ZS"])
         for b in range(4):
             MM(b, 128, "qw", 128 * b, z, None, True, False)
-            MM(b, 128, "qce", 128 * b, z, None, False, True)
+            MM(b, 128, "qce", 128 * b, z, [z, "qce%d" % b], False, True)
         if last:
             for k, li in enumerate((laid, kept)):
                 ACT(T.ow[:, 128 * k:128 * k + 128], "ow", T.colw[:].indirect(li), ["colw", "ll%d" % r])
             ACT(T.opw[:], "opw", T.ow[:].indirect(L("lP")), ["ow", "lsE"])
             emit("Y", lambda: g.sync.dma_start(T.op[:], T.opw[0:128:16, :]), ["opw"], ["op"], dma=True)
         else:
-            QT("qb0", 0, 128, T.B[:, 0:512], "B0")
-            for bank, c in ((5, 0), (7, 128)):
-                MM(bank, 128, "qcs", c, "qb0")
+            spread(0)
             if r == 0:
                 FILL(T.r16[:], "r160", 1.0)
+                FILL(T.wrow[:, 256:384], "wrow1", 1.0)
+                FILL(T.pm[:, 0:128], "pm", 0.0)
+                FILL(T.e1[:], "e1", 0.0)
                 TS(L("lR1"), "lsD", L("lR0"), "lsB", 0.5, None, A.mult)
                 TS(L("lD1"), "lsD", L("lD0"), "lsB", 0.5, None, A.mult)
                 FILL(T.cra[:], "cra0", U)
-                FILL(T.pm[:, 128:656:16], ["pfar", "cap0"], FAR)
+                FILL(T.pm[:, 128:1184:16], ["pfar", "cap0"], FAR)
                 FILL(T.r16[:, 0:128:16], "r16", 0.0, "r160")
-                FILL(T.crow[:, 271:384:16], "crow", U + GONE, "crow0")
+                FILL(T.crow[:, 143:256:16], "crow", 2 * GONE, "crow0")
+                FILL(T.wrow[:, 271:384:16], "wrow", 4096.0, "wrow1")
                 FILL(T.cra[:, 15:128:16], "cra", 16 * GONE, "cra0")
-                ACT(T.pc[:, 16:32], "pc", T.rows[:, 96:112], ["rowq", "jq"], AF.Identity, bias=C("jq"))
+                ACT(T.pc[:, 16:32], "pc", T.rows[:, 40:56], ["rowq", "jq"], AF.Identity, bias=C("jq"))
                 ACT(T.pl1[:], "pl1", T.pl1[:], ["pl10", "q6"], AF.Identity, bias=C("q6"))
             else:
                 turn("lp", "lp", "zcD", "zrD")
                 QT("qv", 0, 128, T.vs[:], "vs")
-                TS(L("lF"), "lsE", T.rows[:, 96:112], ["rowq", "zcA"], C("jj"), None, A.add)
-                TS(L("lP"), "lsE", T.rows[:, 16:32], ["rows2", "zcD"], C("lp"), None, A.add)
+                TS(L("lF"), "lsE", T.rows[:, 40:56], ["rowq", "zcA"], C("jj"), None, A.add)
+                TS(L("lP"), "lsE", T.rows[:, 24:40], ["rows2", "zcD"], C("lp"), None, A.add)
         for b in range(4):
             o, i = T.X[:, 512 + b:1024:4], T["ps%d" % b][:, 0:128]
             if b >= HV:
                 TS(o, "X1V", i, "ps%d" % b, 0.0078125, None, A.mult)
             else:
                 ACT(o, "X1S", i, "ps%d" % b, scale=0.0078125)
-        if not last:
-            rows_V(0, T.crow[:, 256:384])
         QT("nb%d" % (r + 1), 0, 128, T.X[:, 512:1024], ["X1V", "X1S"])
         if not last:
-            scores(r + 1, 1)
+            MM(4, 128, "qu", 0, "nb%d" % (r + 1))
             send_codes(r + 1, 128, 256, ["nb%d" % (r + 1)], 4)
-            sy, first = symbols(0, 7, slice(0, 16, 2)), firsts((0,))
+            sy = symbols(0, slice(0, 16, 2))
+            rows_V(0, T.crow[:, 128:256])
             SCAN(T.pt[:], "pt", T.r16[:], T.ps5[:, 0:128], ["r16", "ps5"], 0.0, A.mult, A.add)
-            first[0]()
-            sy[0]()
-            first[1]()
+            above(T.pb, "pb0", back(T.dz, 0, 128), "dz0", 0, 128)
             ACT(T.pt8[:, 0:8], "pt8", T.pt[:, 15:128:16], "pt", AF.Identity, bias=16 * U)
             ACT(T.pt8[:, 8:16], "pt9", T.pt[:, 15:128:16], "pt", AF.Identity, bias=16 * U - 8 * GONE)
-            sy[1]()
-            TS(T.B[:, 512:1024:4], "B1", T.ps4[:, 0:128], "ps4", 0.0, None, A.is_gt)
-            TT(T.e1[:, 0:128:16], "e1", T.pb[:, 0:128:16], T.pt8[:, 0:8], ["pb0", "pt8"], A.min)
+            own_state(r + 1, 0, FE)
+            signs(1)
             TS(T.pt8[:, 16:24], "pta", T.pb[:, 0:128:16], "pb0", DROP, 8 * GONE + U, A.is_ge, A.mult)
-            QT("qb1", 0, 128, T.B[:, 512:1024], "B1")
-            for bank, c in ((6, 0), (7, 128)):
-                MM(bank, 128, "qcs", c, "qb1")
+            spread(1)
+            TT(T.e1[:, 0:128:16], "e1", T.pb[:, 0:128:16], T.pt8[:, 0:8], ["pb0", "pt8"], A.min)
+            sy[0]()
             TT(T.cra[:, 0:128:16], "cra", T.pt8[:, 8:16], T.pt8[:, 16:24], ["pt9", "pta"], A.add)
             RED(T.ab[:, 256:257], "abk", T.pt8[:, 16:24], "pta", A.min)
             ACT(T.pkr[:], "pkr", T.e1[:].indirect(L("lR1")), ["e1", "lsD"])
-            for o in both:
-                a = slice(64 * o, 64 * o + 64)
-                TS(T.ab[:, 128 + 64 * o:192 + 64 * o], ["ab1", "ac%d" % o], T.ps6[:, a], ["ps6", "nb"], C("nb"), GONE, A.not_equal, A.mult)
-                TT(T.dz[:, 128 + 64 * o:192 + 64 * o], ["dz1", "dc%d" % o], T.ps6[:, a], T.cra[:, a], ["ps6", "cra"], A.add)
+            above(T.fs, "fs0", back(T.wrow, 256, 384), "wrow", 0, 128)
+            sy[1]()
+            rows_V(1, T.cra[:], "cra")
     MM(5, 128, "qv", 0, "nb3")
     (oc, osc), (ic, isc) = K("qp", 0, 256), K("qn3", 0, 256)
     emit("V", lambda: v.tensor_copy(oc.bitcast(dt.uint32), ic.bitcast(dt.uint32).indirect(L("lF"))), ["na3", "nb3", "lsE"], ["qp"])
     emit("S", lambda: s.activation(osc, isc.indirect(L("lF")), AF.Copy), ["na3", "nb3", "lsE"], ["sqp"])
-    emit("Y", lambda: g.sync.dma_start(T.oc[:, 0:1024], oc.bitcast(dt.uint8)), ["qp"], ["oc"], dma=True)
     ACT(T.ysb[:, :, 16:32], "ysb1", T.ps5[:, 0:128], "ps5")
+    emit("Y", lambda: g.sync.dma_start(T.oc[:, 0:1024], oc.bitcast(dt.uint8)), ["qp"], ["oc"], dma=True)
     emit("S", lambda: s.dma_start(T.y[:], T.ysb[:]), ["ysb", "ysb1"], ["y"], dma=True)
     for k in range(4):
         emit("Y" if k < 3 else "S", lambda: (g.sync if k < 3 else s).dma_start(T.osc[4 * k:4 * k + 4, 0:256], T.sqp[32 * k:32 * k + 4, 0:256]),

@@ -1,23 +1,24 @@
 from concourse.mybir import dt, AluOpType as A, AxisListType, ActivationFunctionType as AF
 
 NR = 3
-U = 8.0
-GONE = float(1 << 23)
-DROP = float(1 << 22)
+GONE = 2048.0
+UP = 2048.0
+RISE = 8192.0
+FAR = float(1 << 30)
+PL = 1 / 4096
+ROUND = 1.5 * float(1 << 20)
 DK = 16384.0
 HOLD = 512.0
-FAR = float(1 << 30)
-ROUND256 = 1.5 * float(1 << 31)
 HV = 3
-XV, ZV = 1, 2
-GE = (0, 2, 2)
+XV, ZV = 2, 2
+GE = 2
 FE = 1
-NV = 9
+NV = 10
 NS = 16 - NV
-COLS = ["jj", "us", "w2", "lR", "lD", "lW", "k4", "lp"]
-LISTS = {"lW": (0, 4), "lD0": (4, 4), "lR0": (8, 8), "lP": (16, 16), "lF": (32, 16), "lD1": (48, 4), "lR1": (52, 8)}
-SMALL = ["pf", "wu", "g0", "nb", "mn", "km", "rn", "pn", "q5", "q6", "jq", "ku", "kb", "gp", "jr"]
-E40, TRP = 0, 80
+COLS = ["jj", "us", "wu", "lD", "k4", "lp"]
+LISTS = {"lD": (0, 4), "lP": (4, 16), "lF": (20, 16)}
+SMALL = ["pf", "g0", "nb", "km", "rn", "pn", "q5", "q6", "jq", "ku", "kb", "gp", "jr"]
+E0, TRP = 0, 80
 GG, FO, HS = 512, 1600, 2624
 
 SCRATCH = {}
@@ -28,8 +29,7 @@ def _b(name, n, d="float32"):
 
 
 for _n, _k, _d in (
-        ("xs", 1024, "bfloat16"), ("us", 512, "bfloat16"), ("vs", 512, "bfloat16"),
-        ("one", 128, "bfloat16"), ("idn", 128, "bfloat16"), ("prm", 128, "bfloat16"),
+        ("xs", 1024, "bfloat16"), ("us", 512, "bfloat16"), ("vs", 512, "bfloat16"), ("one", 128, "bfloat16"), ("idn", 128, "bfloat16"),
         ("ce", 516, "bfloat16"), ("cg", 516, "bfloat16"), ("cs", 1024, "bfloat16"), ("vg", 128, "float32"),
         ("zr", 32 * len(COLS), "float32"), ("zc", 32 * len(COLS), "float32"), ("sm", 8 * len(SMALL), "float32"),
         ("ls", 60, "uint16"), ("rows", 56, "float32"), ("cc", 32, "float32"),
@@ -40,14 +40,14 @@ for _n, _k, _d in (
         ("rq", 74, "float32"), ("pl0", 256, "float32"), ("pl1", 256, "float32"), ("colw", 768, "bfloat16"),
         ("B", 1024, "bfloat16"), ("dz", 256, "bfloat16"), ("ab", 258, "bfloat16"), ("dr", 256, "bfloat16"),
         ("sd", 256, "float32"), ("LG", 16, "uint16"), ("fr", 256, "uint16"), ("fd", 256, "uint16"),
-        ("pb", 2368, "bfloat16"), ("fs", 256, "bfloat16"), ("e1", 128, "bfloat16"), ("pkr", 128, "bfloat16"), ("pm", 1184, "bfloat16"), ("pt", 128, "float32"),
-        ("pt8", 24, "float32"), ("ck", 16, "float32"), ("R", 128, "bfloat16"), ("al", 128, "bfloat16"),
+        ("pb", 128, "bfloat16"), ("p0", 2368, "bfloat16"), ("p1", 1184, "bfloat16"), ("rk", 36, "bfloat16"), ("ek", 16, "float32"),
+        ("fs", 256, "bfloat16"), ("e1", 16, "bfloat16"), ("pm", 1184, "bfloat16"), ("pt", 128, "float32"),
+        ("pt8", 24, "float32"), ("ck", 16, "float32"), ("R", 100, "bfloat16"), ("al", 64, "bfloat16"),
         ("val", 64, "float32"), ("bd", 64, "float32"), ("yi", 64, "float32"), ("Y", 592, "float32"),
+        ("w2r", 64, "uint16"), ("rp1", 74, "uint16"), ("kv", 64, "float32"), ("cv", 65, "float32"), ("d2", 64, "float32"),
         ("pr", 8, "float32"), ("be", 9, "float32"), ("er", 74, "float32"), ("k0", 8, "float32"), ("rep", 74, "float32"), ("c1", 8, "float32"),
-        ("k1", 8, "float32"), ("k16", 480, "uint16"), ("jb", 4, "bfloat16"), ("k2", 8, "float32"), ("pen", 2, "float32"),
-        ("lf", 32 * NR, "uint16"), ("fa", 32 * NR, "uint16"),
-        ("wr", 256, "uint16"), ("od", 256, "float32"), ("oh", 16 * NV, "bfloat16"), ("ol", 16, "bfloat16"),
-        ("js", 256 * NS, "bfloat16"), ("jv", 256 * NV, "bfloat16"), ("acc", 16, "float32"), ("pl", 2048, "uint16"),
+        ("k16", 480, "uint16"), ("jb", 4, "bfloat16"), ("k2", 8, "float32"), ("lf", 32 * NR, "uint16"), ("fa", 32 * NR, "uint16"),
+        ("wr", 256, "uint16"), ("ou", 256, "uint16"), ("js", 256 * NS, "bfloat16"), ("jv", 256 * NV, "bfloat16"), ("acc", 16, "float32"), ("pl", 2048, "uint16"),
         ("win", 256, "float32"), ("dl", 256 * NR, "uint16"), ("la", 16 * NR, "uint16"), ("ow", 256, "float32"), ("opw", 256, "float32"),
         ("D", 3648, "bfloat16"), ("gz", 1024, "bfloat16"), ("Z", 512, "bfloat16"),
         ("X", 1024, "bfloat16"), ("ysb", (8, 32), "float32")):
@@ -181,8 +181,8 @@ def rank_program(g, core, T, topo):
     def TR(o, ok, i, ik):
         return emit("V", lambda: v.transpose(o, i), pt(ik), pt(ok))
 
-    def RED(o, ok, i, ik, op):
-        return emit("V", lambda: v.tensor_reduce(o, i, AxisListType.X, op), pt(ik), pt(ok))
+    def RED(o, ok, i, ik, op, negate=False):
+        return emit("V", lambda: v.tensor_reduce(o, i, AxisListType.X, op, negate=negate), pt(ik), pt(ok))
 
     def SCAN(o, ok, a, b, ik, init, o0, o1):
         return emit("V", lambda: v.tensor_tensor_scan(o, a, b, init, o0, o1), pt(ik), pt(ok))
@@ -200,9 +200,6 @@ def rank_program(g, core, T, topo):
 
     def IOTA(ap, ok, pat, base, cm=0):
         return emit("G", lambda: g.iota(ap, pat, base, cm, allow_small_or_imprecise_dtypes=True), [], pt(ok))
-
-    def AFF(o, ok, i, ik, pat, op, base, cm):
-        return emit("G", lambda: g.affine_select(o, i, pat, op, 0.0, base, cm), pt(ik), pt(ok))
 
     def row(n, a=0, b=32, st=1, p=128):
         k = 32 * COLS.index(n)
@@ -242,10 +239,11 @@ def rank_program(g, core, T, topo):
         for bank, c in ((5 + o, 0), ((7, 4)[o], 128)):
             MM(bank, 128, "qcs", c, "qb%d" % o)
 
-    def rows_V(o, c, ck="crow"):
-        a, ps = slice(128 * o, 128 * o + 128), "ps%d" % (5 + o)
-        TS(T.ab[:, a], "ab%d" % o, T[ps][:, 0:128], [ps, "nb"], C("nb"), GONE, A.not_equal, A.mult)
-        TT(T.dz[:, a], "dz%d" % o, T[ps][:, 0:128], c, [ps, ck], A.add)
+    def others(o, a=0, b=128, more=()):
+        TS(T.ab[:, 128 * o + a:128 * o + b], ["ab%d" % o] + pt(more), T["ps%d" % (5 + o)][:, a:b], ["ps%d" % (5 + o), "nb"], C("nb"), GONE, A.not_equal, A.mult)
+
+    def steps(o, c, ck="crow", a=0, b=128, more=()):
+        TT(T.dz[:, 128 * o + a:128 * o + b], ["dz%d" % o] + pt(more), T["ps%d" % (5 + o)][:, a:b], c, ["ps%d" % (5 + o), ck], A.add)
 
     def above(o, ok, w, wk, a, n):
         SCAN(back(o, a, a + n), ok, w, back(T.ab, a, a + n), pt(wk) + ["ab%d" % h for h in range(a // 128, (a + n) // 128)], 0.0, A.add, A.min)
@@ -255,10 +253,10 @@ def rank_program(g, core, T, topo):
         return [lambda: SCAN(T.sd[:, 128 * o:128 * o + 128], "sd%d" % o, T.ar[:], T[ps][:, 0:128], ["ar", ps], 0.0, A.add, A.max),
                 lambda: TT(T.LG[:, cols], "LG%d" % o, T.sd[:, 128 * o + 15:128 * o + 128:16], T.lc[:, cols], ["sd%d" % o, "lc"], A.add)]
 
-    def own_state(r, a, b):
+    def own_state(r, a, b, k=0):
         for t in range(a, b):
-            MM(t, 256, "qce", 128 * t, "qn%d" % r, ["na%d" % r, "nb%d" % r, "qce%d" % t])
-            ACT(T.D[:, FO + 256 * t:FO + 256 * t + 256], "Fo%d" % t, T["ps%d" % t][:, 0:256], "ps%d" % t, scale=1 / 128)
+            MM(t + k, 256, "qce", 128 * t, "qn%d" % r, ["na%d" % r, "nb%d" % r, "qce%d" % t])
+            ACT(T.D[:, FO + 256 * t:FO + 256 * t + 256], "Fo%d" % t, T["ps%d" % (t + k)][:, 0:256], "ps%d" % (t + k), scale=1 / 128)
 
     def weave(main, fill):
         for m, fs in zip(main, fill):
@@ -266,88 +264,86 @@ def rank_program(g, core, T, topo):
             for f in fs:
                 f()
 
-    def level(o, p0, p1, tk):
-        return [lambda: TT(T.yi[:], "yi", T.zf[:, TRP:TRP + 64].indirect(L("lW")), T.val[:], ["trp0", "trp1", "trp2", "val", "lsW"], A.mult),
-                lambda: SCAN(T.Y[:, 0:64], "Y", T.bd[:], T.yi[:], ["bd", "bd0", "yi"], -FAR, A.add, A.max),
-                lambda: SCAN(o[p0:p1, :], tk, T.er[p0:p1, :], T.Y[p0:p1, 7:592:8], ["Y", "Yc", "cap", "er", "erc"], FAR, A.add, A.min)]
-
     both = (0, 1)
     emit("Y", lambda: g.sync.dma_start(T.xs[:, 0:512], T.x[:, 0:512]), [], ["xs0"], dma=True)
     emit("S", lambda: s.dma_start(T.us[:], T.u[:]), [], ["us"], dma=True)
     emit("Y", lambda: g.sync.dma_start(T.xs[:, 512:1024], T.x[:, 512:1024]), [], ["xs1"], dma=True)
-    emit("Y", lambda: g.sync.dma_start(T.qw[:, 0:512].bitcast(dt.uint8), T.wc[:, 0:2048]), ["xs1", "us"], ["qw"], dma=True)
-    emit("Y", lambda: g.sync.dma_start(T.sqw[:, 0:512], T.ws[:, 0:512]), [], ["sqw"], dma=True)
+    emit("Y", lambda: g.sync.dma_start(T.qw[:, 0:256].bitcast(dt.uint8), T.wc[:, 0:1024]), ["xs1", "us"], ["qw"], dma=True)
 
     FILL(T.one[:], "one", 128.0)
-    FILL(row("w2"), "zr0", 0.0)
+    FILL(row("wu"), "zr0", 0.0)
     FILL(T.B[:], ["zer", "B0", "B1"], 0.0)
     IOTA(row("jj"), "zrA", [[0, 2], [1, 16]], 0)
-    IOTA(row("us"), "zrA", [[0, 2], [int(U), 8], [0, 2]], int(U))
+    IOTA(row("us"), "zrA", [[0, 4], [1, 8]], 1)
     IOTA(C("pf"), "pf", [[0, 1]], 0, 1)
     IOTA(T.vg[:], "vg", [[16, 8], [0, 16]], 0)
-    AFF(T.idn[:], "idn", T.one[:], "one", [[-1, 128]], A.is_equal, 0, 1)
+    emit("G", lambda: g.affine_select(T.idn[:], T.one[:], [[-1, 128]], A.is_equal, 0.0, 0, 1), ["one"], ["idn"])
     IOTA(T.i16[:], "i16", [[0, 10], [1, 16]], 0)
-    IOTA(row("lR"), "zrB", [[32, 2], [0, 16]], 0)
-    IOTA(row("lD"), "zrB", [[0, 2], [32, 2], [0, 8]], 0)
-    IOTA(row("lW"), "zrB", [[0, 2], [1, 2], [2, 8]], 0)
-    IOTA(row("k4"), "zrB", [[2, 2], [0, 8], [1, 2]], 0)
-    IOTA(T.rows[:, 0:8], "rows", [[64, 4], [0, 2]], 0)
-    for k in both:
-        IOTA(T.rows[:, 8 + 8 * k:16 + 8 * k], "rowl", [[16, 2], [1, 2], [0, 2]], 32 * k)
+    IOTA(row("lD"), "zrB", [[0, 2], [16, 2], [0, 8]], 0)
+    IOTA(row("k4"), "zrB", [[1, 4], [0, 8]], 0)
+    IOTA(T.rows[:, 8:24], "rowl", [[8, 8], [0, 2]], 0)
+    IOTA(T.dT[:], "dT", [[0, 16], [8, 8]], 8)
     for i in range(3):
-        FILL(row("w2", i, 32, 16), "zrV", float(8 >> i), "zr0")
+        FILL(row("wu", i, 32, 16), "zrV", float(4 >> i), "zr0")
     FILL(T.cs[:], "cs0", 0.0)
-    turn("jj", "w2", "zcA", ["zrA", "zrV"])
-    SET(T.ce[:, 0:512], "ce0", 512, 0.0)
-    SET(T.ce[:, 512:516], "ce0", 4, 0.0)
-    SET(T.crow[:], "crow0", 256, U)
+    turn("jj", "wu", "zcA", ["zrA", "zrV"])
+    for t, k in ((T.ce, "ce0"), (T.cg, "cg0")):
+        SET(t[:, 0:512], k, 512, 0.0)
+        SET(t[:, 512:516], k, 4, 0.0)
     ACT(T.ce[:, 3:512:4], "ce", T.idn[:], ["idn", "ce0"])
+    for a, b, n in ((0, 112, 16), (16, 0, 32), (48, 16, 32), (80, 32, 32), (112, 48, 16)):
+        ACT(T.cg[:, 4 * a + 3:4 * (a + n):4], "cg", T.idn[:, b:b + n], ["idn", "cg0"])
+    SET(T.crow[:], "crow0", 256, 1.0)
+    ACT(C("nb"), "nb", C("us"), "zcA", AF.Identity, bias=-1.0)
+    SET(T.r15[:], "r150", 64, 0.0)
+    SET(T.wrow[:, 0:256], "wrow0", 256, PL)
     SET(T.crow[:, 31:128:32], "crow", 4, GONE, "crow0")
-    ACT(C("nb"), "nb", C("us"), "zcA", AF.Identity, bias=-U)
-    SET(T.cg[:, 0:512], "cg0", 512, 0.0)
-    SET(T.cg[:, 512:516], "cg0", 4, 0.0)
-    FILL(T.zf[:], ["zf0", "trp1", "trp2"], 0.0)
-    QT("qu", 0, 128, T.us[:], "us")
-    TS(C("wu"), "wu", C("w2"), "zcA", U / 2, None, A.mult)
+    SET(T.Y[:, 71:592:8], ["Yc", "cap"], 66, FAR)
+    SET(T.pm[:, 0:128], "pm", 128, 0.0)
+    SET(T.pm[:, 128:1184:16], ["pfar", "cap0"], 66, FAR)
+    SET(T.rk[:, 5:36], "rk0", 31, 0.0)
+    SET(T.er[:], "er0", 74, 0.0)
+    SET(T.cv[:, 64:65], "cv0", 1, 0.0)
+    SET(T.bd[:, 0:1], "bd0", 1, 0.0)
+    FILL(T.zf[:], ["zf0", "trp1"], 0.0)
+    FILL(T.p0[:, 0:2368:32], ["pz", "pa0", "pa1"], 0.0)
     TS(C("gp"), "gp", C("pf"), ["pf", "zcA"], C("jj"), None, A.subtract)
-    TS(C("q5"), "q5", C("jj"), "zcA", 15.0, HOLD, A.is_lt, A.mult)
-    FILL(T.Y[:, 71:592:8], ["Yc", "cap"], FAR)
-    FILL(T.pb[:, 256:2368:32], ["pfar", "cap0"], FAR)
-    QT("na0", 0, 128, T.xs[:, 0:512], "xs0")
+    QT("qu", 0, 128, T.us[:], "us")
     for k in both:
-        TS(T.cs[:, 4 * k:512:8], "cs", T.vg[:, 0:64], ["vg", "gp", "wu", "cs0"], C("gp"), C("wu"), A.is_equal, A.mult)
-    TS(T.cs[:, 512:1024:4], "cs", T.vg[:], ["vg", "gp", "zcA", "cs0"], C("gp"), C("w2"), A.is_equal, A.mult)
-    QT("nb0", 0, 128, T.xs[:, 512:1024], "xs1")
+        TS(T.cs[:, 4 * k:512:8], "cs", T.vg[:, 0:64], ["vg", "gp", "zcA", "cs0"], C("gp"), C("wu"), A.is_equal, A.mult)
+    TS(T.cs[:, 512:1024:4], "cs", T.vg[:], ["vg", "gp", "zcA", "cs0"], C("gp"), C("wu"), A.is_equal, A.mult)
+    QT("na0", 0, 128, T.xs[:, 0:512], "xs0")
     QT("qcs", 0, 256, T.cs[:], "cs")
+    tile_E = [lambda b=b: QT("qce", 128 * b, 128 * b + 128, T.ce[:, 3 - b:515 - b], "ce", "qce%d" % b) for b in range(4)]
+    tile_G = [lambda b=b: QT("qcg", 128 * b, 128 * b + 128, T.cg[:, 3 - b:515 - b], "cg", "qcg%d" % b) for b in range(4)]
+    for b in range(3):
+        tile_G[b]()
+    QT("nb0", 0, 128, T.xs[:, 512:1024], "xs1")
     for o in both:
         MM(4 * o, 128, "qu", 0, ("na0", "nb0")[o])
-    tiles = [lambda b=b: QT("qce", 128 * b, 128 * b + 128, T.ce[:, 3 - b:515 - b], "ce", "qce%d" % b) for b in range(4)]
-    signs(0, 0)
     TS(T.eq[:], "eq", T.i16[:], ["i16", "zcA"], C("jj"), None, A.is_equal)
-    TS(C("g0"), "g0", C("pf"), "pf", 16.0, 64.0, A.is_lt, A.mult)
+    signs(0, 0)
+    tile_E[0]()
+    TS(C("q5"), "q5", C("jj"), "zcA", 15.0, HOLD, A.is_lt, A.mult)
     spread(0)
     signs(1)
-    turn("lR", "k4", "zcB", "zrB")
-    tiles[0]()
+    turn("lD", "k4", "zcB", "zrB")
+    TS(C("g0"), "g0", C("pf"), "pf", 16.0, 64.0, A.is_lt, A.mult)
+    tile_E[1]()
     spread(1)
     ACT(T.a1[:], "a1", T.eq[:, 15:143], "eq", scale=-0.25)
     ACT(T.a2[:], "a2", T.eq[:, 16:144], "eq", scale=-4 * HOLD)
-    ACT(T.zf[:, E40 + 8:E40 + 9], "e40", C("us"), ["zcA", "zf0"])
-    ACT(T.cc[:, 24:32], "ramp", T.i16[:, 0:8], "i16", scale=2 * GONE)
-    SET(T.er[:], "er0", 74, 0.0)
-    SET(T.bd[:, 0:1], "bd0", 1, 0.0)
-    ACT(T.be[:, 8:9], "be8", C("us"), "zcA", scale=-1.0)
-    ACT(C("pn"), "pn", C("us"), "zcA", AF.Identity, bias=254.0 / FAR, scale=2 / U / FAR)
-    for k in range(4):
-        ACT(T.dT[:, 32 * k:32 * k + 32], "dT", row("us"), "zrA")
+    ACT(T.zf[:, E0 + 8:E0 + 9], "e0", C("us"), ["zcA", "zf0"], AF.Identity, bias=-GONE)
+    SET(T.zf[:, E0 + 9:E0 + 10], "e0", 1, GONE, "zf0")
+    ACT(T.cc[:, 24:32], "ramp", T.i16[:, 0:8], "i16", scale=RISE)
+    ACT(T.be[0:64, 8:9], "be8", C("us", 0, 64), "zcA", scale=-1.0)
+    ACT(T.be[64:128, 8:9], "be8", C("us", 64), "zcA", AF.Identity, bias=UP, scale=-1.0)
+    ACT(C("pn"), "pn", C("us"), "zcA", AF.Identity, bias=255.0 / FAR, scale=1 / FAR)
     SET(T.tr2[:, 64:128], "tr2c", 64, 0.0)
-    SET(T.r15[:], "r150", 64, 0.0)
     SET(T.r15[:, 15:64:16], "r15", 4, HOLD / FAR, "r150")
-    SET(T.wrow[:, 0:256], "wrow", 256, 1.0)
-    AFF(T.prm[:, 0:16], "prm", T.one[:, 0:16], "one", [[-1, 16]], A.is_equal, -112, 1)
-    AFF(T.prm[:, 16:32], "prm", T.one[:, 0:16], "one", [[-1, 16]], A.is_equal, 0, 1)
-    AFF(T.prm[:, 32:128], "prm", T.one[:, 0:96], "one", [[-16, 3], [0, 2], [-1, 16]], A.is_equal, -16, 1)
     send_codes(0, 0, 256, ["na0", "nb0"], 2)
+    emit("Y", lambda: g.sync.dma_start(T.qw[:, 256:512].bitcast(dt.uint8), T.wc[:, 1024:2048]), ["qa0"], ["qw2"], dma=True)
+    emit("Y", lambda: g.sync.dma_start(T.sqw[:, 0:512], T.ws[:, 0:512]), [], ["sqw"], dma=True)
     IOTA(T.pl0[:], "pl00", [[1, 256]], 0)
     IOTA(T.win[:], "win", [[0, 256]], 0)
     IOTA(T.D[:, 0:512], "Dp", [[0, 512]], 0)
@@ -355,82 +351,79 @@ def rank_program(g, core, T, topo):
     IOTA(T.pl1[:], "pl10", [[16, 8], [128, 2], [1, 16]], 0)
     IOTA(T.rows[:, 24:40], "rows2", [[128, 2], [2, 8]], 0)
     IOTA(row("lp"), "zrD", [[0, 2], [1, 2], [16, 8]], 0)
-    tiles[1]()
-    rows_V(0, T.crow[:, 0:128])
+    TS(T.ek[:, 0:5], "ek", T.i16[:, 0:5], ["i16", "zcB"], C("k4"), -16 * GONE, A.is_equal, A.mult)
+    TS(T.ek[:, 8:13], "ek", T.i16[:, 15:20], ["i16", "zcB"], C("k4"), 2 * GONE, A.is_equal, A.mult)
+    others(0, more="ac0")
+    steps(0, T.crow[:, 0:128], more="dc0")
     SCAN(T.ar[:], "ar", T.a1[:], T.a2[:], ["a1", "a2"], 0.0, A.mult, A.add)
-    TS(L("lR0"), "lsB", T.rows[:, 0:8], ["rows", "zcB"], C("lR"), None, A.add)
-    TS(L("lD0"), "lsB", T.i16[:, 0:4], ["i16", "zcB"], 64.0, C("lD"), A.mult, A.add)
+    TT(T.rk[:, 0:5], "rk1", T.ek[:, 0:5], T.ek[:, 8:13], "ek", A.add)
+    TS(L("lD"), "lsB", T.i16[:, 0:4], ["i16", "zcB"], 32.0, C("lD"), A.mult, A.add)
     TS(T.lc[:], "lc", T.rows[:, 8:24], ["rowl", "g0", "q5"], C("g0"), C("q5"), A.add, A.subtract)
-    ACT(C("kb"), "kb", C("k4"), "zcB", scale=2 * GONE)
-    ACT(C("ku"), "ku", C("k4"), ["zcA", "zcB"], AF.Identity, bias=C("us"))
+    ACT(T.rk[:, 4:5], "rk", T.rk[:, 4:5], ["rk0", "rk1"], AF.Identity, bias=-2 * GONE)
+    ACT(C("kb"), "kb", C("k4"), "zcB", scale=RISE)
+    ACT(C("ku"), "ku", C("k4"), ["zcA", "zcB"], AF.Identity, bias=C("us"), scale=0.125)
     for k in both:
-        ACT(T.zf[0:32, TRP + 32 * k:TRP + 32 * k + 32], "trp0", row("k4", p=32), ["zrB", "zf0"], AF.Identity, bias=8 * GONE * k, scale=2 * GONE)
-    for o, a, ok in ((T.zf, 0, "e40"), (T.er, 32, "erc")):
-        SET(o[a:a + 32, 42:43], ok, 1, 8 * GONE, ["zf0", "er0"], a, a + 32)
+        ACT(T.zf[0:32, TRP + 32 * k:TRP + 32 * k + 32], "trp0", row("k4", p=32), ["zrB", "zf0"], AF.Identity, bias=4 * RISE * k, scale=RISE)
+    for o, a, ok in ((T.zf, 0, "e0"), (T.er, 32, "erc")):
+        SET(o[a:a + 32, 42:43], ok, 1, 4 * RISE, ["zf0", "er0"], a, a + 32)
         ACT(o[a:a + 32, 10:11], ok, C("kb", a, a + 32), ["kb", "zf0", "er0"])
-    rows_V(1, T.crow[:, 0:128])
-    RED(T.ab[:, 256:257], "abk", T.ab[:, 0:128], "ab0", A.min)
+    SET(T.wrow[:, 31:256:32], "wrow", 8, 2 * GONE, "wrow0")
+    SET(T.er[64:128, 42:43], "erc", 1, 0.5, "er0", 64)
+    SET(T.tie[:, 0:32], "tie0", 32, C("ku"), "ku")
+    ACT(T.er[64:128, 10:11], "erc", C("ku", 64), ["ku", "er0"])
+    for k, (sc, bi) in enumerate(((0.125 + 32 * PL, 0.0), (0.125 + 16 * PL, 0.0), (0.125 + 16 * PL, 128 * PL))):
+        ACT(T.cc[:, 8 * k:8 * k + 8], "cc", T.i16[:, 0:8], "i16", AF.Identity, bias=bi, scale=sc)
+    ACT(T.tie[:, 32:64], "tie", T.tie[:, 0:32], "tie0", AF.Identity, bias=0.5)
+    ACT(C("jq"), "jq", C("jj"), "zcA", AF.Identity, bias=HOLD)
+    ACT(C("q6"), "q6", C("q5"), "q5", AF.Identity, bias=HOLD, scale=-1.0)
+    ACT(T.mk[:], "mk", T.eq[:], "eq", AF.Identity, bias=1.0, scale=-1.0)
+    SET(T.lf[:, 17:32 * NR:32], ["lf%d" % k for k in range(NR)], NR, 0.0)
+    ACT(C("jr"), "jr", C("jj"), "zcA", AF.Identity, bias=120.0)
+    for y in both:
+        ACT(T.jb[:, 2 * y:2 * y + 1], "jb", C("jj"), "zcA", AF.Identity, bias=16.0 * y)
+    ACT(T.pc[:, 0:16], "pc", T.i16[:, 0:16], ["i16", "jq"], AF.Identity, bias=C("jq"), scale=16.0)
     s0 = symbols(0, slice(0, 8))
-    s0[0]()
-
-    def later():
-        SET(T.er[64:128, 42:43], "erc", 1, 4.0, "er0", 64)
-        SET(T.tie[:, 0:32], "tie0", 32, C("ku"), "ku")
-        ACT(T.er[64:128, 10:11], "erc", C("ku", 64), ["ku", "er0"])
-        for k, (sc, bi) in enumerate(((288.0, -127.5), (272.0, -127.5), (272.0, 0.5))):
-            ACT(T.cc[:, 8 * k:8 * k + 8], "cc", T.i16[:, 0:8], "i16", AF.Identity, bias=bi, scale=sc)
-        ACT(T.tie[:, 32:64], "tie", T.tie[:, 0:32], "tie0", AF.Identity, bias=4.0)
-        ACT(C("jq"), "jq", C("jj"), "zcA", AF.Identity, bias=HOLD)
-        ACT(C("q6"), "q6", C("q5"), "q5", AF.Identity, bias=HOLD, scale=-1.0)
-        ACT(T.mk[:], "mk", T.eq[:], "eq", AF.Identity, bias=1.0, scale=-1.0)
-        SET(T.pen[:], "pen", 2, 127.5)
-        ACT(C("jr"), "jr", C("jj"), "zcA", AF.Identity, bias=120.0)
-        for y in both:
-            ACT(T.jb[:, 2 * y:2 * y + 1], "jb", C("jj"), "zcA", AF.Identity, bias=16.0 * y)
-        ACT(T.pc[:, 0:16], "pc", T.i16[:, 0:16], ["i16", "jq"], AF.Identity, bias=C("jq"), scale=16.0)
+    others(1, more="ac1")
+    steps(1, T.crow[:, 0:128], more="dc1")
 
     for r in range(NR):
         last = r == NR - 1
         p0, n = (128, 128) if r else (0, 256)
         sy = symbols(1, slice(1, 16, 2) if r else slice(8, 16))
-        lR, lD = L("lR%d" % min(r, 1)), L("lD%d" % min(r, 1))
-        pb, pk, st = (T.pb, ["pbc"], 32) if r == 0 else (T.pm, ["pm"], 16)
-        ends = pb[:, 0:8 * st:st]
-        if r:
-            sy[0]()
-        above(T.pb, ["pb1", "pbc"] + ["pb0"] * (r == 0), back(T.dz, p0, p0 + n), ["dz0", "dz1"], p0, n)
-        RED(C("mn"), "mn", T.ab[:, 128:257], ["ab1", "abk"], A.min)
-        for o, ok in ((T.pm[:, 144:145] if r else T.pb[:, 288:289], "cap0"), (T.Y[:, 79:80], "cap")):
-            ACT(o, ok, C("mn"), "mn", AF.Relu, bias=FAR, scale=-FAR / GONE)
+        pa, st = (T.p1, 16) if r else (T.p0, 32)
+        for o in both:
+            a = p0 + o * n // 2
+            SCAN(back(pa, 37 * st * o, 37 * st * o + n // 2), "pa%d" % o, back(T.dz, a, a + n // 2), back(T.ab, a, a + n // 2), ["dc%d" % o, "ac%d" % o, "pz"],
+                 0.0, A.add, A.min)
+            if o == 0 and r == 0:
+                RED(T.ab[:, 256:257], "abk", T.ab[:, 0:128], "ab0", A.min)
+        cap = T.pm[:, 144:145]
+        RED(cap, "cap0", T.ab[:, 128:257], ["ab1", "abk"], A.min, True)
+        ACT(T.Y[:, 79:80], "cap", cap, "cap0", AF.Relu, bias=FAR, scale=FAR / GONE)
+        own_state(r, FE if r else 0, 4 if r else 2)
+        for o in both:
+            SCAN((T.R[:, 28:64], T.R[:, 99:63:-1])[o], "R%d" % o, T.rk[:], pa[:, 37 * st * o:37 * st * o + 36 * st:st], ["rk", "pa%d" % o, "pz", "ks%d" % o],
+                 0.0, A.add, A.max)
+            tops, ends = pa[:, 37 * st * o:37 * st * o + 4 * st:st], T.pm[:, 64 * o:64 * o + 64:16]
+            if r:
+                TT(ends, "pm", tops, T.e1[:, 8 * o:8 * o + 4], ["e1", "pa%d" % o], A.max)
+            else:
+                CP(ends, "pm", tops, "pa%d" % o)
+        sy[0]()
         if r == 0:
-            CP(T.R[:], "R", T.pb[:, 0:256].indirect(lR), ["pbc", "lsB"])
-            own_state(0, 0, 2)
-            later()
-            ACT(T.cg[:, 3:512:4], "cg", T.prm[:], ["prm", "cg0"])
-            sy[0]()
+            s0[0]()
+        TR(T.al[:], "al", T.R[:, 32:96], ["R0", "R1"])
+        SCAN(T.rep[0:32, :], "rep0", T.pm[0:32, 0:1184:16], T.zf[0:32, E0:E0 + 74], ["pm", "cap0", "pfar", "e0"], FAR, A.min, A.add)
+        TT(T.pr[:], "pr", T.pm[:, 0:128:16], T.cc[:, 24:32], ["pm", "ramp"], A.subtract)
+        sy[1]()
+        TT(T.val[:], "val", T.pm[:, 0:128].indirect(L("lD")), T.al[:], ["pm", "al", "lsB"], A.is_ge)
+        TR(T.zf[32:64, TRP:TRP + 64], "trp1", T.rep[0:32, 10:74], "rep0")
+        if r == 0:
             s0[1]()
-        else:
-            TT(T.R[:], "R", T.pb[:, 128:256].indirect(lR), T.pkr[:], ["pbc", "pkr", "lsD"], A.max)
-            TT(ends, "pm", T.pb[:, 128:256:16], T.e1[:, 0:128:16], ["e1", "pbc"], A.max)
-            own_state(r, FE, 4)
-            sy[1]()
-        zero = [lambda: SCAN(T.rep[0:32, :], "rep0", pb[0:32, 0:74 * st:st], T.zf[0:32, E40:E40 + 74], pk + ["cap0", "pfar", "e40"], FAR, A.min, A.add),
-                lambda: TR(T.zf[32:64, TRP:TRP + 64], "trp1", T.rep[0:32, 10:74], "rep0")]
-        if r == 0:
-            zero[0]()
-            TS(L("lW"), "lsW", T.i16[:, 0:4], ["i16", "zcB"], 16.0, C("lW"), A.mult, A.add)
-        TR(T.al[:], "al", T.R[:], "R")
+        TT(T.bd[0:64, 1:64], "bd", T.al[0:64, 1:64], T.al[0:64, 0:63], "al", A.subtract)
+        TT(T.be[0:64, 0:8], "be", T.pr[0:64, :], T.al[0:64, 7:64:8], ["pr", "al"], A.subtract)
         if r:
-            zero[0]()
-        TT(T.pr[:], "pr", ends, T.cc[:, 24:32], pk + ["ramp"], A.subtract)
-        if r == 0:
-            zero[1]()
-            sy[1]()
-        TT(T.val[:], "val", pb[:, 0:n].indirect(lD), T.al[:, 0:128:2], pk + ["al", "lsB", "lsD"], A.is_ge)
-        if r:
-            zero[1]()
-        TT(T.bd[:, 1:64], "bd", T.al[:, 2:128:2], T.al[:, 0:126:2], "al", A.subtract)
-        TT(T.be[:, 0:8], "be", T.pr[:], T.al[:, 14:128:16], ["pr", "al"], A.subtract)
+            ACT(T.kv[:], "kv", T.val[:], "val", scale=UP)
         ACT(T.dr[:], "dr", T.dT[:].indirect(T.LG[:]), ["dT", "LG0", "LG1"])
         lf = 32 * r
         flags = [lambda: TS(T.rp2[:], "rp2", T.r15[:], ["r15", "pn", "cap"], C("pn"), T.Y[:, 79:80], A.add, A.mult),
@@ -438,79 +431,93 @@ def rank_program(g, core, T, topo):
                  lambda: [SET(T.dr[:, 0:256:32], "dr", 8, -DK, "dr"),
                           ACT(T.fr[:], "fr", T.tr2[:].indirect(T.LG[:]), ["tr2", "tr2c", "LG0", "LG1"])]]
         mate = [lambda o=o: SCAN(T.fd[:, 128 * o:128 * o + 128], "fd", T.ar[:], T.fr[:, 128 * o:128 * o + 128], ["ar", "fr"], 0.0, A.add, A.max) for o in both]
-        down = lambda: TT(T.er[:, 1:9], "er", T.be[:, 0:8], T.be[:, 1:9], ["be", "be8", "er0"], A.subtract)
-        ties = lambda: TS(T.rq[0:64, 10:74], "rq1", T.tie[0:64, :], ["tie", "rep0", "rep1"], T.rep[0:64, 9:10], None, A.add)
-        least = [lambda: TT(T.k0[:], "k0", T.Y[:, 7:64:8], T.be[:, 0:8], ["Y", "be"], A.add),
-                 lambda: TS(T.k1[:], "k1", T.k0[:], "k0", 256.0, DROP, A.mult, A.min)]
-        depth = lambda: above(T.fs, ["fs1"] + ["fs0"] * (r == 0), back(T.wrow, 256 - p0 - n + 256 * (r > 0), 256 + 128 * (r > 0)), "wrow", p0, n)
-
+        down = lambda: TT(T.er[32:64, 1:9], "er", T.be[32:64, 0:8], T.be[32:64, 1:9], ["be", "be8", "er0"], A.subtract)
+        second = [lambda: TT(T.cv[64:128, 0:64], "cv", T.kv[64:128, :], T.al[64:128, :], ["kv", "al"], A.subtract),
+                  lambda: TT(T.d2[64:128, :], "d2", T.cv[64:128, 0:64], T.cv[64:128, 1:65], ["cv", "cv0"], A.subtract),
+                  lambda: TT(T.be[64:128, 0:8], "be2", T.pr[64:128, :], T.cv[64:128, 8:65:8], ["pr", "cv", "cv0"], A.add),
+                  lambda: TT(T.er[64:128, 1:9], "er2", T.be[64:128, 0:8], T.be[64:128, 1:9], ["be2", "be8", "er0"], A.subtract)]
+        ties = [lambda a=a, o=o, k=k: TS(T.rq[a:a + 32, 10:74], "rq1", T.tie[a:a + 32, :], ["tie", k], o[a:a + 32, 9:10], None, A.add)
+                for a, o, k in ((0, T.rep, "rep0"), (32, T.rp1, "rep1"))]
+        least = [lambda: TT(T.k0[:], "k0", T.Y[:, 7:64:8], T.be[:, 0:8], ["Y", "Y2", "be", "be2"], A.add),
+                 lambda: TT(T.k2[:], "k2", T.k0[:], T.c1[:], ["k0", "c1"], A.add)]
+        depth = lambda: above(T.fs, ["fs1"] + ["fs0"] * (r == 0), back(T.wrow, 2 * p0, 2 * p0 + n), "wrow", p0, n)
         if r == 0:
-            late = [lambda b=b: QT("qcg", 128 * b, 128 * b + 128, T.cg[:, 3 - b:515 - b], "cg", "qcg%d" % b) for b in range(4)]
-            fill = [[down, flags[0], tiles[2]], [depth, tiles[3]], flags[1:] + [lambda: own_state(0, 2, 4), late[0]], [late[3]],
-                    [late[1], lambda: TT(T.c1[:], "c1", T.fs[:, 0:256:32], T.cc[:, 0:8], ["fs0", "fs1", "cc"], A.add), ties],
-                    [late[2], lambda: TR(T.tf[:, 64:128], "tfc", T.tie[:], "tie")]]
+            fill = [[lambda: TS(T.kv[:], "kv", T.val[:], "val", UP, None, A.mult), down, flags[0]], [second[0], tile_G[3]], flags[1:] + [second[2], second[1]],
+                    [second[3], depth], ties + [lambda: TT(T.c1[:], "c1", T.fs[:, 0:256:32], T.cc[:, 0:8], ["fs0", "fs1", "cc"], A.add)],
+                    [least[0], lambda: TR(T.tf[:, 64:128], "tfc", T.tie[:], "tie"), tile_E[2]], [least[1], tile_E[3]]]
         else:
-            fill = [[down, flags[0]], [depth], flags[1:],
-                    [lambda: TT(T.ck[:], "ck", T.fs[:, 0:256:16], T.cc[:, 8:24], ["fs0", "fs1", "cc"], A.add)],
-                    [lambda: TT(T.c1[:], "c1", T.ck[:, 0:8], T.ck[:, 8:16], "ck", A.min), ties], []]
-        weave(level(T.rep, 32, 64, "rep1") + [lambda: [TR(T.zf[p:p + 32, TRP:TRP + 64], "trp2", T.rep[32:64, 10:74], "rep1") for p in (64, 96)]]
-              + level(T.rq, 64, 128, "rq2") + [lambda: TR(T.tf[:, 0:64], "tf", T.rq[:, 10:74], ["rq1", "rq2"])],
-              fill + [least[0:1], least[1:] + mate])
-        for c, k in (("qcg", 0), ("qce", 4)):
+            fill = [[flags[0], down], [second[0], depth], flags[1:] + [second[2], second[1]],
+                    [second[3], lambda: TT(T.ck[:], "ck", T.fs[:, 0:256:16], T.cc[:, 8:24], ["fs0", "fs1", "cc"], A.add), ties[0]],
+                    [ties[1], lambda: TT(T.c1[:], "c1", T.ck[:, 0:8], T.ck[:, 8:16], "ck", A.min)], [least[0]], [least[1]] + mate]
+        weave([lambda: TT(T.yi[0:64, :], "yi", T.zf[0:64, TRP:TRP + 64], T.val[0:64, :], ["trp0", "trp1", "val"], A.mult),
+               lambda: SCAN(T.Y[0:64, 0:64], "Y", T.bd[0:64, :], T.yi[0:64, :], ["bd", "bd0", "yi"], -FAR, A.add, A.max),
+               lambda: SCAN(T.rp1[32:64, :], "rep1", T.er[32:64, :], T.Y[32:64, 7:592:8], ["Y", "Yc", "cap", "er", "erc"], FAR, A.add, A.min),
+               lambda: [TR(T.w2r[p:p + 32, :], "w2r", T.rp1[32:64, 10:74], "rep1") for p in (64, 96)],
+               lambda: SCAN(T.Y[64:128, 0:64], "Y2", T.w2r[64:128, :], T.d2[64:128, :], ["w2r", "d2"], -FAR, A.max, A.add),
+               lambda: SCAN(T.rq[64:128, :], "rq2", T.er[64:128, :], T.Y[64:128, 7:592:8], ["Y2", "Yc", "cap", "er2", "erc"], FAR, A.add, A.min),
+               lambda: TR(T.tf[:, 0:64], "tf", T.rq[:, 10:74], ["rq1", "rq2"])], fill)
+
+        def unpack(c, k):
             for b in range(4):
                 MM(k + b, 256, c, 128 * b, "qa%d" % r, ["qa%d" % r, "%s%d" % (c, b)])
 
         def copy_G(t):
             ACT(T.D[:, GG + 272 * t:GG + 272 * t + 256], "G%d" % t, T["ps%d" % t][:, 0:256], "ps%d" % t)
 
-        for t in range(GE[r]):
+        unpack("qcg", 0)
+        if r:
+            unpack("qce", 4)
+        for t in range(GE):
             copy_G(t)
-        CP(T.wr[:, 0:128], "wr0", T.tf[:].indirect(T.LG[:, 0:8]), ["tf", "tfc", "LG0", "LG1"])
-        ACT(T.wr[:, 128:256], "wr1", T.tf[:].indirect(T.LG[:, 8:16]), ["tf", "tfc", "LG0", "LG1"])
-        for t in range(GE[r], 4):
+        TS(T.wr[:, 0:128], "wr0", T.tf[:].indirect(T.LG[:, 0:8]), ["tf", "tfc", "LG0", "LG1"], 8.0, None, A.mult)
+        ACT(T.wr[:, 128:256], "wr1", T.tf[:].indirect(T.LG[:, 8:16]), ["tf", "tfc", "LG0", "LG1"], scale=8.0)
+        for t in range(GE, 4):
             copy_G(t)
-        TT(T.k2[:], "k2", T.k1[:], T.c1[:], ["k1", "c1"], A.add)
         if r == 0:
-            TT(T.lf[:, lf:lf + 16], "lf%d" % r, T.fd[:, 15:256:16], T.pc[:, 0:16], ["fd", "pc"], A.max)
+            own_state(0, 2, 3, 2)
+        RED(C("km"), "km", T.k2[:], "k2", A.min)
+        if r == 0:
+            mate[0]()
+            mate[1]()
         else:
             for y in both:
                 TT(T.lf[:, lf + 8 * y:lf + 8 * y + 8], "lf%d" % r, T.fd[:, 15 + 16 * y:256:32], T.pc[:, 16 + y:32:2], ["fd", "pc"], A.max)
-        for o in both:
-            a = slice(128 * o, 128 * o + 128)
-            SCAN(T.k16[:, a], "key%d" % o, T.dr[:, a], T.wr[:, a], ["wr%d" % o, "dr"], 0.0, A.add, A.max)
-        RED(C("km"), "km", T.k2[:], "k2", A.min)
 
-        def own(o, ok, c, a, b):
-            SCAN(back(o, c, c + b - a), ok, back(T.mk, 0, b - a), back(T.k16, a, b), ["mk"] + ["key%d" % h for h in range(a // 128, (b - 1) // 128 + 1)],
+        def keys(k, o, a, b):
+            SCAN(T.k16[:, o + a:o + b], "key%d" % k, T.dr[:, a:b], T.wr[:, a:b], ["wr%d" % (a // 128), "dr"], 0.0, A.add, A.max)
+
+        def own(ok, a, b):
+            SCAN(back(T.ou, a, b), ok, back(T.mk, 0, b - a), back(T.k16, a, b), ["mk"] + ["key%d" % h for h in range(a // 128, (b - 1) // 128 + 1)],
                  0.0, A.mult, A.max)
 
-        def again(a, b):
-            SCAN(T.k16[:, 256 + a:256 + b], "key%d" % (2 + (a > 0)), T.dr[:, a:b], T.wr[:, a:b], ["wr0", "wr1", "dr"], 0.0, A.add, A.max)
-
-        own(T.od, "od0", 0, 0, 16 * NS)
-        again(0, 128)
-        own(T.oh, "oh", 0, 16 * NS, 256)
-        own(T.od, "od1", 16 * NS, 16 * NS, 256)
-        again(128, 224)
-        TS(C("rn"), "rn", C("km"), "km", ROUND256, -ROUND256, A.add, A.add)
-        TT(T.ol[:, 0:NV], "ol", T.od[:, 16 * NS:256:16], T.oh[:, 0:16 * NV:16], ["od0", "od1", "oh"], A.subtract)
-        TS(T.lf[:, lf + 16:lf + 18], "lf%d" % r, T.pen[:], ["pen", "km", "rn"], C("km"), C("rn"), A.add, A.subtract)
+        keys(0, 0, 0, 128)
+        keys(1, 0, 128, 256)
+        keys(2, 256, 0, 128)
+        TS(C("rn"), "rn", C("km"), "km", ROUND, -ROUND, A.add, A.add)
+        own("od0", 0, 16 * NS)
+        own("od1", 16 * NS, 256)
+        keys(3, 256, 128, 224)
+        if r == 0:
+            TT(T.lf[:, lf:lf + 16], "lf%d" % r, T.fd[:, 15:256:16], T.pc[:, 0:16], ["fd", "pc"], A.max)
+        TS(T.lf[:, lf + 16:lf + 17], "lf%d" % r, C("km"), ["km", "rn"], C("rn"), 1 / PL, A.subtract, A.mult)
         send(T.fa[:, lf:lf + 18], T.lf[:, lf:lf + 18], "f", r)
         for b in range(NS):
             a = 32 * (b // 2) + 16 + 16 * (b % 2)
             ACT(T.js[:, 256 * b:256 * b + 240], "acc", T.k16[:, a:a + 240], ["key0", "key1", "od0"] + ["key2"] * (b > 0), AF.Sign,
-                bias=T.od[:, 16 * b:16 * b + 1], scale=-1.0, accum_out=T.acc[:, b:b + 1])
+                bias=T.ou[:, 16 * b:16 * b + 1], scale=-1.0, accum_out=T.acc[:, b:b + 1])
         if r == 0:
-            ACT(T.pl0[:], "pl0", T.pl0[:], ["pl00", "q6"], AF.Identity, bias=C("q6"))
+            ACT(T.pl0[:], "vpl0", T.pl0[:], ["pl00", "q6"], AF.Identity, bias=C("q6"))
+            own_state(0, 3, 4, 2)
+            unpack("qce", 4)
         for b in range(NV):
             a = 32 * ((NS + b) // 2) + 32
-            TS(T.jv[:, 256 * b:256 * b + 224], "jv%d" % b, T.k16[:, a:a + 224], ["key0", "key1", "key2", "key3", "oh", "ol"], T.oh[:, 16 * b:16 * b + 1], T.ol[:, b:b + 1],
-               A.subtract, A.is_lt)
+            TS(T.jv[:, 256 * b:256 * b + 224], "jv%d" % b, T.k16[:, a:a + 224], ["key0", "key1", "key2", "od1"] + ["key3"] * (a > 160),
+               T.ou[:, 16 * (NS + b):16 * (NS + b) + 1], None, A.is_lt)
         for b in range(NV):
             y = (NS + b) % 2
             SCAN(T.pl[:, 1776 + NS + b::-16], "pl", T.jv[:, 256 * b:256 * b + 112], T.jv[:, 256 * b + 112:256 * b + 224], ["jv%d" % b, "jb"], T.jb[:, 2 * y:2 * y + 1],
                  A.add, A.add)
-        TS(T.pl[:, 0:NS], "pl", T.acc[:, 0:NS], ["acc", "jr"], 0.5, C("jr"), A.mult, A.add)
+        TS(T.pl[:, 0:NS], "plS", T.acc[:, 0:NS], ["acc", "jr"], 0.5, C("jr"), A.mult, A.add)
         for t in range(4):
             a = GG + 272 * t
             ACT(T.D[:, a + 256:a + 272], "Gf%d" % t, T.D[:, a:a + 256].indirect(T.fa[:, lf + 16:lf + 17]), ["G%d" % t, "fa%d" % r])
@@ -523,7 +530,12 @@ def rank_program(g, core, T, topo):
             TT(T.D[:, HS + 256 * t:HS + 256 * t + 256], "H%d" % t, T["ps%d" % (4 + t)][:, 0:256], T.gz[:, 256 * t:256 * t + 256], ["ps%d" % (4 + t), "gz%d" % t], A.add)
 
         pl = ("pl0", "pl1")[min(r, 1)]
-        emit("V", lambda: v.tensor_copy(T.win[:].indirect(T.pl[:, 0:16]), T[pl][:]), ["pl", pl, "win"], ["win"])
+        spare = [[lambda: FILL(T.r16[:], "r160", 1.0), lambda: FILL(T.e1[:], "e10", 0.0)],
+                 [lambda: turn("lp", "lp", "zcD", "zrD"), lambda: TS(L("lP"), "lsE", T.rows[:, 24:40], ["rows2", "zcD"], C("lp"), None, A.add)],
+                 [lambda: TS(L("lF"), "lsF", T.rows[:, 40:56], ["rowq", "zcA"], C("jj"), None, A.add), lambda: QT("qv", 0, 128, T.vs[:], "vs")]][r]
+        spare[0]()
+        emit("V", lambda: v.tensor_copy(T.win[:].indirect(T.pl[:, 0:16]), T[pl][:]), ["pl", "plS", "v" + pl], ["win"])
+        spare[1]()
         for h in range(8):
             SCAN(T.dl[:, 256 * r + h:256 * r + 256:8], "ll%d" % r, T.ar[:, 0:32], T.win[:, h:256:8], ["ar", "win"], 0.0, A.add, A.max)
         la, laid, kept = T.la[:, 16 * r:16 * r + 8], T.dl[:, 256 * r + 120:256 * r + 128], T.dl[:, 256 * r + 248:256 * r + 256]
@@ -543,10 +555,6 @@ def rank_program(g, core, T, topo):
         if r == 0:
             emit("Y", lambda: g.sync.dma_start(T.vs[:], T.v[:]), ["la0"], ["vs"], dma=True)
             IOTA(T.colw[:], "colw", [[16, 6], [32, 8], [1, 16]], -64)
-        QT("na%d" % (r + 1), 0, 128, T.X[:, 0:512], ["X0V", "X0S"])
-        MM(4, 128, "qv" if last else "qu", 0, "na%d" % (r + 1))
-        if not last:
-            send_codes(r + 1, 0, 128, ["na%d" % (r + 1)], 2)
         z = "qz%d" % r
         for t in range(4):
             a = HS + 256 * t
@@ -555,13 +563,17 @@ def rank_program(g, core, T, topo):
                 TS(o, "ZV", i, ik, 1 / 256, None, A.mult)
             else:
                 ACT(o, "ZS", i, ik, scale=1 / 256)
+        QT("na%d" % (r + 1), 0, 128, T.X[:, 0:512], ["X0V", "X0S"])
+        MM(4, 128, "qv" if last else "qu", 0, "na%d" % (r + 1))
+        if not last:
+            send_codes(r + 1, 0, 128, ["na%d" % (r + 1)], 2)
+        QT(z, 0, 128, T.Z[:], ["ZV", "ZS"])
         if last:
             CP(T.ysb[:, :, 0:16], "ysb", T.ps4[:, 0:128], "ps4")
         else:
             signs(0)
-        QT(z, 0, 128, T.Z[:], ["ZV", "ZS"])
         for b in range(4):
-            MM(b, 128, "qw", 128 * b, z, None, True, False)
+            MM(b, 128, "qw", 128 * b, z, [z, "qw2"], True, False)
             MM(b, 128, "qce", 128 * b, z, [z, "qce%d" % b], False, True)
         if last:
             for k, li in enumerate((laid, kept)):
@@ -570,58 +582,54 @@ def rank_program(g, core, T, topo):
             emit("Y", lambda: g.sync.dma_start(T.op[:], T.opw[0:128:16, :]), ["opw"], ["op"], dma=True)
         else:
             spread(0)
-            if r == 0:
-                FILL(T.r16[:], "r160", 1.0)
-                FILL(T.wrow[:, 256:384], "wrow1", 1.0)
-                FILL(T.pm[:, 0:128], "pm", 0.0)
-                FILL(T.e1[:], "e1", 0.0)
-                TS(L("lR1"), "lsD", L("lR0"), "lsB", 0.5, None, A.mult)
-                TS(L("lD1"), "lsD", L("lD0"), "lsB", 0.5, None, A.mult)
-                FILL(T.cra[:], "cra0", U)
-                FILL(T.pm[:, 128:1184:16], ["pfar", "cap0"], FAR)
-                FILL(T.r16[:, 0:128:16], "r16", 0.0, "r160")
-                FILL(T.crow[:, 143:256:16], "crow", 2 * GONE, "crow0")
-                FILL(T.wrow[:, 271:384:16], "wrow", 4096.0, "wrow1")
-                FILL(T.cra[:, 15:128:16], "cra", 16 * GONE, "cra0")
-                ACT(T.pc[:, 16:32], "pc", T.rows[:, 40:56], ["rowq", "jq"], AF.Identity, bias=C("jq"))
-                ACT(T.pl1[:], "pl1", T.pl1[:], ["pl10", "q6"], AF.Identity, bias=C("q6"))
-            else:
-                turn("lp", "lp", "zcD", "zrD")
-                QT("qv", 0, 128, T.vs[:], "vs")
-                TS(L("lF"), "lsE", T.rows[:, 40:56], ["rowq", "zcA"], C("jj"), None, A.add)
-                TS(L("lP"), "lsE", T.rows[:, 24:40], ["rows2", "zcD"], C("lp"), None, A.add)
+        if r == 0:
+            FILL(T.wrow[:, 256:384], "wrow1", PL)
+            FILL(T.p1[:, 0:1184:16], "pz", 0.0)
+            FILL(T.cra[:], "cra0", 1.0)
+            FILL(T.r16[:, 0:128:16], "r16", 0.0, "r160")
+            FILL(T.crow[:, 143:256:16], "crow", 2 * GONE, "crow0")
+            FILL(T.wrow[:, 271:384:16], "wrow", 2 * GONE, "wrow1")
+            FILL(T.cra[:, 15:128:16], "cra", 16 * GONE, "cra0")
+            ACT(T.pc[:, 16:32], "pc", T.rows[:, 40:56], ["rowq", "jq"], AF.Identity, bias=C("jq"))
+            ACT(T.pl1[:], "vpl1", T.pl1[:], ["pl10", "q6"], AF.Identity, bias=C("q6"))
         for b in range(4):
             o, i = T.X[:, 512 + b:1024:4], T["ps%d" % b][:, 0:128]
             if b >= HV:
                 TS(o, "X1V", i, "ps%d" % b, 0.0078125, None, A.mult)
             else:
                 ACT(o, "X1S", i, "ps%d" % b, scale=0.0078125)
+        if not last:
+            others(0)
         QT("nb%d" % (r + 1), 0, 128, T.X[:, 512:1024], ["X1V", "X1S"])
         if not last:
             MM(4, 128, "qu", 0, "nb%d" % (r + 1))
             send_codes(r + 1, 128, 256, ["nb%d" % (r + 1)], 4)
             sy = symbols(0, slice(0, 16, 2))
-            rows_V(0, T.crow[:, 128:256])
+            steps(0, T.crow[:, 128:256])
             SCAN(T.pt[:], "pt", T.r16[:], T.ps5[:, 0:128], ["r16", "ps5"], 0.0, A.mult, A.add)
             above(T.pb, "pb0", back(T.dz, 0, 128), "dz0", 0, 128)
-            ACT(T.pt8[:, 0:8], "pt8", T.pt[:, 15:128:16], "pt", AF.Identity, bias=16 * U)
-            ACT(T.pt8[:, 8:16], "pt9", T.pt[:, 15:128:16], "pt", AF.Identity, bias=16 * U - 8 * GONE)
+            sy[0]()
+            above(T.fs, "fs0", back(T.wrow, 256, 384), "wrow", 0, 128)
+            TS(T.pt8[:, 16:24], "pta", T.pb[:, 0:128:16], "pb0", GONE / 2, 8 * GONE + 1, A.is_ge, A.mult)
+            ACT(T.pt8[:, 0:8], "pt8", T.pt[:, 15:128:16], "pt", AF.Identity, bias=16.0)
+            ACT(T.pt8[:, 8:16], "pt9", T.pt[:, 15:128:16], "pt", AF.Identity, bias=16 - 8 * GONE)
             own_state(r + 1, 0, FE)
             signs(1)
-            TS(T.pt8[:, 16:24], "pta", T.pb[:, 0:128:16], "pb0", DROP, 8 * GONE + U, A.is_ge, A.mult)
+            sy[1]()
             spread(1)
-            TT(T.e1[:, 0:128:16], "e1", T.pb[:, 0:128:16], T.pt8[:, 0:8], ["pb0", "pt8"], A.min)
-            sy[0]()
+            for o in both:
+                TT(T.e1[:, 8 * o:8 * o + 4], "e1", T.pb[:, 64 * o:64 * o + 64:16], T.pt8[:, 4 * o:4 * o + 4], ["pb0", "pt8", "e10"], A.min)
             TT(T.cra[:, 0:128:16], "cra", T.pt8[:, 8:16], T.pt8[:, 16:24], ["pt9", "pta"], A.add)
             RED(T.ab[:, 256:257], "abk", T.pt8[:, 16:24], "pta", A.min)
-            ACT(T.pkr[:], "pkr", T.e1[:].indirect(L("lR1")), ["e1", "lsD"])
-            above(T.fs, "fs0", back(T.wrow, 256, 384), "wrow", 0, 128)
-            sy[1]()
-            rows_V(1, T.cra[:], "cra")
+            for o in both:
+                SCAN(T.p1[:, 592 * o + 68:592 * o + 63:-1], "ks%d" % o, T.rk[:, 0:5], T.e1[:, 8 * o:8 * o + 5], ["rk", "e1", "pz"], 0.0, A.add, A.max)
+            for o in both:
+                others(1, 64 * o, 64 * o + 64, "ac%d" % o)
+                steps(1, T.cra[:, 64 * o:64 * o + 64], "cra", 64 * o, 64 * o + 64, "dc%d" % o)
     MM(5, 128, "qv", 0, "nb3")
     (oc, osc), (ic, isc) = K("qp", 0, 256), K("qn3", 0, 256)
-    emit("V", lambda: v.tensor_copy(oc.bitcast(dt.uint32), ic.bitcast(dt.uint32).indirect(L("lF"))), ["na3", "nb3", "lsE"], ["qp"])
-    emit("S", lambda: s.activation(osc, isc.indirect(L("lF")), AF.Copy), ["na3", "nb3", "lsE"], ["sqp"])
+    emit("V", lambda: v.tensor_copy(oc.bitcast(dt.uint32), ic.bitcast(dt.uint32).indirect(L("lF"))), ["na3", "nb3", "lsF"], ["qp"])
+    emit("S", lambda: s.activation(osc, isc.indirect(L("lF")), AF.Copy), ["na3", "nb3", "lsF"], ["sqp"])
     ACT(T.ysb[:, :, 16:32], "ysb1", T.ps5[:, 0:128], "ps5")
     emit("Y", lambda: g.sync.dma_start(T.oc[:, 0:1024], oc.bitcast(dt.uint8)), ["qp"], ["oc"], dma=True)
     emit("S", lambda: s.dma_start(T.y[:], T.ysb[:]), ["ysb", "ysb1"], ["y"], dma=True)

from concourse.mybir import dt, AluOpType as A, AxisListType, ActivationFunctionType as AF

NR = 3
GONE = 2048.0
UP = 2048.0
RISE = 8192.0
FAR = float(1 << 30)
PL = 1 / 4096
ROUND = 1.5 * float(1 << 20)
DK = 16384.0
HOLD = 512.0
HV = 3
XV, ZV = 2, 2
GE = 2
FE = 1
NV = 10
NS = 16 - NV
COLS = ["jj", "us", "wu", "lD", "k4", "lp"]
LISTS = {"lD": (0, 4), "lP": (4, 16), "lF": (20, 16)}
SMALL = ["pf", "g0", "nb", "km", "rn", "pn", "q5", "q6", "jq", "ku", "kb", "gp", "jr"]
E0, TRP = 0, 80
GG, FO, HS = 512, 1600, 2624

SCRATCH = {}


def _b(name, n, d="float32"):
    SCRATCH[name] = ("sbuf", [128] + (list(n) if isinstance(n, tuple) else [n]), d)


for _n, _k, _d in (
        ("xs", 1024, "bfloat16"), ("us", 512, "bfloat16"), ("vs", 512, "bfloat16"), ("one", 128, "bfloat16"), ("idn", 128, "bfloat16"),
        ("ce", 516, "bfloat16"), ("cg", 516, "bfloat16"), ("cs", 1024, "bfloat16"), ("vg", 128, "float32"),
        ("zr", 32 * len(COLS), "float32"), ("zc", 32 * len(COLS), "float32"), ("sm", 8 * len(SMALL), "float32"),
        ("ls", 60, "uint16"), ("rows", 56, "float32"), ("cc", 32, "float32"),
        ("crow", 256, "bfloat16"), ("wrow", 384, "bfloat16"), ("r16", 128, "bfloat16"), ("dT", 128, "bfloat16"),
        ("r15", 64, "float32"), ("zf", 144, "float32"), ("cra", 128, "float32"),
        ("i16", 160, "bfloat16"), ("eq", 160, "bfloat16"), ("a1", 128, "bfloat16"), ("a2", 128, "bfloat16"), ("ar", 128, "bfloat16"), ("mk", 160, "bfloat16"),
        ("lc", 16, "float32"), ("pc", 32, "float32"), ("tie", 64, "float32"), ("tf", 128, "float32"), ("rp2", 64, "float32"), ("tr2", 128, "float32"),
        ("rq", 74, "float32"), ("pl0", 256, "float32"), ("pl1", 256, "float32"), ("colw", 768, "bfloat16"),
        ("B", 1024, "bfloat16"), ("dz", 256, "bfloat16"), ("ab", 258, "bfloat16"), ("dr", 256, "bfloat16"),
        ("sd", 256, "float32"), ("LG", 16, "uint16"), ("fr", 256, "uint16"), ("fd", 256, "uint16"),
        ("pb", 128, "bfloat16"), ("p0", 2368, "bfloat16"), ("p1", 1184, "bfloat16"), ("rk", 36, "bfloat16"), ("ek", 16, "float32"),
        ("fs", 256, "bfloat16"), ("e1", 16, "bfloat16"), ("pm", 1184, "bfloat16"), ("pt", 128, "float32"),
        ("pt8", 24, "float32"), ("ck", 16, "float32"), ("R", 100, "bfloat16"), ("al", 64, "bfloat16"),
        ("val", 64, "float32"), ("bd", 64, "float32"), ("yi", 64, "float32"), ("Y", 592, "float32"),
        ("w2r", 64, "uint16"), ("rp1", 74, "uint16"), ("kv", 64, "float32"), ("cv", 65, "float32"), ("d2", 64, "float32"),
        ("pr", 8, "float32"), ("be", 9, "float32"), ("er", 74, "float32"), ("k0", 8, "float32"), ("rep", 74, "float32"), ("c1", 8, "float32"),
        ("k16", 480, "uint16"), ("jb", 4, "bfloat16"), ("k2", 8, "float32"), ("lf", 32 * NR, "uint16"), ("fa", 32 * NR, "uint16"),
        ("wr", 256, "uint16"), ("ou", 256, "uint16"), ("js", 256 * NS, "bfloat16"), ("jv", 256 * NV, "bfloat16"), ("acc", 16, "float32"), ("pl", 2048, "uint16"),
        ("win", 256, "float32"), ("dl", 256 * NR, "uint16"), ("la", 16 * NR, "uint16"), ("ow", 256, "float32"), ("opw", 256, "float32"),
        ("D", 3648, "bfloat16"), ("gz", 1024, "bfloat16"), ("Z", 512, "bfloat16"),
        ("X", 1024, "bfloat16"), ("ysb", (8, 32), "float32")):
    _b(_n, _k, _d)
for _n, _k in (("qn", 256 * (NR + 1)), ("qa", 256 * NR), ("qp", 256), ("qu", 128), ("qv", 128), ("qw", 512), ("qc", 1280), ("qb", 256),
               ("qz", 128 * NR)):
    _b(_n, _k, "float8_e4m3fn_x4")
    _b("s" + _n, _k, "uint8")
for _k in range(8):
    SCRATCH["ps%d" % _k] = ("psum", [128, 512], "float32")
SEMAPHORES = (["cV", "cS", "cT", "cG", "sent"] + ["arc%d" % k for k in range(NR)] + ["arl%d" % k for k in range(NR)] + ["arf%d" % k for k in range(NR)]
              + ["ld%d" % k for k in range(16)])


def recorder(g, T):
    eng = {"V": g.vector, "S": g.scalar, "T": g.tensor, "G": g, "Y": g.sync}
    count = {"V": 0, "S": 0, "T": 0, "G": 0}
    known = {q: {} for q in eng}
    writer, readers = {}, {}
    nd = [0]

    def need(q, toks):
        todo = {}
        for (sem, val, own, snap) in toks:
            if known[q].get(sem, 0) < val and todo.get(sem, (0, None))[0] < val:
                todo[sem] = (val, snap)
        for sem in list(todo):
            if any(s != sem and todo[s][1].get(sem, 0) >= todo[sem][0] for s in todo):
                continue
            eng[q].wait_ge(T.sem[sem], todo[sem][0])
        for sem, (val, snap) in todo.items():
            for k, v in list(snap.items()) + [(sem, val)]:
                if known[q].get(k, 0) < v:
                    known[q][k] = v

    def toks_of(q, reads, writes):
        t = []
        for r in reads:
            if r in writer:
                t.append(writer[r])
            if r[:2] == "ps":
                t += [x for x in readers.get(r, []) if x[2] != q]
        for w in writes:
            t += readers.get(w, [])
            if w in writer and (writer[w][2] != q or readers.get(w)):
                t.append(writer[w])
        return t

    def note(tok, reads, writes):
        for w in writes:
            writer[w] = tok
            readers[w] = []
        for r in reads:
            if r not in writes:
                readers.setdefault(r, []).append(tok)

    def emit(q, make, reads, writes, dma=False):
        need(q, toks_of(q, reads, writes))
        ins = make()
        if dma:
            sem = "ld%d" % nd[0]
            nd[0] += 1
            ins.then_inc(T.sem[sem], 16)
            tok = (sem, 16, "D" + sem, dict(known[q]))
        else:
            sem = "c" + q
            count[q] += 1
            ins.then_inc(T.sem[sem], 1)
            tok = (sem, count[q], q, dict(known[q]))
        note(tok, reads, writes)
        return tok

    def landed(sem, val, writes):
        note((sem, val, "R" + sem, {}), [], writes)

    return emit, need, toks_of, landed, count, nd


def rank_program(g, core, T, topo):
    rank = T.rank_of(core)
    if rank is None:
        return
    nxt = T.cores[(rank + 1) % len(T.cores)]
    prv = T.cores[(rank - 1) % len(T.cores)]
    emit, need, toks_of, landed, count, nd = recorder(g, T)
    v, s = g.vector, g.scalar

    def C(n, a=0, b=128):
        if n in COLS:
            k = 32 * COLS.index(n)
            return T.zc[a:b, k:k + 1]
        k = 8 * SMALL.index(n)
        return T.sm[a:b, k:k + 1]

    def L(n):
        a, k = LISTS[n]
        return T.ls[:, a:a + k]

    place = {"qcs": ("qc", 0), "qce": ("qc", 256), "qcg": ("qc", 768), "qb0": ("qb", 0), "qb1": ("qb", 128)}
    for k in range(NR + 1):
        place["qn%d" % k] = ("qn", 256 * k)
        place["na%d" % k] = ("qn", 256 * k)
        place["nb%d" % k] = ("qn", 256 * k + 128)
        place["qz%d" % k] = ("qz", 128 * k)
        place["qa%d" % k] = ("qa", 256 * k)

    def K(n, a, b):
        q, o = place.get(n, (n, 0))
        return T[q][:, o + a:o + b], T["s" + q][:, o + a:o + b]

    def pt(n):
        return list(n) if isinstance(n, (list, tuple)) else [n]

    def TS(o, ok, i, ik, s1, s2, o0, o1=None):
        if o1 is None:
            return emit("V", lambda: v.tensor_scalar(o, i, s1, None, o0), pt(ik), pt(ok))
        return emit("V", lambda: v.tensor_scalar(o, i, s1, s2, o0, o1), pt(ik), pt(ok))

    def TT(o, ok, a, b, ik, op):
        return emit("V", lambda: v.tensor_tensor(o, a, b, op), pt(ik), pt(ok))

    def CP(o, ok, i, ik):
        return emit("V", lambda: v.tensor_copy(o, i), pt(ik), pt(ok))

    def ACT(o, ok, i, ik, f=AF.Copy, **kw):
        return emit("S", lambda: s.activation(o, i, f, **kw), pt(ik), pt(ok))

    def SET(o, ok, n, c, ik=(), a=0, b=128):
        return ACT(o, ok, T.B[a:b, 1:2 * n:2], ["zer"] + pt(ik), AF.Identity, bias=c)

    def TR(o, ok, i, ik):
        return emit("V", lambda: v.transpose(o, i), pt(ik), pt(ok))

    def RED(o, ok, i, ik, op, negate=False):
        return emit("V", lambda: v.tensor_reduce(o, i, AxisListType.X, op, negate=negate), pt(ik), pt(ok))

    def SCAN(o, ok, a, b, ik, init, o0, o1):
        return emit("V", lambda: v.tensor_tensor_scan(o, a, b, init, o0, o1), pt(ik), pt(ok))

    def FILL(ap, ok, c, ik=()):
        return emit("V", lambda: v.memset(ap, c), pt(ik), pt(ok))

    def QT(q, a, b, i, ik, ok=None):
        return emit("V", lambda: v.quantize_mx(*K(q, a, b), i), pt(ik), pt(ok or q))

    def MM(bank, n, w, wa, m, mk=None, start=True, stop=True):
        (wt, ws), (mt, ms) = K(w, wa, wa + 128), K(m, 0, n)
        o = T["ps%d" % bank][:, 0:n]
        return emit("T", lambda: g.tensor.matmul_mx(o, wt, ws, mt, ms, start, stop), [w, "s" + w] + pt(mk or m), ["ps%d" % bank])

    def IOTA(ap, ok, pat, base, cm=0):
        return emit("G", lambda: g.iota(ap, pat, base, cm, allow_small_or_imprecise_dtypes=True), [], pt(ok))

    def row(n, a=0, b=32, st=1, p=128):
        k = 32 * COLS.index(n)
        return T.zr[0:p, k + a:k + b:st]

    def turn(a, b, ok, ik):
        i, j = 32 * COLS.index(a), 32 * COLS.index(b) + 32
        TR(T.zc[:, i:j], ok, T.zr[:, i:j], ik)

    rid, pid, _ = topo.addr(nxt)
    mask = topo.mask(core, nxt)
    n_out, n_in = len(topo.engines(core, nxt)), len(topo.engines(prv, core))
    calls = [0]

    def send_codes(r, a, b, keys, got):
        need("G", toks_of("G", keys, []))
        (zc, zs), (ac, asc) = K("qn%d" % r, a, b), K("qa%d" % r, a, b)
        g.remote_dma(ac.bitcast(dt.uint8), zc.bitcast(dt.uint8), T.sem["arc%d" % r], T.sem.sent, pid, rid, mask)
        g.remote_dma(asc, zs, T.sem["arc%d" % r], T.sem.sent, pid, rid, mask)
        calls[0] += 2
        landed("arc%d" % r, got * n_in, ["qa%d" % r])

    def send(dst, src, k, r):
        need("G", toks_of("G", ["l%s%d" % (k, r)], []))
        g.remote_dma(dst, src, T.sem["ar%s%d" % (k, r)], T.sem.sent, pid, rid, mask)
        calls[0] += 1
        landed("ar%s%d" % (k, r), n_in, ["%sa%d" % (k, r)])

    def back(t, a, b):
        return t[:, b - 1::-1] if a == 0 else t[:, b - 1:a - 1:-1]

    def signs(o, bank=4):
        TS(T.B[:, 512 * o:512 * o + 512:4], "B%d" % o, T["ps%d" % bank][:, 0:128], "ps%d" % bank, 0.0, None, A.is_gt)

    def spread(o):
        QT("qb%d" % o, 0, 128, T.B[:, 512 * o:512 * o + 512], "B%d" % o)
        for bank, c in ((5 + o, 0), ((7, 4)[o], 128)):
            MM(bank, 128, "qcs", c, "qb%d" % o)

    def others(o, a=0, b=128, more=()):
        TS(T.ab[:, 128 * o + a:128 * o + b], ["ab%d" % o] + pt(more), T["ps%d" % (5 + o)][:, a:b], ["ps%d" % (5 + o), "nb"], C("nb"), GONE, A.not_equal, A.mult)

    def steps(o, c, ck="crow", a=0, b=128, more=()):
        TT(T.dz[:, 128 * o + a:128 * o + b], ["dz%d" % o] + pt(more), T["ps%d" % (5 + o)][:, a:b], c, ["ps%d" % (5 + o), ck], A.add)

    def above(o, ok, w, wk, a, n):
        SCAN(back(o, a, a + n), ok, w, back(T.ab, a, a + n), pt(wk) + ["ab%d" % h for h in range(a // 128, (a + n) // 128)], 0.0, A.add, A.min)

    def symbols(o, cols):
        ps = "ps%d" % (7, 4)[o]
        return [lambda: SCAN(T.sd[:, 128 * o:128 * o + 128], "sd%d" % o, T.ar[:], T[ps][:, 0:128], ["ar", ps], 0.0, A.add, A.max),
                lambda: TT(T.LG[:, cols], "LG%d" % o, T.sd[:, 128 * o + 15:128 * o + 128:16], T.lc[:, cols], ["sd%d" % o, "lc"], A.add)]

    def own_state(r, a, b, k=0):
        for t in range(a, b):
            MM(t + k, 256, "qce", 128 * t, "qn%d" % r, ["na%d" % r, "nb%d" % r, "qce%d" % t])
            ACT(T.D[:, FO + 256 * t:FO + 256 * t + 256], "Fo%d" % t, T["ps%d" % (t + k)][:, 0:256], "ps%d" % (t + k), scale=1 / 128)

    def weave(main, fill):
        for m, fs in zip(main, fill):
            m()
            for f in fs:
                f()

    both = (0, 1)
    emit("Y", lambda: g.sync.dma_start(T.xs[:, 0:512], T.x[:, 0:512]), [], ["xs0"], dma=True)
    emit("S", lambda: s.dma_start(T.us[:], T.u[:]), [], ["us"], dma=True)
    emit("Y", lambda: g.sync.dma_start(T.xs[:, 512:1024], T.x[:, 512:1024]), [], ["xs1"], dma=True)
    emit("Y", lambda: g.sync.dma_start(T.qw[:, 0:256].bitcast(dt.uint8), T.wc[:, 0:1024]), ["xs1", "us"], ["qw"], dma=True)

    FILL(T.one[:], "one", 128.0)
    FILL(row("wu"), "zr0", 0.0)
    FILL(T.B[:], ["zer", "B0", "B1"], 0.0)
    IOTA(row("jj"), "zrA", [[0, 2], [1, 16]], 0)
    IOTA(row("us"), "zrA", [[0, 4], [1, 8]], 1)
    IOTA(C("pf"), "pf", [[0, 1]], 0, 1)
    IOTA(T.vg[:], "vg", [[16, 8], [0, 16]], 0)
    emit("G", lambda: g.affine_select(T.idn[:], T.one[:], [[-1, 128]], A.is_equal, 0.0, 0, 1), ["one"], ["idn"])
    IOTA(T.i16[:], "i16", [[0, 10], [1, 16]], 0)
    IOTA(row("lD"), "zrB", [[0, 2], [16, 2], [0, 8]], 0)
    IOTA(row("k4"), "zrB", [[1, 4], [0, 8]], 0)
    IOTA(T.rows[:, 8:24], "rowl", [[8, 8], [0, 2]], 0)
    IOTA(T.dT[:], "dT", [[0, 16], [8, 8]], 8)
    for i in range(3):
        FILL(row("wu", i, 32, 16), "zrV", float(4 >> i), "zr0")
    FILL(T.cs[:], "cs0", 0.0)
    turn("jj", "wu", "zcA", ["zrA", "zrV"])
    for t, k in ((T.ce, "ce0"), (T.cg, "cg0")):
        SET(t[:, 0:512], k, 512, 0.0)
        SET(t[:, 512:516], k, 4, 0.0)
    ACT(T.ce[:, 3:512:4], "ce", T.idn[:], ["idn", "ce0"])
    for a, b, n in ((0, 112, 16), (16, 0, 32), (48, 16, 32), (80, 32, 32), (112, 48, 16)):
        ACT(T.cg[:, 4 * a + 3:4 * (a + n):4], "cg", T.idn[:, b:b + n], ["idn", "cg0"])
    SET(T.crow[:], "crow0", 256, 1.0)
    ACT(C("nb"), "nb", C("us"), "zcA", AF.Identity, bias=-1.0)
    SET(T.r15[:], "r150", 64, 0.0)
    SET(T.wrow[:, 0:256], "wrow0", 256, PL)
    SET(T.crow[:, 31:128:32], "crow", 4, GONE, "crow0")
    SET(T.Y[:, 71:592:8], ["Yc", "cap"], 66, FAR)
    SET(T.pm[:, 0:128], "pm", 128, 0.0)
    SET(T.pm[:, 128:1184:16], ["pfar", "cap0"], 66, FAR)
    SET(T.rk[:, 5:36], "rk0", 31, 0.0)
    SET(T.er[:], "er0", 74, 0.0)
    SET(T.cv[:, 64:65], "cv0", 1, 0.0)
    SET(T.bd[:, 0:1], "bd0", 1, 0.0)
    FILL(T.zf[:], ["zf0", "trp1"], 0.0)
    FILL(T.p0[:, 0:2368:32], ["pz", "pa0", "pa1"], 0.0)
    TS(C("gp"), "gp", C("pf"), ["pf", "zcA"], C("jj"), None, A.subtract)
    QT("qu", 0, 128, T.us[:], "us")
    for k in both:
        TS(T.cs[:, 4 * k:512:8], "cs", T.vg[:, 0:64], ["vg", "gp", "zcA", "cs0"], C("gp"), C("wu"), A.is_equal, A.mult)
    TS(T.cs[:, 512:1024:4], "cs", T.vg[:], ["vg", "gp", "zcA", "cs0"], C("gp"), C("wu"), A.is_equal, A.mult)
    QT("na0", 0, 128, T.xs[:, 0:512], "xs0")
    QT("qcs", 0, 256, T.cs[:], "cs")
    tile_E = [lambda b=b: QT("qce", 128 * b, 128 * b + 128, T.ce[:, 3 - b:515 - b], "ce", "qce%d" % b) for b in range(4)]
    tile_G = [lambda b=b: QT("qcg", 128 * b, 128 * b + 128, T.cg[:, 3 - b:515 - b], "cg", "qcg%d" % b) for b in range(4)]
    for b in range(3):
        tile_G[b]()
    QT("nb0", 0, 128, T.xs[:, 512:1024], "xs1")
    for o in both:
        MM(4 * o, 128, "qu", 0, ("na0", "nb0")[o])
    TS(T.eq[:], "eq", T.i16[:], ["i16", "zcA"], C("jj"), None, A.is_equal)
    signs(0, 0)
    tile_E[0]()
    TS(C("q5"), "q5", C("jj"), "zcA", 15.0, HOLD, A.is_lt, A.mult)
    spread(0)
    signs(1)
    turn("lD", "k4", "zcB", "zrB")
    TS(C("g0"), "g0", C("pf"), "pf", 16.0, 64.0, A.is_lt, A.mult)
    tile_E[1]()
    spread(1)
    ACT(T.a1[:], "a1", T.eq[:, 15:143], "eq", scale=-0.25)
    ACT(T.a2[:], "a2", T.eq[:, 16:144], "eq", scale=-4 * HOLD)
    ACT(T.zf[:, E0 + 8:E0 + 9], "e0", C("us"), ["zcA", "zf0"], AF.Identity, bias=-GONE)
    SET(T.zf[:, E0 + 9:E0 + 10], "e0", 1, GONE, "zf0")
    ACT(T.cc[:, 24:32], "ramp", T.i16[:, 0:8], "i16", scale=RISE)
    ACT(T.be[0:64, 8:9], "be8", C("us", 0, 64), "zcA", scale=-1.0)
    ACT(T.be[64:128, 8:9], "be8", C("us", 64), "zcA", AF.Identity, bias=UP, scale=-1.0)
    ACT(C("pn"), "pn", C("us"), "zcA", AF.Identity, bias=255.0 / FAR, scale=1 / FAR)
    SET(T.tr2[:, 64:128], "tr2c", 64, 0.0)
    SET(T.r15[:, 15:64:16], "r15", 4, HOLD / FAR, "r150")
    send_codes(0, 0, 256, ["na0", "nb0"], 2)
    emit("Y", lambda: g.sync.dma_start(T.qw[:, 256:512].bitcast(dt.uint8), T.wc[:, 1024:2048]), ["qa0"], ["qw2"], dma=True)
    emit("Y", lambda: g.sync.dma_start(T.sqw[:, 0:512], T.ws[:, 0:512]), [], ["sqw"], dma=True)
    IOTA(T.pl0[:], "pl00", [[1, 256]], 0)
    IOTA(T.win[:], "win", [[0, 256]], 0)
    IOTA(T.D[:, 0:512], "Dp", [[0, 512]], 0)
    IOTA(T.rows[:, 40:56], "rowq", [[16, 8], [128, 2]], 0)
    IOTA(T.pl1[:], "pl10", [[16, 8], [128, 2], [1, 16]], 0)
    IOTA(T.rows[:, 24:40], "rows2", [[128, 2], [2, 8]], 0)
    IOTA(row("lp"), "zrD", [[0, 2], [1, 2], [16, 8]], 0)
    TS(T.ek[:, 0:5], "ek", T.i16[:, 0:5], ["i16", "zcB"], C("k4"), -16 * GONE, A.is_equal, A.mult)
    TS(T.ek[:, 8:13], "ek", T.i16[:, 15:20], ["i16", "zcB"], C("k4"), 2 * GONE, A.is_equal, A.mult)
    others(0, more="ac0")
    steps(0, T.crow[:, 0:128], more="dc0")
    SCAN(T.ar[:], "ar", T.a1[:], T.a2[:], ["a1", "a2"], 0.0, A.mult, A.add)
    TT(T.rk[:, 0:5], "rk1", T.ek[:, 0:5], T.ek[:, 8:13], "ek", A.add)
    TS(L("lD"), "lsB", T.i16[:, 0:4], ["i16", "zcB"], 32.0, C("lD"), A.mult, A.add)
    TS(T.lc[:], "lc", T.rows[:, 8:24], ["rowl", "g0", "q5"], C("g0"), C("q5"), A.add, A.subtract)
    ACT(T.rk[:, 4:5], "rk", T.rk[:, 4:5], ["rk0", "rk1"], AF.Identity, bias=-2 * GONE)
    ACT(C("kb"), "kb", C("k4"), "zcB", scale=RISE)
    ACT(C("ku"), "ku", C("k4"), ["zcA", "zcB"], AF.Identity, bias=C("us"), scale=0.125)
    for k in both:
        ACT(T.zf[0:32, TRP + 32 * k:TRP + 32 * k + 32], "trp0", row("k4", p=32), ["zrB", "zf0"], AF.Identity, bias=4 * RISE * k, scale=RISE)
    for o, a, ok in ((T.zf, 0, "e0"), (T.er, 32, "erc")):
        SET(o[a:a + 32, 42:43], ok, 1, 4 * RISE, ["zf0", "er0"], a, a + 32)
        ACT(o[a:a + 32, 10:11], ok, C("kb", a, a + 32), ["kb", "zf0", "er0"])
    SET(T.wrow[:, 31:256:32], "wrow", 8, 2 * GONE, "wrow0")
    SET(T.er[64:128, 42:43], "erc", 1, 0.5, "er0", 64)
    SET(T.tie[:, 0:32], "tie0", 32, C("ku"), "ku")
    ACT(T.er[64:128, 10:11], "erc", C("ku", 64), ["ku", "er0"])
    for k, (sc, bi) in enumerate(((0.125 + 32 * PL, 0.0), (0.125 + 16 * PL, 0.0), (0.125 + 16 * PL, 128 * PL))):
        ACT(T.cc[:, 8 * k:8 * k + 8], "cc", T.i16[:, 0:8], "i16", AF.Identity, bias=bi, scale=sc)
    ACT(T.tie[:, 32:64], "tie", T.tie[:, 0:32], "tie0", AF.Identity, bias=0.5)
    ACT(C("jq"), "jq", C("jj"), "zcA", AF.Identity, bias=HOLD)
    ACT(C("q6"), "q6", C("q5"), "q5", AF.Identity, bias=HOLD, scale=-1.0)
    ACT(T.mk[:], "mk", T.eq[:], "eq", AF.Identity, bias=1.0, scale=-1.0)
    SET(T.lf[:, 17:32 * NR:32], ["lf%d" % k for k in range(NR)], NR, 0.0)
    ACT(C("jr"), "jr", C("jj"), "zcA", AF.Identity, bias=120.0)
    for y in both:
        ACT(T.jb[:, 2 * y:2 * y + 1], "jb", C("jj"), "zcA", AF.Identity, bias=16.0 * y)
    ACT(T.pc[:, 0:16], "pc", T.i16[:, 0:16], ["i16", "jq"], AF.Identity, bias=C("jq"), scale=16.0)
    s0 = symbols(0, slice(0, 8))
    others(1, more="ac1")
    steps(1, T.crow[:, 0:128], more="dc1")

    for r in range(NR):
        last = r == NR - 1
        p0, n = (128, 128) if r else (0, 256)
        sy = symbols(1, slice(1, 16, 2) if r else slice(8, 16))
        pa, st = (T.p1, 16) if r else (T.p0, 32)
        for o in both:
            a = p0 + o * n // 2
            SCAN(back(pa, 37 * st * o, 37 * st * o + n // 2), "pa%d" % o, back(T.dz, a, a + n // 2), back(T.ab, a, a + n // 2), ["dc%d" % o, "ac%d" % o, "pz"],
                 0.0, A.add, A.min)
            if o == 0 and r == 0:
                RED(T.ab[:, 256:257], "abk", T.ab[:, 0:128], "ab0", A.min)
        cap = T.pm[:, 144:145]
        RED(cap, "cap0", T.ab[:, 128:257], ["ab1", "abk"], A.min, True)
        ACT(T.Y[:, 79:80], "cap", cap, "cap0", AF.Relu, bias=FAR, scale=FAR / GONE)
        own_state(r, FE if r else 0, 4 if r else 2)
        for o in both:
            SCAN((T.R[:, 28:64], T.R[:, 99:63:-1])[o], "R%d" % o, T.rk[:], pa[:, 37 * st * o:37 * st * o + 36 * st:st], ["rk", "pa%d" % o, "pz", "ks%d" % o],
                 0.0, A.add, A.max)
            tops, ends = pa[:, 37 * st * o:37 * st * o + 4 * st:st], T.pm[:, 64 * o:64 * o + 64:16]
            if r:
                TT(ends, "pm", tops, T.e1[:, 8 * o:8 * o + 4], ["e1", "pa%d" % o], A.max)
            else:
                CP(ends, "pm", tops, "pa%d" % o)
        sy[0]()
        if r == 0:
            s0[0]()
        TR(T.al[:], "al", T.R[:, 32:96], ["R0", "R1"])
        SCAN(T.rep[0:32, :], "rep0", T.pm[0:32, 0:1184:16], T.zf[0:32, E0:E0 + 74], ["pm", "cap0", "pfar", "e0"], FAR, A.min, A.add)
        TT(T.pr[:], "pr", T.pm[:, 0:128:16], T.cc[:, 24:32], ["pm", "ramp"], A.subtract)
        sy[1]()
        TT(T.val[:], "val", T.pm[:, 0:128].indirect(L("lD")), T.al[:], ["pm", "al", "lsB"], A.is_ge)
        TR(T.zf[32:64, TRP:TRP + 64], "trp1", T.rep[0:32, 10:74], "rep0")
        if r == 0:
            s0[1]()
        TT(T.bd[0:64, 1:64], "bd", T.al[0:64, 1:64], T.al[0:64, 0:63], "al", A.subtract)
        TT(T.be[0:64, 0:8], "be", T.pr[0:64, :], T.al[0:64, 7:64:8], ["pr", "al"], A.subtract)
        if r:
            ACT(T.kv[:], "kv", T.val[:], "val", scale=UP)
        ACT(T.dr[:], "dr", T.dT[:].indirect(T.LG[:]), ["dT", "LG0", "LG1"])
        lf = 32 * r
        flags = [lambda: TS(T.rp2[:], "rp2", T.r15[:], ["r15", "pn", "cap"], C("pn"), T.Y[:, 79:80], A.add, A.mult),
                 lambda: TR(T.tr2[:, 0:64], "tr2", T.rp2[:], "rp2"),
                 lambda: [SET(T.dr[:, 0:256:32], "dr", 8, -DK, "dr"),
                          ACT(T.fr[:], "fr", T.tr2[:].indirect(T.LG[:]), ["tr2", "tr2c", "LG0", "LG1"])]]
        mate = [lambda o=o: SCAN(T.fd[:, 128 * o:128 * o + 128], "fd", T.ar[:], T.fr[:, 128 * o:128 * o + 128], ["ar", "fr"], 0.0, A.add, A.max) for o in both]
        down = lambda: TT(T.er[32:64, 1:9], "er", T.be[32:64, 0:8], T.be[32:64, 1:9], ["be", "be8", "er0"], A.subtract)
        second = [lambda: TT(T.cv[64:128, 0:64], "cv", T.kv[64:128, :], T.al[64:128, :], ["kv", "al"], A.subtract),
                  lambda: TT(T.d2[64:128, :], "d2", T.cv[64:128, 0:64], T.cv[64:128, 1:65], ["cv", "cv0"], A.subtract),
                  lambda: TT(T.be[64:128, 0:8], "be2", T.pr[64:128, :], T.cv[64:128, 8:65:8], ["pr", "cv", "cv0"], A.add),
                  lambda: TT(T.er[64:128, 1:9], "er2", T.be[64:128, 0:8], T.be[64:128, 1:9], ["be2", "be8", "er0"], A.subtract)]
        ties = [lambda a=a, o=o, k=k: TS(T.rq[a:a + 32, 10:74], "rq1", T.tie[a:a + 32, :], ["tie", k], o[a:a + 32, 9:10], None, A.add)
                for a, o, k in ((0, T.rep, "rep0"), (32, T.rp1, "rep1"))]
        least = [lambda: TT(T.k0[:], "k0", T.Y[:, 7:64:8], T.be[:, 0:8], ["Y", "Y2", "be", "be2"], A.add),
                 lambda: TT(T.k2[:], "k2", T.k0[:], T.c1[:], ["k0", "c1"], A.add)]
        depth = lambda: above(T.fs, ["fs1"] + ["fs0"] * (r == 0), back(T.wrow, 2 * p0, 2 * p0 + n), "wrow", p0, n)
        if r == 0:
            fill = [[lambda: TS(T.kv[:], "kv", T.val[:], "val", UP, None, A.mult), down, flags[0]], [second[0], tile_G[3]], flags[1:] + [second[2], second[1]],
                    [second[3], depth], ties + [lambda: TT(T.c1[:], "c1", T.fs[:, 0:256:32], T.cc[:, 0:8], ["fs0", "fs1", "cc"], A.add)],
                    [least[0], lambda: TR(T.tf[:, 64:128], "tfc", T.tie[:], "tie"), tile_E[2]], [least[1], tile_E[3]]]
        else:
            fill = [[flags[0], down], [second[0], depth], flags[1:] + [second[2], second[1]],
                    [second[3], lambda: TT(T.ck[:], "ck", T.fs[:, 0:256:16], T.cc[:, 8:24], ["fs0", "fs1", "cc"], A.add), ties[0]],
                    [ties[1], lambda: TT(T.c1[:], "c1", T.ck[:, 0:8], T.ck[:, 8:16], "ck", A.min)], [least[0]], [least[1]] + mate]
        weave([lambda: TT(T.yi[0:64, :], "yi", T.zf[0:64, TRP:TRP + 64], T.val[0:64, :], ["trp0", "trp1", "val"], A.mult),
               lambda: SCAN(T.Y[0:64, 0:64], "Y", T.bd[0:64, :], T.yi[0:64, :], ["bd", "bd0", "yi"], -FAR, A.add, A.max),
               lambda: SCAN(T.rp1[32:64, :], "rep1", T.er[32:64, :], T.Y[32:64, 7:592:8], ["Y", "Yc", "cap", "er", "erc"], FAR, A.add, A.min),
               lambda: [TR(T.w2r[p:p + 32, :], "w2r", T.rp1[32:64, 10:74], "rep1") for p in (64, 96)],
               lambda: SCAN(T.Y[64:128, 0:64], "Y2", T.w2r[64:128, :], T.d2[64:128, :], ["w2r", "d2"], -FAR, A.max, A.add),
               lambda: SCAN(T.rq[64:128, :], "rq2", T.er[64:128, :], T.Y[64:128, 7:592:8], ["Y2", "Yc", "cap", "er2", "erc"], FAR, A.add, A.min),
               lambda: TR(T.tf[:, 0:64], "tf", T.rq[:, 10:74], ["rq1", "rq2"])], fill)

        def unpack(c, k):
            for b in range(4):
                MM(k + b, 256, c, 128 * b, "qa%d" % r, ["qa%d" % r, "%s%d" % (c, b)])

        def copy_G(t):
            ACT(T.D[:, GG + 272 * t:GG + 272 * t + 256], "G%d" % t, T["ps%d" % t][:, 0:256], "ps%d" % t)

        unpack("qcg", 0)
        if r:
            unpack("qce", 4)
        for t in range(GE):
            copy_G(t)
        TS(T.wr[:, 0:128], "wr0", T.tf[:].indirect(T.LG[:, 0:8]), ["tf", "tfc", "LG0", "LG1"], 8.0, None, A.mult)
        ACT(T.wr[:, 128:256], "wr1", T.tf[:].indirect(T.LG[:, 8:16]), ["tf", "tfc", "LG0", "LG1"], scale=8.0)
        for t in range(GE, 4):
            copy_G(t)
        if r == 0:
            own_state(0, 2, 3, 2)
        RED(C("km"), "km", T.k2[:], "k2", A.min)
        if r == 0:
            mate[0]()
            mate[1]()
        else:
            for y in both:
                TT(T.lf[:, lf + 8 * y:lf + 8 * y + 8], "lf%d" % r, T.fd[:, 15 + 16 * y:256:32], T.pc[:, 16 + y:32:2], ["fd", "pc"], A.max)

        def keys(k, o, a, b):
            SCAN(T.k16[:, o + a:o + b], "key%d" % k, T.dr[:, a:b], T.wr[:, a:b], ["wr%d" % (a // 128), "dr"], 0.0, A.add, A.max)

        def own(ok, a, b):
            SCAN(back(T.ou, a, b), ok, back(T.mk, 0, b - a), back(T.k16, a, b), ["mk"] + ["key%d" % h for h in range(a // 128, (b - 1) // 128 + 1)],
                 0.0, A.mult, A.max)

        keys(0, 0, 0, 128)
        keys(1, 0, 128, 256)
        keys(2, 256, 0, 128)
        TS(C("rn"), "rn", C("km"), "km", ROUND, -ROUND, A.add, A.add)
        own("od0", 0, 16 * NS)
        own("od1", 16 * NS, 256)
        keys(3, 256, 128, 224)
        if r == 0:
            TT(T.lf[:, lf:lf + 16], "lf%d" % r, T.fd[:, 15:256:16], T.pc[:, 0:16], ["fd", "pc"], A.max)
        TS(T.lf[:, lf + 16:lf + 17], "lf%d" % r, C("km"), ["km", "rn"], C("rn"), 1 / PL, A.subtract, A.mult)
        send(T.fa[:, lf:lf + 18], T.lf[:, lf:lf + 18], "f", r)
        for b in range(NS):
            a = 32 * (b // 2) + 16 + 16 * (b % 2)
            ACT(T.js[:, 256 * b:256 * b + 240], "acc", T.k16[:, a:a + 240], ["key0", "key1", "od0"] + ["key2"] * (b > 0), AF.Sign,
                bias=T.ou[:, 16 * b:16 * b + 1], scale=-1.0, accum_out=T.acc[:, b:b + 1])
        if r == 0:
            ACT(T.pl0[:], "vpl0", T.pl0[:], ["pl00", "q6"], AF.Identity, bias=C("q6"))
            own_state(0, 3, 4, 2)
            unpack("qce", 4)
        for b in range(NV):
            a = 32 * ((NS + b) // 2) + 32
            TS(T.jv[:, 256 * b:256 * b + 224], "jv%d" % b, T.k16[:, a:a + 224], ["key0", "key1", "key2", "od1"] + ["key3"] * (a > 160),
               T.ou[:, 16 * (NS + b):16 * (NS + b) + 1], None, A.is_lt)
        for b in range(NV):
            y = (NS + b) % 2
            SCAN(T.pl[:, 1776 + NS + b::-16], "pl", T.jv[:, 256 * b:256 * b + 112], T.jv[:, 256 * b + 112:256 * b + 224], ["jv%d" % b, "jb"], T.jb[:, 2 * y:2 * y + 1],
                 A.add, A.add)
        TS(T.pl[:, 0:NS], "plS", T.acc[:, 0:NS], ["acc", "jr"], 0.5, C("jr"), A.mult, A.add)
        for t in range(4):
            a = GG + 272 * t
            ACT(T.D[:, a + 256:a + 272], "Gf%d" % t, T.D[:, a:a + 256].indirect(T.fa[:, lf + 16:lf + 17]), ["G%d" % t, "fa%d" % r])
        for t in range(4):
            a = GG + 272 * t
            ACT(T.gz[:, 256 * t:256 * t + 256], "gz%d" % t, T.D[:, a - 512:a + 272].indirect(T.fa[:, lf:lf + 16]),
                ["Dp", "fa%d" % r] + [k + str(j) for k in ("G", "Gf") for j in range(t + 1)])

        def pairs(t):
            TT(T.D[:, HS + 256 * t:HS + 256 * t + 256], "H%d" % t, T["ps%d" % (4 + t)][:, 0:256], T.gz[:, 256 * t:256 * t + 256], ["ps%d" % (4 + t), "gz%d" % t], A.add)

        pl = ("pl0", "pl1")[min(r, 1)]
        spare = [[lambda: FILL(T.r16[:], "r160", 1.0), lambda: FILL(T.e1[:], "e10", 0.0)],
                 [lambda: turn("lp", "lp", "zcD", "zrD"), lambda: TS(L("lP"), "lsE", T.rows[:, 24:40], ["rows2", "zcD"], C("lp"), None, A.add)],
                 [lambda: TS(L("lF"), "lsF", T.rows[:, 40:56], ["rowq", "zcA"], C("jj"), None, A.add), lambda: QT("qv", 0, 128, T.vs[:], "vs")]][r]
        spare[0]()
        emit("V", lambda: v.tensor_copy(T.win[:].indirect(T.pl[:, 0:16]), T[pl][:]), ["pl", "plS", "v" + pl], ["win"])
        spare[1]()
        for h in range(8):
            SCAN(T.dl[:, 256 * r + h:256 * r + 256:8], "ll%d" % r, T.ar[:, 0:32], T.win[:, h:256:8], ["ar", "win"], 0.0, A.add, A.max)
        la, laid, kept = T.la[:, 16 * r:16 * r + 8], T.dl[:, 256 * r + 120:256 * r + 128], T.dl[:, 256 * r + 248:256 * r + 256]
        send(la, laid, "l", r)
        before = ["G%d" % t for t in range(4)] + ["Gf%d" % t for t in range(4)] + ["Fo%d" % t for t in range(4)]

        def stay(t):
            a = FO + 256 * t
            (CP if t < XV else ACT)(T.X[:, t:512:4], "X0" + "VS"[t >= XV], T.D[:, a - 512:a + 256].indirect(kept), before + ["ll%d" % r])

        pairs(0)
        pairs(1)
        for t in range(4):
            stay(t)
        pairs(2)
        pairs(3)
        if r == 0:
            emit("Y", lambda: g.sync.dma_start(T.vs[:], T.v[:]), ["la0"], ["vs"], dma=True)
            IOTA(T.colw[:], "colw", [[16, 6], [32, 8], [1, 16]], -64)
        z = "qz%d" % r
        for t in range(4):
            a = HS + 256 * t
            o, i, ik = T.Z[:, t:512:4], T.D[:, a - 512:a + 256].indirect(la), ["Fo2", "Fo3"] + ["H%d" % k for k in range(t + 1)] + ["la%d" % r]
            if t < ZV:
                TS(o, "ZV", i, ik, 1 / 256, None, A.mult)
            else:
                ACT(o, "ZS", i, ik, scale=1 / 256)
        QT("na%d" % (r + 1), 0, 128, T.X[:, 0:512], ["X0V", "X0S"])
        MM(4, 128, "qv" if last else "qu", 0, "na%d" % (r + 1))
        if not last:
            send_codes(r + 1, 0, 128, ["na%d" % (r + 1)], 2)
        QT(z, 0, 128, T.Z[:], ["ZV", "ZS"])
        if last:
            CP(T.ysb[:, :, 0:16], "ysb", T.ps4[:, 0:128], "ps4")
        else:
            signs(0)
        for b in range(4):
            MM(b, 128, "qw", 128 * b, z, [z, "qw2"], True, False)
            MM(b, 128, "qce", 128 * b, z, [z, "qce%d" % b], False, True)
        if last:
            for k, li in enumerate((laid, kept)):
                ACT(T.ow[:, 128 * k:128 * k + 128], "ow", T.colw[:].indirect(li), ["colw", "ll%d" % r])
            ACT(T.opw[:], "opw", T.ow[:].indirect(L("lP")), ["ow", "lsE"])
            emit("Y", lambda: g.sync.dma_start(T.op[:], T.opw[0:128:16, :]), ["opw"], ["op"], dma=True)
        else:
            spread(0)
        if r == 0:
            FILL(T.wrow[:, 256:384], "wrow1", PL)
            FILL(T.p1[:, 0:1184:16], "pz", 0.0)
            FILL(T.cra[:], "cra0", 1.0)
            FILL(T.r16[:, 0:128:16], "r16", 0.0, "r160")
            FILL(T.crow[:, 143:256:16], "crow", 2 * GONE, "crow0")
            FILL(T.wrow[:, 271:384:16], "wrow", 2 * GONE, "wrow1")
            FILL(T.cra[:, 15:128:16], "cra", 16 * GONE, "cra0")
            ACT(T.pc[:, 16:32], "pc", T.rows[:, 40:56], ["rowq", "jq"], AF.Identity, bias=C("jq"))
            ACT(T.pl1[:], "vpl1", T.pl1[:], ["pl10", "q6"], AF.Identity, bias=C("q6"))
        for b in range(4):
            o, i = T.X[:, 512 + b:1024:4], T["ps%d" % b][:, 0:128]
            if b >= HV:
                TS(o, "X1V", i, "ps%d" % b, 0.0078125, None, A.mult)
            else:
                ACT(o, "X1S", i, "ps%d" % b, scale=0.0078125)
        if not last:
            others(0)
        QT("nb%d" % (r + 1), 0, 128, T.X[:, 512:1024], ["X1V", "X1S"])
        if not last:
            MM(4, 128, "qu", 0, "nb%d" % (r + 1))
            send_codes(r + 1, 128, 256, ["nb%d" % (r + 1)], 4)
            sy = symbols(0, slice(0, 16, 2))
            steps(0, T.crow[:, 128:256])
            SCAN(T.pt[:], "pt", T.r16[:], T.ps5[:, 0:128], ["r16", "ps5"], 0.0, A.mult, A.add)
            above(T.pb, "pb0", back(T.dz, 0, 128), "dz0", 0, 128)
            sy[0]()
            above(T.fs, "fs0", back(T.wrow, 256, 384), "wrow", 0, 128)
            TS(T.pt8[:, 16:24], "pta", T.pb[:, 0:128:16], "pb0", GONE / 2, 8 * GONE + 1, A.is_ge, A.mult)
            ACT(T.pt8[:, 0:8], "pt8", T.pt[:, 15:128:16], "pt", AF.Identity, bias=16.0)
            ACT(T.pt8[:, 8:16], "pt9", T.pt[:, 15:128:16], "pt", AF.Identity, bias=16 - 8 * GONE)
            own_state(r + 1, 0, FE)
            signs(1)
            sy[1]()
            spread(1)
            for o in both:
                TT(T.e1[:, 8 * o:8 * o + 4], "e1", T.pb[:, 64 * o:64 * o + 64:16], T.pt8[:, 4 * o:4 * o + 4], ["pb0", "pt8", "e10"], A.min)
            TT(T.cra[:, 0:128:16], "cra", T.pt8[:, 8:16], T.pt8[:, 16:24], ["pt9", "pta"], A.add)
            RED(T.ab[:, 256:257], "abk", T.pt8[:, 16:24], "pta", A.min)
            for o in both:
                SCAN(T.p1[:, 592 * o + 68:592 * o + 63:-1], "ks%d" % o, T.rk[:, 0:5], T.e1[:, 8 * o:8 * o + 5], ["rk", "e1", "pz"], 0.0, A.add, A.max)
            for o in both:
                others(1, 64 * o, 64 * o + 64, "ac%d" % o)
                steps(1, T.cra[:, 64 * o:64 * o + 64], "cra", 64 * o, 64 * o + 64, "dc%d" % o)
    MM(5, 128, "qv", 0, "nb3")
    (oc, osc), (ic, isc) = K("qp", 0, 256), K("qn3", 0, 256)
    emit("V", lambda: v.tensor_copy(oc.bitcast(dt.uint32), ic.bitcast(dt.uint32).indirect(L("lF"))), ["na3", "nb3", "lsF"], ["qp"])
    emit("S", lambda: s.activation(osc, isc.indirect(L("lF")), AF.Copy), ["na3", "nb3", "lsF"], ["sqp"])
    ACT(T.ysb[:, :, 16:32], "ysb1", T.ps5[:, 0:128], "ps5")
    emit("Y", lambda: g.sync.dma_start(T.oc[:, 0:1024], oc.bitcast(dt.uint8)), ["qp"], ["oc"], dma=True)
    emit("S", lambda: s.dma_start(T.y[:], T.ysb[:]), ["ysb", "ysb1"], ["y"], dma=True)
    for k in range(4):
        emit("Y" if k < 3 else "S", lambda: (g.sync if k < 3 else s).dma_start(T.osc[4 * k:4 * k + 4, 0:256], T.sqp[32 * k:32 * k + 4, 0:256]),
             ["sqp"], ["osc%d" % k], dma=True)
    for k in range(nd[0]):
        g.wait_ge(T.sem["ld%d" % k], 16)
    g.wait_ge(T.sem.sent, calls[0] * n_out)
    for k in "VSTG":
        g.wait_ge(T.sem["c" + k], count[k])
